import numpy as np, ml_dtypes
CORES = [35,38,43,46]
N = 4
BF = ml_dtypes.bfloat16
W, L, S, J, TB, D = 4096, 256, 16, 16, 3, 3
NE = (TB + 1) // 2 * L
def cands(u, k):
    return ((u * u >> 5)[..., None] + (2 * np.arange(J) + 1) * u[..., None] + k) & (W - 1)
def pairs(rng, n, pen):
    s = np.arange(W) % S
    kv = rng.random(W) + pen * ((s < TB) & (s % 2 == 0)); ky = rng.random(W) + pen * ((s < TB) & (s % 2 == 1))
    row = np.full(W, -1, np.int64); row[rng.permutation(np.argsort(kv)[:n])] = np.argsort(ky)[:n]
    return row
def filled(rng, lo, hi):
    return np.stack([np.stack([pairs(rng, int(W * (lo + (hi - lo) * rng.random())), 0.6) for g in range(8)]) for r in range(N)])
def pack(x, a, w):
    b = np.full((N, 8, W), -1, np.int64)
    for r in range(N):
        for g in range(8):
            v = np.flatnonzero(a[r, g] >= 0); b[(r + 1) % N, g, a[r, g, v]] = v
    return {"x": np.ascontiguousarray(x).reshape(N, 128, W).astype(np.float32).astype(BF), "pa": a.astype(np.int32), "pb": b.astype(np.int32), "wt": np.ascontiguousarray(w).reshape(N, 128, 1).astype(np.int32)}
def some(rng, m):
    us = np.flatnonzero(m)
    return int(us[int(rng.integers(0, us.size))]) if us.size else 0
def hashed(z, w, u):
    z = np.array(z); z[:2] = 0; rho = (u - int(np.sum(w * z))) & (W - 1); z[0] = rho & 255; z[1] = rho >> 8
    return z
def firststep(x, a, w, r):
    q = (r + 1) % N; v = S * np.arange(L); z = x[r][:, :, v]; u = np.sum(w[q][:, :, None] * z, axis=1) & (W - 1); c = cands(u, 0)
    col = np.take_along_axis(x[q], c.reshape(8, 1, L * J), 2).reshape(8, 16, L, J); key = np.sum(np.abs(col - z[..., None]), axis=1) * W + c
    y = np.take_along_axis(c, np.argmin(key, axis=2)[..., None], 2)[..., 0]; taken = np.zeros((8, W), bool)
    for g in range(8): taken[g, a[r, g][a[r, g] >= 0]] = True
    return y, (a[r][:, v] < 0) & ~np.take_along_axis(taken, y, 1), taken
def setup_inputs(rng):
    return pack(rng.integers(0, 256, (N, 8, 16, W)), filled(rng, 0.4, 0.85), rng.integers(1, 4096, (N, 8, 16)))
def setup_inputs_spread(rng):
    x = np.minimum(np.exp2(8 * rng.random((N, 8, 1, W))) * rng.random((N, 8, 16, W)) * 1.25, 255).astype(np.int64) * (rng.random((N, 8, 1, W)) > 0.0625)
    w = np.minimum(np.maximum(np.exp2(12 * rng.random((N, 8, 16))).astype(np.int64), 1), 4095)
    return pack(x, filled(rng, 0.05, 0.95), w)
def setup_inputs_ties(rng):
    recs = rng.integers(0, 256, (1, 8, 16, 12)); recs[..., 0] = 0; recs[..., 1] = 0; recs[:, :, 0, 1] = 1
    pick = rng.integers(0, 12, (N, 8, W)); w = rng.integers(1, 4096, (N, 8, 16)); w[:, :, 0] = 2048
    x = np.take_along_axis(np.ascontiguousarray(np.broadcast_to(recs, (N, 8, 16, 12))), pick[:, :, None, :], 3)
    return pack(x, filled(rng, 0.3, 0.9), w)
def setup_inputs_corners(rng):
    x = rng.integers(0, 256, (N, 8, 16, W)); col = rng.random((N, 8, 1, W)); x = np.where(col < 0.06, 0, np.where(col > 0.94, 255, x))
    w = rng.integers(1, 4096, (N, 8, 16)); k = rng.integers(0, 4, (N, 8, 1)); w = np.where(k == 0, 1, np.where(k == 1, 4095, w))
    off = int(rng.integers(0, 8)); a = np.full((N, 8, W), -1, np.int64); s = np.arange(W)
    for r in range(N):
        for g in range(8):
            m = (r + g + off) % 8
            if m == 1: a[r, g] = rng.permutation(W)
            elif m == 2: a[r, g] = pairs(rng, W - NE, 2.0)
            elif m == 3: a[r, g, np.delete(s, W - S)] = rng.permutation(W - 1)
            elif m == 4 or m == 5:
                v = np.flatnonzero(pairs(rng, W // 2 if m == 4 else 3 * W // 4, 0.6) >= 0); a[r, g, v] = v if m == 4 else W - 1 - v
            elif m == 6:
                a[r, g] = pairs(rng, 3 * W // 4, 2.0); rec = rng.integers(0, 256, (16, 1))
                for t in range(0, TB, 2): x[r, g][:, t::S] = rec
    tab = cands(np.arange(W), 0); starter = (s % S < TB) & (s % S % 2 == 0)
    for r in range(N):
        g = (7 - r - off) % 8; q = (r + 1) % N; w[q, g, 0] = 1; w[q, g, 1] = 256
        lanes = np.concatenate([np.arange(0, 32, 2 - r % 2), np.arange(32, 96)]); pl = np.where(lanes < 32, 97 + lanes, 128 + lanes)
        held = a[r - 1, g]; held = held[held >= 0]; held = held[held % S >= TB]; h = rng.permutation(held)[:lanes.size]
        row = np.full(W, -1, np.int64); row[h] = pl[:h.size]; fv = ~starter; fv[h] = False; fy = np.ones(W, bool); fy[96:129] = False; fy[160:224] = False
        row[rng.permutation(np.flatnonzero(fv))[:W // 2]] = rng.permutation(np.flatnonzero(fy))[:W // 2]; a[r, g] = row
        for e in range(h.size):
            k = int(lanes[e]); P = int(pl[e]); z = hashed(rng.integers(0, 256, 16), w[q, g], some(rng, np.any(tab == P, axis=1)))
            if k < 32: there = z; back = np.zeros(16, np.int64)
            else:
                kk = (k - 32) >> 1 if r % 2 == 1 else 2 * ((k - 32) >> 2)
                hit = ((tab + 97 + kk) & (W - 1)) == P; there = hashed(z, w[q, g], some(rng, np.any(hit, axis=1) & ~np.all(hit, axis=1))); back = there
            x[r, g][:, S * k] = z; x[q, g][:, P] = there; x[r, g][:, int(h[e])] = back
    for r in range(0, N, 2):
        g = (7 - r - off) % 8; y, go, taken = firststep(x, a, w, r); n = 0
        for b in range(8): n = n + int(np.unique(y[b][go[b]]).size)
        if n % 2 == 1:
            cnt = np.bincount(y[g][go[g]], minlength=W); one = np.flatnonzero(go[g] & (cnt[y[g]] == 1) & (np.arange(L) >= 96))
            fr = ~taken[g]; fr[y[g]] = False; fr[96:129] = False; fr[160:224] = False; fr = np.flatnonzero(fr)
            if one.size and fr.size: a[r, g, S * int(one[int(rng.integers(0, one.size))])] = int(fr[int(rng.integers(0, fr.size))])
    return pack(x, a, w)
def setup_inputs_ends(rng):
    kind = (7 - np.arange(8)[None, :] + N - 1 - np.arange(N)[:, None]) % 4
    w = np.where(rng.random((N, 8, 16)) < 0.5, 1, 4095); w[kind == 0] = 4095; w[kind == 3] = 1
    x = 255 * (rng.random((N, 8, 16, W)) < rng.choice(np.array([0.0, 0.25, 0.5, 0.75, 1.0]), (N, 8, 1, W))).astype(np.int64)
    pick = rng.random((N, 8, L)) < 0.25; pick[:, :, L - 1] = True; x[:, :, :, ::S] = np.where(pick[:, :, None, :], 255, x[:, :, :, ::S])
    tab = cands(np.arange(W), 0); top = np.max(tab, axis=1); pool = np.flatnonzero(top == np.max(top))
    a = np.full((N, 8, W), -1, np.int64); n = 3 * W // 8
    for r in range(N):
        for g in range(8):
            if kind[r, g] == 1:
                need = int(pool[int(rng.integers(0, pool.size))]) * 3839; i = int(rng.integers(0, 16)); o = (i + 1) % 16; w[r, g, i] = 0
                if (need - int(np.sum(w[r, g]))) & (W - 1) == 0: w[r, g, o] = 4096 - w[r, g, o]
                w[r, g, i] = (need - int(np.sum(w[r, g]))) & (W - 1)
            c = cands(np.array([255 * int(np.sum(w[r, g])) & (W - 1)]), 0)[0]; c = c[c % S != 0]
            if c.size:
                x[r, g][:, c] = 0
                if kind[r, g] == 2: x[r, g][:, int(np.max(c))] = 255
            v = rng.permutation(W); v = v[(v != 0) & (v != W - 1) & (v != W - S)][:n]; y = rng.permutation(W); y = y[(y != 0) & (y != W - 1)][:n]
            a[r, g, v] = y
            if g % 2 == 0: a[r, g, 0] = W - 1; a[r, g, W - 1] = 0
    return pack(x, a, w)
def setup_inputs_paths(rng):
    x = rng.integers(0, 256, (N, 8, 16, W)); w = rng.integers(1, 4096, (N, 8, 16)); w[:, :, 0] = 1; w[:, :, 1] = 256
    tab = cands(np.arange(W), 0); s = np.arange(W); gs = rng.permutation(8); lanes = np.argsort(rng.random((N, 8, L)), axis=-1); cnt = np.zeros((N, 8), np.int64)
    use = np.zeros((N, 8, W), bool); use[:, :, s % S < TB] = True; use[:, :, 1850:1920] = True; use[:, :, 3770:3840] = True
    for o in range(0, W, 1024): use[:, :, o + 96:o + 256] = True
    fv = [[[] for g in range(8)] for r in range(N)]; fy = [[[] for g in range(8)] for r in range(N)]; link = [[[] for g in range(8)] for r in range(N)]
    k0 = np.zeros(N, np.int64); k1 = np.zeros(N, np.int64)
    def start(r, g):
        v = S * int(lanes[r, g, cnt[r, g]]); cnt[r, g] += 1; fv[r][g].append(v)
        return v
    def spot(r, g):
        c = np.flatnonzero(~use[r, g]); p = int(c[int(rng.integers(0, c.size))]); use[r, g, p] = True
        return p
    def reach(r, g, k, v=None, u=0):
        z = rng.integers(0, 256, 16)
        for e in range(40):
            z = rng.integers(0, 256, 16)
            if v is not None: z = hashed(z, v, u)
            c = cands(np.array([int(np.sum(w[r, g] * z)) & (W - 1)]), k)[0]; c = c[~use[r, g, c]]
            if c.size:
                p = int(c[int(rng.integers(0, c.size))]); use[r, g, p] = True
                return z, p
        return z, -1
    def visit(r, g, P, rec, b):
        q = (r + 1) % N; m = np.any(tab == P, axis=1)
        if not np.any(m): return None
        z = hashed(rng.integers(0, 256, 16), w[q, g], some(rng, m)); v = start(r, g)
        if b < 0: b = spot(r, g)
        x[r, g][:, v] = z; x[q, g][:, P] = z; x[r, g][:, b] = rec; link[r][g].append((b, P))
        return z
    for r in range(N):
        q = (r + 1) % N; g = int(gs[0])
        for i in range(L):
            z, p = reach(q, g, 0)
            if p >= 0: x[r, g][:, S * i] = z; x[q, g][:, p] = z; fv[r][g].append(S * i); fy[r][g].append(p); k0[q] += 1
        g = int(gs[1]); xq = x[q, g]
        z = hashed(rng.integers(200, 256, 16), w[q, g], 4095); x[r, g][:, start(r, g)] = z; c = cands(np.array([4095]), 0)[0]
        j = 2 * int(rng.integers(1, J // 2)); xq[:, c] = 0; xq[5, c[j]] = 8; xq[5, c[j - 1]] = 8; fy[r][g].append(int(c[j])); fy[r][g].append(int(c[j - 1]))
        z = hashed(rng.integers(200, 256, 16), w[q, g], 2047); x[r, g][:, start(r, g)] = z; c = cands(np.array([2047]), 0)[0]
        xq[:, c] = 0; xq[6, c] = (int(np.sum(z)) - 4) & 15; xq[5, c[0]] = 1; fy[r][g].append(int(c[0])); k0[q] += 2
    ka = [int(k) & 31 for k in k0]
    for r in range(N):
        q = (r + 1) % N; g = int(gs[2])
        if q % 2 == 1:
            w[q, g, 2] = 0; need = (1024 + 2048 * int(rng.integers(0, 2))) * 3839
            if (need - int(np.sum(w[q, g]))) & (W - 1) == 0: w[q, g, 3] += 1 if w[q, g, 3] < 4095 else -1
            w[q, g, 2] = (need - int(np.sum(w[q, g]))) & (W - 1)
            if visit(r, g, 1024 + 97 + ka[q], np.full(16, 255, np.int64), -1) is not None:
                x[q, g][:, 3072 + 97 + ka[q]] = 0; fy[r][g].append(3072 + 97 + ka[q]); k1[q] += 1
        g = int(gs[4])
        if r % 2 == 1:
            for o in (0, 2048):
                rb, b = reach(r, g, 97 + ka[r], w[q, g], o); z, p = reach(r, g, 0)
                if b >= 0 and p >= 0 and visit(r, g, o + 97 + ka[q], rb, b) is not None:
                    fy[r][g].append(o + 194); v = start(r - 1, g); e = spot(r - 1, g)
                    x[r - 1, g][:, v] = z; x[r, g][:, p] = z; x[r - 1, g][:, e] = rb; link[r - 1][g].append((e, p)); fy[r - 1][g].append(b); k1[r] += 1
    kb = [int(k) & 31 for k in k1]
    for r in range(N):
        q = (r + 1) % N; g = int(gs[3])
        for o in (0, 2048):
            if visit(r, g, o + 97 + ka[q], hashed(rng.integers(0, 256, 16), w[q, g], o), -1) is not None: fy[r][g].append(o + 194 + kb[q])
        g = int(gs[5]); z1, p = reach(q, g, 97 + ka[q])
        if p >= 0:
            z = visit(r, g, 1024 + 194 + kb[q], z1, -1)
            if z is not None:
                z = hashed(z, w[q, g], 1024); b = spot(r, g); x[q, g][:, p] = z1; x[r, g][:, b] = z; link[r][g].append((b, p))
                x[q, g][:, 3072 + 194 + kb[q]] = np.where(z < 128, 255, 0); fy[r][g].append(3072 + 194 + kb[q])
    a = np.full((N, 8, W), -1, np.int64)
    for r in range(N):
        for g in range(8):
            mv = np.ones(W, bool); my = np.ones(W, bool); mv[np.array(fv[r][g], np.int64)] = False; my[np.array(fy[r][g], np.int64)] = False
            for v, y in link[r][g]: mv[v] = False; my[y] = False; a[r, g, v] = y
            vs = np.flatnonzero(mv); vs = np.concatenate([vs[vs % S == 0], rng.permutation(vs[vs % S != 0])[:W // 2]])
            a[r, g, vs] = rng.permutation(np.flatnonzero(my))[:vs.size]
    return pack(x, a, w)
def check_inputs(d):
    bad = []; xx = np.asarray(d["x"]).astype(np.float32)
    if not (np.min(xx) >= 0 and np.max(xx) <= 255): bad.append("range of x")
    if np.any(xx != np.floor(xx)): bad.append("x not whole")
    for k, lo, hi in (("pa", -1, W - 1), ("pb", -1, W - 1), ("wt", 1, 4095)):
        if not (np.min(d[k]) >= lo and np.max(d[k]) <= hi): bad.append("range of " + k)
    own = np.arange(W)[None, :]; off = False
    for r in range(N):
        a = np.asarray(d["pa"])[r].astype(np.int64); b = np.asarray(d["pb"])[(r + 1) % N].astype(np.int64)
        for c, e in ((a, b), (b, a)):
            if np.any((c >= 0) & (np.take_along_axis(e, np.clip(c, 0, W - 1), 1) != own)): off = True
    if off: bad.append("pa and pb not mutual")
    return bad
def reference(x, pa, pb, wt):
    X = x.astype(np.float32).astype(np.int32).reshape(N, 8, 16, W); A = pa.astype(np.int64); B = pb.astype(np.int64); w = wt.astype(np.int64).reshape(N, 8, 16, 1)
    kap = np.zeros(N, np.int64); lane = np.arange(L)
    for t in range(TB):
        q = (np.arange(N) + (1 if t % 2 == 0 else -1)) % N
        near, far = (A, B) if t % 2 == 0 else (B, A)
        v = S * lane + t; x0 = X[:, :, :, v]; z = x0; live = near[:, :, v] < 0; last = np.full((N, 8, L), -1, np.int64)
        for d in range(D):
            u = np.sum(w[q] * z, axis=2) & (W - 1)
            c = cands(u, (97 * d + kap[q])[:, None, None, None])
            col = np.take_along_axis(X[q], c.reshape(N, 8, 1, L * J), 3).reshape(N, 8, 16, L, J)
            dist = np.sum(np.abs(col - z[..., None]), axis=2)
            key = np.where(c == last[..., None], 2 ** 24, dist.astype(np.int64) * W + c)
            y = np.take_along_axis(c, np.argmin(key, axis=3)[..., None], 3)[..., 0]
            go = live & (np.take_along_axis(far[q], y, 2) < 0)
            rr, gg, ii = np.nonzero(go); low = np.full((N, 8, W), L, np.int64); np.minimum.at(low, (rr, gg, y[go]), ii)
            win = go & (np.take_along_axis(low, y, 2) == lane)
            rr, gg, ii = np.nonzero(win); yy = y[win]; qq = q[rr]; vv = S * ii + t
            X[qq, gg, :, yy] = (X[qq, gg, :, yy] + x0[rr, gg, :, ii]) >> 1
            far[qq, gg, yy] = vv; near[rr, gg, vv] = yy
            live = live & ~win; kap = np.bincount(qq, minlength=N).astype(np.int64) & 31; last = y
            p = np.maximum(np.take_along_axis(far[q], y, 2), 0)
            z = np.where(live[:, :, None, :], np.take_along_axis(X, p[:, :, None, :], 3), z)
    return {"yx": X.reshape(N, 128, W).astype(np.float32).astype(BF), "ya": A.astype(np.float32), "yb": B.astype(np.float32)}

@@ -1,0 +1,606 @@
+from concourse.mybir import AluOpType, AxisListType, ActivationFunctionType
+
+W = 4096
+WX = 4608
+DEAD = 4096.0
+DUM = 4352
+NB, ND = 3, 3
+BAR = 4095.0 * 4096.0
+
+_B = {}
+
+
+def _sb(name, cols, dtype):
+    _B[name] = ("sbuf", [128, cols], dtype)
+
+
+_sb("X", WX, "bfloat16"); _sb("XC0", WX, "bfloat16"); _sb("XC1", WX, "bfloat16")
+_sb("TA", WX, "float32"); _sb("TB", WX, "float32")
+_sb("PAI", 256, "int32"); _sb("PBI", 256, "int32"); _sb("PF", 512, "float32"); _sb("PG4", 512, "float32")
+_sb("BI", 384, "int32"); _sb("BF", 448, "float32")
+_sb("WI", 8, "int32"); _sb("WF2", 8, "float32")
+_sb("CI5", 256, "int32"); _sb("CT1", 256, "int32"); _sb("CT2", 256, "int32"); _sb("CA", 512, "float32"); _sb("CB", 256, "float32")
+_sb("PI", 8, "int32"); _sb("PT", 16, "int32"); _sb("PC", 16, "float32"); _sb("CF", 256, "float32")
+_sb("WH", 512, "bfloat16"); _sb("WL", 512, "bfloat16")
+_sb("OB", 8, "bfloat16"); _sb("IDF", 128, "float32"); _sb("PEN", 128, "bfloat16"); _sb("ZB", 256, "bfloat16")
+_sb("DIAG", 256, "float32"); _sb("DG2", 256, "float32"); _sb("M1", 128, "float32"); _sb("RS1", 32, "float32")
+_sb("CL", 256, "float32"); _sb("CR", 256, "float32"); _sb("RC", 256, "float32"); _sb("TH2", 256, "float32")
+_sb("RHL", 24, "bfloat16")
+_sb("SR14", 128, "float32")
+_sb("SRB", 384, "bfloat16")
+_sb("IBN", 256, "bfloat16")
+_sb("GBH", 128, "bfloat16"); _sb("ONES", 128, "bfloat16")
+_sb("RS8", 256, "float32"); _sb("RS16", 256, "float32")
+_sb("LX1", 8, "uint16"); _sb("LX2", 16, "uint16"); _sb("LX3", 8, "uint16"); _sb("LX4", 16, "uint16"); _sb("LX5", 16, "uint16")
+_sb("LXI", 16, "int32"); _sb("LXJ", 16, "int32")
+_sb("SCOL", 4, "float32"); _sb("ABASE", 4, "float32"); _sb("ACOL", 4, "float32"); _sb("ATMP", 4, "float32")
+_sb("FBC", 16, "float32"); _sb("FB4C", 64, "float32")
+_sb("SSND", 256 * NB, "bfloat16"); _sb("SLAND", 256 * NB, "bfloat16")
+_sb("DSND", 16 * NB, "float32"); _sb("DLAND", 16 * NB, "float32")
+_sb("NSND", 256 * NB * ND, "bfloat16"); _sb("NLAND", 256 * NB * ND, "bfloat16")
+_sb("LSND", 16 * NB * ND, "uint16"); _sb("LLAND", 16 * NB * ND, "uint16")
+_sb("RSND", 32 * NB, "float32"); _sb("RLAND", 32 * NB, "float32")
+_sb("Z", 256, "bfloat16"); _sb("Z4", 1024, "bfloat16"); _sb("SH", 256, "float32")
+_sb("NI", 64, "int32"); _sb("UF", 64, "float32"); _sb("SQ", 256, "float32"); _sb("FI", 256, "int32"); _sb("CI", 256, "int32")
+_sb("OFF", 256, "uint16"); _sb("CFL", 256, "float32"); _sb("EQ", 256, "bfloat16")
+_sb("DF", 4096, "bfloat16"); _sb("AB", 4096, "bfloat16")
+_sb("R", 256, "float32"); _sb("E1", 128, "float32"); _sb("R4", 128, "float32")
+_sb("MN", 16, "float32"); _sb("YI", 16, "int32"); _sb("YA", 16, "int32"); _sb("YQ", 16, "float32"); _sb("YU", 16, "uint16")
+_sb("FB", 16, "float32"); _sb("FB4", 64, "float32"); _sb("L1", 64, "float32"); _sb("L2", 64, "int32"); _sb("LAST", 64, "int32")
+_sb("QL", 256, "bfloat16"); _sb("QR", 256, "bfloat16"); _sb("QE", 256, "bfloat16"); _sb("QO", 256, "bfloat16")
+_sb("TT", 256, "float32"); _sb("T2", 256, "float32"); _sb("FL", 16, "float32"); _sb("JK", 1280, "bfloat16")
+_sb("E2", 256, "bfloat16"); _sb("LF", 16, "float32"); _sb("UP", 256, "float32"); _sb("PG", 256, "bfloat16")
+_sb("DM", 256, "float32"); _sb("SC", 256, "float32"); _sb("PU", 16, "uint16"); _sb("E3", 512, "bfloat16"); _sb("E4", 256, "bfloat16")
+_sb("W1", 16, "float32"); _sb("W2", 16, "float32"); _sb("W3", 16, "float32"); _sb("WB", 16, "bfloat16")
+_sb("DEADL", 16, "float32"); _sb("RES", 16, "float32"); _sb("KP", 8, "float32"); _sb("KI", 8, "int32")
+for _n in ["G0", "G1", "G2", "G3", "G4", "G5", "K6", "C7"]:
+    _B[_n] = ("psum", [128, 512], "float32")
+_B["BD"] = ("dram", [14, 128, 32], "float32")
+_B["PD"] = ("dram", [4, 128, 256], "float32")
+SCRATCH = _B
+
+_MSG = []
+for _t in range(NB):
+    _MSG += ["s%d" % _t, "b%d" % _t, "e%d" % _t, "r%d" % _t]
+    for _d in range(ND - 1):
+        _MSG += ["n%d%d" % (_t, _d), "l%d%d" % (_t, _d)]
+SEMAPHORES = ["cv", "cs", "cp", "cg"] + ["rx" + m for m in _MSG] + ["tx" + m for m in _MSG] + ["dm%d" % i for i in range(16)]
+
+
+def rank_program(g, core, T, topo):
+    rank = T.rank_of(core)
+    if rank is None:
+        return
+    A = AluOpType
+    F = ActivationFunctionType
+    RH, RL0, RL1 = T.RHL[:, 0:8], T.RHL[:, 8:16], T.RHL[:, 16:24]
+    SRP, SRH, SRL = [T.SRB[:, 128 * i:128 * i + 128] for i in range(3)]
+    n_ranks = len(T.cores)
+    nxt, prv = (rank + 1) % n_ranks, (rank - 1) % n_ranks
+    Q = {"v": g.vector, "s": g.scalar, "p": g.tensor, "g": g, "y": g.sync}
+    cnt = {"v": 0, "s": 0, "p": 0, "g": 0}
+    waited = {q: {} for q in Q}
+    wr = {}
+    rd = {}
+    nd = [0]
+    last = {}
+
+    def need(q, toks):
+        for sem in sorted(toks):
+            if waited[q].get(sem, 0) < toks[sem]:
+                Q[q].wait_ge(T.sem[sem], toks[sem])
+                waited[q][sem] = toks[sem]
+
+    def deps(reads, writes, own=None):
+        toks = {}
+        for k in reads:
+            for s, v in wr.get(k, {}).items():
+                toks[s] = max(toks.get(s, 0), v)
+        for k in writes:
+            for m in (wr, rd):
+                for s, v in m.get(k, {}).items():
+                    if s != own:
+                        toks[s] = max(toks.get(s, 0), v)
+        return toks
+
+    def note(reads, writes, sem, val):
+        for k in writes:
+            wr[k] = {sem: val}
+            rd[k] = {}
+        for k in reads:
+            if k not in writes:
+                m = rd.setdefault(k, {})
+                m[sem] = max(m.get(sem, 0), val)
+        last[sem] = max(last.get(sem, 0), val)
+
+    def op(q, fns, reads, writes, acc=False):
+        need(q, deps(reads, writes, "c" + q if acc else None))
+        for fn in (fns if isinstance(fns, list) else [fns]):
+            cnt[q] += 1
+            fn().then_inc(T.sem["c" + q], 1)
+        note(reads, writes, "c" + q, cnt[q])
+
+    def dma(q, pieces, reads, writes):
+        need(q, deps(reads, writes))
+        sem = "dm%d" % nd[0]
+        nd[0] += 1
+        for out, in_ in pieces:
+            Q[q].dma_start(out, in_).then_inc(T.sem[sem], 16)
+        note(reads, writes, sem, 16 * len(pieces))
+
+    def engs(src, dst):
+        e = topo.engines(src, dst)
+        m = 0
+        for x in e:
+            m |= 1 << x
+        return m, len(e)
+
+    def send(to, msg, out, in_, reads):
+        need("g", deps(reads, []))
+        dst = T.cores[to]
+        rid, pid, _se = topo.addr(dst)
+        m, n = engs(core, dst)
+        g.remote_dma(out, in_, T.sem["rx" + msg], T.sem["tx" + msg], pid, rid, m)
+        note(reads, [], "tx" + msg, n)
+
+    def landed(frm, msg, keys):
+        note([], keys, "rx" + msg, engs(T.cores[frm], core)[1])
+
+    def ts(out, in0, s1, o0, r, w, s2=None, o1=None):
+        if o1 is None:
+            op("v", lambda: g.vector.tensor_scalar(out, in0, s1, None, o0), r, w)
+        else:
+            op("v", lambda: g.vector.tensor_scalar(out, in0, s1, s2, o0, o1), r, w)
+
+    def tt(out, a, b, o, r, w):
+        op("v", lambda: g.vector.tensor_tensor(out, a, b, o), r, w)
+
+    def cp(out, a, r, w):
+        op("v", lambda: g.vector.tensor_copy(out, a), r, w)
+
+    def scan(out, d0, d1, o0, o1, r, w):
+        op("v", lambda: g.vector.tensor_tensor_scan(out, d0, d1, 0.0, o0, o1), r, w)
+
+    def ms(ap, c, w):
+        op("v", lambda: g.vector.memset(ap, c), [], w)
+
+    def act(out, in_, f, r, w, **kw):
+        op("s", lambda: g.scalar.activation(out, in_, f, **kw), r, w)
+
+    def mm(out, lhsT, rhs, start, stop):
+        return lambda: g.tensor.matmul(out, lhsT, rhs, start, stop)
+
+    def row_to_list(src, lhsT, rows, bank, bkey, fin, *between):
+        op("p", mm(bank[:, 0:256], lhsT, src, True, True), rows, [bkey])
+        tt(T.DM[:], bank[:, 0:256], T.DIAG[:], A.mult, [bkey, "DIAG"], ["DM"])
+        for f in between[0:1]:
+            f()
+        scan(T.SC[:], T.RS16[:], T.DM[:], A.mult, A.add, ["RS16", "DM"], ["SC"])
+        for f in between[1:]:
+            f()
+        fin(T.SC[:, 15:256:16])
+
+    def dead_done(t):
+        def fin(ap):
+            ts(T.DSND[:, 16 * t:16 * t + 16], ap, 1.0, A.min, ["SC"], ["DSND%d" % t], DEAD, A.mult)
+            send(nxt if t % 2 == 0 else prv, "e%d" % t, T.DLAND[:, 16 * t:16 * t + 16], T.DSND[:, 16 * t:16 * t + 16], ["DSND%d" % t])
+        return fin
+
+    def start_batch(t):
+        to = nxt if t % 2 == 0 else prv
+        act(T.SSND[:, 256 * t:256 * t + 256], T.X[:, t:W:16], F.Copy, ["X"], ["SSND%d" % t])
+        send(to, "s%d" % t, T.SLAND[:, 256 * t:256 * t + 256], T.SSND[:, 256 * t:256 * t + 256], ["SSND%d" % t])
+        xc = T.XC0 if t % 2 == 0 else T.XC1
+        send(to, "b%d" % t, xc[:, 0:W], T.X[:, 0:W], ["X"])
+        landed(prv if t % 2 == 0 else nxt, "s%d" % t, ["SLAND%d" % t])
+
+    def near_send(t):
+        hi, lo = T.RSND[:, 32 * t:32 * t + 16], T.RSND[:, 32 * t + 16:32 * t + 32]
+        if t == NB - 1:
+            cp(hi, T.RES[:], ["RES"], ["RSH%d" % t])
+            send(prv if t % 2 == 0 else nxt, "r%d" % t, T.RLAND[:, 32 * t:32 * t + 16], hi, ["RSH%d" % t])
+            return
+        ts(T.LXJ[:], T.RES[:], -1.0, A.add, ["RES"], ["LXJ"])
+        ts(T.LXI[:], T.LXJ[:], 4, A.arith_shift_right, ["LXJ"], ["LXI"])
+        ts(hi, T.LXI[:], 0.0, A.max, ["LXI"], ["RSH%d" % t])
+        ts(T.W2[:], hi, -16.0, A.mult, ["RSH%d" % t], ["W2"])
+        tt(lo, T.RES[:], T.W2[:], A.add, ["RES", "W2"], ["RSL%d" % t])
+        send(prv if t % 2 == 0 else nxt, "r%d" % t, T.RLAND[:, 32 * t:32 * t + 32], T.RSND[:, 32 * t:32 * t + 32], ["RSH%d" % t, "RSL%d" % t])
+
+    def near_rows(t):
+        landed(nxt if t % 2 == 0 else prv, "r%d" % t, ["RLAND%d" % t])
+        for i in range(2):
+            tt(T.E3[:, 256 * i:256 * i + 256], T.RLAND[:, 32 * t + 16 * i:32 * t + 16 * i + 16].indirect(T.LX4[:]), T.DIAG[:], A.mult,
+               ["RLAND%d" % t, "LX4", "DIAG"], ["E3_%d" % i])
+        op("p", [mm(T.G4[:, 0:256], SRH, T.E3[:, 0:256], True, False), mm(T.G4[:, 0:256], SRL, T.E3[:, 256:512], False, True)],
+           ["SRH", "SRL", "E3_0", "E3_1"], ["G4"])
+
+    def near_add(t):
+        near, nk = (T.TA, "TA") if t % 2 == 0 else (T.TB, "TB")
+        tt(near[:, t:W:16], T.G4[:, 0:256], near[:, t:W:16], A.add, ["G4", nk], [nk])
+
+    dma("s", [(T.PAI[:], T.pa[:])], [], ["PAI"])
+    dma("y", [(T.X[:, 0:W], T.x[:])], [], ["X"])
+    dma("s", [(T.PBI[:], T.pb[:])], [], ["PBI"])
+    dma("s", [(T.WI[:, 0:1], T.wt[:])], [], ["WI"])
+    op("g", lambda: g.iota(T.PI[:, 0:1], [[0, 1]], 0, 1), [], ["PI"])
+    op("g", lambda: g.iota(T.BI[:, 0:32], [[1, 32]], 0, 32), [], ["BI0"])
+    op("g", lambda: g.iota(T.CI5[:], [[1, 256]], 0, 0), [], ["CI5"])
+    op("g", lambda: g.iota(T.LXI[:, 0:8], [[32, 8]], 7, 0), [], ["LXI"])
+    for nm in ("X", "XC0", "XC1"):
+        op("g", lambda: g.iota(T[nm][:, W:WX], [[0, WX - W]], 0, 0, allow_small_or_imprecise_dtypes=True), [], [nm + "x"])
+    for c, k, v in [(0, "s", 4), (1, "a", 15), (2, "a", 3), (3, "s", 2)]:
+        ts(T.PT[:, c:c + 1], T.PI[:, 0:1], v, A.arith_shift_right if k == "s" else A.bitwise_and, ["PI"], ["PT%d" % c])
+    cp(T.PC[:, 0:4], T.PT[:, 0:4], ["PT0", "PT1", "PT2", "PT3"], ["PC0"])
+    cp(T.PC[:, 4:5], T.PI[:, 0:1], ["PI"], ["PC4"])
+    PGRP, PLOW, PL3, PS2, PP = T.PC[:, 0:1], T.PC[:, 1:2], T.PC[:, 2:3], T.PC[:, 3:4], T.PC[:, 4:5]
+    for i, r in enumerate((12, 13, 14, 15)):
+        ts(T.PC[:, 8 + i:9 + i], PLOW, float(r), A.is_equal, ["PC0"], ["PC%d" % (8 + i)])
+    I12, I13, I14, I15 = [T.PC[:, 8 + i:9 + i] for i in range(4)]
+    ts(T.PT[:, 4:5], T.PI[:, 0:1], 4, A.arith_shift_right, ["PI"], ["PT4"], 1, A.bitwise_and)
+    ECOL, OCOL = T.WF2[:, 6:7], T.WF2[:, 5:6]
+    for f in range(1, 12):
+        ts(T.BI[:, 32 * f:32 * f + 32], T.BI[:, 0:32], f, A.arith_shift_right, ["BI0"], ["BI%d" % f], 1, A.bitwise_and)
+    ts(T.BI[:, 0:32], T.BI[:, 0:32], 1, A.bitwise_and, ["BI0"], ["BI0"])
+    ts(T.BF[:, 0:384], T.BI[:], 2.0, A.mult, ["BI%d" % f for f in range(12)], ["BFA"], -1.0, A.add)
+    ms(T.BF[:, 384:448], 1.0, ["BFB"])
+    dma("y", [(T.BD[f], T.BF[:, 32 * f:32 * f + 32]) for f in range(14)], ["BFA", "BFB"], ["BD"])
+    ts(T.CT1[:], T.CI5[:], 15, A.bitwise_and, ["CI5"], ["CT1"])
+    ts(T.CT2[:], T.CI5[:], 4, A.arith_shift_right, ["CI5"], ["CT2"])
+    ts(T.GBH[:], T.CT2[:, 0:128], PGRP, A.is_equal, ["CT2", "PC0"], ["GBH"])
+    ts(T.DG2[:], T.CT2[:], PLOW, A.is_equal, ["CT2", "PC0"], ["DG2"])
+    ms(T.CA[:, 0:16], 0.0, ["CA"])
+    ts(T.LX5[:], T.CA[:, 0:16], PLOW, A.add, ["CA", "PC0"], ["LX5"])
+    ts(T.W1[:], T.PAI[:, 0:256:16], 0.0, A.is_ge, ["PAI"], ["W1"])
+    tt(T.E4[:], T.W1[:, 0:16].indirect(T.LX5[:]), T.DG2[:], A.mult, ["W1", "LX5", "DG2"], ["E4"])
+    ts(T.RS16[:], T.CT1[:], 0.0, A.not_equal, ["CT1"], ["RS16"])
+    ts(T.DIAG[:], T.CT1[:], PLOW, A.is_equal, ["CT1", "PC0"], ["DIAG"])
+    row_to_list(T.E4[:], T.GBH[:], ["E4", "GBH"], T.G3, "G3", dead_done(0))
+    start_batch(0)
+    wr["X"] = deps(["X", "Xx"], [])
+    def table_rows(pin, pk, i):
+        hi, lo = T.PF[:, 256 * i:256 * i + 256], T.PG4[:, 256 * i:256 * i + 256]
+        ts(T.CT1[:], pin[:], 4, A.arith_shift_right, [pk], ["CT1"])
+        ts(hi, T.CT1[:], 0.0, A.max, ["CT1"], ["PF%d" % i])
+        ts(T.CB[:], hi, -16.0, A.mult, ["PF%d" % i], ["CB"], 1.0, A.add)
+        tt(lo, T.CB[:], pin[:], A.add, ["CB", pk], ["PG4%d" % i])
+        dma("y", [(T.PD[2 * i], hi), (T.PD[2 * i + 1], lo)], ["PF%d" % i, "PG4%d" % i], ["PD%d" % i])
+
+    def fill_table(tab, key, pv, pf, pk):
+        pieces = [(tab[16 * b:16 * b + 14, 0:W], T.BD[:]) for b in range(8)]
+        pieces += [(tab[15:128:16, 0:W], pv), (tab[14:128:16, 0:W], pf)]
+        dma("y", pieces, ["BD", pk], [key])
+
+    table_rows(T.PBI, "PBI", 0)
+    fill_table(T.TB, "TBd", T.PD[0], T.PD[1], "PD0")
+    ts(T.WI[:, 2:3], T.WI[:, 0:1], 3840, A.bitwise_and, ["WI"], ["WI2"])
+    ts(T.WI[:, 3:4], T.WI[:, 0:1], 255, A.bitwise_and, ["WI"], ["WI3"])
+    ts(T.WF2[:, 0:2], T.WI[:, 2:4], 1.0 / 4096, A.mult, ["WI2", "WI3"], ["WF2"])
+    ts(T.CA[:, 0:128], T.CT2[:, 0:128], PGRP, A.is_equal, ["CT2", "PC0"], ["CA"], 100.0, A.mult)
+    ts(T.CT1[:, 0:128], T.CI5[:, 0:128], 2, A.arith_shift_right, ["CI5"], ["CT1"], 3, A.bitwise_and)
+    tt(T.CB[:, 0:128], T.CT1[:, 0:128], T.CA[:, 0:128], A.add, ["CT1", "CA"], ["CB"])
+    for ll in range(4):
+        for wm, wc in ((T.WH, 0), (T.WL, 1)):
+            ts(wm[:, 128 * ll:128 * ll + 128], T.CB[:, 0:128], 100.0 + ll, A.is_equal, ["CB", "WF2"], ["WHL%d%d" % (ll, wc)], T.WF2[:, wc:wc + 1], A.mult)
+    WHL = ["WHL%d%d" % (i, j) for i in range(4) for j in range(2)]
+    ts(T.M1[:], T.CT1[:, 0:128], PL3, A.is_equal, ["CT1", "PC0"], ["M1"])
+    for ch in range(4):
+        ts(T.SCOL[:, ch:ch + 1], PL3, 32.0, A.mult, ["PC0"], ["SCOL"], 128.0 * ch + 16.0, A.add)
+    tt(T.ATMP[:], T.SCOL[:], T.SCOL[:], A.mult, ["SCOL"], ["ATMP"])
+    ts(T.ABASE[:], T.ATMP[:], -1.0, A.mult, ["ATMP"], ["ABASE"], 262144.0 - 12.0, A.add)
+    ts(T.ACOL[:], T.ABASE[:], 0.0, A.add, ["ABASE"], ["ACOL"])
+    cp(T.CF[:], T.CI5[:], ["CI5"], ["CF"])
+    ts(T.IDF[:], T.CF[:, 0:128], PP, A.is_equal, ["CF", "PC4"], ["IDF"])
+    ts(T.PC[:, 12:13], PLOW, 12.0, A.is_lt, ["PC0"], ["PC12"])
+    ts(T.PC[:, 7:8], I12, -1.0, A.mult, ["PC8"], ["PC7"])
+    ts(T.PC[:, 13:14], T.PC[:, 12:13], 128.0, A.mult, ["PC12", "PC8"], ["PC13"], I12, A.add)
+    ts(T.PC[:, 14:15], I14, 2048.0, A.mult, ["PC10"], ["PC14"])
+    tt(T.PC[:, 13:14], T.PC[:, 13:14], T.PC[:, 14:15], A.add, ["PC13", "PC14"], ["PC13"])
+    ts(T.PC[:, 15:16], T.PC[:, 12:13], I13, A.add, ["PC12", "PC9", "PC10"], ["PC15"], I14, A.add)
+    ts(T.WF2[:, 4:5], PLOW, 14.0, A.is_lt, ["PC0", "PC10"], ["WF4"], -2.0, A.mult)
+    tt(T.WF2[:, 4:5], T.WF2[:, 4:5], I14, A.add, ["WF4", "PC10"], ["WF4"])
+    ts(T.WF2[:, 3:4], I15, 16.0, A.mult, ["PC11", "PC10"], ["WF3"], I14, A.add)
+    cp(T.WF2[:, 5:6], T.PT[:, 4:5], ["PT4"], ["WF5"])
+    ts(T.WF2[:, 6:7], T.WF2[:, 5:6], -1.0, A.mult, ["WF5"], ["WF6"], 1.0, A.add)
+    ts(T.OB[:], T.CF[:, 0:8], PGRP, A.is_equal, ["CF", "PC0"], ["OB"], 4096.0, A.mult)
+    ms(T.ZB[:], 0.0, ["ZB"])
+    ts(T.CT1[:], T.CI5[:], 7, A.bitwise_and, ["CI5"], ["CT1"])
+    ts(T.RS8[:], T.CT1[:], 0.0, A.is_equal, ["CT1"], ["RS8"], float(2 ** 26), A.mult)
+    ts(T.RS1[:], T.CF[:, 0:32], PS2, A.is_equal, ["CF", "PC0"], ["RS1"])
+    ts(T.PC[:, 5:6], PL3, 8.0, A.mult, ["PC0"], ["PC5"])
+    ts(T.LX1[:], T.LXI[:, 0:8], T.PC[:, 5:6], A.add, ["LXI", "PC5"], ["LX1"])
+    ts(T.PT[:, 6:7], T.PI[:, 0:1], 2, A.arith_shift_right, ["PI"], ["PT6"], 3, A.bitwise_and)
+    ts(T.PC[:, 6:7], T.PT[:, 6:7], 8.0, A.mult, ["PT6"], ["PC6"])
+    ts(T.LX3[:], T.LXI[:, 0:8], T.PC[:, 6:7], A.add, ["LXI", "PC6"], ["LX3"])
+    ms(T.FBC[:], 16777215.0, ["FBC"])
+    ms(T.FB4C[:], 16777215.0, ["FB4C"])
+    act(T.IBN[:, 0:128], T.IDF[:], F.Identity, ["IDF"], ["IBN0"])
+    act(T.IBN[:, 128:256], T.IDF[:], F.Identity, ["IDF"], ["IBN1"], scale=-1.0)
+    act(T.CL[:], T.CF[:], F.Identity, ["CF", "PC9", "PC13"], ["CL"], scale=I13, bias=T.PC[:, 13:14])
+    act(T.CR[:], T.CF[:], F.Identity, ["CF", "PC7", "PC15"], ["CR"], scale=T.PC[:, 7:8], bias=T.PC[:, 15:16])
+    for i in range(2):
+        act(T.TB[:, W + 256 * i:W + 256 * i + 256], T.CF[:], F.Identity, ["CF", "PC10"], ["TBx%d" % i], scale=0.0, bias=I14)
+    wr["TB"] = deps(["TBd", "TBx0", "TBx1"], [])
+
+    def scalar_constants():
+        act(T.PEN[:], T.IDF[:], F.Identity, ["IDF"], ["PEN"], scale=float(2 ** 25))
+        act(T.RC[:], T.CF[:], F.Identity, ["CF", "PC11", "WF4"], ["RC"], scale=I15, bias=T.WF2[:, 4:5])
+        act(SRP, T.GBH[:], F.Identity, ["GBH", "WF3"], ["SRP"], scale=T.WF2[:, 3:4])
+        act(T.SR14[:], T.GBH[:], F.Identity, ["GBH", "PC10"], ["SR14"], scale=I14)
+        for i in range(2):
+            act(T.TA[:, W + 256 * i:W + 256 * i + 256], T.CF[:], F.Identity, ["CF", "PC10"], ["TAx%d" % i], scale=0.0, bias=I14)
+
+    def later_constants():
+        ts(T.CT2[:, 0:16], T.CI5[:, 0:16], 7, A.bitwise_and, ["CI5"], ["CT2"])
+        cp(T.LX2[:], T.CT2[:, 0:16], ["CT2"], ["LX2"])
+        ts(T.CT1[:], T.CI5[:], 4, A.arith_shift_right, ["CI5"], ["CT1"], 7, A.bitwise_and)
+        for h in range(2):
+            ts(T.CA[:, 128 * h:128 * h + 128], T.CT1[:, 128 * h:128 * h + 128], 4.0 + h, A.is_lt, ["CT1"], ["CA"], 1536.0, A.mult)
+        ts(T.CB[:], T.DIAG[:], 0.0, A.is_equal, ["DIAG"], ["CB"], 1e25, A.mult)
+        tt(T.TH2[:], T.CA[:, 0:256], T.CB[:], A.max, ["CA", "CB"], ["TH2"])
+        ts(RH, T.CF[:, 0:8], PGRP, A.is_equal, ["CF", "PC0"], ["RH"], float(DUM), A.mult)
+        ts(RL0, T.CF[:, 0:8], PGRP, A.is_equal, ["CF", "PC0", "PC4"], ["RL0"], PP, A.mult)
+        ts(T.WF2[:, 7:8], PP, 128.0, A.add, ["PC4"], ["WF7"])
+        ts(RL1, T.CF[:, 0:8], PGRP, A.is_equal, ["CF", "PC0", "WF7"], ["RL1"], T.WF2[:, 7:8], A.mult)
+
+    def last_constants():
+        ms(T.ONES[:], 1.0, ["ONES"])
+        ts(T.CT2[:, 0:128], T.CI5[:, 0:128], 15, A.bitwise_and, ["CI5"], ["CT2"])
+        for i, sel in ((15, SRH), (14, SRL)):
+            ts(T.CA[:, 0:128], T.CT2[:, 0:128], float(i), A.is_equal, ["CT2"], ["CA"])
+            tt(sel, T.CA[:, 0:128], T.GBH[:], A.mult, ["CA", "GBH"], ["SRH" if i == 15 else "SRL"])
+        cp(T.LX4[:], T.CI5[:, 0:16], ["CI5"], ["LX4"])
+        table_rows(T.PAI, "PAI", 1)
+        fill_table(T.TA, "TAd", T.PD[2], T.PD[3], "PD1")
+        wr["TA"] = deps(["TAd", "TAx0", "TAx1"], [])
+
+    BANKS = [T.G0, T.G1, T.G2, T.G3, T.G4, T.G5]
+    for t in range(NB):
+        frm, to = (prv, nxt) if t % 2 == 0 else (nxt, prv)
+        far, fk = (T.TB, "TB") if t % 2 == 0 else (T.TA, "TA")
+        XC, xk = (T.XC0, "XC0") if t % 2 == 0 else (T.XC1, "XC1")
+        for d in range(ND):
+            m = t * ND + d
+            tail = d == ND - 1
+            if d == 0:
+                z, zk = T.SLAND[:, 256 * t:256 * t + 256], "SLAND%d" % t
+            else:
+                z, zk = T.Z[:], "Z"
+                pm = m - 1
+                msg = "%d%d" % (t, d - 1)
+                if d == 1:
+                    landed(frm, "b%d" % t, [xk + "b"])
+                    wr[xk] = deps([xk + "b", xk + "x"], [])
+                landed(frm, "n" + msg, ["NLAND%d" % pm])
+                landed(frm, "l" + msg, ["LLAND%d" % pm])
+                cp(XC[:, 0:WX].indirect(T.LLAND[:, 16 * pm:16 * pm + 16]), T.NLAND[:, 256 * pm:256 * pm + 256],
+                   ["NLAND%d" % pm, "LLAND%d" % pm], [xk])
+                cp(T.Z[:], XC[:, 0:WX].indirect(T.PU[:]), [xk, "PU"], ["Z"])
+
+            result = (lambda: ts(T.W3[:], T.YQ[:], 1.0, A.add, ["YQ"], ["W3"]),
+                      lambda: tt(T.W2[:], T.W3[:], T.WB[:], A.mult, ["W3", "WB"], ["W2"]),
+                      lambda: tt(T.RES[:], T.RES[:], T.W2[:], A.add, ["RES", "W2"], ["RES"]))
+
+            fs = []
+            for ll in range(4):
+                zs = T.SLAND[:, 256 * t + ll:256 * t + 256:4] if d == 0 else T.Z[:, ll:256:4]
+                fs.append(mm(T.K6[:, 0:64], T.WH[:, 128 * ll:128 * ll + 128], zs, ll == 0, False))
+                fs.append(mm(T.K6[:, 0:64], T.WL[:, 128 * ll:128 * ll + 128], zs, False, ll == 3))
+            op("p", fs, WHL + [zk], ["K6"])
+            for cl in range(4):
+                cp(T.Z4[:, cl:1024:4], z, [zk], ["Z4_%d" % cl])
+            ts(T.NI[:], T.K6[:, 0:64], -0.5, A.add, ["K6"], ["NI"])
+            tt(T.UF[:], T.K6[:, 0:64], T.NI[:], A.subtract, ["K6", "NI"], ["UF"])
+            for ch in range(4):
+                act(T.SQ[:, 64 * ch:64 * ch + 64], T.UF[:], F.Square, ["UF", "SCOL"], ["SQ%d" % ch], bias=T.SCOL[:, ch:ch + 1], scale=4096.0)
+
+            def floors(ch):
+                ts(T.FI[:, 64 * ch:64 * ch + 64], T.SQ[:, 64 * ch:64 * ch + 64], T.ACOL[:, ch:ch + 1], A.add, ["SQ%d" % ch, "ACOL"], ["FI%d" % ch], 1.0 / 32, A.mult)
+
+            def places(c0, c1):
+                keys = [str(ch) for ch in range(c0, c1)]
+                ts(T.CI[:, 64 * c0:64 * c1], T.FI[:, 64 * c0:64 * c1], 4095, A.bitwise_and, ["FI" + c for c in keys], ["CI" + c for c in keys])
+
+            def bars(ch):
+                tt(T.EQ[:, 64 * ch:64 * ch + 64], T.CI[:, 64 * ch:64 * ch + 64], T.LAST[:], A.is_equal, ["CI%d" % ch, "LAST"], ["EQ%d" % ch])
+
+            def lists(c0, c1):
+                keys = [str(ch) for ch in range(c0, c1)]
+                cp(T.OFF[:, 64 * c0:64 * c1], T.CI[:, 64 * c0:64 * c1], ["CI" + c for c in keys], ["OFF" + c for c in keys])
+
+            if d == 0:
+                act(T.SH[:], z, F.Copy, [zk], ["SH"], bias=-0.5)
+
+            def gather(c0, n):
+                a, b, zo = 16 * c0, 16 * (c0 + n), 16 * (c0 % 64)
+                tt(T.DF[:, a:b], T.X[:, 0:WX].indirect(T.OFF[:, c0:c0 + n]), T.Z4[:, zo:zo + 16 * n], A.subtract,
+                   ["X", "OFF%d" % (c0 // 64), "Z4_0", "Z4_1", "Z4_2", "Z4_3"], ["DF%d" % c0])
+                act(T.AB[:, a:b], T.DF[:, a:b], F.Abs, ["DF%d" % c0], ["AB%d" % c0])
+
+            def dsum(c0, n, p0, pr, keys):
+                fs = []
+                for part in range(16):
+                    o = 2 * part + pr
+                    fs.append(mm(T.K6[p0:p0 + n, o:256:32], T.AB[:, 16 * c0 + part:16 * (c0 + n):16], T.OB[:], False, False))
+                op("p", fs, keys + ["OB"], ["K6"], True)
+
+            floors(0)
+            floors(1)
+            places(0, 1)
+            floors(2)
+            lists(0, 1)
+            floors(3)
+            act(T.DF[:, 512:1024], T.X[:, 0:WX].indirect(T.OFF[:, 32:64]), F.Copy, ["X", "OFF0"], ["DF32"])
+            op("p", [mm(T.G0[:], T.IBN[:, 0:128], T.DF[:, 512:1024], True, False), mm(T.G0[:], T.IBN[:, 128:256], T.Z4[:, 512:1024], False, True)],
+               ["IBN0", "IBN1", "DF32", "Z4_0", "Z4_1", "Z4_2", "Z4_3"], ["G0"])
+            gather(0, 32)
+            act(T.AB[:, 512:1024], T.G0[:], F.Abs, ["G0"], ["AB32"])
+            places(1, 4)
+            if d > 0:
+                bars(0)
+            lists(1, 4)
+            cis = ["CI0", "CI1", "CI2", "CI3"]
+            cp(T.CFL[:], T.CI[:], cis, ["CFL"])
+            op("p", [mm(T.K6[:, 0:256], T.ZB[:, 0:128], T.ZB[:], True, False)] +
+               [mm(T.K6[:, pr:256:2], T.CFL[:, 128 * pr:128 * pr + 128], T.IDF[:], False, False) for pr in range(2)], ["ZB", "CFL", "IDF"], ["K6"])
+            gather(64, 64)
+            dsum(0, 128, 0, 0, ["AB0", "AB32", "AB64"])
+            gather(128, 32)
+            gather(160, 32)
+            dsum(128, 64, 0, 1, ["AB128", "AB160"])
+            if d == 0 and t > 0:
+                near_rows(t - 1)
+            gather(192, 32)
+            dsum(192, 32, 64, 1, ["AB192"])
+            gather(224, 16)
+            gather(240, 16)
+            if d > 0:
+                for ch in range(1, 4):
+                    bars(ch)
+            dsum(224, 32, 96, 1, ["AB224", "AB240"])
+            if d > 0:
+                op("p", [mm(T.K6[:, pr:256:2], T.EQ[:, 128 * pr:128 * pr + 128], T.PEN[:], False, False) for pr in range(2)], ["EQ0", "EQ1", "EQ2", "EQ3", "PEN"], ["K6"], True)
+            op("p", mm(T.K6[:, 0:256], T.ZB[:, 0:128], T.ZB[:], False, True), ["ZB"], ["K6"], True)
+            if d == 0:
+                landed(frm, "e%d" % t, ["DLAND%d" % t])
+                cp(T.DEADL[:], T.DLAND[:, 16 * t:16 * t + 16], ["DLAND%d" % t], ["DEADL"])
+                ms(T.RES[:], 0.0, ["RES"])
+                if t > 0:
+                    near_add(t - 1)
+                    ts(T.RC[:], T.RC[:], I14, A.add, ["RC", "PC10"], ["RC"])
+                else:
+                    later_constants()
+            else:
+                ts(T.W1[:], T.WB[:], DEAD, A.mult, ["WB"], ["W1"])
+                tt(T.DEADL[:], T.DEADL[:], T.W1[:], A.max, ["DEADL", "W1"], ["DEADL"])
+                ts(T.FB[:], T.YA[:], BAR, A.add, ["YA"], ["FB"])
+            if m == 0:
+                scalar_constants()
+            scan(T.R[:], T.RS8[:], T.K6[:, 0:256], A.max, A.min, ["RS8", "K6"], ["R"])
+            tt(T.E1[:], T.R[:, 0:256].indirect(T.LX1[:]), T.M1[:], A.mult, ["R", "LX1", "M1"], ["E1"])
+            op("p", mm(T.C7[:, 0:32], T.E1[:], T.RS1[:], True, True), ["E1", "RS1"], ["C7"])
+            if not tail:
+                act(T.R4[:], T.R[:, 0:256].indirect(T.LX3[:]), F.Copy, ["R", "LX3"], ["R4"])
+                op("p", mm(T.K6[:, 0:128], T.R4[:], T.IDF[:], True, True), ["R4", "IDF"], ["K6"])
+            fb, fbk = (T.FBC, "FBC") if d == 0 else (T.FB, "FB")
+            rs = list(result) if d > 0 else [lambda: None] * 3
+            tt(T.MN[:], T.C7[:, 16:32], fb[:], A.min, ["C7", fbk], ["MN"])
+            rs[0]()
+            tt(T.YI[:], T.C7[:, 0:16], T.MN[:], A.min, ["C7", "MN"], ["YI"])
+            rs[1]()
+            ts(T.YA[:], T.YI[:], 4095, A.bitwise_and, ["YI"], ["YA"])
+            rs[2]()
+            tt(T.YQ[:], T.YA[:], T.DEADL[:], A.max, ["YA", "DEADL"], ["YQ"])
+            cp(T.YU[:], T.YQ[:], ["YQ"], ["YU"])
+            for h in range(2):
+                a, b, yl = 128 * h, 128 * h + 128, T.YU[:, 8 * h:8 * h + 8]
+                tt(T.QL[:, a:b], far[:, 0:WX].indirect(yl), T.CL[:, a:b], A.mult, [fk, "YU", "CL"], ["QL%d" % h])
+                act(T.QE[:, a:b], T.QL[:, a:b], F.Copy, ["QL%d" % h, "WF6"], ["QE%d" % h], scale=ECOL)
+                tt(T.QR[:, a:b], far[:, 0:WX].indirect(yl), T.CR[:, a:b], A.mult, [fk, "YU", "CR"], ["QR%d" % h])
+                ts(T.QO[:, a:b], T.QL[:, a:b], OCOL, A.mult, ["QL%d" % h, "WF5"], ["QO%d" % h])
+            if m == 0:
+                last_constants()
+
+            def unit(gr, h, b, c):
+                qa, qk = (T.QE, "QE%d" % h) if gr % 2 == 0 else (T.QO, "QO%d" % h)
+                p0 = 32 * (gr // 2)
+                return mm(b[:, c:c + 128 + 128 * h], qa[p0:p0 + 32, 128 * h:128 * h + 128], T.QR[p0:p0 + 32, 0:128 + 128 * h], True, True)
+
+            def reduce(gr, h, b, bk, c, vec):
+                src = b[:, c:c + 128 + 128 * h]
+                o = T.FL[:, 8 * h + gr:8 * h + gr + 1]
+                if vec:
+                    op("v", lambda: g.vector.tensor_reduce(o, src, AxisListType.X, A.max), [bk], ["FL%d_%d" % (gr, h)])
+                else:
+                    j = 128 * (gr - 4) if h == 0 else 512 + 256 * (gr - 5)
+                    act(T.JK[:, j:j + 128 + 128 * h], src, F.Relu, [bk], ["JK%d_%d" % (gr, h), "FL%d_%d" % (gr, h)], bias=-1536.0, accum_out=o)
+
+            def unpaired(h):
+                tt(T.E2[:, 128 * h:128 * h + 128], T.FL[:, 8 * h:8 * h + 8].indirect(T.LX2[:, 8 * h:8 * h + 8]), T.TH2[:, 128 * h:128 * h + 128], A.is_gt,
+                   ["FL%d_%d" % (i, h) for i in range(8)] + ["LX2", "TH2"], ["E2_%d" % h])
+
+            for i, (ga, gb) in enumerate(((4, 5), (0, 1), (6, 7), (2, 3))):
+                b, bk = BANKS[i], "G%d" % i
+                op("p", [unit(ga, 0, b, 0), unit(gb, 0, b, 128)], ["QE0", "QO0", "QR0"], [bk])
+                reduce(ga, 0, b, bk, 0, ga < 4)
+                reduce(gb, 0, b, bk, 128, gb < 4)
+            tt(T.TT[:], T.X[:, 0:WX].indirect(T.YU[:]), T.SH[:], A.add, ["X", "YU", "SH"], ["TT"])
+            ns = T.NSND[:, 256 * m:256 * m + 256]
+            for n, gr in enumerate((5, 0, 6, 1, 7, 2, 3, 4)):
+                b, bk = BANKS[(4 + n) % 6], "G%d" % ((4 + n) % 6)
+                op("p", unit(gr, 1, b, 0), ["QE1" if gr % 2 == 0 else "QO1", "QR0", "QR1"], [bk])
+                reduce(gr, 1, b, bk, 0, gr < 5)
+                if n == 0:
+                    act(T.T2[:], T.TT[:], F.Copy, ["TT"], ["T2"], scale=0.5, bias=8388608.0)
+                    act(ns, T.T2[:], F.Copy, ["T2"], ["NSND%d" % m], bias=-8388608.0)
+                    if not tail:
+                        send(to, "n%d%d" % (t, d), T.NLAND[:, 256 * m:256 * m + 256], ns, ["NSND%d" % m])
+                if n == 1:
+                    unpaired(0)
+                if not tail:
+                    f4, f4k = (T.FB4C, "FB4C") if d == 0 else (T.FB4, "FB4")
+                    if n == 3:
+                        tt(T.L1[:], T.K6[:, 64:128], f4[:], A.min, ["K6", f4k], ["L1"])
+                    if n == 5:
+                        tt(T.L2[:], T.K6[:, 0:64], T.L1[:], A.min, ["K6", "L1"], ["L2"])
+                    if n == 6:
+                        ts(T.LAST[:], T.L2[:], 4095, A.bitwise_and, ["L2"], ["LAST"])
+                    if n == 7 and d == 0:
+                        ts(T.FB4[:], T.LAST[:], BAR, A.add, ["LAST"], ["FB4"])
+            unpaired(1)
+            fs = []
+            for h in range(2):
+                fs.append(mm(T.C7[:, 64 + 8 * h:72 + 8 * h], T.E2[:, 128 * h:128 * h + 128], RH, True, False))
+                fs.append(mm(T.C7[:, 64 + 8 * h:72 + 8 * h], T.E2[:, 128 * h:128 * h + 128], RL0 if h == 0 else RL1, False, True))
+            op("p", fs, ["E2_0", "E2_1", "RH", "RL0", "RL1"], ["C7"])
+            if m == ND * NB - 2:
+                dma("y", [(T.PG4[:, 0:256], T.TA[15:128:16, 0:W]), (T.PG4[:, 256:512], T.TA[14:128:16, 0:W])], ["TA"], ["PG4n"])
+                ts(T.CB[:], T.PG4[:, 0:256], 16.0, A.mult, ["PG4n"], ["CB"], -1.0, A.add)
+                tt(T.PF[:, 0:256], T.CB[:], T.PG4[:, 256:512], A.add, ["CB", "PG4n"], ["YA0"])
+            act(T.UP[:], far[:, 0:WX].indirect(T.YU[:]), F.Copy, [fk, "YU"], ["UP"])
+            tt(T.LF[:], T.C7[:, 64:80], T.YQ[:], A.max, ["C7", "YQ"], ["LF"])
+            ls = T.LSND[:, 16 * m:16 * m + 16]
+            lk = "LSND%d" % m
+            cp(ls, T.LF[:], ["LF"], [lk])
+            if not tail:
+                send(to, "l%d%d" % (t, d), T.LLAND[:, 16 * m:16 * m + 16], ls, [lk])
+            if tail:
+                cp(T.X[:, 0:WX].indirect(ls), ns, [lk, "NSND%d" % m], ["X"])
+                if t + 1 < NB:
+                    start_batch(t + 1)
+            ts(T.WB[:], T.LF[:], float(DUM), A.is_lt, ["LF"], ["WB"])
+            if not (tail and t + 1 == NB):
+                op("p", mm(T.G0[:, 0:16], T.ONES[:], T.WB[:], True, True), ["ONES", "WB"], ["G0"])
+            if tail:
+                for r in result:
+                    r()
+                near_send(t)
+            tt(far[:, 0:WX].indirect(ls), T.UP[:], T.RC[:], A.max, ["UP", "RC", lk], [fk])
+            if not tail:
+                act(T.PG[:], far[:, 0:WX].indirect(T.YU[:]), F.Copy, [fk, "YU"], ["PG"])
+                cp(T.X[:, 0:WX].indirect(ls), ns, [lk, "NSND%d" % m], ["X"])
+            if not (tail and t + 1 == NB):
+                op("v", lambda: g.vector.tensor_reduce(T.KP[:, 0:1], T.G0[:, 0:16], AxisListType.X, A.add), ["G0"], ["KP0"])
+                k1 = lambda: cp(T.KI[:, 0:1], T.KP[:, 0:1], ["KP0"], ["KI0"])
+                k2 = lambda: ts(T.KI[:, 1:2], T.KI[:, 0:1], 31, A.bitwise_and, ["KI0"], ["KI1"])
+                if not tail:
+                    row_to_list(T.PG[:], SRP, ["PG", "SRP"], T.G2, "G2",
+                                lambda ap: ts(T.PU[:], ap, -1.0, A.add, ["SC"], ["PU"]), k1, k2)
+                else:
+                    row_to_list(far[:, t + 1:W:16], T.SR14[:], [fk, "SR14"], T.G3, "G3", dead_done(t + 1), k1, k2)
+                ts(T.KP[:, 1:2], T.KI[:, 1:2], 32.0, A.mult, ["KI1"], ["KP1"])
+                ts(T.ACOL[:], T.ABASE[:], T.KP[:, 1:2], A.add, ["ABASE", "KP1"], ["ACOL"], 3104.0 * ((d + 1) % ND), A.add)
+    dma("y", [(T.yx[:], T.X[:, 0:W])], ["X"], ["yx"])
+
+    dma("y", [(T.PG4[:, 0:256], T.TB[15:128:16, 0:W]), (T.PG4[:, 256:512], T.TB[14:128:16, 0:W])], ["TB", "YA0"], ["PG4f"])
+    t = NB - 1
+    landed(nxt if t % 2 == 0 else prv, "r%d" % t, ["RLAND%d" % t])
+    tt(T.E1[:], T.RLAND[:, 32 * t:32 * t + 16].indirect(T.LX5[:, 0:8]), T.GBH[:], A.mult, ["RLAND%d" % t, "LX5", "GBH"], ["E1"])
+    op("p", mm(T.G4[:, 0:16], T.E1[:], T.DIAG[:, 0:16], True, True), ["E1", "DIAG"], ["G4"])
+    ts(T.CB[:], T.PG4[:, 0:256], 16.0, A.mult, ["PG4f"], ["CB"], -1.0, A.add)
+    tt(T.PF[:, 256:512], T.CB[:], T.PG4[:, 256:512], A.add, ["CB", "PG4f"], ["YB0"])
+    tt(T.PF[:, t:256:16], T.G4[:, 0:16], T.PF[:, t:256:16], A.add, ["G4", "YA0"], ["YA0"])
+    dma("y", [(T.yb[:], T.PF[:, 256:512])], ["YB0"], ["yb"])
+    dma("y", [(T.ya[:], T.PF[:, 0:256])], ["YA0"], ["ya"])
+    for sem in sorted(last):
+        need("g", {sem: last[sem]})

@@ -1,11 +1,13 @@
-from concourse.mybir import AluOpType, AxisListType, ActivationFunctionType
+from concourse.mybir import AluOpType, ActivationFunctionType
 
 W = 4096
-WX = 4608
 DEAD = 4096.0
-DUM = 4352
+DUM = 4112
+WX = DUM + 256
 NB, ND = 3, 3
-BAR = 4095.0 * 4096.0
+SC = 8192.0
+MAGIC = 1.5 * 2 ** 23
+NV = 72
 
 _B = {}
 
@@ -14,49 +16,40 @@ def _sb(name, cols, dtype):
     _B[name] = ("sbuf", [128, cols], dtype)
 
 
-_sb("X", WX, "bfloat16"); _sb("XC0", WX, "bfloat16"); _sb("XC1", WX, "bfloat16")
-_sb("TA", WX, "float32"); _sb("TB", WX, "float32")
-_sb("PAI", 256, "int32"); _sb("PBI", 256, "int32"); _sb("PF", 512, "float32"); _sb("PG4", 512, "float32")
-_sb("BI", 384, "int32"); _sb("BF", 448, "float32")
-_sb("WI", 8, "int32"); _sb("WF2", 8, "float32")
-_sb("CI5", 256, "int32"); _sb("CT1", 256, "int32"); _sb("CT2", 256, "int32"); _sb("CA", 512, "float32"); _sb("CB", 256, "float32")
-_sb("PI", 8, "int32"); _sb("PT", 16, "int32"); _sb("PC", 16, "float32"); _sb("CF", 256, "float32")
-_sb("WH", 512, "bfloat16"); _sb("WL", 512, "bfloat16")
-_sb("OB", 8, "bfloat16"); _sb("IDF", 128, "float32"); _sb("PEN", 128, "bfloat16"); _sb("ZB", 256, "bfloat16")
-_sb("DIAG", 256, "float32"); _sb("DG2", 256, "float32"); _sb("M1", 128, "float32"); _sb("RS1", 32, "float32")
-_sb("CL", 256, "float32"); _sb("CR", 256, "float32"); _sb("RC", 256, "float32"); _sb("TH2", 256, "float32")
-_sb("RHL", 24, "bfloat16")
-_sb("SR14", 128, "float32")
-_sb("SRB", 384, "bfloat16")
-_sb("IBN", 256, "bfloat16")
-_sb("GBH", 128, "bfloat16"); _sb("ONES", 128, "bfloat16")
-_sb("RS8", 256, "float32"); _sb("RS16", 256, "float32")
-_sb("LX1", 8, "uint16"); _sb("LX2", 16, "uint16"); _sb("LX3", 8, "uint16"); _sb("LX4", 16, "uint16"); _sb("LX5", 16, "uint16")
-_sb("LXI", 16, "int32"); _sb("LXJ", 16, "int32")
-_sb("SCOL", 4, "float32"); _sb("ABASE", 4, "float32"); _sb("ACOL", 4, "float32"); _sb("ATMP", 4, "float32")
-_sb("FBC", 16, "float32"); _sb("FB4C", 64, "float32")
+for _n in ("X", "XC0", "XC1", "TA", "TB"):
+    _sb(_n, WX, "bfloat16")
+_sb("PAI", 256, "int32"); _sb("PBI", 256, "int32"); _sb("CT1", 256, "int32")
+_sb("HL", 1024, "bfloat16"); _sb("CB", 256, "float32"); _sb("PF", 512, "float32")
+_sb("WI", 8, "int32"); _sb("WF", 8, "float32")
+_sb("PI", 8, "int32"); _sb("PT", 8, "int32"); _sb("PC", 32, "float32"); _sb("SG", 16, "float32")
+_sb("CF", 264, "float32"); _sb("LANE", 256, "float32"); _sb("C8", 128, "float32"); _sb("CB1", 128, "float32"); _sb("SPI", 128, "float32")
+_sb("WH", 256, "bfloat16"); _sb("WL", 256, "bfloat16")
+_sb("OB", 16, "bfloat16"); _sb("IDF", 128, "float32"); _sb("PEN", 264, "bfloat16"); _sb("ZB", 128, "bfloat16")
+_sb("IBN", 384, "bfloat16")
+_sb("CQ", 512, "bfloat16")
+_sb("M1", 128, "float32"); _sb("MSP", 128, "float32"); _sb("RS1", 16, "float32"); _sb("RS", 256, "float32")
+_sb("CR", 256, "bfloat16"); _sb("RC", 256 * NB, "bfloat16"); _sb("TH", 512, "float32"); _sb("SW", 144, "bfloat16")
+_sb("ONES", 128, "bfloat16"); _sb("DIAG", 256, "float32"); _sb("SRB", 256, "bfloat16"); _sb("GBH", 128, "float32"); _sb("D16", 16, "float32")
+_sb("LX1", 8, "uint16"); _sb("LX2", 8, "uint16"); _sb("LX3", 8, "uint16"); _sb("LX4", 32, "uint16"); _sb("LX5", 16, "uint16")
+_sb("LT", 64, "float32"); _sb("LXI", 16, "int32"); _sb("LXJ", 16, "int32")
+_sb("SCOL", 4, "float32"); _sb("ABASE", 8, "float32"); _sb("ACOL", 4, "float32")
 _sb("SSND", 256 * NB, "bfloat16"); _sb("SLAND", 256 * NB, "bfloat16")
-_sb("DSND", 16 * NB, "float32"); _sb("DLAND", 16 * NB, "float32")
+_sb("DSND", 16 * NB, "bfloat16"); _sb("DLAND", 16 * NB, "bfloat16")
 _sb("NSND", 256 * NB * ND, "bfloat16"); _sb("NLAND", 256 * NB * ND, "bfloat16")
 _sb("LSND", 16 * NB * ND, "uint16"); _sb("LLAND", 16 * NB * ND, "uint16")
 _sb("RSND", 32 * NB, "float32"); _sb("RLAND", 32 * NB, "float32")
-_sb("Z", 256, "bfloat16"); _sb("Z4", 1024, "bfloat16"); _sb("SH", 256, "float32")
-_sb("NI", 64, "int32"); _sb("UF", 64, "float32"); _sb("SQ", 256, "float32"); _sb("FI", 256, "int32"); _sb("CI", 256, "int32")
-_sb("OFF", 256, "uint16"); _sb("CFL", 256, "float32"); _sb("EQ", 256, "bfloat16")
+_sb("Z", 256, "bfloat16"); _sb("Z8", 2048, "bfloat16")
+_sb("NI", 128, "int32"); _sb("UF", 128, "float32"); _sb("SQ", 256, "float32"); _sb("FI", 256, "int32"); _sb("CI", 256, "int32")
+_sb("OFF", 256, "uint16"); _sb("CFL", 256, "float32"); _sb("NE", 256, "bfloat16")
 _sb("DF", 4096, "bfloat16"); _sb("AB", 4096, "bfloat16")
-_sb("R", 256, "float32"); _sb("E1", 128, "float32"); _sb("R4", 128, "float32")
-_sb("MN", 16, "float32"); _sb("YI", 16, "int32"); _sb("YA", 16, "int32"); _sb("YQ", 16, "float32"); _sb("YU", 16, "uint16")
-_sb("FB", 16, "float32"); _sb("FB4", 64, "float32"); _sb("L1", 64, "float32"); _sb("L2", 64, "int32"); _sb("LAST", 64, "int32")
-_sb("QL", 256, "bfloat16"); _sb("QR", 256, "bfloat16"); _sb("QE", 256, "bfloat16"); _sb("QO", 256, "bfloat16")
-_sb("TT", 256, "float32"); _sb("T2", 256, "float32"); _sb("FL", 16, "float32"); _sb("JK", 1280, "bfloat16")
-_sb("E2", 256, "bfloat16"); _sb("LF", 16, "float32"); _sb("UP", 256, "float32"); _sb("PG", 256, "bfloat16")
-_sb("DM", 256, "float32"); _sb("SC", 256, "float32"); _sb("PU", 16, "uint16"); _sb("E3", 512, "bfloat16"); _sb("E4", 256, "bfloat16")
-_sb("W1", 16, "float32"); _sb("W2", 16, "float32"); _sb("W3", 16, "float32"); _sb("WB", 16, "bfloat16")
-_sb("DEADL", 16, "float32"); _sb("RES", 16, "float32"); _sb("KP", 8, "float32"); _sb("KI", 8, "int32")
-for _n in ["G0", "G1", "G2", "G3", "G4", "G5", "K6", "C7"]:
+_sb("R", 256, "float32"); _sb("RI", 16, "int32"); _sb("RA", 16, "int32"); _sb("E1", 128, "float32"); _sb("DE", 128, "float32")
+_sb("R4", 128, "float32"); _sb("E2", 128, "float32"); _sb("YU", 16, "uint16")
+_sb("UP", 256, "bfloat16"); _sb("QR", 256, "bfloat16"); _sb("QO", 256, "bfloat16"); _sb("GX", 256, "bfloat16")
+_sb("FL", 2056, "float32"); _sb("JK", 1024, "bfloat16"); _sb("PG", 256, "bfloat16"); _sb("PU", 16, "uint16"); _sb("E3", 512, "bfloat16")
+_sb("WB", 16 * ND, "bfloat16"); _sb("RES", 16, "float32"); _sb("W1", 16, "float32"); _sb("W2", 16, "float32"); _sb("W3", 16, "float32")
+_sb("KP", 8, "float32"); _sb("KJ", 16, "float32"); _sb("KI", 8, "int32")
+for _n in ["G0", "G1", "G2", "G3", "G4", "K6", "C7", "LB"]:
     _B[_n] = ("psum", [128, 512], "float32")
-_B["BD"] = ("dram", [14, 128, 32], "float32")
-_B["PD"] = ("dram", [4, 128, 256], "float32")
 SCRATCH = _B
 
 _MSG = []
@@ -73,8 +66,6 @@ def rank_program(g, core, T, topo):
         return
     A = AluOpType
     F = ActivationFunctionType
-    RH, RL0, RL1 = T.RHL[:, 0:8], T.RHL[:, 8:16], T.RHL[:, 16:24]
-    SRP, SRH, SRL = [T.SRB[:, 128 * i:128 * i + 128] for i in range(3)]
     n_ranks = len(T.cores)
     nxt, prv = (rank + 1) % n_ranks, (rank - 1) % n_ranks
     Q = {"v": g.vector, "s": g.scalar, "p": g.tensor, "g": g, "y": g.sync}
@@ -82,6 +73,7 @@ def rank_program(g, core, T, topo):
     waited = {q: {} for q in Q}
     wr = {}
     rd = {}
+    bank = {}
     nd = [0]
     last = {}
 
@@ -93,28 +85,30 @@ def rank_program(g, core, T, topo):
 
     def deps(reads, writes, own=None):
         toks = {}
-        for k in reads:
-            for s, v in wr.get(k, {}).items():
-                toks[s] = max(toks.get(s, 0), v)
-        for k in writes:
-            for m in (wr, rd):
-                for s, v in m.get(k, {}).items():
-                    if s != own:
-                        toks[s] = max(toks.get(s, 0), v)
+        for k in reads + writes:
+            if k[0] == "@":
+                ms_ = [{s: v for s, v in bank.get(k, {}).items() if s != own}]
+            else:
+                ms_ = [wr.get(k, {})] + ([rd.get(k, {})] if k in writes else [])
+            for m in ms_:
+                for s, v in m.items():
+                    toks[s] = max(toks.get(s, 0), v)
         return toks
 
     def note(reads, writes, sem, val):
-        for k in writes:
-            wr[k] = {sem: val}
-            rd[k] = {}
-        for k in reads:
-            if k not in writes:
+        for k in reads + writes:
+            if k[0] == "@":
+                bank.setdefault(k, {})[sem] = val
+            elif k in writes:
+                wr[k] = {sem: val}
+                rd[k] = {}
+            else:
                 m = rd.setdefault(k, {})
                 m[sem] = max(m.get(sem, 0), val)
         last[sem] = max(last.get(sem, 0), val)
 
-    def op(q, fns, reads, writes, acc=False):
-        need(q, deps(reads, writes, "c" + q if acc else None))
+    def op(q, fns, reads, writes):
+        need(q, deps(reads, writes, "c" + q))
         for fn in (fns if isinstance(fns, list) else [fns]):
             cnt[q] += 1
             fn().then_inc(T.sem["c" + q], 1)
@@ -128,23 +122,18 @@ def rank_program(g, core, T, topo):
             Q[q].dma_start(out, in_).then_inc(T.sem[sem], 16)
         note(reads, writes, sem, 16 * len(pieces))
 
-    def engs(src, dst):
-        e = topo.engines(src, dst)
-        m = 0
-        for x in e:
-            m |= 1 << x
-        return m, len(e)
-
     def send(to, msg, out, in_, reads):
         need("g", deps(reads, []))
         dst = T.cores[to]
         rid, pid, _se = topo.addr(dst)
-        m, n = engs(core, dst)
-        g.remote_dma(out, in_, T.sem["rx" + msg], T.sem["tx" + msg], pid, rid, m)
-        note(reads, [], "tx" + msg, n)
+        g.remote_dma(out, in_, T.sem["rx" + msg], T.sem["tx" + msg], pid, rid, topo.mask(core, dst))
+        note(reads, [], "tx" + msg, len(topo.engines(core, dst)))
 
     def landed(frm, msg, keys):
-        note([], keys, "rx" + msg, engs(T.cores[frm], core)[1])
+        note([], keys, "rx" + msg, len(topo.engines(T.cores[frm], core)))
+
+    def join(key, parts):
+        wr[key] = deps(parts, [])
 
     def ts(out, in0, s1, o0, r, w, s2=None, o1=None):
         if o1 is None:
@@ -167,440 +156,463 @@ def rank_program(g, core, T, topo):
     def act(out, in_, f, r, w, **kw):
         op("s", lambda: g.scalar.activation(out, in_, f, **kw), r, w)
 
+    def iota(out, pattern, base, mult, key):
+        if out.dtype == "int32" or key in ("PI",):
+            op("g", lambda: g.iota(out, pattern, base, mult), [], [key])
+        else:
+            op("g", lambda: g.iota(out, pattern, base, mult, allow_small_or_imprecise_dtypes=True), [], [key])
+
     def mm(out, lhsT, rhs, start, stop):
         return lambda: g.tensor.matmul(out, lhsT, rhs, start, stop)
 
-    def row_to_list(src, lhsT, rows, bank, bkey, fin, *between):
-        op("p", mm(bank[:, 0:256], lhsT, src, True, True), rows, [bkey])
-        tt(T.DM[:], bank[:, 0:256], T.DIAG[:], A.mult, [bkey, "DIAG"], ["DM"])
-        for f in between[0:1]:
-            f()
-        scan(T.SC[:], T.RS16[:], T.DM[:], A.mult, A.add, ["RS16", "DM"], ["SC"])
-        for f in between[1:]:
-            f()
-        fin(T.SC[:, 15:256:16])
+    IB, IN, IH = T.IBN[:, 0:128], T.IBN[:, 128:256], T.IBN[:, 256:384]
 
-    def dead_done(t):
-        def fin(ap):
-            ts(T.DSND[:, 16 * t:16 * t + 16], ap, 1.0, A.min, ["SC"], ["DSND%d" % t], DEAD, A.mult)
-            send(nxt if t % 2 == 0 else prv, "e%d" % t, T.DLAND[:, 16 * t:16 * t + 16], T.DSND[:, 16 * t:16 * t + 16], ["DSND%d" % t])
-        return fin
+    def to_list(cols, keys):
+        op("p", [mm(T.C7[:, 32:48], T.SW[:, 16 - b:144 - b], cols(b), b == 0, b == 15) for b in range(16)], ["SW"] + keys, ["@C7"])
 
-    def start_batch(t):
-        to = nxt if t % 2 == 0 else prv
-        act(T.SSND[:, 256 * t:256 * t + 256], T.X[:, t:W:16], F.Copy, ["X"], ["SSND%d" % t])
-        send(to, "s%d" % t, T.SLAND[:, 256 * t:256 * t + 256], T.SSND[:, 256 * t:256 * t + 256], ["SSND%d" % t])
-        xc = T.XC0 if t % 2 == 0 else T.XC1
-        send(to, "b%d" % t, xc[:, 0:W], T.X[:, 0:W], ["X"])
+    def starters_send(t):
+        s = T.SSND[:, 256 * t:256 * t + 256]
+        cp(s[:, 0:256:2], T.X[:, t:W // 2:16], ["X"], ["SS0_%d" % t])
+        act(s[:, 1:256:2], T.X[:, W // 2 + t:W:16], F.Copy, ["X"], ["SS1_%d" % t])
+        send(nxt if t % 2 == 0 else prv, "s%d" % t, T.SLAND[:, 256 * t:256 * t + 256], s, ["SS0_%d" % t, "SS1_%d" % t])
         landed(prv if t % 2 == 0 else nxt, "s%d" % t, ["SLAND%d" % t])
+
+    def dead_list(t):
+        near, nk = (T.TA, "TA") if t % 2 == 0 else (T.TB, "TB")
+        to_list(lambda b: near[:, 2048 * (b % 2) + 16 * (b // 2) + t:2048 * (b % 2) + 2048:128], [nk])
+
+    def dead_send(t):
+        to = nxt if t % 2 == 0 else prv
+        e = T.DSND[:, 16 * t:16 * t + 16]
+        ts(e, T.C7[:, 32:48], 1.0, A.min, ["@C7"], ["DSND%d" % t], DEAD, A.mult)
+        send(to, "e%d" % t, T.DLAND[:, 16 * t:16 * t + 16], e, ["DSND%d" % t])
+        landed(prv if t % 2 == 0 else nxt, "e%d" % t, ["DLAND%d" % t])
+
+    def records_send(t):
+        xc = T.XC0 if t % 2 == 0 else T.XC1
+        send(nxt if t % 2 == 0 else prv, "b%d" % t, xc[:, 0:W], T.X[:, 0:W], ["X"])
 
     def near_send(t):
         hi, lo = T.RSND[:, 32 * t:32 * t + 16], T.RSND[:, 32 * t + 16:32 * t + 32]
+        home = prv if t % 2 == 0 else nxt
+        ts(T.W1[:], T.RES[:], DEAD, A.is_lt, ["RES"], ["W1"])
         if t == NB - 1:
-            cp(hi, T.RES[:], ["RES"], ["RSH%d" % t])
-            send(prv if t % 2 == 0 else nxt, "r%d" % t, T.RLAND[:, 32 * t:32 * t + 16], hi, ["RSH%d" % t])
+            ts(T.W2[:], T.RES[:], 1.0, A.add, ["RES"], ["W2"])
+            tt(hi, T.W1[:], T.W2[:], A.mult, ["W1", "W2"], ["RSH%d" % t])
+            send(home, "r%d" % t, T.RLAND[:, 32 * t:32 * t + 16], hi, ["RSH%d" % t])
             return
-        ts(T.LXJ[:], T.RES[:], -1.0, A.add, ["RES"], ["LXJ"])
+        cp(T.LXJ[:], T.RES[:], ["RES"], ["LXJ"])
+        ts(T.W2[:], T.RES[:], 1.0, A.add, ["RES"], ["W2"])
         ts(T.LXI[:], T.LXJ[:], 4, A.arith_shift_right, ["LXJ"], ["LXI"])
-        ts(hi, T.LXI[:], 0.0, A.max, ["LXI"], ["RSH%d" % t])
+        tt(T.W3[:], T.W1[:], T.W2[:], A.mult, ["W1", "W2"], ["W3"])
+        tt(hi, T.LXI[:], T.W1[:], A.mult, ["LXI", "W1"], ["RSH%d" % t])
         ts(T.W2[:], hi, -16.0, A.mult, ["RSH%d" % t], ["W2"])
-        tt(lo, T.RES[:], T.W2[:], A.add, ["RES", "W2"], ["RSL%d" % t])
-        send(prv if t % 2 == 0 else nxt, "r%d" % t, T.RLAND[:, 32 * t:32 * t + 32], T.RSND[:, 32 * t:32 * t + 32], ["RSH%d" % t, "RSL%d" % t])
+        tt(lo, T.W3[:], T.W2[:], A.add, ["W3", "W2"], ["RSL%d" % t])
+        send(home, "r%d" % t, T.RLAND[:, 32 * t:32 * t + 32], T.RSND[:, 32 * t:32 * t + 32], ["RSH%d" % t, "RSL%d" % t])
 
-    def near_rows(t):
-        landed(nxt if t % 2 == 0 else prv, "r%d" % t, ["RLAND%d" % t])
-        for i in range(2):
-            tt(T.E3[:, 256 * i:256 * i + 256], T.RLAND[:, 32 * t + 16 * i:32 * t + 16 * i + 16].indirect(T.LX4[:]), T.DIAG[:], A.mult,
-               ["RLAND%d" % t, "LX4", "DIAG"], ["E3_%d" % i])
-        op("p", [mm(T.G4[:, 0:256], SRH, T.E3[:, 0:256], True, False), mm(T.G4[:, 0:256], SRL, T.E3[:, 256:512], False, True)],
-           ["SRH", "SRL", "E3_0", "E3_1"], ["G4"])
+    def near_rows(t, i):
+        if i == 0:
+            landed(nxt if t % 2 == 0 else prv, "r%d" % t, ["RLAND%d" % t])
+        tt(T.E3[:, 256 * i:256 * i + 256], T.RLAND[:, 32 * t:32 * t + 32].indirect(T.LX4[:, 16 * i:16 * i + 16]), T.DIAG[:], A.mult,
+           ["RLAND%d" % t, "LX4", "DIAG"], ["E3_%d" % i])
+        if i == 1:
+            op("p", [mm(T.LB[:, 0:256], T.SRB[:, 128 * h:128 * h + 128], T.E3[:, 256 * h:256 * h + 256], h == 0, h == 1) for h in range(2)],
+               ["SRB0", "SRB1", "E3_0", "E3_1"], ["@LB"])
 
     def near_add(t):
         near, nk = (T.TA, "TA") if t % 2 == 0 else (T.TB, "TB")
-        tt(near[:, t:W:16], T.G4[:, 0:256], near[:, t:W:16], A.add, ["G4", nk], [nk])
+        tt(near[:, t:W:16], T.LB[:, 0:256], near[:, t:W:16], A.add, ["@LB", nk], [nk])
 
-    dma("s", [(T.PAI[:], T.pa[:])], [], ["PAI"])
-    dma("y", [(T.X[:, 0:W], T.x[:])], [], ["X"])
-    dma("s", [(T.PBI[:], T.pb[:])], [], ["PBI"])
+    dma("y", [(T.X[:, 0:W], T.x[:])], [], ["Xd"])
     dma("s", [(T.WI[:, 0:1], T.wt[:])], [], ["WI"])
+    dma("s", [(T.PAI[:], T.pa[:])], [], ["PAI"])
+    dma("s", [(T.PBI[:], T.pb[:])], [], ["PBI"])
     op("g", lambda: g.iota(T.PI[:, 0:1], [[0, 1]], 0, 1), [], ["PI"])
-    op("g", lambda: g.iota(T.BI[:, 0:32], [[1, 32]], 0, 32), [], ["BI0"])
-    op("g", lambda: g.iota(T.CI5[:], [[1, 256]], 0, 0), [], ["CI5"])
-    op("g", lambda: g.iota(T.LXI[:, 0:8], [[32, 8]], 7, 0), [], ["LXI"])
-    for nm in ("X", "XC0", "XC1"):
-        op("g", lambda: g.iota(T[nm][:, W:WX], [[0, WX - W]], 0, 0, allow_small_or_imprecise_dtypes=True), [], [nm + "x"])
-    for c, k, v in [(0, "s", 4), (1, "a", 15), (2, "a", 3), (3, "s", 2)]:
-        ts(T.PT[:, c:c + 1], T.PI[:, 0:1], v, A.arith_shift_right if k == "s" else A.bitwise_and, ["PI"], ["PT%d" % c])
-    cp(T.PC[:, 0:4], T.PT[:, 0:4], ["PT0", "PT1", "PT2", "PT3"], ["PC0"])
-    cp(T.PC[:, 4:5], T.PI[:, 0:1], ["PI"], ["PC4"])
-    PGRP, PLOW, PL3, PS2, PP = T.PC[:, 0:1], T.PC[:, 1:2], T.PC[:, 2:3], T.PC[:, 3:4], T.PC[:, 4:5]
-    for i, r in enumerate((12, 13, 14, 15)):
-        ts(T.PC[:, 8 + i:9 + i], PLOW, float(r), A.is_equal, ["PC0"], ["PC%d" % (8 + i)])
-    I12, I13, I14, I15 = [T.PC[:, 8 + i:9 + i] for i in range(4)]
-    ts(T.PT[:, 4:5], T.PI[:, 0:1], 4, A.arith_shift_right, ["PI"], ["PT4"], 1, A.bitwise_and)
-    ECOL, OCOL = T.WF2[:, 6:7], T.WF2[:, 5:6]
-    for f in range(1, 12):
-        ts(T.BI[:, 32 * f:32 * f + 32], T.BI[:, 0:32], f, A.arith_shift_right, ["BI0"], ["BI%d" % f], 1, A.bitwise_and)
-    ts(T.BI[:, 0:32], T.BI[:, 0:32], 1, A.bitwise_and, ["BI0"], ["BI0"])
-    ts(T.BF[:, 0:384], T.BI[:], 2.0, A.mult, ["BI%d" % f for f in range(12)], ["BFA"], -1.0, A.add)
-    ms(T.BF[:, 384:448], 1.0, ["BFB"])
-    dma("y", [(T.BD[f], T.BF[:, 32 * f:32 * f + 32]) for f in range(14)], ["BFA", "BFB"], ["BD"])
-    ts(T.CT1[:], T.CI5[:], 15, A.bitwise_and, ["CI5"], ["CT1"])
-    ts(T.CT2[:], T.CI5[:], 4, A.arith_shift_right, ["CI5"], ["CT2"])
-    ts(T.GBH[:], T.CT2[:, 0:128], PGRP, A.is_equal, ["CT2", "PC0"], ["GBH"])
-    ts(T.DG2[:], T.CT2[:], PLOW, A.is_equal, ["CT2", "PC0"], ["DG2"])
-    ms(T.CA[:, 0:16], 0.0, ["CA"])
-    ts(T.LX5[:], T.CA[:, 0:16], PLOW, A.add, ["CA", "PC0"], ["LX5"])
-    ts(T.W1[:], T.PAI[:, 0:256:16], 0.0, A.is_ge, ["PAI"], ["W1"])
-    tt(T.E4[:], T.W1[:, 0:16].indirect(T.LX5[:]), T.DG2[:], A.mult, ["W1", "LX5", "DG2"], ["E4"])
-    ts(T.RS16[:], T.CT1[:], 0.0, A.not_equal, ["CT1"], ["RS16"])
-    ts(T.DIAG[:], T.CT1[:], PLOW, A.is_equal, ["CT1", "PC0"], ["DIAG"])
-    row_to_list(T.E4[:], T.GBH[:], ["E4", "GBH"], T.G3, "G3", dead_done(0))
-    start_batch(0)
-    wr["X"] = deps(["X", "Xx"], [])
-    def table_rows(pin, pk, i):
-        hi, lo = T.PF[:, 256 * i:256 * i + 256], T.PG4[:, 256 * i:256 * i + 256]
-        ts(T.CT1[:], pin[:], 4, A.arith_shift_right, [pk], ["CT1"])
-        ts(hi, T.CT1[:], 0.0, A.max, ["CT1"], ["PF%d" % i])
-        ts(T.CB[:], hi, -16.0, A.mult, ["PF%d" % i], ["CB"], 1.0, A.add)
-        tt(lo, T.CB[:], pin[:], A.add, ["CB", pk], ["PG4%d" % i])
-        dma("y", [(T.PD[2 * i], hi), (T.PD[2 * i + 1], lo)], ["PF%d" % i, "PG4%d" % i], ["PD%d" % i])
-
-    def fill_table(tab, key, pv, pf, pk):
-        pieces = [(tab[16 * b:16 * b + 14, 0:W], T.BD[:]) for b in range(8)]
-        pieces += [(tab[15:128:16, 0:W], pv), (tab[14:128:16, 0:W], pf)]
-        dma("y", pieces, ["BD", pk], [key])
-
-    table_rows(T.PBI, "PBI", 0)
-    fill_table(T.TB, "TBd", T.PD[0], T.PD[1], "PD0")
+    for key, pattern, base, mult in (("CF", [[1, 264]], 0, 0), ("C8", [[1, 16], [0, 8]], 0, 0), ("LANE", [[1, 128], [128, 2]], 0, 0),
+                                     ("CB1", [[0, 8], [1, 8], [0, 2]], 0, 0), ("SPI", [[0, 64], [1, 2]], DUM, 2)):
+        op("g", lambda: g.iota(T[key][:], pattern, base, mult, allow_small_or_imprecise_dtypes=True), [], [key])
+    ms(T.TA[:, 0:1], 1.0, ["TAb"])
+    ms(T.X[:, W:WX], 0.0, ["Xx"])
+    join("X", ["Xd", "Xx"])
+    for c, (sh, mask) in enumerate(((4, 7), (0, 15), (0, 7), (3, 15), (0, 1), (3, 1), (4, 1), (0, 127))):
+        ts(T.PT[:, c:c + 1], T.PI[:, 0:1], sh, A.arith_shift_right, ["PI"], ["PT%d" % c], mask, A.bitwise_and)
+    ms(T.ZB[:], 0.0, ["ZB"])
+    cp(T.PC[:, 0:8], T.PT[:, 0:8], ["PT%d" % c for c in range(8)], ["PC"])
+    PGRP, PLOW, PL7, P8, P1, PLL, OCOL, PP = [T.PC[:, c:c + 1] for c in range(8)]
+    ms(T.RS[:], -2.0 ** 26, ["RS"])
+    ts(T.LT[:, 0:12], T.CF[:, 0:12], PLOW, A.not_equal, ["CF", "PC"], ["LT"], 2.0, A.mult)
+    ts(T.PC[:, 8:12], T.CF[:, 12:16], PLOW, A.is_equal, ["CF", "PC"], ["PCI"])
+    I12, I14, I15 = T.PC[:, 8:9], T.PC[:, 10:11], T.PC[:, 11:12]
+    ts(T.SG[:, 0:12], T.LT[:, 0:12], -1.0, A.add, ["LT"], ["SG"])
+    for r in range(11):
+        n = 1 << r
+        act(T.TA[:, n:2 * n], T.TA[:, 0:n], F.Copy, ["TAb", "SG"], ["TAb"], scale=T.SG[:, r:r + 1])
+    act(T.TA[:, 2048:W], T.TA[:, 0:2048], F.Copy, ["TAb", "SG"], ["TAc"], scale=T.SG[:, 11:12])
+    ts(T.PC[:, 12:13], PGRP, 2.0, A.mult, ["PC"], ["PC12"])
+    ts(T.PC[:, 13:14], PGRP, 2.0, A.mult, ["PC"], ["PC13"], 1.0, A.add)
+    ts(T.PC[:, 14:15], PGRP, 16.0, A.mult, ["PC"], ["PC14"], 16.0, A.add)
+    ts(T.PC[:, 15:16], I15, 16.0, A.mult, ["PCI"], ["PC15"], I14, A.add)
     ts(T.WI[:, 2:3], T.WI[:, 0:1], 3840, A.bitwise_and, ["WI"], ["WI2"])
     ts(T.WI[:, 3:4], T.WI[:, 0:1], 255, A.bitwise_and, ["WI"], ["WI3"])
-    ts(T.WF2[:, 0:2], T.WI[:, 2:4], 1.0 / 4096, A.mult, ["WI2", "WI3"], ["WF2"])
-    ts(T.CA[:, 0:128], T.CT2[:, 0:128], PGRP, A.is_equal, ["CT2", "PC0"], ["CA"], 100.0, A.mult)
-    ts(T.CT1[:, 0:128], T.CI5[:, 0:128], 2, A.arith_shift_right, ["CI5"], ["CT1"], 3, A.bitwise_and)
-    tt(T.CB[:, 0:128], T.CT1[:, 0:128], T.CA[:, 0:128], A.add, ["CT1", "CA"], ["CB"])
-    for ll in range(4):
-        for wm, wc in ((T.WH, 0), (T.WL, 1)):
-            ts(wm[:, 128 * ll:128 * ll + 128], T.CB[:, 0:128], 100.0 + ll, A.is_equal, ["CB", "WF2"], ["WHL%d%d" % (ll, wc)], T.WF2[:, wc:wc + 1], A.mult)
-    WHL = ["WHL%d%d" % (i, j) for i in range(4) for j in range(2)]
-    ts(T.M1[:], T.CT1[:, 0:128], PL3, A.is_equal, ["CT1", "PC0"], ["M1"])
-    for ch in range(4):
-        ts(T.SCOL[:, ch:ch + 1], PL3, 32.0, A.mult, ["PC0"], ["SCOL"], 128.0 * ch + 16.0, A.add)
-    tt(T.ATMP[:], T.SCOL[:], T.SCOL[:], A.mult, ["SCOL"], ["ATMP"])
-    ts(T.ABASE[:], T.ATMP[:], -1.0, A.mult, ["ATMP"], ["ABASE"], 262144.0 - 12.0, A.add)
-    ts(T.ACOL[:], T.ABASE[:], 0.0, A.add, ["ABASE"], ["ACOL"])
-    cp(T.CF[:], T.CI5[:], ["CI5"], ["CF"])
-    ts(T.IDF[:], T.CF[:, 0:128], PP, A.is_equal, ["CF", "PC4"], ["IDF"])
-    ts(T.PC[:, 12:13], PLOW, 12.0, A.is_lt, ["PC0"], ["PC12"])
-    ts(T.PC[:, 7:8], I12, -1.0, A.mult, ["PC8"], ["PC7"])
-    ts(T.PC[:, 13:14], T.PC[:, 12:13], 128.0, A.mult, ["PC12", "PC8"], ["PC13"], I12, A.add)
-    ts(T.PC[:, 14:15], I14, 2048.0, A.mult, ["PC10"], ["PC14"])
-    tt(T.PC[:, 13:14], T.PC[:, 13:14], T.PC[:, 14:15], A.add, ["PC13", "PC14"], ["PC13"])
-    ts(T.PC[:, 15:16], T.PC[:, 12:13], I13, A.add, ["PC12", "PC9", "PC10"], ["PC15"], I14, A.add)
-    ts(T.WF2[:, 4:5], PLOW, 14.0, A.is_lt, ["PC0", "PC10"], ["WF4"], -2.0, A.mult)
-    tt(T.WF2[:, 4:5], T.WF2[:, 4:5], I14, A.add, ["WF4", "PC10"], ["WF4"])
-    ts(T.WF2[:, 3:4], I15, 16.0, A.mult, ["PC11", "PC10"], ["WF3"], I14, A.add)
-    cp(T.WF2[:, 5:6], T.PT[:, 4:5], ["PT4"], ["WF5"])
-    ts(T.WF2[:, 6:7], T.WF2[:, 5:6], -1.0, A.mult, ["WF5"], ["WF6"], 1.0, A.add)
-    ts(T.OB[:], T.CF[:, 0:8], PGRP, A.is_equal, ["CF", "PC0"], ["OB"], 4096.0, A.mult)
-    ms(T.ZB[:], 0.0, ["ZB"])
-    ts(T.CT1[:], T.CI5[:], 7, A.bitwise_and, ["CI5"], ["CT1"])
-    ts(T.RS8[:], T.CT1[:], 0.0, A.is_equal, ["CT1"], ["RS8"], float(2 ** 26), A.mult)
-    ts(T.RS1[:], T.CF[:, 0:32], PS2, A.is_equal, ["CF", "PC0"], ["RS1"])
-    ts(T.PC[:, 5:6], PL3, 8.0, A.mult, ["PC0"], ["PC5"])
-    ts(T.LX1[:], T.LXI[:, 0:8], T.PC[:, 5:6], A.add, ["LXI", "PC5"], ["LX1"])
-    ts(T.PT[:, 6:7], T.PI[:, 0:1], 2, A.arith_shift_right, ["PI"], ["PT6"], 3, A.bitwise_and)
-    ts(T.PC[:, 6:7], T.PT[:, 6:7], 8.0, A.mult, ["PT6"], ["PC6"])
-    ts(T.LX3[:], T.LXI[:, 0:8], T.PC[:, 6:7], A.add, ["LXI", "PC6"], ["LX3"])
-    ms(T.FBC[:], 16777215.0, ["FBC"])
-    ms(T.FB4C[:], 16777215.0, ["FB4C"])
-    act(T.IBN[:, 0:128], T.IDF[:], F.Identity, ["IDF"], ["IBN0"])
-    act(T.IBN[:, 128:256], T.IDF[:], F.Identity, ["IDF"], ["IBN1"], scale=-1.0)
-    act(T.CL[:], T.CF[:], F.Identity, ["CF", "PC9", "PC13"], ["CL"], scale=I13, bias=T.PC[:, 13:14])
-    act(T.CR[:], T.CF[:], F.Identity, ["CF", "PC7", "PC15"], ["CR"], scale=T.PC[:, 7:8], bias=T.PC[:, 15:16])
-    for i in range(2):
-        act(T.TB[:, W + 256 * i:W + 256 * i + 256], T.CF[:], F.Identity, ["CF", "PC10"], ["TBx%d" % i], scale=0.0, bias=I14)
-    wr["TB"] = deps(["TBd", "TBx0", "TBx1"], [])
+    ts(T.SW[:], T.CF[:, 0:144], T.PC[:, 14:15], A.is_equal, ["CF", "PC14", "PC15"], ["SW"], T.PC[:, 15:16], A.mult)
+    ts(T.WF[:, 0:2], T.WI[:, 2:4], 1.0 / 4096, A.mult, ["WI2", "WI3"], ["WF"])
 
-    def scalar_constants():
-        act(T.PEN[:], T.IDF[:], F.Identity, ["IDF"], ["PEN"], scale=float(2 ** 25))
-        act(T.RC[:], T.CF[:], F.Identity, ["CF", "PC11", "WF4"], ["RC"], scale=I15, bias=T.WF2[:, 4:5])
-        act(SRP, T.GBH[:], F.Identity, ["GBH", "WF3"], ["SRP"], scale=T.WF2[:, 3:4])
-        act(T.SR14[:], T.GBH[:], F.Identity, ["GBH", "PC10"], ["SR14"], scale=I14)
+    def table_rows(pin, pk, i):
+        hi, lo = T.HL[:, 512 * i:512 * i + 256], T.HL[:, 512 * i + 256:512 * i + 512]
+        return (lambda: ts(T.CT1[:], pin[:], 4, A.arith_shift_right, [pk], ["CT1"]),
+                lambda: ts(hi, T.CT1[:], 0.0, A.max, ["CT1"], ["HI%d" % i]),
+                lambda: ts(T.CB[:], hi, -16.0, A.mult, ["HI%d" % i], ["CB"], 1.0, A.add),
+                lambda: tt(lo, T.CB[:], pin[:], A.add, ["CB", pk], ["LO%d" % i]))
+
+    def fill_rows(tab, key, i, after):
+        dma("y", [(tab[15:128:16, 0:W], T.HL[:, 512 * i:512 * i + 256]), (tab[14:128:16, 0:W], T.HL[:, 512 * i + 256:512 * i + 512])],
+            ["HI%d" % i, "LO%d" % i], after + [key])
+
+    rows_a, rows_b = table_rows(T.PAI, "PAI", 0), table_rows(T.PBI, "PBI", 1)
+    for ll in range(2):
+        rows_a[2 * ll]()
+        ts(T.WH[:, 128 * ll:128 * ll + 128], T.C8[:], T.PC[:, 12 + ll:13 + ll], A.is_equal, ["C8", "PC12", "PC13", "WF"], ["WH%d" % ll], T.WF[:, 0:1], A.mult)
+        rows_a[2 * ll + 1]()
+        ts(T.WL[:, 128 * ll:128 * ll + 128], T.C8[:], T.PC[:, 12 + ll:13 + ll], A.is_equal, ["C8", "PC12", "PC13", "WF"], ["WL%d" % ll], T.WF[:, 1:2], A.mult)
+    WHL = ["WH0", "WH1", "WL0", "WL1"]
+    for ch in range(2):
+        ts(T.SCOL[:, ch:ch + 1], PL7, 32.0, A.mult, ["PC"], ["SCOL%d" % ch], 256.0 * ch + 16.0, A.add)
+    ts(T.IDF[:], T.CF[:, 0:128], PP, A.is_equal, ["CF", "PC"], ["IDF"])
+    tt(T.SCOL[:, 2:4], T.SCOL[:, 0:2], T.SCOL[:, 0:2], A.mult, ["SCOL0", "SCOL1"], ["SCOL2"])
+    ts(IB, T.CF[:, 0:128], PP, A.is_equal, ["CF", "PC"], ["IB"])
+    for d in range(ND):
+        ts(T.ABASE[:, 2 * d:2 * d + 2], T.SCOL[:, 2:4], -1.0, A.mult, ["SCOL2"], ["ABASE%d" % d], 262144.0 - 12.0 + 32.0 * 97 * d, A.add)
+    ts(IN, T.CF[:, 0:128], PP, A.is_equal, ["CF", "PC"], ["IN"], -1.0, A.mult)
+    cp(T.ACOL[:, 0:2], T.ABASE[:, 0:2], ["ABASE0"], ["ACOL0", "ACOL1"])
+    starters_send(0)
+    cp(T.TB[:, 0:2048], T.TA[:, 0:2048], ["TAb"], ["TBb"])
+    ts(T.TB[:, 2048:W], T.TA[:, 0:2048], T.SG[:, 11:12], A.mult, ["TAb", "SG"], ["TBc"])
+    fill_rows(T.TA, "TAd", 0, ["TAb", "TAc"])
+    ts(T.PC[:, 16:17], I14, 40.0, A.mult, ["PCI"], ["PC16"])
+    for i in range(4):
+        rows_b[i]()
+        ts(T.OB[:, 8 * (i % 2):8 * (i % 2) + 8], T.CF[:, 0:8], PGRP, A.is_equal, ["CF", "PC"], ["OB%d" % (i % 2)], 4096.0 * (1 - 2 * (i % 2)), A.mult) if i < 2 else None
+        ms(T["XC%d" % (i - 2)][:, W:WX], 0.0, ["XC%dx" % (i - 2)]) if i >= 2 else None
+    fill_rows(T.TB, "TBd", 1, ["TBb", "TBc"])
+    for tab in ("TA", "TB"):
+        act(T[tab][:, W:WX], T.X[:, W:WX], F.Identity, ["Xx", "PC16"], [tab + "x"], bias=T.PC[:, 16:17])
+        join(tab, [tab + "d", tab + "x"])
+    dead_list(0)
+    ms(T.RS[:, 0:256:16], 2.0 ** 26, ["RS"])
+    ts(T.M1[:], T.CB1[:], PL7, A.is_equal, ["CB1", "PC"], ["M1"])
+    ts(T.RS1[:], T.CF[:, 0:16], P8, A.is_equal, ["CF", "PC"], ["RS1"])
+    ts(T.LX1[:], T.CF[:, 0:16:2], P1, A.add, ["CF", "PC"], ["LX1"])
+    ts(T.LX3[:], T.CF[:, 0:16:2], PLL, A.add, ["CF", "PC"], ["LX3"])
+    tt(T.MSP[:], T.M1[:], T.SPI[:], A.mult, ["M1", "SPI"], ["MSP"])
+    ts(T.PC[:, 17:18], PLOW, 12.0, A.is_lt, ["PC"], ["PC17"], 128.0 * SC, A.mult)
+    ts(T.PC[:, 18:19], I12, -SC, A.mult, ["PCI"], ["PC18"])
+    ts(T.PC[:, 20:23], T.CF[:, 1:4], I14, A.mult, ["CF", "PCI"], ["PC20"])
+    ts(T.PC[:, 19:20], I14, SC, A.mult, ["PCI", "PC17"], ["PC19"], T.PC[:, 17:18], A.add)
+    ts(T.PC[:, 23:24], PP, 2.0, A.mult, ["PC"], ["PC23"], 1.0, A.add)
+    ms(T.TH[:], 0.0, ["TH"])
+    act(T.CR[:], T.LANE[:], F.Identity, ["LANE", "PC18", "PC19"], ["CR"], scale=T.PC[:, 18:19], bias=T.PC[:, 19:20])
+    for t in range(NB):
+        act(T.RC[:, 256 * t:256 * t + 256], T.LANE[:], F.Identity, ["LANE", "PCI", "PC20"], ["RC%d" % t], scale=I15, bias=T.PC[:, 20 + t:21 + t])
+    act(IH, T.IDF[:], F.Copy, ["IDF"], ["IH"], scale=0.5)
+    ts(T.PEN[:], T.CF[:], T.PC[:, 23:24], A.is_equal, ["CF", "PC23"], ["PEN"], -2.0 ** 24, A.mult)
+    ms(T.CQ[:, 0:256], -0.5, ["CQ0"])
+    ms(T.CQ[:, 256:512], 2 * MAGIC, ["CQ1"])
+    ts(T.TH[:, 255:256], PP, SC, A.mult, ["PC", "TH"], ["TH1"], (128 - 1536) * SC, A.add)
+    for c in (383, 511):
+        ts(T.TH[:, c:c + 1], PP, SC, A.mult, ["PC", "TH"], ["TH%d" % c], -1536 * SC, A.add)
+    join("THS", ["TH", "TH1", "TH383", "TH511"])
+    for i, (c0, step, base) in enumerate(((0, 512.0, 383.0), (1, 512.0, 511.0), (8, 512.0, 255.0), (9, 1.0, 2048.0))):
+        ts(T.LT[:, 16 + c0:16 + c0 + 7:2], T.CF[:, 0:4], step, A.mult, ["CF"], ["LT%d" % i], base, A.add)
+    ms(T.ONES[:], 1.0, ["ONES"])
+    ms(T.FL[:, 2048:2056], 0.0, ["FL4", "FL5", "FL6", "FL7"])
+    tt(T.LT[:, 32:40], T.LT[:, 24:32], T.LT[:, 16:24], A.subtract, ["LT0", "LT1", "LT2", "LT3"], ["LT4"])
+    dead_send(0)
+    records_send(0)
+    ts(T.LT[:, 40:48], T.LT[:, 32:40], P1, A.mult, ["LT4", "PC"], ["LT5"])
+    ts(T.GBH[:], T.C8[:], T.PC[:, 12:13], A.subtract, ["C8", "PC12"], ["GBH"])
+    tt(T.LT[:, 32:40], T.LT[:, 40:48], T.LT[:, 16:24], A.add, ["LT5", "LT0", "LT1"], ["LT4"])
+    cp(T.LX2[:], T.LT[:, 32:40], ["LT4"], ["LX2"])
+
+    def late_constants():
+        yield lambda: ts(T.CB[:, 0:128], T.GBH[:], 0.0, A.is_ge, ["GBH"], ["CB"])
+        yield lambda: ts(T.CB[:, 128:256], T.GBH[:], 1.0, A.is_le, ["GBH"], ["CBb"])
+        yield lambda: tt(T.GBH[:], T.CB[:, 0:128], T.CB[:, 128:256], A.mult, ["CB", "CBb"], ["GBH"])
+        yield lambda: cp(T.CT1[:], T.CF[:, 0:256], ["CF"], ["CT1"])
+        yield lambda: ts(T.PAI[:], T.CT1[:], 7, A.bitwise_and, ["CT1"], ["PAI"])
+        yield lambda: ts(T.PBI[:], T.CT1[:], 15, A.bitwise_and, ["CT1"], ["PBI"])
+        for ll in range(2):
+            yield lambda ll=ll: ts(T.CB[:, 128 * ll:128 * ll + 128], T.PAI[:, 0:128], 2.0, A.mult, ["PAI"], ["CB" if ll == 0 else "CBb"], float(ll), A.add)
+        yield lambda: ts(T.DIAG[:], T.CB[:], PLOW, A.is_equal, ["CB", "CBb", "PC"], ["DIAG"])
         for i in range(2):
-            act(T.TA[:, W + 256 * i:W + 256 * i + 256], T.CF[:], F.Identity, ["CF", "PC10"], ["TAx%d" % i], scale=0.0, bias=I14)
+            yield lambda i=i: ts(T.CB[:, 128 * i:128 * i + 128], T.PBI[:, 0:128], 15.0 - i, A.is_equal, ["PBI"], ["CB" if i == 0 else "CBb"])
+        for i in range(2):
+            yield lambda i=i: tt(T.SRB[:, 128 * i:128 * i + 128], T.CB[:, 128 * i:128 * i + 128], T.GBH[:], A.mult, ["CB", "CBb", "GBH"], ["SRB%d" % i])
+        for h in range(4):
+            yield lambda h=h: ts(T.LX4[:, 8 * h:8 * h + 8], T.CF[:, 0:16:2], PLL, A.add, ["CF", "PC"], ["LX4_%d" % h], 16.0 * (h // 2), A.add)
+        yield lambda: join("LX4", ["LX4_%d" % h for h in range(4)])
+        yield lambda: ts(T.CB1[:], T.C8[:], T.PC[:, 12:13], A.subtract, ["C8", "PC12"], ["CB1"], P1, A.is_equal)
+        yield lambda: ts(T.LT[:, 0:2], T.CF[:, 0:2], PL7, A.add, ["CF", "PC"], ["LT"], PL7, A.add)
+        yield lambda: ts(T.WF[:, 2:3], PLOW, P1, A.subtract, ["PC"], ["WF2"], 0.5, A.mult)
+        for o in range(2):
+            yield lambda o=o: ts(T.LX5[:, 8 * o:8 * o + 8], T.TH[:, 0:8], T.LT[:, o:o + 1], A.add, ["THS", "LT"], ["LX5_%d" % o])
+        yield lambda: ts(T.D16[:, 0:8], T.CF[:, 0:8], T.WF[:, 2:3], A.is_equal, ["CF", "WF2"], ["D16"])
 
-    def later_constants():
-        ts(T.CT2[:, 0:16], T.CI5[:, 0:16], 7, A.bitwise_and, ["CI5"], ["CT2"])
-        cp(T.LX2[:], T.CT2[:, 0:16], ["CT2"], ["LX2"])
-        ts(T.CT1[:], T.CI5[:], 4, A.arith_shift_right, ["CI5"], ["CT1"], 7, A.bitwise_and)
-        for h in range(2):
-            ts(T.CA[:, 128 * h:128 * h + 128], T.CT1[:, 128 * h:128 * h + 128], 4.0 + h, A.is_lt, ["CT1"], ["CA"], 1536.0, A.mult)
-        ts(T.CB[:], T.DIAG[:], 0.0, A.is_equal, ["DIAG"], ["CB"], 1e25, A.mult)
-        tt(T.TH2[:], T.CA[:, 0:256], T.CB[:], A.max, ["CA", "CB"], ["TH2"])
-        ts(RH, T.CF[:, 0:8], PGRP, A.is_equal, ["CF", "PC0"], ["RH"], float(DUM), A.mult)
-        ts(RL0, T.CF[:, 0:8], PGRP, A.is_equal, ["CF", "PC0", "PC4"], ["RL0"], PP, A.mult)
-        ts(T.WF2[:, 7:8], PP, 128.0, A.add, ["PC4"], ["WF7"])
-        ts(RL1, T.CF[:, 0:8], PGRP, A.is_equal, ["CF", "PC0", "WF7"], ["RL1"], T.WF2[:, 7:8], A.mult)
+    late = list(late_constants())
+    gaps = {(1, 0): late[0:5], (1, 1): late[5:9], (2, 0): late[9:14], (2, 1): late[14:18], (4, 0): late[18:21], (4, 1): late[21:24]}
 
-    def last_constants():
-        ms(T.ONES[:], 1.0, ["ONES"])
-        ts(T.CT2[:, 0:128], T.CI5[:, 0:128], 15, A.bitwise_and, ["CI5"], ["CT2"])
-        for i, sel in ((15, SRH), (14, SRL)):
-            ts(T.CA[:, 0:128], T.CT2[:, 0:128], float(i), A.is_equal, ["CT2"], ["CA"])
-            tt(sel, T.CA[:, 0:128], T.GBH[:], A.mult, ["CA", "GBH"], ["SRH" if i == 15 else "SRL"])
-        cp(T.LX4[:], T.CI5[:, 0:16], ["CI5"], ["LX4"])
-        table_rows(T.PAI, "PAI", 1)
-        fill_table(T.TA, "TAd", T.PD[2], T.PD[3], "PD1")
-        wr["TA"] = deps(["TAd", "TAx0", "TAx1"], [])
-
-    BANKS = [T.G0, T.G1, T.G2, T.G3, T.G4, T.G5]
     for t in range(NB):
         frm, to = (prv, nxt) if t % 2 == 0 else (nxt, prv)
         far, fk = (T.TB, "TB") if t % 2 == 0 else (T.TA, "TA")
         XC, xk = (T.XC0, "XC0") if t % 2 == 0 else (T.XC1, "XC1")
+        s_, sk = T.SLAND[:, 256 * t:256 * t + 256], "SLAND%d" % t
         for d in range(ND):
             m = t * ND + d
             tail = d == ND - 1
-            if d == 0:
-                z, zk = T.SLAND[:, 256 * t:256 * t + 256], "SLAND%d" % t
-            else:
-                z, zk = T.Z[:], "Z"
-                pm = m - 1
-                msg = "%d%d" % (t, d - 1)
-                if d == 1:
-                    landed(frm, "b%d" % t, [xk + "b"])
-                    wr[xk] = deps([xk + "b", xk + "x"], [])
-                landed(frm, "n" + msg, ["NLAND%d" % pm])
-                landed(frm, "l" + msg, ["LLAND%d" % pm])
-                cp(XC[:, 0:WX].indirect(T.LLAND[:, 16 * pm:16 * pm + 16]), T.NLAND[:, 256 * pm:256 * pm + 256],
-                   ["NLAND%d" % pm, "LLAND%d" % pm], [xk])
-                cp(T.Z[:], XC[:, 0:WX].indirect(T.PU[:]), [xk, "PU"], ["Z"])
+            end = m == NB * ND - 1
+            z, zk = (s_, sk) if d == 0 else (T.Z[:], "Z")
 
-            result = (lambda: ts(T.W3[:], T.YQ[:], 1.0, A.add, ["YQ"], ["W3"]),
-                      lambda: tt(T.W2[:], T.W3[:], T.WB[:], A.mult, ["W3", "WB"], ["W2"]),
-                      lambda: tt(T.RES[:], T.RES[:], T.W2[:], A.add, ["RES", "W2"], ["RES"]))
+            op("p", [mm(T.G4[:, 0:128], wm[:, 128 * ll:128 * ll + 128], z[:, ll:256:2], ll == 0 and wm is T.WH, ll == 1 and wm is T.WL)
+                     for ll in range(2) for wm in (T.WH, T.WL)], WHL + [zk], ["@G4"])
+            Z8 = ["Z8_%d" % cl for cl in range(8)]
 
-            fs = []
-            for ll in range(4):
-                zs = T.SLAND[:, 256 * t + ll:256 * t + 256:4] if d == 0 else T.Z[:, ll:256:4]
-                fs.append(mm(T.K6[:, 0:64], T.WH[:, 128 * ll:128 * ll + 128], zs, ll == 0, False))
-                fs.append(mm(T.K6[:, 0:64], T.WL[:, 128 * ll:128 * ll + 128], zs, False, ll == 3))
-            op("p", fs, WHL + [zk], ["K6"])
-            for cl in range(4):
-                cp(T.Z4[:, cl:1024:4], z, [zk], ["Z4_%d" % cl])
-            ts(T.NI[:], T.K6[:, 0:64], -0.5, A.add, ["K6"], ["NI"])
-            tt(T.UF[:], T.K6[:, 0:64], T.NI[:], A.subtract, ["K6", "NI"], ["UF"])
-            for ch in range(4):
-                act(T.SQ[:, 64 * ch:64 * ch + 64], T.UF[:], F.Square, ["UF", "SCOL"], ["SQ%d" % ch], bias=T.SCOL[:, ch:ch + 1], scale=4096.0)
+            def z8(cl):
+                cp(T.Z8[:, cl:2048:8], z, [zk], ["Z8_%d" % cl])
+
+            def acol(ch):
+                ts(T.ACOL[:, ch:ch + 1], T.KI[:, 1:2], 32.0, A.mult, ["KI1", "ABASE%d" % d], ["ACOL%d" % ch], T.ABASE[:, 2 * d + ch:2 * d + ch + 1], A.add)
 
             def floors(ch):
-                ts(T.FI[:, 64 * ch:64 * ch + 64], T.SQ[:, 64 * ch:64 * ch + 64], T.ACOL[:, ch:ch + 1], A.add, ["SQ%d" % ch, "ACOL"], ["FI%d" % ch], 1.0 / 32, A.mult)
+                ts(T.FI[:, 128 * ch:128 * ch + 128], T.SQ[:, 128 * ch:128 * ch + 128], T.ACOL[:, ch:ch + 1], A.add, ["SQ%d" % ch, "ACOL%d" % ch], ["FI%d" % ch], 1.0 / 32, A.mult)
 
-            def places(c0, c1):
-                keys = [str(ch) for ch in range(c0, c1)]
-                ts(T.CI[:, 64 * c0:64 * c1], T.FI[:, 64 * c0:64 * c1], 4095, A.bitwise_and, ["FI" + c for c in keys], ["CI" + c for c in keys])
+            def places(ch):
+                ts(T.CI[:, 128 * ch:128 * ch + 128], T.FI[:, 128 * ch:128 * ch + 128], 4095, A.bitwise_and, ["FI%d" % ch], ["CI%d" % ch])
 
-            def bars(ch):
-                tt(T.EQ[:, 64 * ch:64 * ch + 64], T.CI[:, 64 * ch:64 * ch + 64], T.LAST[:], A.is_equal, ["CI%d" % ch, "LAST"], ["EQ%d" % ch])
+            def lists(ch):
+                cp(T.OFF[:, 128 * ch:128 * ch + 128], T.CI[:, 128 * ch:128 * ch + 128], ["CI%d" % ch], ["OFF%d" % ch])
 
-            def lists(c0, c1):
-                keys = [str(ch) for ch in range(c0, c1)]
-                cp(T.OFF[:, 64 * c0:64 * c1], T.CI[:, 64 * c0:64 * c1], ["CI" + c for c in keys], ["OFF" + c for c in keys])
-
-            if d == 0:
-                act(T.SH[:], z, F.Copy, [zk], ["SH"], bias=-0.5)
-
-            def gather(c0, n):
-                a, b, zo = 16 * c0, 16 * (c0 + n), 16 * (c0 % 64)
-                tt(T.DF[:, a:b], T.X[:, 0:WX].indirect(T.OFF[:, c0:c0 + n]), T.Z4[:, zo:zo + 16 * n], A.subtract,
-                   ["X", "OFF%d" % (c0 // 64), "Z4_0", "Z4_1", "Z4_2", "Z4_3"], ["DF%d" % c0])
-                act(T.AB[:, a:b], T.DF[:, a:b], F.Abs, ["DF%d" % c0], ["AB%d" % c0])
-
-            def dsum(c0, n, p0, pr, keys):
-                fs = []
-                for part in range(16):
-                    o = 2 * part + pr
-                    fs.append(mm(T.K6[p0:p0 + n, o:256:32], T.AB[:, 16 * c0 + part:16 * (c0 + n):16], T.OB[:], False, False))
-                op("p", fs, keys + ["OB"], ["K6"], True)
-
+            for cl in range(2):
+                act(T.Z8[:, cl:2048:8], z, F.Copy, [zk], ["Z8_%d" % cl])
+            for cl in (2, 3, 4):
+                z8(cl)
+            ts(T.NI[:], T.G4[:, 0:128], -0.5, A.add, ["@G4"], ["NI"])
+            z8(5)
+            tt(T.UF[:], T.G4[:, 0:128], T.NI[:], A.subtract, ["@G4", "NI"], ["UF"])
+            for ch in range(2):
+                act(T.SQ[:, 128 * ch:128 * ch + 128], T.UF[:], F.Square, ["UF", "SCOL%d" % ch], ["SQ%d" % ch], bias=T.SCOL[:, ch:ch + 1], scale=4096.0)
+            z8(6)
+            if m > 0:
+                acol(0)
+                acol(1)
             floors(0)
+            z8(7)
+            places(0)
             floors(1)
-            places(0, 1)
-            floors(2)
-            lists(0, 1)
-            floors(3)
-            act(T.DF[:, 512:1024], T.X[:, 0:WX].indirect(T.OFF[:, 32:64]), F.Copy, ["X", "OFF0"], ["DF32"])
-            op("p", [mm(T.G0[:], T.IBN[:, 0:128], T.DF[:, 512:1024], True, False), mm(T.G0[:], T.IBN[:, 128:256], T.Z4[:, 512:1024], False, True)],
-               ["IBN0", "IBN1", "DF32", "Z4_0", "Z4_1", "Z4_2", "Z4_3"], ["G0"])
-            gather(0, 32)
-            act(T.AB[:, 512:1024], T.G0[:], F.Abs, ["G0"], ["AB32"])
-            places(1, 4)
-            if d > 0:
-                bars(0)
-            lists(1, 4)
-            cis = ["CI0", "CI1", "CI2", "CI3"]
-            cp(T.CFL[:], T.CI[:], cis, ["CFL"])
-            op("p", [mm(T.K6[:, 0:256], T.ZB[:, 0:128], T.ZB[:], True, False)] +
-               [mm(T.K6[:, pr:256:2], T.CFL[:, 128 * pr:128 * pr + 128], T.IDF[:], False, False) for pr in range(2)], ["ZB", "CFL", "IDF"], ["K6"])
-            gather(64, 64)
-            dsum(0, 128, 0, 0, ["AB0", "AB32", "AB64"])
-            gather(128, 32)
-            gather(160, 32)
-            dsum(128, 64, 0, 1, ["AB128", "AB160"])
+            lists(0)
+            places(1)
+
+            def v_gather(ch, c0, c1):
+                a, b = 2048 * ch + 16 * c0, 2048 * ch + 16 * c1
+                tt(T.DF[:, a:b], T.X[:, 0:WX].indirect(T.OFF[:, 128 * ch + c0:128 * ch + c1]), T.Z8[:, 16 * c0:16 * c1], A.subtract,
+                   ["X", "OFF%d" % ch] + Z8, ["DF%d_%d" % (ch, c0)])
+
+            def v_half(ch, c0, c1):
+                a, b = 2048 * ch + 16 * c0, 2048 * ch + 16 * c1
+                ts(T.AB[:, a:b], T.DF[:, a:b], 0.0, A.max, ["DF%d_%d" % (ch, c0)], ["AB%d_%d" % (ch, c0)], 2.0, A.mult)
+
+            def s_gather(ch, c0, c1):
+                a, b = 2048 * ch + 16 * c0, 2048 * ch + 16 * c1
+                act(T.DF[:, a:b], T.X[:, 0:WX].indirect(T.OFF[:, 128 * ch + c0:128 * ch + c1]), F.Copy, ["X", "OFF%d" % ch], ["DF%d_%d" % (ch, c0)])
+
+            def p_diff(ch, c0, c1, bk):
+                a, b = 2048 * ch + 16 * c0, 2048 * ch + 16 * c1
+                op("p", [mm(T[bk][:, 0:b - a], IN, T.Z8[:, 16 * c0:16 * c1], True, False), mm(T[bk][:, 0:b - a], IB, T.DF[:, a:b], False, True)],
+                   ["IB", "IN", "DF%d_%d" % (ch, c0)] + Z8, ["@" + bk])
+
+            def s_abs(ch, c0, c1, bk):
+                a, b = 2048 * ch + 16 * c0, 2048 * ch + 16 * c1
+                act(T.AB[:, a:b], T[bk][:, 0:b - a], F.Abs, ["@" + bk], ["AB%d_%d" % (ch, c0)])
+
+            def dsum(src, ch, n, ob, keys):
+                op("p", [mm(T.K6[0:n, 2 * b + ch:256:32], src[:, 2048 * ch + b:2048 * ch + 16 * n:16], T.OB[:, 8 * ob:8 * ob + 8], False, False)
+                         for b in range(16)], keys + ["OB%d" % ob], ["@K6"])
+
+            def unbarred(ch):
+                if d > 0:
+                    tt(T.NE[:, 128 * ch:128 * ch + 128], T.LB[:, 0:128], T.CI[:, 128 * ch:128 * ch + 128], A.not_equal, ["@LB", "CI%d" % ch], ["NE%d" % ch])
+
+            def bar(ch):
+                ne = T.NE[:, 128 * ch:128 * ch + 128] if d > 0 else T.ZB[:]
+                op("p", mm(T.K6[:, 0:256], ne, T.PEN[:, 1 - ch:257 - ch], ch == 0, ch == 1), ["NE%d" % ch if d > 0 else "ZB", "PEN"], ["@K6"])
+
+            def number(ch):
+                op("p", mm(T.K6[:, ch:256:2], T.CFL[:, 128 * ch:128 * ch + 128], T.IDF[:], False, False), ["CFL", "IDF"], ["@K6"])
+
+            H, SM = NV // 2, NV + 32
+            sc = [(0, NV, SM, "G0"), (0, SM, 128, "G1"), (1, NV, SM, "G2"), (1, SM, 128, "G3")]
+            s_gather(*sc[0][:3])
+            lists(1)
+            s_gather(*sc[1][:3])
+            p_diff(*sc[0])
+            v_gather(0, 0, NV)
+            s_abs(*sc[0])
+            p_diff(*sc[1])
+            unbarred(0)
+            bar(0)
+            dsum(T.DF, 0, NV, 1, ["DF0_0"])
+            cp(T.CFL[:], T.CI[:], ["CI0", "CI1"], ["CFL"])
+            s_gather(*sc[2][:3])
+            v_gather(1, 0, H)
+            s_abs(*sc[1])
+            p_diff(*sc[2])
+            number(1)
+            v_half(0, 0, NV)
+            s_gather(*sc[3][:3])
+            dsum(T.AB, 0, 128, 0, ["AB0_0", "AB0_%d" % NV, "AB0_%d" % SM])
+            p_diff(*sc[3])
+            v_gather(1, H, NV)
+            s_abs(*sc[2])
+            number(0)
+            dsum(T.DF, 1, NV, 1, ["DF1_0", "DF1_%d" % H])
+            v_half(1, 0, H)
+            s_abs(*sc[3])
+            v_half(1, H, NV)
+            unbarred(1)
+            dsum(T.AB, 1, 128, 0, ["AB1_0", "AB1_%d" % H, "AB1_%d" % NV, "AB1_%d" % SM])
+            bar(1)
+            dead = [(T.DLAND[:, 16 * t:16 * t + 16], "DLAND%d" % t)] + [(T.WB[:, 16 * i:16 * i + 16], "WB%d" % i) for i in range(d)]
+            op("p", [mm(T.C7[:, 0:16], IB, a, i == 0, False) for i, (a, k) in enumerate(dead)], ["IB"] + [k for a, k in dead], ["@C7"])
             if d == 0 and t > 0:
-                near_rows(t - 1)
-            gather(192, 32)
-            dsum(192, 32, 64, 1, ["AB192"])
-            gather(224, 16)
-            gather(240, 16)
-            if d > 0:
-                for ch in range(1, 4):
-                    bars(ch)
-            dsum(224, 32, 96, 1, ["AB224", "AB240"])
-            if d > 0:
-                op("p", [mm(T.K6[:, pr:256:2], T.EQ[:, 128 * pr:128 * pr + 128], T.PEN[:], False, False) for pr in range(2)], ["EQ0", "EQ1", "EQ2", "EQ3", "PEN"], ["K6"], True)
-            op("p", mm(T.K6[:, 0:256], T.ZB[:, 0:128], T.ZB[:], False, True), ["ZB"], ["K6"], True)
-            if d == 0:
-                landed(frm, "e%d" % t, ["DLAND%d" % t])
-                cp(T.DEADL[:], T.DLAND[:, 16 * t:16 * t + 16], ["DLAND%d" % t], ["DEADL"])
-                ms(T.RES[:], 0.0, ["RES"])
-                if t > 0:
-                    near_add(t - 1)
-                    ts(T.RC[:], T.RC[:], I14, A.add, ["RC", "PC10"], ["RC"])
-                else:
-                    later_constants()
-            else:
-                ts(T.W1[:], T.WB[:], DEAD, A.mult, ["WB"], ["W1"])
-                tt(T.DEADL[:], T.DEADL[:], T.W1[:], A.max, ["DEADL", "W1"], ["DEADL"])
-                ts(T.FB[:], T.YA[:], BAR, A.add, ["YA"], ["FB"])
-            if m == 0:
-                scalar_constants()
-            scan(T.R[:], T.RS8[:], T.K6[:, 0:256], A.max, A.min, ["RS8", "K6"], ["R"])
-            tt(T.E1[:], T.R[:, 0:256].indirect(T.LX1[:]), T.M1[:], A.mult, ["R", "LX1", "M1"], ["E1"])
-            op("p", mm(T.C7[:, 0:32], T.E1[:], T.RS1[:], True, True), ["E1", "RS1"], ["C7"])
+                near_rows(t - 1, 0)
+                near_rows(t - 1, 1)
+            for f in gaps.get((m, 0), []):
+                f()
+            scan(T.R[:], T.RS[:], T.K6[:, 0:256], A.max, A.min, ["RS", "@K6"], ["R"])
+            cp(T.RI[:], T.R[:, 15:256:16], ["R"], ["RI"])
+            ts(T.RA[:], T.RI[:], 4095, A.bitwise_and, ["RI"], ["RA"])
+            tt(T.E1[:], T.RA[:, 0:16].indirect(T.LX1[:]), T.M1[:], A.mult, ["RA", "LX1", "M1"], ["E1"])
+            op("p", mm(T.C7[:, 0:16], T.E1[:], T.RS1[:], False, True), ["E1", "RS1"], ["@C7"])
+            if d == 0 and t > 0:
+                near_add(t - 1)
             if not tail:
-                act(T.R4[:], T.R[:, 0:256].indirect(T.LX3[:]), F.Copy, ["R", "LX3"], ["R4"])
-                op("p", mm(T.K6[:, 0:128], T.R4[:], T.IDF[:], True, True), ["R4", "IDF"], ["K6"])
-            fb, fbk = (T.FBC, "FBC") if d == 0 else (T.FB, "FB")
-            rs = list(result) if d > 0 else [lambda: None] * 3
-            tt(T.MN[:], T.C7[:, 16:32], fb[:], A.min, ["C7", fbk], ["MN"])
-            rs[0]()
-            tt(T.YI[:], T.C7[:, 0:16], T.MN[:], A.min, ["C7", "MN"], ["YI"])
-            rs[1]()
-            ts(T.YA[:], T.YI[:], 4095, A.bitwise_and, ["YI"], ["YA"])
-            rs[2]()
-            tt(T.YQ[:], T.YA[:], T.DEADL[:], A.max, ["YA", "DEADL"], ["YQ"])
-            cp(T.YU[:], T.YQ[:], ["YQ"], ["YU"])
-            for h in range(2):
-                a, b, yl = 128 * h, 128 * h + 128, T.YU[:, 8 * h:8 * h + 8]
-                tt(T.QL[:, a:b], far[:, 0:WX].indirect(yl), T.CL[:, a:b], A.mult, [fk, "YU", "CL"], ["QL%d" % h])
-                act(T.QE[:, a:b], T.QL[:, a:b], F.Copy, ["QL%d" % h, "WF6"], ["QE%d" % h], scale=ECOL)
-                tt(T.QR[:, a:b], far[:, 0:WX].indirect(yl), T.CR[:, a:b], A.mult, [fk, "YU", "CR"], ["QR%d" % h])
-                ts(T.QO[:, a:b], T.QL[:, a:b], OCOL, A.mult, ["QL%d" % h, "WF5"], ["QO%d" % h])
-            if m == 0:
-                last_constants()
-
-            def unit(gr, h, b, c):
-                qa, qk = (T.QE, "QE%d" % h) if gr % 2 == 0 else (T.QO, "QO%d" % h)
-                p0 = 32 * (gr // 2)
-                return mm(b[:, c:c + 128 + 128 * h], qa[p0:p0 + 32, 128 * h:128 * h + 128], T.QR[p0:p0 + 32, 0:128 + 128 * h], True, True)
-
-            def reduce(gr, h, b, bk, c, vec):
-                src = b[:, c:c + 128 + 128 * h]
-                o = T.FL[:, 8 * h + gr:8 * h + gr + 1]
-                if vec:
-                    op("v", lambda: g.vector.tensor_reduce(o, src, AxisListType.X, A.max), [bk], ["FL%d_%d" % (gr, h)])
-                else:
-                    j = 128 * (gr - 4) if h == 0 else 512 + 256 * (gr - 5)
-                    act(T.JK[:, j:j + 128 + 128 * h], src, F.Relu, [bk], ["JK%d_%d" % (gr, h), "FL%d_%d" % (gr, h)], bias=-1536.0, accum_out=o)
-
-            def unpaired(h):
-                tt(T.E2[:, 128 * h:128 * h + 128], T.FL[:, 8 * h:8 * h + 8].indirect(T.LX2[:, 8 * h:8 * h + 8]), T.TH2[:, 128 * h:128 * h + 128], A.is_gt,
-                   ["FL%d_%d" % (i, h) for i in range(8)] + ["LX2", "TH2"], ["E2_%d" % h])
-
-            for i, (ga, gb) in enumerate(((4, 5), (0, 1), (6, 7), (2, 3))):
-                b, bk = BANKS[i], "G%d" % i
-                op("p", [unit(ga, 0, b, 0), unit(gb, 0, b, 128)], ["QE0", "QO0", "QR0"], [bk])
-                reduce(ga, 0, b, bk, 0, ga < 4)
-                reduce(gb, 0, b, bk, 128, gb < 4)
-            tt(T.TT[:], T.X[:, 0:WX].indirect(T.YU[:]), T.SH[:], A.add, ["X", "YU", "SH"], ["TT"])
-            ns = T.NSND[:, 256 * m:256 * m + 256]
-            for n, gr in enumerate((5, 0, 6, 1, 7, 2, 3, 4)):
-                b, bk = BANKS[(4 + n) % 6], "G%d" % ((4 + n) % 6)
-                op("p", unit(gr, 1, b, 0), ["QE1" if gr % 2 == 0 else "QO1", "QR0", "QR1"], [bk])
-                reduce(gr, 1, b, bk, 0, gr < 5)
-                if n == 0:
-                    act(T.T2[:], T.TT[:], F.Copy, ["TT"], ["T2"], scale=0.5, bias=8388608.0)
-                    act(ns, T.T2[:], F.Copy, ["T2"], ["NSND%d" % m], bias=-8388608.0)
-                    if not tail:
-                        send(to, "n%d%d" % (t, d), T.NLAND[:, 256 * m:256 * m + 256], ns, ["NSND%d" % m])
-                if n == 1:
-                    unpaired(0)
-                if not tail:
-                    f4, f4k = (T.FB4C, "FB4C") if d == 0 else (T.FB4, "FB4")
-                    if n == 3:
-                        tt(T.L1[:], T.K6[:, 64:128], f4[:], A.min, ["K6", f4k], ["L1"])
-                    if n == 5:
-                        tt(T.L2[:], T.K6[:, 0:64], T.L1[:], A.min, ["K6", "L1"], ["L2"])
-                    if n == 6:
-                        ts(T.LAST[:], T.L2[:], 4095, A.bitwise_and, ["L2"], ["LAST"])
-                    if n == 7 and d == 0:
-                        ts(T.FB4[:], T.LAST[:], BAR, A.add, ["LAST"], ["FB4"])
-            unpaired(1)
-            fs = []
-            for h in range(2):
-                fs.append(mm(T.C7[:, 64 + 8 * h:72 + 8 * h], T.E2[:, 128 * h:128 * h + 128], RH, True, False))
-                fs.append(mm(T.C7[:, 64 + 8 * h:72 + 8 * h], T.E2[:, 128 * h:128 * h + 128], RL0 if h == 0 else RL1, False, True))
-            op("p", fs, ["E2_0", "E2_1", "RH", "RL0", "RL1"], ["C7"])
-            if m == ND * NB - 2:
-                dma("y", [(T.PG4[:, 0:256], T.TA[15:128:16, 0:W]), (T.PG4[:, 256:512], T.TA[14:128:16, 0:W])], ["TA"], ["PG4n"])
-                ts(T.CB[:], T.PG4[:, 0:256], 16.0, A.mult, ["PG4n"], ["CB"], -1.0, A.add)
-                tt(T.PF[:, 0:256], T.CB[:], T.PG4[:, 256:512], A.add, ["CB", "PG4n"], ["YA0"])
+                cp(T.R4[:], T.RA[:, 0:16].indirect(T.LX3[:]), ["RA", "LX3"], ["R4"])
+            tt(T.DE[:], T.MSP[:], T.E1[:], A.subtract, ["MSP", "E1"], ["DE"])
+            ts(T.YU[:], T.C7[:, 0:16], DEAD, A.min, ["@C7"], ["YU"])
             act(T.UP[:], far[:, 0:WX].indirect(T.YU[:]), F.Copy, [fk, "YU"], ["UP"])
-            tt(T.LF[:], T.C7[:, 64:80], T.YQ[:], A.max, ["C7", "YQ"], ["LF"])
+            tt(T.QR[:], far[:, 0:WX].indirect(T.YU[:]), T.CR[:], A.mult, [fk, "YU", "CR"], ["QR"])
+            act(T.GX[:], T.X[:, 0:WX].indirect(T.YU[:]), F.Copy, ["X", "YU"], ["GX"])
+            ts(T.QO[:], T.QR[:], OCOL, A.mult, ["QR", "PC"], ["QO"])
+
+            def unit(gr, ll, b, c):
+                p0, k = 32 * (gr // 2), 16 + 16 * (gr % 2)
+                q = T.QO if gr % 2 else T.QR
+                return mm(b[:, c:c + 128 + 128 * ll], T.UP[p0:p0 + k, ll:256:2], q[p0:p0 + k, 0:256:2 - ll], True, True)
+
+            def v_units(q):
+                bk = ("G0", "G1", "G2", "G3")[q]
+                op("p", [unit(2 * q, 1, T[bk], 0), unit(2 * q, 0, T[bk], 256), unit(2 * q + 1, 0, T[bk], 384)], ["UP", "QR", "QO"], ["@" + bk])
+                scan(T.FL[:, 512 * q:512 * q + 512], T[bk][:], T.TH[:], A.max, A.add, ["@" + bk, "THS"], ["FL%d" % q])
+
+            def s_unit(q):
+                bk = ("G4", "K6")[q % 2]
+                op("p", unit(2 * q + 1, 1, T[bk], 0), ["UP", "QO"], ["@" + bk])
+                act(T.JK[:, 256 * q:256 * q + 256], T[bk][:, 0:256], F.Relu, ["@" + bk, "THS"], ["JK%d" % q, "FL%d" % (4 + q)],
+                    bias=T.TH[:, 255:256], accum_out=T.FL[:, 2048 + q:2049 + q])
+
+            ns = T.NSND[:, 256 * m:256 * m + 256]
+            v_units(0)
+            s_unit(0)
+            v_units(1)
+            op("p", [mm(T.C7[:, 256:512], IH, a, i == 0, i == 3) for i, a in enumerate((T.GX[:], s_, T.CQ[:, 0:256], T.CQ[:, 256:512]))],
+               ["IH", "GX", sk, "CQ0", "CQ1"], ["@C7"])
+            s_unit(1)
+            act(ns, T.C7[:, 256:512], F.Copy, ["@C7"], ["NSND%d" % m], bias=-MAGIC)
+            if not tail:
+                send(to, "n%d%d" % (t, d), T.NLAND[:, 256 * m:256 * m + 256], ns, ["NSND%d" % m])
+            v_units(2)
+            s_unit(2)
+            v_units(3)
+            s_unit(3)
+            op("p", mm(T.C7[:, 16:32], T.E1[:], T.RS1[:], True, False), ["E1", "RS1"], ["@C7"])
+            if not tail:
+                op("p", mm(T.LB[:, 0:128], T.R4[:], T.IDF[:], True, True), ["R4", "IDF"], ["@LB"])
+            tt(T.E2[:], T.FL[:, 0:2056].indirect(T.LX2[:]), T.DE[:], A.min, ["FL%d" % i for i in range(8)] + ["LX2", "DE"], ["E2"])
+            op("p", mm(T.C7[:, 16:32], T.E2[:], T.RS1[:], False, True), ["E2", "RS1"], ["@C7"])
+            for f in gaps.get((m, 1), []):
+                f()
+            if end:
+                ts(T.CB[:], T.HL[:, 0:256], 16.0, A.mult, ["HI0"], ["CB", "CBb"], -1.0, A.add)
             ls = T.LSND[:, 16 * m:16 * m + 16]
             lk = "LSND%d" % m
-            cp(ls, T.LF[:], ["LF"], [lk])
+            cp(ls, T.C7[:, 16:32], ["@C7"], [lk])
             if not tail:
                 send(to, "l%d%d" % (t, d), T.LLAND[:, 16 * m:16 * m + 16], ls, [lk])
-            if tail:
-                cp(T.X[:, 0:WX].indirect(ls), ns, [lk, "NSND%d" % m], ["X"])
-                if t + 1 < NB:
-                    start_batch(t + 1)
-            ts(T.WB[:], T.LF[:], float(DUM), A.is_lt, ["LF"], ["WB"])
-            if not (tail and t + 1 == NB):
-                op("p", mm(T.G0[:, 0:16], T.ONES[:], T.WB[:], True, True), ["ONES", "WB"], ["G0"])
-            if tail:
-                for r in result:
-                    r()
-                near_send(t)
-            tt(far[:, 0:WX].indirect(ls), T.UP[:], T.RC[:], A.max, ["UP", "RC", lk], [fk])
-            if not tail:
-                act(T.PG[:], far[:, 0:WX].indirect(T.YU[:]), F.Copy, [fk, "YU"], ["PG"])
-                cp(T.X[:, 0:WX].indirect(ls), ns, [lk, "NSND%d" % m], ["X"])
-            if not (tail and t + 1 == NB):
-                op("v", lambda: g.vector.tensor_reduce(T.KP[:, 0:1], T.G0[:, 0:16], AxisListType.X, A.add), ["G0"], ["KP0"])
-                k1 = lambda: cp(T.KI[:, 0:1], T.KP[:, 0:1], ["KP0"], ["KI0"])
-                k2 = lambda: ts(T.KI[:, 1:2], T.KI[:, 0:1], 31, A.bitwise_and, ["KI0"], ["KI1"])
-                if not tail:
-                    row_to_list(T.PG[:], SRP, ["PG", "SRP"], T.G2, "G2",
-                                lambda ap: ts(T.PU[:], ap, -1.0, A.add, ["SC"], ["PU"]), k1, k2)
-                else:
-                    row_to_list(far[:, t + 1:W:16], T.SR14[:], [fk, "SR14"], T.G3, "G3", dead_done(t + 1), k1, k2)
-                ts(T.KP[:, 1:2], T.KI[:, 1:2], 32.0, A.mult, ["KI1"], ["KP1"])
-                ts(T.ACOL[:], T.ABASE[:], T.KP[:, 1:2], A.add, ["ABASE", "KP1"], ["ACOL"], 3104.0 * ((d + 1) % ND), A.add)
-    dma("y", [(T.yx[:], T.X[:, 0:W])], ["X"], ["yx"])
+            wb = T.WB[:, 16 * d:16 * d + 16]
 
-    dma("y", [(T.PG4[:, 0:256], T.TB[15:128:16, 0:W]), (T.PG4[:, 256:512], T.TB[14:128:16, 0:W])], ["TB", "YA0"], ["PG4f"])
+            def result():
+                if d == 0:
+                    cp(T.RES[:], T.C7[:, 16:32], ["@C7"], ["RES"])
+                else:
+                    tt(T.RES[:], T.C7[:, 16:32], T.RES[:], A.min, ["@C7", "RES"], ["RES"])
+
+            def own_records():
+                cp(T.X[:, 0:WX].indirect(ls), ns, [lk, "NSND%d" % m], ["X"])
+
+            def far_table():
+                tt(far[:, 0:WX].indirect(ls), T.UP[:], T.RC[:, 256 * t:256 * t + 256], A.add, ["UP", "RC%d" % t, lk], [fk])
+
+            if end:
+                result()
+                own_records()
+                dma("y", [(T.yx[:], T.X[:, 0:W])], ["X"], ["yx"])
+                near_send(t)
+                far_table()
+                break
+            ts(wb, T.C7[:, 16:32], DEAD, A.is_lt, ["@C7"], ["WB%d" % d], DEAD, A.mult)
+            op("p", mm(T.G0[:, 0:16], T.ONES[:], wb, True, True), ["ONES", "WB%d" % d], ["@G0"])
+            act(T.KJ[:], T.G0[:, 0:16], F.Copy, ["@G0"], ["KJ", "KP"], scale=1.0 / DEAD, accum_out=T.KP[:, 0:1])
+            k1 = lambda: cp(T.KI[:, 0:1], T.KP[:, 0:1], ["KP"], ["KI0"])
+            k2 = lambda: ts(T.KI[:, 1:2], T.KI[:, 0:1], 31, A.bitwise_and, ["KI0"], ["KI1"])
+            if tail:
+                own_records()
+                result()
+                starters_send(t + 1)
+                far_table()
+                dead_list(t + 1)
+                k1()
+                near_send(t)
+                k2()
+                dead_send(t + 1)
+                records_send(t + 1)
+                continue
+            far_table()
+            act(T.PG[:], far[:, 0:WX].indirect(T.YU[:]), F.Copy, [fk, "YU"], ["PG"])
+            result()
+            to_list(lambda b: T.PG[:, b:256:16], ["PG"])
+            own_records()
+            if m == ND * NB - 2:
+                dma("y", [(T.HL[:, 0:256], T.TA[15:128:16, 0:W]), (T.HL[:, 256:512], T.TA[14:128:16, 0:W])], ["TA"], ["HI0", "LO0"])
+            k1()
+            ts(T.PU[:], T.C7[:, 32:48], -1.0, A.add, ["@C7"], ["PU"])
+            k2()
+            msg = "%d%d" % (t, d)
+            if d == 0:
+                landed(frm, "b%d" % t, [xk + "b"])
+                join(xk, [xk + "b", xk + "x"])
+            landed(frm, "n" + msg, ["NLAND%d" % m])
+            landed(frm, "l" + msg, ["LLAND%d" % m])
+            cp(XC[:, 0:WX].indirect(T.LLAND[:, 16 * m:16 * m + 16]), T.NLAND[:, 256 * m:256 * m + 256], ["NLAND%d" % m, "LLAND%d" % m], [xk])
+            cp(T.Z[:], XC[:, 0:WX].indirect(T.PU[:]), [xk, "PU"], ["Z"])
+    dma("y", [(T.HL[:, 512:768], T.TB[15:128:16, 0:W]), (T.HL[:, 768:1024], T.TB[14:128:16, 0:W])], ["TB"], ["HI1", "LO1"])
     t = NB - 1
+    tt(T.PF[:, 0:256], T.CB[:], T.HL[:, 256:512], A.add, ["CB", "CBb", "LO0"], ["YA0"])
     landed(nxt if t % 2 == 0 else prv, "r%d" % t, ["RLAND%d" % t])
-    tt(T.E1[:], T.RLAND[:, 32 * t:32 * t + 16].indirect(T.LX5[:, 0:8]), T.GBH[:], A.mult, ["RLAND%d" % t, "LX5", "GBH"], ["E1"])
-    op("p", mm(T.G4[:, 0:16], T.E1[:], T.DIAG[:, 0:16], True, True), ["E1", "DIAG"], ["G4"])
-    ts(T.CB[:], T.PG4[:, 0:256], 16.0, A.mult, ["PG4f"], ["CB"], -1.0, A.add)
-    tt(T.PF[:, 256:512], T.CB[:], T.PG4[:, 256:512], A.add, ["CB", "PG4f"], ["YB0"])
-    tt(T.PF[:, t:256:16], T.G4[:, 0:16], T.PF[:, t:256:16], A.add, ["G4", "YA0"], ["YA0"])
-    dma("y", [(T.yb[:], T.PF[:, 256:512])], ["YB0"], ["yb"])
+    for o, e in enumerate(("E1", "E2")):
+        tt(T[e][:], T.RLAND[:, 32 * t:32 * t + 16].indirect(T.LX5[:, 8 * o:8 * o + 8]), T.CB1[:], A.mult, ["RLAND%d" % t, "LX5_%d" % o, "CB1"], [e])
+        op("p", mm(T.G4[:, 8 * o:8 * o + 8], T[e][:], T.D16[:, 0:8], True, True), [e, "D16"], ["@G4"])
+    ts(T.DIAG[:], T.HL[:, 512:768], 16.0, A.mult, ["HI1"], ["DIAG"], -1.0, A.add)
+    tt(T.PF[:, t:256:16], T.G4[:, 0:16], T.PF[:, t:256:16], A.add, ["@G4", "YA0"], ["YA0"])
+    tt(T.PF[:, 256:512], T.DIAG[:], T.HL[:, 768:1024], A.add, ["DIAG", "LO1"], ["YB0"])
     dma("y", [(T.ya[:], T.PF[:, 0:256])], ["YA0"], ["ya"])
+    dma("s", [(T.yb[:], T.PF[:, 256:512])], ["YB0"], ["yb"])
     for sem in sorted(last):
         need("g", {sem: last[sem]})

@@ -18,23 +18,23 @@ def _sb(name, cols, dtype):
 
 for _n in ("X", "XC0", "XC1", "TA", "TB"):
     _sb(_n, WX, "bfloat16")
-_sb("PAI", 256, "int32"); _sb("PBI", 256, "int32"); _sb("CT1", 256, "int32")
+_sb("PAI", 256, "int32"); _sb("PBI", 256, "int32"); _sb("CT1", 256, "int32"); _sb("CT2", 256, "int32")
 _sb("HL", 1024, "bfloat16"); _sb("CB", 256, "float32"); _sb("PF", 512, "float32")
 _sb("WI", 8, "int32"); _sb("WF", 8, "float32")
 _sb("PI", 8, "int32"); _sb("PT", 8, "int32"); _sb("PC", 32, "float32"); _sb("SG", 16, "float32")
 _sb("CF", 264, "float32"); _sb("LANE", 256, "float32"); _sb("C8", 128, "float32"); _sb("CB1", 128, "float32"); _sb("SPI", 128, "float32")
-_sb("WH", 256, "bfloat16"); _sb("WL", 256, "bfloat16")
+_sb("CG", 128, "float32"); _sb("WH", 256, "bfloat16"); _sb("WL", 256, "bfloat16")
 _sb("OB", 16, "bfloat16"); _sb("IDF", 128, "float32"); _sb("PEN", 264, "bfloat16"); _sb("ZB", 128, "bfloat16")
 _sb("IBN", 384, "bfloat16")
 _sb("CQ", 512, "bfloat16")
 _sb("M1", 128, "float32"); _sb("MSP", 128, "float32"); _sb("RS1", 16, "float32"); _sb("RS", 256, "float32")
 _sb("CR", 256, "bfloat16"); _sb("RC", 256 * NB, "bfloat16"); _sb("TH", 512, "float32"); _sb("SW", 144, "bfloat16")
 _sb("ONES", 128, "bfloat16"); _sb("DIAG", 256, "float32"); _sb("SRB", 256, "bfloat16"); _sb("GBH", 128, "float32"); _sb("D16", 16, "float32")
-_sb("LX1", 8, "uint16"); _sb("LX2", 8, "uint16"); _sb("LX3", 8, "uint16"); _sb("LX4", 32, "uint16"); _sb("LX5", 16, "uint16")
+_sb("LX0", 16, "uint16"); _sb("LX1", 8, "uint16"); _sb("LX2", 8, "uint16"); _sb("LX3", 8, "uint16"); _sb("LX4", 32, "uint16"); _sb("LX5", 16, "uint16")
 _sb("LT", 64, "float32"); _sb("LXI", 16, "int32"); _sb("LXJ", 16, "int32")
 _sb("SCOL", 4, "float32"); _sb("ABASE", 8, "float32"); _sb("ACOL", 4, "float32")
 _sb("SSND", 256 * NB, "bfloat16"); _sb("SLAND", 256 * NB, "bfloat16")
-_sb("DSND", 16 * NB, "bfloat16"); _sb("DLAND", 16 * NB, "bfloat16")
+_sb("DSND", 16 * NB, "bfloat16"); _sb("DLAND", 16 * (NB + 1), "bfloat16")
 _sb("NSND", 256 * NB * ND, "bfloat16"); _sb("NLAND", 256 * NB * ND, "bfloat16")
 _sb("LSND", 16 * NB * ND, "uint16"); _sb("LLAND", 16 * NB * ND, "uint16")
 _sb("RSND", 32 * NB, "float32"); _sb("RLAND", 32 * NB, "float32")
@@ -156,11 +156,8 @@ def rank_program(g, core, T, topo):
     def act(out, in_, f, r, w, **kw):
         op("s", lambda: g.scalar.activation(out, in_, f, **kw), r, w)
 
-    def iota(out, pattern, base, mult, key):
-        if out.dtype == "int32" or key in ("PI",):
-            op("g", lambda: g.iota(out, pattern, base, mult), [], [key])
-        else:
-            op("g", lambda: g.iota(out, pattern, base, mult, allow_small_or_imprecise_dtypes=True), [], [key])
+    def iota(key, pattern, base, mult):
+        op("g", lambda: g.iota(T[key][:], pattern, base, mult, allow_small_or_imprecise_dtypes=True), [], [key])
 
     def mm(out, lhsT, rhs, start, stop):
         return lambda: g.tensor.matmul(out, lhsT, rhs, start, stop)
@@ -194,13 +191,7 @@ def rank_program(g, core, T, topo):
 
     def near_send(t):
         hi, lo = T.RSND[:, 32 * t:32 * t + 16], T.RSND[:, 32 * t + 16:32 * t + 32]
-        home = prv if t % 2 == 0 else nxt
         ts(T.W1[:], T.RES[:], DEAD, A.is_lt, ["RES"], ["W1"])
-        if t == NB - 1:
-            ts(T.W2[:], T.RES[:], 1.0, A.add, ["RES"], ["W2"])
-            tt(hi, T.W1[:], T.W2[:], A.mult, ["W1", "W2"], ["RSH%d" % t])
-            send(home, "r%d" % t, T.RLAND[:, 32 * t:32 * t + 16], hi, ["RSH%d" % t])
-            return
         cp(T.LXJ[:], T.RES[:], ["RES"], ["LXJ"])
         ts(T.W2[:], T.RES[:], 1.0, A.add, ["RES"], ["W2"])
         ts(T.LXI[:], T.LXJ[:], 4, A.arith_shift_right, ["LXJ"], ["LXI"])
@@ -208,7 +199,7 @@ def rank_program(g, core, T, topo):
         tt(hi, T.LXI[:], T.W1[:], A.mult, ["LXI", "W1"], ["RSH%d" % t])
         ts(T.W2[:], hi, -16.0, A.mult, ["RSH%d" % t], ["W2"])
         tt(lo, T.W3[:], T.W2[:], A.add, ["W3", "W2"], ["RSL%d" % t])
-        send(home, "r%d" % t, T.RLAND[:, 32 * t:32 * t + 32], T.RSND[:, 32 * t:32 * t + 32], ["RSH%d" % t, "RSL%d" % t])
+        send(prv if t % 2 == 0 else nxt, "r%d" % t, T.RLAND[:, 32 * t:32 * t + 32], T.RSND[:, 32 * t:32 * t + 32], ["RSH%d" % t, "RSL%d" % t])
 
     def near_rows(t, i):
         if i == 0:
@@ -223,15 +214,16 @@ def rank_program(g, core, T, topo):
         near, nk = (T.TA, "TA") if t % 2 == 0 else (T.TB, "TB")
         tt(near[:, t:W:16], T.LB[:, 0:256], near[:, t:W:16], A.add, ["@LB", nk], [nk])
 
-    dma("y", [(T.X[:, 0:W], T.x[:])], [], ["Xd"])
+    dma("y", [(T.PAI[:], T.pa[:])], [], ["PAI"])
     dma("s", [(T.WI[:, 0:1], T.wt[:])], [], ["WI"])
-    dma("s", [(T.PAI[:], T.pa[:])], [], ["PAI"])
+    dma("y", [(T.X[:, 0:W], T.x[:])], [], ["Xd"])
     dma("s", [(T.PBI[:], T.pb[:])], [], ["PBI"])
     op("g", lambda: g.iota(T.PI[:, 0:1], [[0, 1]], 0, 1), [], ["PI"])
-    for key, pattern, base, mult in (("CF", [[1, 264]], 0, 0), ("C8", [[1, 16], [0, 8]], 0, 0), ("LANE", [[1, 128], [128, 2]], 0, 0),
-                                     ("CB1", [[0, 8], [1, 8], [0, 2]], 0, 0), ("SPI", [[0, 64], [1, 2]], DUM, 2)):
-        op("g", lambda: g.iota(T[key][:], pattern, base, mult, allow_small_or_imprecise_dtypes=True), [], [key])
-    ms(T.TA[:, 0:1], 1.0, ["TAb"])
+    iota("CF", [[1, 264]], 0, 0)
+    iota("C8", [[1, 16], [0, 8]], 0, 0)
+    iota("CB1", [[0, 8], [1, 8], [0, 2]], 0, 0)
+    iota("LANE", [[1, 128], [128, 2]], 0, 0)
+    ms(T.TB[:, 0:1], 1.0, ["TBb"])
     ms(T.X[:, W:WX], 0.0, ["Xx"])
     join("X", ["Xd", "Xx"])
     for c, (sh, mask) in enumerate(((4, 7), (0, 15), (0, 7), (3, 15), (0, 1), (3, 1), (4, 1), (0, 127))):
@@ -244,107 +236,128 @@ def rank_program(g, core, T, topo):
     ts(T.PC[:, 8:12], T.CF[:, 12:16], PLOW, A.is_equal, ["CF", "PC"], ["PCI"])
     I12, I14, I15 = T.PC[:, 8:9], T.PC[:, 10:11], T.PC[:, 11:12]
     ts(T.SG[:, 0:12], T.LT[:, 0:12], -1.0, A.add, ["LT"], ["SG"])
-    for r in range(11):
+    for r in range(12):
         n = 1 << r
-        act(T.TA[:, n:2 * n], T.TA[:, 0:n], F.Copy, ["TAb", "SG"], ["TAb"], scale=T.SG[:, r:r + 1])
-    act(T.TA[:, 2048:W], T.TA[:, 0:2048], F.Copy, ["TAb", "SG"], ["TAc"], scale=T.SG[:, 11:12])
+        act(T.TB[:, n:2 * n], T.TB[:, 0:n], F.Copy, ["TBb", "SG"], ["TBb"], scale=T.SG[:, r:r + 1])
     ts(T.PC[:, 12:13], PGRP, 2.0, A.mult, ["PC"], ["PC12"])
     ts(T.PC[:, 13:14], PGRP, 2.0, A.mult, ["PC"], ["PC13"], 1.0, A.add)
     ts(T.PC[:, 14:15], PGRP, 16.0, A.mult, ["PC"], ["PC14"], 16.0, A.add)
     ts(T.PC[:, 15:16], I15, 16.0, A.mult, ["PCI"], ["PC15"], I14, A.add)
+    ts(T.IDF[:], T.CF[:, 0:128], PP, A.is_equal, ["CF", "PC"], ["IDF"])
+    ts(T.DSND[:, 0:16], T.PAI[:, 0:256:16], 0.0, A.is_ge, ["PAI"], ["DSND0"], DEAD, A.mult)
+    send(nxt, "e0", T.DLAND[:, 16 * NB:16 * NB + 16], T.DSND[:, 0:16], ["DSND0"])
+    landed(prv, "e0", ["DRAW"])
+    iota("SPI", [[0, 64], [1, 2]], DUM, 2)
+    iota("CG", [[2, 8], [0, 8], [1, 2]], 0, 0)
     ts(T.WI[:, 2:3], T.WI[:, 0:1], 3840, A.bitwise_and, ["WI"], ["WI2"])
     ts(T.WI[:, 3:4], T.WI[:, 0:1], 255, A.bitwise_and, ["WI"], ["WI3"])
     ts(T.SW[:], T.CF[:, 0:144], T.PC[:, 14:15], A.is_equal, ["CF", "PC14", "PC15"], ["SW"], T.PC[:, 15:16], A.mult)
     ts(T.WF[:, 0:2], T.WI[:, 2:4], 1.0 / 4096, A.mult, ["WI2", "WI3"], ["WF"])
-
-    def table_rows(pin, pk, i):
-        hi, lo = T.HL[:, 512 * i:512 * i + 256], T.HL[:, 512 * i + 256:512 * i + 512]
-        return (lambda: ts(T.CT1[:], pin[:], 4, A.arith_shift_right, [pk], ["CT1"]),
-                lambda: ts(hi, T.CT1[:], 0.0, A.max, ["CT1"], ["HI%d" % i]),
-                lambda: ts(T.CB[:], hi, -16.0, A.mult, ["HI%d" % i], ["CB"], 1.0, A.add),
-                lambda: tt(lo, T.CB[:], pin[:], A.add, ["CB", pk], ["LO%d" % i]))
-
-    def fill_rows(tab, key, i, after):
-        dma("y", [(tab[15:128:16, 0:W], T.HL[:, 512 * i:512 * i + 256]), (tab[14:128:16, 0:W], T.HL[:, 512 * i + 256:512 * i + 512])],
-            ["HI%d" % i, "LO%d" % i], after + [key])
-
-    rows_a, rows_b = table_rows(T.PAI, "PAI", 0), table_rows(T.PBI, "PBI", 1)
-    for ll in range(2):
-        rows_a[2 * ll]()
-        ts(T.WH[:, 128 * ll:128 * ll + 128], T.C8[:], T.PC[:, 12 + ll:13 + ll], A.is_equal, ["C8", "PC12", "PC13", "WF"], ["WH%d" % ll], T.WF[:, 0:1], A.mult)
-        rows_a[2 * ll + 1]()
-        ts(T.WL[:, 128 * ll:128 * ll + 128], T.C8[:], T.PC[:, 12 + ll:13 + ll], A.is_equal, ["C8", "PC12", "PC13", "WF"], ["WL%d" % ll], T.WF[:, 1:2], A.mult)
-    WHL = ["WH0", "WH1", "WL0", "WL1"]
     for ch in range(2):
         ts(T.SCOL[:, ch:ch + 1], PL7, 32.0, A.mult, ["PC"], ["SCOL%d" % ch], 256.0 * ch + 16.0, A.add)
-    ts(T.IDF[:], T.CF[:, 0:128], PP, A.is_equal, ["CF", "PC"], ["IDF"])
+    for ll in range(2):
+        for wm, c in (("WH", 0), ("WL", 1)):
+            ts(T[wm][:, 128 * ll:128 * ll + 128], T.C8[:], T.PC[:, 12 + ll:13 + ll], A.is_equal, ["C8", "PC12", "PC13", "WF"], ["%s%d" % (wm, ll)], T.WF[:, c:c + 1], A.mult)
+    WHL = ["WH0", "WH1", "WL0", "WL1"]
     tt(T.SCOL[:, 2:4], T.SCOL[:, 0:2], T.SCOL[:, 0:2], A.mult, ["SCOL0", "SCOL1"], ["SCOL2"])
     ts(IB, T.CF[:, 0:128], PP, A.is_equal, ["CF", "PC"], ["IB"])
     for d in range(ND):
         ts(T.ABASE[:, 2 * d:2 * d + 2], T.SCOL[:, 2:4], -1.0, A.mult, ["SCOL2"], ["ABASE%d" % d], 262144.0 - 12.0 + 32.0 * 97 * d, A.add)
     ts(IN, T.CF[:, 0:128], PP, A.is_equal, ["CF", "PC"], ["IN"], -1.0, A.mult)
     cp(T.ACOL[:, 0:2], T.ABASE[:, 0:2], ["ABASE0"], ["ACOL0", "ACOL1"])
-    starters_send(0)
-    cp(T.TB[:, 0:2048], T.TA[:, 0:2048], ["TAb"], ["TBb"])
-    ts(T.TB[:, 2048:W], T.TA[:, 0:2048], T.SG[:, 11:12], A.mult, ["TAb", "SG"], ["TBc"])
-    fill_rows(T.TA, "TAd", 0, ["TAb", "TAc"])
-    ts(T.PC[:, 16:17], I14, 40.0, A.mult, ["PCI"], ["PC16"])
-    for i in range(4):
-        rows_b[i]()
-        ts(T.OB[:, 8 * (i % 2):8 * (i % 2) + 8], T.CF[:, 0:8], PGRP, A.is_equal, ["CF", "PC"], ["OB%d" % (i % 2)], 4096.0 * (1 - 2 * (i % 2)), A.mult) if i < 2 else None
-        ms(T["XC%d" % (i - 2)][:, W:WX], 0.0, ["XC%dx" % (i - 2)]) if i >= 2 else None
-    fill_rows(T.TB, "TBd", 1, ["TBb", "TBc"])
-    for tab in ("TA", "TB"):
-        act(T[tab][:, W:WX], T.X[:, W:WX], F.Identity, ["Xx", "PC16"], [tab + "x"], bias=T.PC[:, 16:17])
+    for i in range(2):
+        ts(T.OB[:, 8 * i:8 * i + 8], T.CF[:, 0:8], PGRP, A.is_equal, ["CF", "PC"], ["OB%d" % i], 4096.0 * (1 - 2 * i), A.mult)
+    ts(T.PC[:, 23:24], PP, 2.0, A.mult, ["PC"], ["PC23"], 1.0, A.add)
+
+    def table_rows(pin, pk, i):
+        hi, lo = T.HL[:, 512 * i:512 * i + 256], T.HL[:, 512 * i + 256:512 * i + 512]
+        return [lambda: ts(T.CT1[:], pin[:], 4, A.arith_shift_right, [pk], ["CT1"]),
+                lambda: ts(hi, T.CT1[:], 0.0, A.max, ["CT1"], ["HI%d" % i]),
+                lambda: ts(T.CB[:], hi, -16.0, A.mult, ["HI%d" % i], ["CB", "CBb"], 1.0, A.add),
+                lambda: tt(lo, T.CB[:], pin[:], A.add, ["CB", "CBb", pk], ["LO%d" % i])]
+
+    def fill_rows(tab, i):
+        dma("y", [(T[tab][15:128:16, 0:W], T.HL[:, 512 * i:512 * i + 256]), (T[tab][14:128:16, 0:W], T.HL[:, 512 * i + 256:512 * i + 512])],
+            ["HI%d" % i, "LO%d" % i], [tab + "b", tab + "c", tab + "d"])
         join(tab, [tab + "d", tab + "x"])
-    dead_list(0)
+
+    def spare_columns(tab):
+        act(T[tab][:, W:WX], T.XC1[:, W:WX], F.Identity, ["XC1x", "PC16"], [tab + "x"], bias=T.PC[:, 16:17])
+
+    def starter_rows(t):
+        act(T.RC[:, 256 * t:256 * t + 256], T.LANE[:], F.Identity, ["LANE", "PCI", "PC20"], ["RC%d" % t], scale=I15, bias=T.PC[:, 20 + t:21 + t])
+
+    rows_b = table_rows(T.PBI, "PBI", 1)
+    rows_b[0]()
+    ts(T.PEN[:], T.CF[:], T.PC[:, 23:24], A.is_equal, ["CF", "PC23"], ["PEN"], -2.0 ** 24, A.mult)
+    rows_b[1]()
+    ms(T.XC1[:, W:WX], 0.0, ["XC1x"])
+    rows_b[2]()
+    ts(T.PC[:, 16:17], I14, 40.0, A.mult, ["PCI"], ["PC16"])
+    ts(T.PC[:, 17:18], PLOW, 12.0, A.is_lt, ["PC"], ["PC17"], 128.0 * SC, A.mult)
+    rows_b[3]()
+    ts(T.PC[:, 18:19], I12, -SC, A.mult, ["PCI"], ["PC18"])
+    ts(T.PC[:, 20:23], T.CF[:, 1:4], I14, A.mult, ["CF", "PCI"], ["PC20"])
+    ts(T.PC[:, 19:20], I14, SC, A.mult, ["PCI", "PC17"], ["PC19"], T.PC[:, 17:18], A.add)
+    starters_send(0)
+    spare_columns("TB")
+    need("y", deps([], ["SS0_0"]))
+    fill_rows("TB", 1)
+    need("g", deps(["TBd"], []))
+    records_send(0)
+    act(T.CR[:], T.LANE[:], F.Identity, ["LANE", "PC18", "PC19"], ["CR"], scale=T.PC[:, 18:19], bias=T.PC[:, 19:20])
+    act(IH, T.IDF[:], F.Copy, ["IDF"], ["IH"], scale=0.5)
+    starter_rows(0)
+    ts(T.WF[:, 2:3], PLOW, P1, A.subtract, ["PC"], ["WF2"], 0.5, A.mult)
+    ts(T.WB[:, 0:8], T.CF[:, 0:8], PL7, A.is_equal, ["CF", "PC"], ["WB0"])
+    ts(T.R4[:], T.CG[:], P8, A.is_equal, ["CG", "PC"], ["R4"])
+    for o in range(2):
+        ts(T.LX0[:, 8 * o:8 * o + 8], T.ZB[:, 0:8], T.WF[:, 2:3], A.add, ["ZB", "WF2"], ["LX0_%d" % o], 8.0 * o, A.add)
     ms(T.RS[:, 0:256:16], 2.0 ** 26, ["RS"])
+    for o in range(2):
+        tt(T.E3[:, 128 * o:128 * o + 128], T.DLAND[:, 16 * NB:16 * NB + 16].indirect(T.LX0[:, 8 * o:8 * o + 8]), T.R4[:], A.mult,
+           ["DRAW", "LX0_%d" % o, "R4"], ["E3_%d" % o])
+        op("p", mm(T.C7[:, 32 + o:48:2], T.E3[:, 128 * o:128 * o + 128], T.WB[:, 0:8], True, True), ["E3_%d" % o, "WB0"], ["@C7"])
     ts(T.M1[:], T.CB1[:], PL7, A.is_equal, ["CB1", "PC"], ["M1"])
     ts(T.RS1[:], T.CF[:, 0:16], P8, A.is_equal, ["CF", "PC"], ["RS1"])
     ts(T.LX1[:], T.CF[:, 0:16:2], P1, A.add, ["CF", "PC"], ["LX1"])
     ts(T.LX3[:], T.CF[:, 0:16:2], PLL, A.add, ["CF", "PC"], ["LX3"])
+    cp(T.DLAND[:, 0:16], T.C7[:, 32:48], ["@C7"], ["DLAND0"])
     tt(T.MSP[:], T.M1[:], T.SPI[:], A.mult, ["M1", "SPI"], ["MSP"])
-    ts(T.PC[:, 17:18], PLOW, 12.0, A.is_lt, ["PC"], ["PC17"], 128.0 * SC, A.mult)
-    ts(T.PC[:, 18:19], I12, -SC, A.mult, ["PCI"], ["PC18"])
-    ts(T.PC[:, 20:23], T.CF[:, 1:4], I14, A.mult, ["CF", "PCI"], ["PC20"])
-    ts(T.PC[:, 19:20], I14, SC, A.mult, ["PCI", "PC17"], ["PC19"], T.PC[:, 17:18], A.add)
-    ts(T.PC[:, 23:24], PP, 2.0, A.mult, ["PC"], ["PC23"], 1.0, A.add)
     ms(T.TH[:], 0.0, ["TH"])
-    act(T.CR[:], T.LANE[:], F.Identity, ["LANE", "PC18", "PC19"], ["CR"], scale=T.PC[:, 18:19], bias=T.PC[:, 19:20])
-    for t in range(NB):
-        act(T.RC[:, 256 * t:256 * t + 256], T.LANE[:], F.Identity, ["LANE", "PCI", "PC20"], ["RC%d" % t], scale=I15, bias=T.PC[:, 20 + t:21 + t])
-    act(IH, T.IDF[:], F.Copy, ["IDF"], ["IH"], scale=0.5)
-    ts(T.PEN[:], T.CF[:], T.PC[:, 23:24], A.is_equal, ["CF", "PC23"], ["PEN"], -2.0 ** 24, A.mult)
-    ms(T.CQ[:, 0:256], -0.5, ["CQ0"])
-    ms(T.CQ[:, 256:512], 2 * MAGIC, ["CQ1"])
-    ts(T.TH[:, 255:256], PP, SC, A.mult, ["PC", "TH"], ["TH1"], (128 - 1536) * SC, A.add)
-    for c in (383, 511):
-        ts(T.TH[:, c:c + 1], PP, SC, A.mult, ["PC", "TH"], ["TH%d" % c], -1536 * SC, A.add)
-    join("THS", ["TH", "TH1", "TH383", "TH511"])
-    for i, (c0, step, base) in enumerate(((0, 512.0, 383.0), (1, 512.0, 511.0), (8, 512.0, 255.0), (9, 1.0, 2048.0))):
-        ts(T.LT[:, 16 + c0:16 + c0 + 7:2], T.CF[:, 0:4], step, A.mult, ["CF"], ["LT%d" % i], base, A.add)
-    ms(T.ONES[:], 1.0, ["ONES"])
-    ms(T.FL[:, 2048:2056], 0.0, ["FL4", "FL5", "FL6", "FL7"])
-    tt(T.LT[:, 32:40], T.LT[:, 24:32], T.LT[:, 16:24], A.subtract, ["LT0", "LT1", "LT2", "LT3"], ["LT4"])
-    dead_send(0)
-    records_send(0)
-    ts(T.LT[:, 40:48], T.LT[:, 32:40], P1, A.mult, ["LT4", "PC"], ["LT5"])
-    ts(T.GBH[:], T.C8[:], T.PC[:, 12:13], A.subtract, ["C8", "PC12"], ["GBH"])
-    tt(T.LT[:, 32:40], T.LT[:, 40:48], T.LT[:, 16:24], A.add, ["LT5", "LT0", "LT1"], ["LT4"])
-    cp(T.LX2[:], T.LT[:, 32:40], ["LT4"], ["LX2"])
+
+    def first_constants():
+        yield lambda: ms(T.CQ[:, 0:256], -0.5, ["CQ0"])
+        yield lambda: ms(T.CQ[:, 256:512], 2 * MAGIC, ["CQ1"])
+        yield lambda: ts(T.TH[:, 255:256], PP, SC, A.mult, ["PC", "TH"], ["TH1"], (128 - 1536) * SC, A.add)
+        for c in (383, 511):
+            yield lambda c=c: ts(T.TH[:, c:c + 1], PP, SC, A.mult, ["PC", "TH"], ["TH%d" % c], -1536 * SC, A.add)
+        yield lambda: join("THS", ["TH", "TH1", "TH383", "TH511"])
+        for i, (c0, step, base) in enumerate(((0, 512.0, 383.0), (1, 512.0, 511.0), (8, 512.0, 255.0), (9, 1.0, 2048.0))):
+            yield lambda i=i, c0=c0, step=step, base=base: ts(T.LT[:, 16 + c0:16 + c0 + 7:2], T.CF[:, 0:4], step, A.mult, ["CF"], ["LT%d" % i], base, A.add)
+        yield lambda: ms(T.FL[:, 2048:2056], 0.0, ["FL4", "FL5", "FL6", "FL7"])
+        yield lambda: tt(T.LT[:, 32:40], T.LT[:, 24:32], T.LT[:, 16:24], A.subtract, ["LT0", "LT1", "LT2", "LT3"], ["LT4"])
+        yield lambda: ts(T.LT[:, 40:48], T.LT[:, 32:40], P1, A.mult, ["LT4", "PC"], ["LT5"])
+        yield lambda: tt(T.LT[:, 32:40], T.LT[:, 40:48], T.LT[:, 16:24], A.add, ["LT5", "LT0", "LT1"], ["LT4"])
+        yield lambda: cp(T.LX2[:], T.LT[:, 32:40], ["LT4"], ["LX2"])
+        yield lambda: ms(T.ONES[:], 1.0, ["ONES"])
+        yield lambda: ms(T.XC0[:, W:WX], 0.0, ["XC0x"])
 
     def late_constants():
+        for f in table_rows(T.PAI, "PAI", 0):
+            yield f
+        yield lambda: ts(T.GBH[:], T.C8[:], T.PC[:, 12:13], A.subtract, ["C8", "PC12"], ["GBH"])
+        yield lambda: cp(T.CT1[:], T.CF[:, 0:256], ["CF"], ["CT1"])
         yield lambda: ts(T.CB[:, 0:128], T.GBH[:], 0.0, A.is_ge, ["GBH"], ["CB"])
         yield lambda: ts(T.CB[:, 128:256], T.GBH[:], 1.0, A.is_le, ["GBH"], ["CBb"])
+        yield lambda: ts(T.CT2[:, 0:128], T.CT1[:, 0:128], 7, A.bitwise_and, ["CT1"], ["CT2"])
         yield lambda: tt(T.GBH[:], T.CB[:, 0:128], T.CB[:, 128:256], A.mult, ["CB", "CBb"], ["GBH"])
-        yield lambda: cp(T.CT1[:], T.CF[:, 0:256], ["CF"], ["CT1"])
-        yield lambda: ts(T.PAI[:], T.CT1[:], 7, A.bitwise_and, ["CT1"], ["PAI"])
-        yield lambda: ts(T.PBI[:], T.CT1[:], 15, A.bitwise_and, ["CT1"], ["PBI"])
+        yield lambda: ts(T.CT2[:, 128:256], T.CT1[:, 0:128], 15, A.bitwise_and, ["CT1"], ["CT2b"])
         for ll in range(2):
-            yield lambda ll=ll: ts(T.CB[:, 128 * ll:128 * ll + 128], T.PAI[:, 0:128], 2.0, A.mult, ["PAI"], ["CB" if ll == 0 else "CBb"], float(ll), A.add)
+            yield lambda ll=ll: ts(T.CB[:, 128 * ll:128 * ll + 128], T.CT2[:, 0:128], 2.0, A.mult, ["CT2"], ["CB" if ll == 0 else "CBb"], float(ll), A.add)
         yield lambda: ts(T.DIAG[:], T.CB[:], PLOW, A.is_equal, ["CB", "CBb", "PC"], ["DIAG"])
         for i in range(2):
-            yield lambda i=i: ts(T.CB[:, 128 * i:128 * i + 128], T.PBI[:, 0:128], 15.0 - i, A.is_equal, ["PBI"], ["CB" if i == 0 else "CBb"])
+            yield lambda i=i: ts(T.CB[:, 128 * i:128 * i + 128], T.CT2[:, 128:256], 15.0 - i, A.is_equal, ["CT2b"], ["CB" if i == 0 else "CBb"])
         for i in range(2):
             yield lambda i=i: tt(T.SRB[:, 128 * i:128 * i + 128], T.CB[:, 128 * i:128 * i + 128], T.GBH[:], A.mult, ["CB", "CBb", "GBH"], ["SRB%d" % i])
         for h in range(4):
@@ -352,14 +365,19 @@ def rank_program(g, core, T, topo):
         yield lambda: join("LX4", ["LX4_%d" % h for h in range(4)])
         yield lambda: ts(T.CB1[:], T.C8[:], T.PC[:, 12:13], A.subtract, ["C8", "PC12"], ["CB1"], P1, A.is_equal)
         yield lambda: ts(T.LT[:, 0:2], T.CF[:, 0:2], PL7, A.add, ["CF", "PC"], ["LT"], PL7, A.add)
-        yield lambda: ts(T.WF[:, 2:3], PLOW, P1, A.subtract, ["PC"], ["WF2"], 0.5, A.mult)
-        for o in range(2):
-            yield lambda o=o: ts(T.LX5[:, 8 * o:8 * o + 8], T.TH[:, 0:8], T.LT[:, o:o + 1], A.add, ["THS", "LT"], ["LX5_%d" % o])
         yield lambda: ts(T.D16[:, 0:8], T.CF[:, 0:8], T.WF[:, 2:3], A.is_equal, ["CF", "WF2"], ["D16"])
+        for o in range(2):
+            yield lambda o=o: ts(T.LX5[:, 8 * o:8 * o + 8], T.ZB[:, 0:8], T.LT[:, o:o + 1], A.add, ["ZB", "LT"], ["LX5_%d" % o])
 
     late = list(late_constants())
-    gaps = {(1, 0): late[0:5], (1, 1): late[5:9], (2, 0): late[9:14], (2, 1): late[14:18], (4, 0): late[18:21], (4, 1): late[21:24]}
+    first = list(first_constants())
+    gaps = {(0, 0): first[0:12], (0, 3): first[12:13], (0, 4): first[13:14], (0, 5): first[14:15], (0, 1): first[15:17], (0, 2): late[0:1],
+            (1, 0): late[1:4], (1, 1): late[4:6], (1, 2): late[6:7], (2, 0): late[7:13], (2, 1): late[13:15],
+            (2, 2): late[15:23], (4, 0): late[23:26], (4, 1): late[26:28]}
 
+    pending = []
+    SZ8 = 2
+    FILL = [(4, 5), (0, 1)]
     for t in range(NB):
         frm, to = (prv, nxt) if t % 2 == 0 else (nxt, prv)
         far, fk = (T.TB, "TB") if t % 2 == 0 else (T.TA, "TA")
@@ -371,12 +389,16 @@ def rank_program(g, core, T, topo):
             end = m == NB * ND - 1
             z, zk = (s_, sk) if d == 0 else (T.Z[:], "Z")
 
-            op("p", [mm(T.G4[:, 0:128], wm[:, 128 * ll:128 * ll + 128], z[:, ll:256:2], ll == 0 and wm is T.WH, ll == 1 and wm is T.WL)
-                     for ll in range(2) for wm in (T.WH, T.WL)], WHL + [zk], ["@G4"])
+            def gap(i):
+                for f in gaps.get((m, i), []):
+                    f()
+
+            op("p", [mm(T.G4[:, 0:128], T[wm][:, 128 * ll:128 * ll + 128], z[:, ll:256:2], ll == 0 and wm == "WH", ll == 1 and wm == "WL")
+                     for ll in range(2) for wm in ("WH", "WL")], WHL + [zk], ["@G4"])
             Z8 = ["Z8_%d" % cl for cl in range(8)]
 
             def z8(cl):
-                cp(T.Z8[:, cl:2048:8], z, [zk], ["Z8_%d" % cl])
+                cp(T.Z8[:, cl:16 * NV:8], z[:, 0:2 * NV], [zk], ["Z8_%d" % cl])
 
             def acol(ch):
                 ts(T.ACOL[:, ch:ch + 1], T.KI[:, 1:2], 32.0, A.mult, ["KI1", "ABASE%d" % d], ["ACOL%d" % ch], T.ABASE[:, 2 * d + ch:2 * d + ch + 1], A.add)
@@ -390,25 +412,26 @@ def rank_program(g, core, T, topo):
             def lists(ch):
                 cp(T.OFF[:, 128 * ch:128 * ch + 128], T.CI[:, 128 * ch:128 * ch + 128], ["CI%d" % ch], ["OFF%d" % ch])
 
-            for cl in range(2):
-                act(T.Z8[:, cl:2048:8], z, F.Copy, [zk], ["Z8_%d" % cl])
-            for cl in (2, 3, 4):
-                z8(cl)
+            for cl in range(SZ8):
+                act(T.Z8[:, cl:16 * NV:8], z[:, 0:2 * NV], F.Copy, [zk], ["Z8_%d" % cl])
+            fill = pending[:] + [lambda cl=cl: z8(cl) for cl in range(SZ8, 8)]
+            del pending[:]
+            n0, n1 = FILL[min(d, 1)]
+            for f in fill[0:n0]:
+                f()
             ts(T.NI[:], T.G4[:, 0:128], -0.5, A.add, ["@G4"], ["NI"])
-            z8(5)
+            for f in fill[n0:n1]:
+                f()
             tt(T.UF[:], T.G4[:, 0:128], T.NI[:], A.subtract, ["@G4", "NI"], ["UF"])
             for ch in range(2):
                 act(T.SQ[:, 128 * ch:128 * ch + 128], T.UF[:], F.Square, ["UF", "SCOL%d" % ch], ["SQ%d" % ch], bias=T.SCOL[:, ch:ch + 1], scale=4096.0)
-            z8(6)
-            if m > 0:
-                acol(0)
-                acol(1)
+            for f in fill[n1:]:
+                f()
             floors(0)
-            z8(7)
-            places(0)
             floors(1)
-            lists(0)
+            places(0)
             places(1)
+            lists(0)
 
             def v_gather(ch, c0, c1):
                 a, b = 2048 * ch + 16 * c0, 2048 * ch + 16 * c1
@@ -425,30 +448,28 @@ def rank_program(g, core, T, topo):
 
             def p_diff(ch, c0, c1, bk):
                 a, b = 2048 * ch + 16 * c0, 2048 * ch + 16 * c1
-                op("p", [mm(T[bk][:, 0:b - a], IN, T.Z8[:, 16 * c0:16 * c1], True, False), mm(T[bk][:, 0:b - a], IB, T.DF[:, a:b], False, True)],
-                   ["IB", "IN", "DF%d_%d" % (ch, c0)] + Z8, ["@" + bk])
+                op("p", mm(T[bk][:, 0:b - a], IB, T.DF[:, a:b], False, True), ["IB", "DF%d_%d" % (ch, c0)], ["@" + bk])
 
             def s_abs(ch, c0, c1, bk):
                 a, b = 2048 * ch + 16 * c0, 2048 * ch + 16 * c1
                 act(T.AB[:, a:b], T[bk][:, 0:b - a], F.Abs, ["@" + bk], ["AB%d_%d" % (ch, c0)])
 
-            def dsum(src, ch, n, ob, keys):
-                op("p", [mm(T.K6[0:n, 2 * b + ch:256:32], src[:, 2048 * ch + b:2048 * ch + 16 * n:16], T.OB[:, 8 * ob:8 * ob + 8], False, False)
+            def dsum(src, ch, c0, c1, ob, keys):
+                op("p", [mm(T.K6[c0:c1, 2 * b + ch:256:32], src[:, 2048 * ch + 16 * c0 + b:2048 * ch + 16 * c1:16], T.OB[:, 8 * ob:8 * ob + 8], False, False)
                          for b in range(16)], keys + ["OB%d" % ob], ["@K6"])
 
             def unbarred(ch):
                 if d > 0:
                     tt(T.NE[:, 128 * ch:128 * ch + 128], T.LB[:, 0:128], T.CI[:, 128 * ch:128 * ch + 128], A.not_equal, ["@LB", "CI%d" % ch], ["NE%d" % ch])
 
-            def bar(ch):
-                ne = T.NE[:, 128 * ch:128 * ch + 128] if d > 0 else T.ZB[:]
-                op("p", mm(T.K6[:, 0:256], ne, T.PEN[:, 1 - ch:257 - ch], ch == 0, ch == 1), ["NE%d" % ch if d > 0 else "ZB", "PEN"], ["@K6"])
-
             def number(ch):
                 op("p", mm(T.K6[:, ch:256:2], T.CFL[:, 128 * ch:128 * ch + 128], T.IDF[:], False, False), ["CFL", "IDF"], ["@K6"])
 
             H, SM = NV // 2, NV + 32
             sc = [(0, NV, SM, "G0"), (0, SM, 128, "G1"), (1, NV, SM, "G2"), (1, SM, 128, "G3")]
+            op("p", mm(T.K6[:, 0:256], T.ZB[:], T.PEN[:, 0:256], True, False), ["ZB", "PEN"], ["@K6"])
+            for ch, c0, c1, bk in sc:
+                op("p", [mm(T[bk][:, cl:16 * (c1 - c0):8], IN, z[:, 2 * c0:2 * c1], cl == 0, False) for cl in range(8)], ["IN", zk], ["@" + bk])
             s_gather(*sc[0][:3])
             lists(1)
             s_gather(*sc[1][:3])
@@ -456,89 +477,102 @@ def rank_program(g, core, T, topo):
             v_gather(0, 0, NV)
             s_abs(*sc[0])
             p_diff(*sc[1])
-            unbarred(0)
-            bar(0)
-            dsum(T.DF, 0, NV, 1, ["DF0_0"])
             cp(T.CFL[:], T.CI[:], ["CI0", "CI1"], ["CFL"])
+            dsum(T.DF, 0, 0, NV, 1, ["DF0_0"])
             s_gather(*sc[2][:3])
             v_gather(1, 0, H)
             s_abs(*sc[1])
+            number(0)
             p_diff(*sc[2])
             number(1)
             v_half(0, 0, NV)
             s_gather(*sc[3][:3])
-            dsum(T.AB, 0, 128, 0, ["AB0_0", "AB0_%d" % NV, "AB0_%d" % SM])
+            dsum(T.AB, 0, 0, 128, 0, ["AB0_0", "AB0_%d" % NV, "AB0_%d" % SM])
             p_diff(*sc[3])
             v_gather(1, H, NV)
             s_abs(*sc[2])
-            number(0)
-            dsum(T.DF, 1, NV, 1, ["DF1_0", "DF1_%d" % H])
+            dsum(T.DF, 1, 0, NV, 1, ["DF1_0", "DF1_%d" % H])
             v_half(1, 0, H)
             s_abs(*sc[3])
             v_half(1, H, NV)
+            unbarred(0)
             unbarred(1)
-            dsum(T.AB, 1, 128, 0, ["AB1_0", "AB1_%d" % H, "AB1_%d" % NV, "AB1_%d" % SM])
-            bar(1)
+            dsum(T.AB, 1, 0, 128, 0, ["AB1_0", "AB1_%d" % H, "AB1_%d" % NV, "AB1_%d" % SM])
+            if d > 0:
+                op("p", mm(T.K6[:, 0:256:2], T.NE[:, 0:128], T.PEN[:, 1:256:2], False, False), ["NE0", "PEN"], ["@K6"])
+            op("p", mm(T.K6[:, 0:256], T.NE[:, 128:256] if d > 0 else T.ZB[:], T.PEN[:, 0:256], False, True), ["NE1" if d > 0 else "ZB", "PEN"], ["@K6"])
             dead = [(T.DLAND[:, 16 * t:16 * t + 16], "DLAND%d" % t)] + [(T.WB[:, 16 * i:16 * i + 16], "WB%d" % i) for i in range(d)]
             op("p", [mm(T.C7[:, 0:16], IB, a, i == 0, False) for i, (a, k) in enumerate(dead)], ["IB"] + [k for a, k in dead], ["@C7"])
             if d == 0 and t > 0:
                 near_rows(t - 1, 0)
                 near_rows(t - 1, 1)
-            for f in gaps.get((m, 0), []):
-                f()
+            gap(0)
+            op("p", [mm(T.LB[:, 256:512], IH, a, i == 0, False) for i, a in enumerate((s_, T.CQ[:, 0:256]))], ["IH", sk, "CQ0"], ["@LB"])
+            if m < 2:
+                act(T.TA[:, 2048 * m:2048 * m + 2048], T.TB[:, 2048 * m:2048 * m + 2048], F.Copy, ["TB"], ["TA" + "bc"[m]])
+            if m == 2:
+                starter_rows(1)
+                starter_rows(2)
             scan(T.R[:], T.RS[:], T.K6[:, 0:256], A.max, A.min, ["RS", "@K6"], ["R"])
+            gap(3)
             cp(T.RI[:], T.R[:, 15:256:16], ["R"], ["RI"])
+            gap(4)
             ts(T.RA[:], T.RI[:], 4095, A.bitwise_and, ["RI"], ["RA"])
+            gap(5)
             tt(T.E1[:], T.RA[:, 0:16].indirect(T.LX1[:]), T.M1[:], A.mult, ["RA", "LX1", "M1"], ["E1"])
             op("p", mm(T.C7[:, 0:16], T.E1[:], T.RS1[:], False, True), ["E1", "RS1"], ["@C7"])
             if d == 0 and t > 0:
                 near_add(t - 1)
-            if not tail:
-                cp(T.R4[:], T.RA[:, 0:16].indirect(T.LX3[:]), ["RA", "LX3"], ["R4"])
-            tt(T.DE[:], T.MSP[:], T.E1[:], A.subtract, ["MSP", "E1"], ["DE"])
+            else:
+                tt(T.DE[:], T.MSP[:], T.E1[:], A.subtract, ["MSP", "E1"], ["DE"])
             ts(T.YU[:], T.C7[:, 0:16], DEAD, A.min, ["@C7"], ["YU"])
             act(T.UP[:], far[:, 0:WX].indirect(T.YU[:]), F.Copy, [fk, "YU"], ["UP"])
             tt(T.QR[:], far[:, 0:WX].indirect(T.YU[:]), T.CR[:], A.mult, [fk, "YU", "CR"], ["QR"])
             act(T.GX[:], T.X[:, 0:WX].indirect(T.YU[:]), F.Copy, ["X", "YU"], ["GX"])
             ts(T.QO[:], T.QR[:], OCOL, A.mult, ["QR", "PC"], ["QO"])
+            if not tail:
+                cp(T.R4[:], T.RA[:, 0:16].indirect(T.LX3[:]), ["RA", "LX3"], ["R4"])
+            if d == 0 and t > 0:
+                tt(T.DE[:], T.MSP[:], T.E1[:], A.subtract, ["MSP", "E1"], ["DE"])
 
-            def unit(gr, ll, b, c):
+            def unit(gr, ll, bk, c):
                 p0, k = 32 * (gr // 2), 16 + 16 * (gr % 2)
-                q = T.QO if gr % 2 else T.QR
-                return mm(b[:, c:c + 128 + 128 * ll], T.UP[p0:p0 + k, ll:256:2], q[p0:p0 + k, 0:256:2 - ll], True, True)
+                q = "QO" if gr % 2 else "QR"
+                op("p", mm(T[bk][:, c:c + 128 + 128 * ll], T.UP[p0:p0 + k, ll:256:2], T[q][p0:p0 + k, 0:256:2 - ll], True, True), ["UP", q], ["@" + bk])
 
-            def v_units(q):
-                bk = ("G0", "G1", "G2", "G3")[q]
-                op("p", [unit(2 * q, 1, T[bk], 0), unit(2 * q, 0, T[bk], 256), unit(2 * q + 1, 0, T[bk], 384)], ["UP", "QR", "QO"], ["@" + bk])
-                scan(T.FL[:, 512 * q:512 * q + 512], T[bk][:], T.TH[:], A.max, A.add, ["@" + bk, "THS"], ["FL%d" % q])
+            def pv(q):
+                unit(2 * q, 1, "G%d" % q, 0)
+                unit(2 * q, 0, "G%d" % q, 256)
+                unit(2 * q + 1, 0, "G%d" % q, 384)
 
-            def s_unit(q):
+            def vv(q):
+                scan(T.FL[:, 512 * q:512 * q + 512], T["G%d" % q][:], T.TH[:], A.max, A.add, ["@G%d" % q, "THS"], ["FL%d" % q])
+
+            def ps(q):
+                unit(2 * q + 1, 1, ("G4", "K6")[q % 2], 0)
+
+            def ss(q):
                 bk = ("G4", "K6")[q % 2]
-                op("p", unit(2 * q + 1, 1, T[bk], 0), ["UP", "QO"], ["@" + bk])
                 act(T.JK[:, 256 * q:256 * q + 256], T[bk][:, 0:256], F.Relu, ["@" + bk, "THS"], ["JK%d" % q, "FL%d" % (4 + q)],
                     bias=T.TH[:, 255:256], accum_out=T.FL[:, 2048 + q:2049 + q])
 
             ns = T.NSND[:, 256 * m:256 * m + 256]
-            v_units(0)
-            s_unit(0)
-            v_units(1)
-            op("p", [mm(T.C7[:, 256:512], IH, a, i == 0, i == 3) for i, a in enumerate((T.GX[:], s_, T.CQ[:, 0:256], T.CQ[:, 256:512]))],
-               ["IH", "GX", sk, "CQ0", "CQ1"], ["@C7"])
-            s_unit(1)
-            act(ns, T.C7[:, 256:512], F.Copy, ["@C7"], ["NSND%d" % m], bias=-MAGIC)
-            if not tail:
-                send(to, "n%d%d" % (t, d), T.NLAND[:, 256 * m:256 * m + 256], ns, ["NSND%d" % m])
-            v_units(2)
-            s_unit(2)
-            v_units(3)
-            s_unit(3)
+
+            def pn():
+                op("p", [mm(T.LB[:, 256:512], IH, a, False, i == 1) for i, a in enumerate((T.GX[:], T.CQ[:, 256:512]))], ["IH", "GX", "CQ1"], ["@LB"])
+
+            def sn():
+                act(ns, T.LB[:, 256:512], F.Copy, ["@LB"], ["NSND%d" % m], bias=-MAGIC)
+                if not tail:
+                    send(to, "n%d%d" % (t, d), T.NLAND[:, 256 * m:256 * m + 256], ns, ["NSND%d" % m])
+
+            pv(0); vv(0); ps(0); ss(0); pv(1); vv(1); ps(1); ss(1); pv(2); vv(2); pn(); sn(); ps(2); ss(2); pv(3); vv(3); ps(3); ss(3)
             op("p", mm(T.C7[:, 16:32], T.E1[:], T.RS1[:], True, False), ["E1", "RS1"], ["@C7"])
             if not tail:
                 op("p", mm(T.LB[:, 0:128], T.R4[:], T.IDF[:], True, True), ["R4", "IDF"], ["@LB"])
             tt(T.E2[:], T.FL[:, 0:2056].indirect(T.LX2[:]), T.DE[:], A.min, ["FL%d" % i for i in range(8)] + ["LX2", "DE"], ["E2"])
             op("p", mm(T.C7[:, 16:32], T.E2[:], T.RS1[:], False, True), ["E2", "RS1"], ["@C7"])
-            for f in gaps.get((m, 1), []):
-                f()
+            gap(1)
             if end:
                 ts(T.CB[:], T.HL[:, 0:256], 16.0, A.mult, ["HI0"], ["CB", "CBb"], -1.0, A.add)
             ls = T.LSND[:, 16 * m:16 * m + 16]
@@ -548,11 +582,11 @@ def rank_program(g, core, T, topo):
                 send(to, "l%d%d" % (t, d), T.LLAND[:, 16 * m:16 * m + 16], ls, [lk])
             wb = T.WB[:, 16 * d:16 * d + 16]
 
-            def result():
+            def result(out, key):
                 if d == 0:
-                    cp(T.RES[:], T.C7[:, 16:32], ["@C7"], ["RES"])
+                    cp(out, T.C7[:, 16:32], ["@C7"], [key])
                 else:
-                    tt(T.RES[:], T.C7[:, 16:32], T.RES[:], A.min, ["@C7", "RES"], ["RES"])
+                    tt(out, T.C7[:, 16:32], T.RES[:], A.min, ["@C7", "RES"], [key])
 
             def own_records():
                 cp(T.X[:, 0:WX].indirect(ls), ns, [lk, "NSND%d" % m], ["X"])
@@ -561,58 +595,74 @@ def rank_program(g, core, T, topo):
                 tt(far[:, 0:WX].indirect(ls), T.UP[:], T.RC[:, 256 * t:256 * t + 256], A.add, ["UP", "RC%d" % t, lk], [fk])
 
             if end:
-                result()
+                r_ = T.RSND[:, 32 * t:32 * t + 16]
+                result(r_, "RSH")
+                send(frm, "r%d" % t, T.RLAND[:, 32 * t:32 * t + 16], r_, ["RSH"])
                 own_records()
                 dma("y", [(T.yx[:], T.X[:, 0:W])], ["X"], ["yx"])
-                near_send(t)
                 far_table()
                 break
             ts(wb, T.C7[:, 16:32], DEAD, A.is_lt, ["@C7"], ["WB%d" % d], DEAD, A.mult)
             op("p", mm(T.G0[:, 0:16], T.ONES[:], wb, True, True), ["ONES", "WB%d" % d], ["@G0"])
             act(T.KJ[:], T.G0[:, 0:16], F.Copy, ["@G0"], ["KJ", "KP"], scale=1.0 / DEAD, accum_out=T.KP[:, 0:1])
-            k1 = lambda: cp(T.KI[:, 0:1], T.KP[:, 0:1], ["KP"], ["KI0"])
-            k2 = lambda: ts(T.KI[:, 1:2], T.KI[:, 0:1], 31, A.bitwise_and, ["KI0"], ["KI1"])
+            dn = (d + 1) % ND
+            kappa = [lambda: cp(T.KI[:, 0:1], T.KP[:, 0:1], ["KP"], ["KI0"]),
+                     lambda: ts(T.KI[:, 1:2], T.KI[:, 0:1], 31, A.bitwise_and, ["KI0"], ["KI1"])]
+            kappa += [lambda ch=ch: ts(T.ACOL[:, ch:ch + 1], T.KI[:, 1:2], 32.0, A.mult, ["KI1", "ABASE%d" % dn], ["ACOL%d" % ch],
+                                       T.ABASE[:, 2 * dn + ch:2 * dn + ch + 1], A.add) for ch in range(2)]
             if tail:
                 own_records()
-                result()
+                result(T.RES[:], "RES")
                 starters_send(t + 1)
                 far_table()
                 dead_list(t + 1)
-                k1()
+                kappa[0]()
                 near_send(t)
-                k2()
+                kappa[1]()
                 dead_send(t + 1)
                 records_send(t + 1)
+                kappa[2]()
+                kappa[3]()
+                gap(2)
                 continue
             far_table()
             act(T.PG[:], far[:, 0:WX].indirect(T.YU[:]), F.Copy, [fk, "YU"], ["PG"])
-            result()
+            result(T.RES[:], "RES")
             to_list(lambda b: T.PG[:, b:256:16], ["PG"])
-            own_records()
+            kappa[0]()
+            if m == 1:
+                spare_columns("TA")
+                fill_rows("TA", 0)
             if m == ND * NB - 2:
                 dma("y", [(T.HL[:, 0:256], T.TA[15:128:16, 0:W]), (T.HL[:, 256:512], T.TA[14:128:16, 0:W])], ["TA"], ["HI0", "LO0"])
-            k1()
-            ts(T.PU[:], T.C7[:, 32:48], -1.0, A.add, ["@C7"], ["PU"])
-            k2()
+            kappa[1]()
+            gap(2)
             msg = "%d%d" % (t, d)
             if d == 0:
                 landed(frm, "b%d" % t, [xk + "b"])
                 join(xk, [xk + "b", xk + "x"])
             landed(frm, "n" + msg, ["NLAND%d" % m])
             landed(frm, "l" + msg, ["LLAND%d" % m])
+            kappa[2]()
+            kappa[3]()
             cp(XC[:, 0:WX].indirect(T.LLAND[:, 16 * m:16 * m + 16]), T.NLAND[:, 256 * m:256 * m + 256], ["NLAND%d" % m, "LLAND%d" % m], [xk])
-            cp(T.Z[:], XC[:, 0:WX].indirect(T.PU[:]), [xk, "PU"], ["Z"])
-    dma("y", [(T.HL[:, 512:768], T.TB[15:128:16, 0:W]), (T.HL[:, 768:1024], T.TB[14:128:16, 0:W])], ["TB"], ["HI1", "LO1"])
+            ts(T.PU[:], T.C7[:, 32:48], -1.0, A.add, ["@C7"], ["PU"])
+            act(T.Z[:], XC[:, 0:WX].indirect(T.PU[:]), F.Copy, [xk, "PU"], ["Z"])
+            own_records()
+    op("p", [mm(T.G0[:, 0:256], T.SW[:, 16 - k:144 - k], T.TB[:, 256 * k:256 * k + 256], k == 0, k == 15) for k in range(16)], ["SW", "TB"], ["@G0"])
     t = NB - 1
     tt(T.PF[:, 0:256], T.CB[:], T.HL[:, 256:512], A.add, ["CB", "CBb", "LO0"], ["YA0"])
     landed(nxt if t % 2 == 0 else prv, "r%d" % t, ["RLAND%d" % t])
+    r_ = T.RLAND[:, 32 * t:32 * t + 16]
+    ts(T.W1[:], r_, DEAD, A.is_lt, ["RLAND%d" % t], ["W1"])
+    ts(T.W2[:], r_, 1.0, A.add, ["RLAND%d" % t], ["W2"])
+    tt(T.W3[:], T.W1[:], T.W2[:], A.mult, ["W1", "W2"], ["W3"])
     for o, e in enumerate(("E1", "E2")):
-        tt(T[e][:], T.RLAND[:, 32 * t:32 * t + 16].indirect(T.LX5[:, 8 * o:8 * o + 8]), T.CB1[:], A.mult, ["RLAND%d" % t, "LX5_%d" % o, "CB1"], [e])
+        tt(T[e][:], T.W3[:, 0:16].indirect(T.LX5[:, 8 * o:8 * o + 8]), T.CB1[:], A.mult, ["W3", "LX5_%d" % o, "CB1"], [e])
         op("p", mm(T.G4[:, 8 * o:8 * o + 8], T[e][:], T.D16[:, 0:8], True, True), [e, "D16"], ["@G4"])
-    ts(T.DIAG[:], T.HL[:, 512:768], 16.0, A.mult, ["HI1"], ["DIAG"], -1.0, A.add)
-    tt(T.PF[:, t:256:16], T.G4[:, 0:16], T.PF[:, t:256:16], A.add, ["@G4", "YA0"], ["YA0"])
-    tt(T.PF[:, 256:512], T.DIAG[:], T.HL[:, 768:1024], A.add, ["DIAG", "LO1"], ["YB0"])
-    dma("y", [(T.ya[:], T.PF[:, 0:256])], ["YA0"], ["ya"])
+    act(T.PF[:, 256:512], T.G0[:, 0:256], F.Copy, ["@G0"], ["YB0"], bias=-1.0)
     dma("s", [(T.yb[:], T.PF[:, 256:512])], ["YB0"], ["yb"])
+    tt(T.PF[:, t:256:16], T.G4[:, 0:16], T.PF[:, t:256:16], A.add, ["@G4", "YA0"], ["YA0"])
+    dma("y", [(T.ya[:], T.PF[:, 0:256])], ["YA0"], ["ya"])
     for sem in sorted(last):
         need("g", {sem: last[sem]})

@@ -23,10 +23,10 @@ _sb("HL", 1024, "bfloat16"); _sb("CB", 256, "float32"); _sb("PF", 512, "float32"
 _sb("WI", 8, "int32"); _sb("WF", 8, "float32")
 _sb("PI", 8, "int32"); _sb("PT", 8, "int32"); _sb("PC", 32, "float32"); _sb("SG", 16, "float32")
 _sb("CF", 264, "float32"); _sb("LANE", 256, "float32"); _sb("C8", 128, "float32"); _sb("CB1", 128, "float32"); _sb("SPI", 128, "float32")
-_sb("CG", 128, "float32"); _sb("WH", 256, "bfloat16"); _sb("WL", 256, "bfloat16")
+_sb("CG", 128, "float32"); _sb("WP", 256, "float16"); _sb("WN", 256, "float16")
 _sb("OB", 16, "bfloat16"); _sb("IDF", 128, "float32"); _sb("PEN", 264, "bfloat16"); _sb("ZB", 128, "bfloat16")
 _sb("IBN", 384, "bfloat16")
-_sb("CQ", 512, "bfloat16")
+_sb("CQ", 640, "bfloat16")
 _sb("M1", 128, "float32"); _sb("MSP", 128, "float32"); _sb("RS1", 16, "float32"); _sb("RS", 256, "float32")
 _sb("CR", 256, "bfloat16"); _sb("RC", 256 * NB, "bfloat16"); _sb("TH", 512, "float32"); _sb("SW", 144, "bfloat16")
 _sb("ONES", 128, "bfloat16"); _sb("DIAG", 256, "float32"); _sb("SRB", 256, "bfloat16"); _sb("GBH", 128, "float32"); _sb("D16", 16, "float32")
@@ -39,13 +39,13 @@ _sb("NSND", 256 * NB * ND, "bfloat16"); _sb("NLAND", 256 * NB * ND, "bfloat16")
 _sb("LSND", 16 * NB * ND, "uint16"); _sb("LLAND", 16 * NB * ND, "uint16")
 _sb("RSND", 32 * NB, "float32"); _sb("RLAND", 32 * NB, "float32")
 _sb("Z", 256, "bfloat16"); _sb("Z8", 2048, "bfloat16")
-_sb("NI", 128, "int32"); _sb("UF", 128, "float32"); _sb("SQ", 256, "float32"); _sb("FI", 256, "int32"); _sb("CI", 256, "int32")
+_sb("SQ", 256, "float32"); _sb("FI", 256, "int32"); _sb("CI", 256, "int32")
 _sb("OFF", 256, "uint16"); _sb("CFL", 256, "float32"); _sb("NE", 256, "bfloat16")
 _sb("DF", 4096, "bfloat16"); _sb("AB", 4096, "bfloat16")
 _sb("R", 256, "float32"); _sb("RI", 16, "int32"); _sb("RA", 16, "int32"); _sb("E1", 128, "float32"); _sb("DE", 128, "float32")
 _sb("R4", 128, "float32"); _sb("E2", 128, "float32"); _sb("YU", 16, "uint16")
 _sb("UP", 256, "bfloat16"); _sb("QR", 256, "bfloat16"); _sb("QO", 256, "bfloat16"); _sb("GX", 256, "bfloat16")
-_sb("FL", 2056, "float32"); _sb("JK", 1024, "bfloat16"); _sb("PG", 256, "bfloat16"); _sb("PU", 16, "uint16"); _sb("E3", 512, "bfloat16")
+_sb("FL", 2056, "float32"); _sb("JK", 1152, "bfloat16"); _sb("PG", 256, "bfloat16"); _sb("PU", 16, "uint16"); _sb("E3", 512, "bfloat16")
 _sb("WB", 16 * ND, "bfloat16"); _sb("RES", 16, "float32"); _sb("W1", 16, "float32"); _sb("W2", 16, "float32"); _sb("W3", 16, "float32")
 _sb("KP", 8, "float32"); _sb("KJ", 16, "float32"); _sb("KI", 8, "int32")
 for _n in ["G0", "G1", "G2", "G3", "G4", "K6", "C7", "LB"]:
@@ -170,7 +170,10 @@ def rank_program(g, core, T, topo):
     def starters_send(t):
         s = T.SSND[:, 256 * t:256 * t + 256]
         cp(s[:, 0:256:2], T.X[:, t:W // 2:16], ["X"], ["SS0_%d" % t])
-        act(s[:, 1:256:2], T.X[:, W // 2 + t:W:16], F.Copy, ["X"], ["SS1_%d" % t])
+        if t == 0:
+            cp(s[:, 1:256:2], T.X[:, W // 2 + t:W:16], ["X"], ["SS1_%d" % t])
+        else:
+            act(s[:, 1:256:2], T.X[:, W // 2 + t:W:16], F.Copy, ["X"], ["SS1_%d" % t])
         send(nxt if t % 2 == 0 else prv, "s%d" % t, T.SLAND[:, 256 * t:256 * t + 256], s, ["SS0_%d" % t, "SS1_%d" % t])
         landed(prv if t % 2 == 0 else nxt, "s%d" % t, ["SLAND%d" % t])
 
@@ -241,33 +244,32 @@ def rank_program(g, core, T, topo):
         act(T.TB[:, n:2 * n], T.TB[:, 0:n], F.Copy, ["TBb", "SG"], ["TBb"], scale=T.SG[:, r:r + 1])
     ts(T.PC[:, 12:13], PGRP, 2.0, A.mult, ["PC"], ["PC12"])
     ts(T.PC[:, 13:14], PGRP, 2.0, A.mult, ["PC"], ["PC13"], 1.0, A.add)
-    ts(T.PC[:, 14:15], PGRP, 16.0, A.mult, ["PC"], ["PC14"], 16.0, A.add)
-    ts(T.PC[:, 15:16], I15, 16.0, A.mult, ["PCI"], ["PC15"], I14, A.add)
-    ts(T.IDF[:], T.CF[:, 0:128], PP, A.is_equal, ["CF", "PC"], ["IDF"])
-    ts(T.DSND[:, 0:16], T.PAI[:, 0:256:16], 0.0, A.is_ge, ["PAI"], ["DSND0"], DEAD, A.mult)
-    send(nxt, "e0", T.DLAND[:, 16 * NB:16 * NB + 16], T.DSND[:, 0:16], ["DSND0"])
-    landed(prv, "e0", ["DRAW"])
-    iota("SPI", [[0, 64], [1, 2]], DUM, 2)
-    iota("CG", [[2, 8], [0, 8], [1, 2]], 0, 0)
-    ts(T.WI[:, 2:3], T.WI[:, 0:1], 3840, A.bitwise_and, ["WI"], ["WI2"])
-    ts(T.WI[:, 3:4], T.WI[:, 0:1], 255, A.bitwise_and, ["WI"], ["WI3"])
-    ts(T.SW[:], T.CF[:, 0:144], T.PC[:, 14:15], A.is_equal, ["CF", "PC14", "PC15"], ["SW"], T.PC[:, 15:16], A.mult)
-    ts(T.WF[:, 0:2], T.WI[:, 2:4], 1.0 / 4096, A.mult, ["WI2", "WI3"], ["WF"])
     for ch in range(2):
         ts(T.SCOL[:, ch:ch + 1], PL7, 32.0, A.mult, ["PC"], ["SCOL%d" % ch], 256.0 * ch + 16.0, A.add)
-    for ll in range(2):
-        for wm, c in (("WH", 0), ("WL", 1)):
-            ts(T[wm][:, 128 * ll:128 * ll + 128], T.C8[:], T.PC[:, 12 + ll:13 + ll], A.is_equal, ["C8", "PC12", "PC13", "WF"], ["%s%d" % (wm, ll)], T.WF[:, c:c + 1], A.mult)
-    WHL = ["WH0", "WH1", "WL0", "WL1"]
+    ts(T.PC[:, 23:24], PP, 2.0, A.mult, ["PC"], ["PC23"], 1.0, A.add)
+    ts(IH, T.CF[:, 0:128], PP, A.is_equal, ["CF", "PC"], ["IH"], 0.5, A.mult)
     tt(T.SCOL[:, 2:4], T.SCOL[:, 0:2], T.SCOL[:, 0:2], A.mult, ["SCOL0", "SCOL1"], ["SCOL2"])
-    ts(IB, T.CF[:, 0:128], PP, A.is_equal, ["CF", "PC"], ["IB"])
-    for d in range(ND):
-        ts(T.ABASE[:, 2 * d:2 * d + 2], T.SCOL[:, 2:4], -1.0, A.mult, ["SCOL2"], ["ABASE%d" % d], 262144.0 - 12.0 + 32.0 * 97 * d, A.add)
     ts(IN, T.CF[:, 0:128], PP, A.is_equal, ["CF", "PC"], ["IN"], -1.0, A.mult)
-    cp(T.ACOL[:, 0:2], T.ABASE[:, 0:2], ["ABASE0"], ["ACOL0", "ACOL1"])
+    ts(T.ACOL[:, 0:2], T.SCOL[:, 2:4], -1.0, A.mult, ["SCOL2"], ["ACOL0", "ACOL1"], 262144.0 - 12.0, A.add)
+    ts(T.WF[:, 3:4], T.WI[:, 0:1], 2048.0, A.is_gt, ["WI"], ["WF3"], -4096.0, A.mult)
+    ms(T.ONES[:], 1.0, ["ONES"])
+    ts(T.WF[:, 0:1], T.WI[:, 0:1], T.WF[:, 3:4], A.add, ["WI", "WF3"], ["WF0"], 1.0 / 4096, A.mult)
+    ts(T.WF[:, 1:2], T.WI[:, 0:1], T.WF[:, 3:4], A.add, ["WI", "WF3"], ["WF1"], -1.0 / 4096, A.mult)
+    ts(T.DSND[:, 0:16], T.PAI[:, 0:256:16], 0.0, A.is_ge, ["PAI"], ["DSND0"], DEAD, A.mult)
+    iota("SPI", [[0, 64], [1, 2]], DUM, 2)
+    iota("CG", [[2, 8], [0, 8], [1, 2]], 0, 0)
+    send(nxt, "e0", T.DLAND[:, 16 * NB:16 * NB + 16], T.DSND[:, 0:16], ["DSND0"])
+    landed(prv, "e0", ["DRAW"])
+    for ll in range(2):
+        for wm, c in (("WP", 0), ("WN", 1)):
+            ts(T[wm][:, 128 * ll:128 * ll + 128], T.C8[:], T.PC[:, 12 + ll:13 + ll], A.is_equal, ["C8", "PC12", "PC13", "WF%d" % c], ["%s%d" % (wm, ll)], T.WF[:, c:c + 1], A.mult)
+    ms(T.CQ[:, 256:512], 2 * MAGIC, ["CQ1"])
+    ms(T.CQ[:, 512:640], -2 * MAGIC, ["CQ2"])
+    ts(IB, T.CF[:, 0:128], PP, A.is_equal, ["CF", "PC"], ["IB"])
+    ts(T.IDF[:], T.CF[:, 0:128], PP, A.is_equal, ["CF", "PC"], ["IDF"])
     for i in range(2):
         ts(T.OB[:, 8 * i:8 * i + 8], T.CF[:, 0:8], PGRP, A.is_equal, ["CF", "PC"], ["OB%d" % i], 4096.0 * (1 - 2 * i), A.mult)
-    ts(T.PC[:, 23:24], PP, 2.0, A.mult, ["PC"], ["PC23"], 1.0, A.add)
+    ts(T.PEN[:], T.CF[:], T.PC[:, 23:24], A.is_equal, ["CF", "PC23"], ["PEN"], -2.0 ** 24, A.mult)
 
     def table_rows(pin, pk, i):
         hi, lo = T.HL[:, 512 * i:512 * i + 256], T.HL[:, 512 * i + 256:512 * i + 512]
@@ -279,7 +281,6 @@ def rank_program(g, core, T, topo):
     def fill_rows(tab, i):
         dma("y", [(T[tab][15:128:16, 0:W], T.HL[:, 512 * i:512 * i + 256]), (T[tab][14:128:16, 0:W], T.HL[:, 512 * i + 256:512 * i + 512])],
             ["HI%d" % i, "LO%d" % i], [tab + "b", tab + "c", tab + "d"])
-        join(tab, [tab + "d", tab + "x"])
 
     def spare_columns(tab):
         act(T[tab][:, W:WX], T.XC1[:, W:WX], F.Identity, ["XC1x", "PC16"], [tab + "x"], bias=T.PC[:, 16:17])
@@ -289,59 +290,66 @@ def rank_program(g, core, T, topo):
 
     rows_b = table_rows(T.PBI, "PBI", 1)
     rows_b[0]()
-    ts(T.PEN[:], T.CF[:], T.PC[:, 23:24], A.is_equal, ["CF", "PC23"], ["PEN"], -2.0 ** 24, A.mult)
+    ts(T.WF[:, 2:3], PLOW, P1, A.subtract, ["PC"], ["WF2"], 0.5, A.mult)
+    ts(T.PC[:, 16:17], I14, 40.0, A.mult, ["PCI"], ["PC16"])
     rows_b[1]()
     ms(T.XC1[:, W:WX], 0.0, ["XC1x"])
     rows_b[2]()
-    ts(T.PC[:, 16:17], I14, 40.0, A.mult, ["PCI"], ["PC16"])
     ts(T.PC[:, 17:18], PLOW, 12.0, A.is_lt, ["PC"], ["PC17"], 128.0 * SC, A.mult)
-    rows_b[3]()
     ts(T.PC[:, 18:19], I12, -SC, A.mult, ["PCI"], ["PC18"])
-    ts(T.PC[:, 20:23], T.CF[:, 1:4], I14, A.mult, ["CF", "PCI"], ["PC20"])
-    ts(T.PC[:, 19:20], I14, SC, A.mult, ["PCI", "PC17"], ["PC19"], T.PC[:, 17:18], A.add)
     starters_send(0)
-    spare_columns("TB")
+    rows_b[3]()
+    ts(T.PC[:, 19:20], I14, SC, A.mult, ["PCI", "PC17"], ["PC19"], T.PC[:, 17:18], A.add)
+    ts(T.PC[:, 20:23], T.CF[:, 1:4], I14, A.mult, ["CF", "PCI"], ["PC20"])
     need("y", deps([], ["SS0_0"]))
     fill_rows("TB", 1)
     need("g", deps(["TBd"], []))
     records_send(0)
-    act(T.CR[:], T.LANE[:], F.Identity, ["LANE", "PC18", "PC19"], ["CR"], scale=T.PC[:, 18:19], bias=T.PC[:, 19:20])
-    act(IH, T.IDF[:], F.Copy, ["IDF"], ["IH"], scale=0.5)
-    starter_rows(0)
-    ts(T.WF[:, 2:3], PLOW, P1, A.subtract, ["PC"], ["WF2"], 0.5, A.mult)
     ts(T.WB[:, 0:8], T.CF[:, 0:8], PL7, A.is_equal, ["CF", "PC"], ["WB0"])
     ts(T.R4[:], T.CG[:], P8, A.is_equal, ["CG", "PC"], ["R4"])
     for o in range(2):
         ts(T.LX0[:, 8 * o:8 * o + 8], T.ZB[:, 0:8], T.WF[:, 2:3], A.add, ["ZB", "WF2"], ["LX0_%d" % o], 8.0 * o, A.add)
     ms(T.RS[:, 0:256:16], 2.0 ** 26, ["RS"])
-    for o in range(2):
-        tt(T.E3[:, 128 * o:128 * o + 128], T.DLAND[:, 16 * NB:16 * NB + 16].indirect(T.LX0[:, 8 * o:8 * o + 8]), T.R4[:], A.mult,
-           ["DRAW", "LX0_%d" % o, "R4"], ["E3_%d" % o])
-        op("p", mm(T.C7[:, 32 + o:48:2], T.E3[:, 128 * o:128 * o + 128], T.WB[:, 0:8], True, True), ["E3_%d" % o, "WB0"], ["@C7"])
     ts(T.M1[:], T.CB1[:], PL7, A.is_equal, ["CB1", "PC"], ["M1"])
     ts(T.RS1[:], T.CF[:, 0:16], P8, A.is_equal, ["CF", "PC"], ["RS1"])
     ts(T.LX1[:], T.CF[:, 0:16:2], P1, A.add, ["CF", "PC"], ["LX1"])
-    ts(T.LX3[:], T.CF[:, 0:16:2], PLL, A.add, ["CF", "PC"], ["LX3"])
-    cp(T.DLAND[:, 0:16], T.C7[:, 32:48], ["@C7"], ["DLAND0"])
-    tt(T.MSP[:], T.M1[:], T.SPI[:], A.mult, ["M1", "SPI"], ["MSP"])
-    ms(T.TH[:], 0.0, ["TH"])
+    for o in range(2):
+        tt(T.E3[:, 128 * o:128 * o + 128], T.DLAND[:, 16 * NB:16 * NB + 16].indirect(T.LX0[:, 8 * o:8 * o + 8]), T.R4[:], A.mult,
+           ["DRAW", "LX0_%d" % o, "R4"], ["E3_%d" % o])
+
+    def first_dead_list():
+        for o in range(2):
+            op("p", mm(T.C7[:, 32 + o:48:2], T.E3[:, 128 * o:128 * o + 128], T.WB[:, 0:8], True, True), ["E3_%d" % o, "WB0"], ["@C7"])
+
+    op("g", lambda: g.iota(T.TH[:], [[0, 512]], 0, 0, allow_small_or_imprecise_dtypes=True), [], ["TH"])
+
+    def scalar_constants():
+        spare_columns("TB")
+        join("TB", ["TBd", "TBx"])
+        act(T.CR[:], T.LANE[:], F.Identity, ["LANE", "PC18", "PC19"], ["CR"], scale=T.PC[:, 18:19], bias=T.PC[:, 19:20])
+        starter_rows(0)
 
     def first_constants():
         yield lambda: ms(T.CQ[:, 0:256], -0.5, ["CQ0"])
-        yield lambda: ms(T.CQ[:, 256:512], 2 * MAGIC, ["CQ1"])
+        yield lambda: tt(T.MSP[:], T.M1[:], T.SPI[:], A.mult, ["M1", "SPI"], ["MSP"])
+        yield lambda: ts(T.LX3[:], T.CF[:, 0:16:2], PLL, A.add, ["CF", "PC"], ["LX3"])
         yield lambda: ts(T.TH[:, 255:256], PP, SC, A.mult, ["PC", "TH"], ["TH1"], (128 - 1536) * SC, A.add)
         for c in (383, 511):
             yield lambda c=c: ts(T.TH[:, c:c + 1], PP, SC, A.mult, ["PC", "TH"], ["TH%d" % c], -1536 * SC, A.add)
         yield lambda: join("THS", ["TH", "TH1", "TH383", "TH511"])
         for i, (c0, step, base) in enumerate(((0, 512.0, 383.0), (1, 512.0, 511.0), (8, 512.0, 255.0), (9, 1.0, 2048.0))):
             yield lambda i=i, c0=c0, step=step, base=base: ts(T.LT[:, 16 + c0:16 + c0 + 7:2], T.CF[:, 0:4], step, A.mult, ["CF"], ["LT%d" % i], base, A.add)
-        yield lambda: ms(T.FL[:, 2048:2056], 0.0, ["FL4", "FL5", "FL6", "FL7"])
+        yield lambda: (ms(T.FL[:, 2048:2056], 0.0, ["FL4", "FL5", "FL6", "FL7"]), ms(T.FL[:, 384:512], 0.0, ["FL8"]))
         yield lambda: tt(T.LT[:, 32:40], T.LT[:, 24:32], T.LT[:, 16:24], A.subtract, ["LT0", "LT1", "LT2", "LT3"], ["LT4"])
         yield lambda: ts(T.LT[:, 40:48], T.LT[:, 32:40], P1, A.mult, ["LT4", "PC"], ["LT5"])
         yield lambda: tt(T.LT[:, 32:40], T.LT[:, 40:48], T.LT[:, 16:24], A.add, ["LT5", "LT0", "LT1"], ["LT4"])
         yield lambda: cp(T.LX2[:], T.LT[:, 32:40], ["LT4"], ["LX2"])
-        yield lambda: ms(T.ONES[:], 1.0, ["ONES"])
+        yield lambda: ts(T.PC[:, 14:15], PGRP, 16.0, A.mult, ["PC"], ["PC14"], 16.0, A.add)
+        yield lambda: ts(T.PC[:, 15:16], I15, 16.0, A.mult, ["PCI"], ["PC15"], I14, A.add)
         yield lambda: ms(T.XC0[:, W:WX], 0.0, ["XC0x"])
+        yield lambda: ts(T.SW[:], T.CF[:, 0:144], T.PC[:, 14:15], A.is_equal, ["CF", "PC14", "PC15"], ["SW"], T.PC[:, 15:16], A.mult)
+        for d in range(ND):
+            yield lambda d=d: ts(T.ABASE[:, 2 * d:2 * d + 2], T.SCOL[:, 2:4], -1.0, A.mult, ["SCOL2"], ["ABASE%d" % d], 262144.0 - 12.0 + 32.0 * 97 * d, A.add)
 
     def late_constants():
         for f in table_rows(T.PAI, "PAI", 0):
@@ -371,13 +379,11 @@ def rank_program(g, core, T, topo):
 
     late = list(late_constants())
     first = list(first_constants())
-    gaps = {(0, 0): first[0:12], (0, 3): first[12:13], (0, 4): first[13:14], (0, 5): first[14:15], (0, 1): first[15:17], (0, 2): late[0:1],
+    gaps = {(0, 0): first[0:13], (0, 3): first[13:14], (0, 4): first[14:15], (0, 5): first[15:16], (0, 6): first[16:18], (0, 1): first[18:20],
+            (0, 2): first[20:23] + late[0:1],
             (1, 0): late[1:4], (1, 1): late[4:6], (1, 2): late[6:7], (2, 0): late[7:13], (2, 1): late[13:15],
             (2, 2): late[15:23], (4, 0): late[23:26], (4, 1): late[26:28]}
 
-    pending = []
-    SZ8 = 2
-    FILL = [(4, 5), (0, 1)]
     for t in range(NB):
         frm, to = (prv, nxt) if t % 2 == 0 else (nxt, prv)
         far, fk = (T.TB, "TB") if t % 2 == 0 else (T.TA, "TA")
@@ -393,15 +399,18 @@ def rank_program(g, core, T, topo):
                 for f in gaps.get((m, i), []):
                     f()
 
-            op("p", [mm(T.G4[:, 0:128], T[wm][:, 128 * ll:128 * ll + 128], z[:, ll:256:2], ll == 0 and wm == "WH", ll == 1 and wm == "WL")
-                     for ll in range(2) for wm in ("WH", "WL")], WHL + [zk], ["@G4"])
+            hs = T.G4[:, 0:128]
+            op("p", mm(hs, IH, T.ONES[:], True, False), ["IH", "ONES"], ["@G4"])
+            op("p", [mm(hs, T.WN[:, 128 * ll:128 * ll + 128], z[:, ll:256:2], False, False) for ll in range(2)] +
+               [mm(hs, IH, T.CQ[:, c:c + 128], False, False) for c in (256, 512)] +
+               [mm(hs, T.WP[:, 128 * ll:128 * ll + 128], z[:, ll:256:2], False, ll == 1) for ll in range(2)],
+               ["WN0", "WN1", "WP0", "WP1", "CQ1", "CQ2", zk], ["@G4"])
+            if m == 0:
+                first_dead_list()
             Z8 = ["Z8_%d" % cl for cl in range(8)]
 
             def z8(cl):
                 cp(T.Z8[:, cl:16 * NV:8], z[:, 0:2 * NV], [zk], ["Z8_%d" % cl])
-
-            def acol(ch):
-                ts(T.ACOL[:, ch:ch + 1], T.KI[:, 1:2], 32.0, A.mult, ["KI1", "ABASE%d" % d], ["ACOL%d" % ch], T.ABASE[:, 2 * d + ch:2 * d + ch + 1], A.add)
 
             def floors(ch):
                 ts(T.FI[:, 128 * ch:128 * ch + 128], T.SQ[:, 128 * ch:128 * ch + 128], T.ACOL[:, ch:ch + 1], A.add, ["SQ%d" % ch, "ACOL%d" % ch], ["FI%d" % ch], 1.0 / 32, A.mult)
@@ -412,21 +421,14 @@ def rank_program(g, core, T, topo):
             def lists(ch):
                 cp(T.OFF[:, 128 * ch:128 * ch + 128], T.CI[:, 128 * ch:128 * ch + 128], ["CI%d" % ch], ["OFF%d" % ch])
 
-            for cl in range(SZ8):
+            for cl in range(2):
                 act(T.Z8[:, cl:16 * NV:8], z[:, 0:2 * NV], F.Copy, [zk], ["Z8_%d" % cl])
-            fill = pending[:] + [lambda cl=cl: z8(cl) for cl in range(SZ8, 8)]
-            del pending[:]
-            n0, n1 = FILL[min(d, 1)]
-            for f in fill[0:n0]:
-                f()
-            ts(T.NI[:], T.G4[:, 0:128], -0.5, A.add, ["@G4"], ["NI"])
-            for f in fill[n0:n1]:
-                f()
-            tt(T.UF[:], T.G4[:, 0:128], T.NI[:], A.subtract, ["@G4", "NI"], ["UF"])
             for ch in range(2):
-                act(T.SQ[:, 128 * ch:128 * ch + 128], T.UF[:], F.Square, ["UF", "SCOL%d" % ch], ["SQ%d" % ch], bias=T.SCOL[:, ch:ch + 1], scale=4096.0)
-            for f in fill[n1:]:
-                f()
+                act(T.SQ[:, 128 * ch:128 * ch + 128], hs, F.Square, ["@G4", "SCOL%d" % ch], ["SQ%d" % ch], bias=T.SCOL[:, ch:ch + 1], scale=4096.0)
+            for cl in range(2, 5):
+                act(T.Z8[:, cl:16 * NV:8], z[:, 0:2 * NV], F.Copy, [zk], ["Z8_%d" % cl])
+            for cl in range(5, 8):
+                z8(cl)
             floors(0)
             floors(1)
             places(0)
@@ -497,6 +499,8 @@ def rank_program(g, core, T, topo):
             v_half(1, H, NV)
             unbarred(0)
             unbarred(1)
+            if m == 0:
+                cp(T.DLAND[:, 0:16], T.C7[:, 32:48], ["@C7"], ["DLAND0"])
             dsum(T.AB, 1, 0, 128, 0, ["AB1_0", "AB1_%d" % H, "AB1_%d" % NV, "AB1_%d" % SM])
             if d > 0:
                 op("p", mm(T.K6[:, 0:256:2], T.NE[:, 0:128], T.PEN[:, 1:256:2], False, False), ["NE0", "PEN"], ["@K6"])
@@ -508,8 +512,11 @@ def rank_program(g, core, T, topo):
                 near_rows(t - 1, 1)
             gap(0)
             op("p", [mm(T.LB[:, 256:512], IH, a, i == 0, False) for i, a in enumerate((s_, T.CQ[:, 0:256]))], ["IH", sk, "CQ0"], ["@LB"])
+            if m == 0:
+                scalar_constants()
             if m < 2:
-                act(T.TA[:, 2048 * m:2048 * m + 2048], T.TB[:, 2048 * m:2048 * m + 2048], F.Copy, ["TB"], ["TA" + "bc"[m]])
+                c0, c1 = ((0, 1536), (1536, W))[m]
+                act(T.TA[:, c0:c1], T.TB[:, c0:c1], F.Copy, ["TB"], ["TA" + "bc"[m]])
             if m == 2:
                 starter_rows(1)
                 starter_rows(2)
@@ -529,9 +536,8 @@ def rank_program(g, core, T, topo):
             act(T.UP[:], far[:, 0:WX].indirect(T.YU[:]), F.Copy, [fk, "YU"], ["UP"])
             tt(T.QR[:], far[:, 0:WX].indirect(T.YU[:]), T.CR[:], A.mult, [fk, "YU", "CR"], ["QR"])
             act(T.GX[:], T.X[:, 0:WX].indirect(T.YU[:]), F.Copy, ["X", "YU"], ["GX"])
+            gap(6)
             ts(T.QO[:], T.QR[:], OCOL, A.mult, ["QR", "PC"], ["QO"])
-            if not tail:
-                cp(T.R4[:], T.RA[:, 0:16].indirect(T.LX3[:]), ["RA", "LX3"], ["R4"])
             if d == 0 and t > 0:
                 tt(T.DE[:], T.MSP[:], T.E1[:], A.subtract, ["MSP", "E1"], ["DE"])
 
@@ -543,18 +549,24 @@ def rank_program(g, core, T, topo):
             def pv(q):
                 unit(2 * q, 1, "G%d" % q, 0)
                 unit(2 * q, 0, "G%d" % q, 256)
-                unit(2 * q + 1, 0, "G%d" % q, 384)
+                if q > 0:
+                    unit(2 * q + 1, 0, "G%d" % q, 384)
 
             def vv(q):
-                scan(T.FL[:, 512 * q:512 * q + 512], T["G%d" % q][:], T.TH[:], A.max, A.add, ["@G%d" % q, "THS"], ["FL%d" % q])
+                n = 512 if q > 0 else 384
+                scan(T.FL[:, 512 * q:512 * q + n], T["G%d" % q][:, 0:n], T.TH[:, 0:n], A.max, A.add, ["@G%d" % q, "THS"], ["FL%d" % q])
 
             def ps(q):
                 unit(2 * q + 1, 1, ("G4", "K6")[q % 2], 0)
+                if q == 0:
+                    unit(1, 0, "G4", 256)
 
             def ss(q):
                 bk = ("G4", "K6")[q % 2]
                 act(T.JK[:, 256 * q:256 * q + 256], T[bk][:, 0:256], F.Relu, ["@" + bk, "THS"], ["JK%d" % q, "FL%d" % (4 + q)],
                     bias=T.TH[:, 255:256], accum_out=T.FL[:, 2048 + q:2049 + q])
+                if q == 0:
+                    act(T.JK[:, 1024:1152], T.G4[:, 256:384], F.Relu, ["@G4", "THS"], ["JK4", "FL8"], bias=T.TH[:, 383:384], accum_out=T.FL[:, 511:512])
 
             ns = T.NSND[:, 256 * m:256 * m + 256]
 
@@ -566,12 +578,13 @@ def rank_program(g, core, T, topo):
                 if not tail:
                     send(to, "n%d%d" % (t, d), T.NLAND[:, 256 * m:256 * m + 256], ns, ["NSND%d" % m])
 
-            pv(0); vv(0); ps(0); ss(0); pv(1); vv(1); ps(1); ss(1); pv(2); vv(2); pn(); sn(); ps(2); ss(2); pv(3); vv(3); ps(3); ss(3)
+            pv(0); vv(0); ps(0); ss(0); pv(1); vv(1); ps(1); ss(1); pv(2); vv(2); ps(2); ss(2); pv(3); vv(3); ps(3); ss(3); pn(); sn()
             op("p", mm(T.C7[:, 16:32], T.E1[:], T.RS1[:], True, False), ["E1", "RS1"], ["@C7"])
-            if not tail:
-                op("p", mm(T.LB[:, 0:128], T.R4[:], T.IDF[:], True, True), ["R4", "IDF"], ["@LB"])
-            tt(T.E2[:], T.FL[:, 0:2056].indirect(T.LX2[:]), T.DE[:], A.min, ["FL%d" % i for i in range(8)] + ["LX2", "DE"], ["E2"])
+            tt(T.E2[:], T.FL[:, 0:2056].indirect(T.LX2[:]), T.DE[:], A.min, ["FL%d" % i for i in range(9)] + ["LX2", "DE"], ["E2"])
             op("p", mm(T.C7[:, 16:32], T.E2[:], T.RS1[:], False, True), ["E2", "RS1"], ["@C7"])
+            if not tail:
+                cp(T.R4[:], T.RA[:, 0:16].indirect(T.LX3[:]), ["RA", "LX3"], ["R4"])
+                op("p", mm(T.LB[:, 0:128], T.R4[:], T.IDF[:], True, True), ["R4", "IDF"], ["@LB"])
             gap(1)
             if end:
                 ts(T.CB[:], T.HL[:, 0:256], 16.0, A.mult, ["HI0"], ["CB", "CBb"], -1.0, A.add)
@@ -633,6 +646,7 @@ def rank_program(g, core, T, topo):
             if m == 1:
                 spare_columns("TA")
                 fill_rows("TA", 0)
+                join("TA", ["TAd", "TAx"])
             if m == ND * NB - 2:
                 dma("y", [(T.HL[:, 0:256], T.TA[15:128:16, 0:W]), (T.HL[:, 256:512], T.TA[14:128:16, 0:W])], ["TA"], ["HI0", "LO0"])
             kappa[1]()
@@ -643,10 +657,10 @@ def rank_program(g, core, T, topo):
                 join(xk, [xk + "b", xk + "x"])
             landed(frm, "n" + msg, ["NLAND%d" % m])
             landed(frm, "l" + msg, ["LLAND%d" % m])
-            kappa[2]()
-            kappa[3]()
             cp(XC[:, 0:WX].indirect(T.LLAND[:, 16 * m:16 * m + 16]), T.NLAND[:, 256 * m:256 * m + 256], ["NLAND%d" % m, "LLAND%d" % m], [xk])
             ts(T.PU[:], T.C7[:, 32:48], -1.0, A.add, ["@C7"], ["PU"])
+            kappa[2]()
+            kappa[3]()
             act(T.Z[:], XC[:, 0:WX].indirect(T.PU[:]), F.Copy, [xk, "PU"], ["Z"])
             own_records()
     op("p", [mm(T.G0[:, 0:256], T.SW[:, 16 - k:144 - k], T.TB[:, 256 * k:256 * k + 256], k == 0, k == 15) for k in range(16)], ["SW", "TB"], ["@G0"])

@@ -7,7 +7,7 @@ WX = DUM + 256
 NB, ND = 3, 3
 SC = 8192.0
 MAGIC = 1.5 * 2 ** 23
-NV = 72
+NV = (66, 64)
 
 _B = {}
 
@@ -18,7 +18,7 @@ def _sb(name, cols, dtype):
 
 for _n in ("X", "XC0", "XC1", "TA", "TB"):
     _sb(_n, WX, "bfloat16")
-_sb("PAI", 256, "int32"); _sb("PBI", 256, "int32"); _sb("CT1", 256, "int32"); _sb("CT2", 256, "int32")
+_sb("PAI", 256, "int32"); _sb("PBI", 256, "int32"); _sb("CT1", 256, "int32")
 _sb("HL", 1024, "bfloat16"); _sb("CB", 256, "float32"); _sb("PF", 512, "float32")
 _sb("WI", 8, "int32"); _sb("WF", 8, "float32")
 _sb("PI", 8, "int32"); _sb("PT", 8, "int32"); _sb("PC", 32, "float32"); _sb("SG", 16, "float32")
@@ -26,26 +26,26 @@ _sb("CF", 264, "float32"); _sb("LANE", 256, "float32"); _sb("C8", 128, "float32"
 _sb("CG", 128, "float32"); _sb("WP", 256, "float16"); _sb("WN", 256, "float16")
 _sb("OB", 16, "bfloat16"); _sb("IDF", 128, "float32"); _sb("PEN", 264, "bfloat16"); _sb("ZB", 128, "bfloat16")
 _sb("IBN", 384, "bfloat16")
-_sb("CQ", 640, "bfloat16")
-_sb("M1", 128, "float32"); _sb("MSP", 128, "float32"); _sb("RS1", 16, "float32"); _sb("RS", 256, "float32")
+_sb("CQ", 896, "bfloat16")
+_sb("M1", 128, "float32"); _sb("MSP", 128, "float32"); _sb("RS1", 16, "float32"); _sb("RSN", 16, "float32"); _sb("RS", 256, "float32")
 _sb("CR", 256, "bfloat16"); _sb("RC", 256 * NB, "bfloat16"); _sb("TH", 512, "float32"); _sb("SW", 144, "bfloat16")
-_sb("ONES", 128, "bfloat16"); _sb("DIAG", 256, "float32"); _sb("SRB", 256, "bfloat16"); _sb("GBH", 128, "float32"); _sb("D16", 16, "float32")
+_sb("ONES", 128, "bfloat16"); _sb("DIAG", 256, "float32"); _sb("SRB", 256, "bfloat16"); _sb("D16", 16, "float32")
 _sb("LX0", 16, "uint16"); _sb("LX1", 8, "uint16"); _sb("LX2", 8, "uint16"); _sb("LX3", 8, "uint16"); _sb("LX4", 32, "uint16"); _sb("LX5", 16, "uint16")
 _sb("LT", 64, "float32"); _sb("LXI", 16, "int32"); _sb("LXJ", 16, "int32")
 _sb("SCOL", 4, "float32"); _sb("ABASE", 8, "float32"); _sb("ACOL", 4, "float32")
 _sb("SSND", 256 * NB, "bfloat16"); _sb("SLAND", 256 * NB, "bfloat16")
 _sb("DSND", 16 * NB, "bfloat16"); _sb("DLAND", 16 * (NB + 1), "bfloat16")
-_sb("NSND", 256 * NB * ND, "bfloat16"); _sb("NLAND", 256 * NB * ND, "bfloat16")
+_sb("FLAND", 256 * NB, "bfloat16"); _sb("YSND", 16 * NB * ND, "uint16"); _sb("YLAND", 16 * NB * ND, "uint16")
 _sb("LSND", 16 * NB * ND, "uint16"); _sb("LLAND", 16 * NB * ND, "uint16")
 _sb("RSND", 32 * NB, "float32"); _sb("RLAND", 32 * NB, "float32")
 _sb("Z", 256, "bfloat16"); _sb("Z8", 2048, "bfloat16")
 _sb("SQ", 256, "float32"); _sb("FI", 256, "int32"); _sb("CI", 256, "int32")
-_sb("OFF", 256, "uint16"); _sb("CFL", 256, "float32"); _sb("NE", 256, "bfloat16")
+_sb("OFF", 256, "uint16"); _sb("CFL", 256, "float16"); _sb("NE", 256, "bfloat16")
 _sb("DF", 4096, "bfloat16"); _sb("AB", 4096, "bfloat16")
 _sb("R", 256, "float32"); _sb("RI", 16, "int32"); _sb("RA", 16, "int32"); _sb("E1", 128, "float32"); _sb("DE", 128, "float32")
-_sb("R4", 128, "float32"); _sb("E2", 128, "float32"); _sb("YU", 16, "uint16")
-_sb("UP", 256, "bfloat16"); _sb("QR", 256, "bfloat16"); _sb("QO", 256, "bfloat16"); _sb("GX", 256, "bfloat16")
-_sb("FL", 2056, "float32"); _sb("JK", 1152, "bfloat16"); _sb("PG", 256, "bfloat16"); _sb("PU", 16, "uint16"); _sb("E3", 512, "bfloat16")
+_sb("R4", 128, "float32"); _sb("E2", 128, "float32"); _sb("NS", 512, "bfloat16"); _sb("FO", WX, "float32")
+_sb("UP", 256, "bfloat16"); _sb("QR", 256, "bfloat16"); _sb("QO", 256, "bfloat16"); _sb("GX", 512, "bfloat16")
+_sb("FL", 2056, "float32"); _sb("JK", 1280, "bfloat16"); _sb("PG", 256, "bfloat16"); _sb("PU", 16, "uint16"); _sb("E3", 512, "bfloat16")
 _sb("WB", 16 * ND, "bfloat16"); _sb("RES", 16, "float32"); _sb("W1", 16, "float32"); _sb("W2", 16, "float32"); _sb("W3", 16, "float32")
 _sb("KP", 8, "float32"); _sb("KJ", 16, "float32"); _sb("KI", 8, "int32")
 for _n in ["G0", "G1", "G2", "G3", "G4", "K6", "C7", "LB"]:
@@ -54,9 +54,9 @@ SCRATCH = _B
 
 _MSG = []
 for _t in range(NB):
-    _MSG += ["s%d" % _t, "b%d" % _t, "e%d" % _t, "r%d" % _t]
+    _MSG += ["s%d" % _t, "f%d" % _t, "b%d" % _t, "e%d" % _t, "r%d" % _t]
     for _d in range(ND - 1):
-        _MSG += ["n%d%d" % (_t, _d), "l%d%d" % (_t, _d)]
+        _MSG += ["y%d%d" % (_t, _d), "l%d%d" % (_t, _d)]
 SEMAPHORES = ["cv", "cs", "cp", "cg"] + ["rx" + m for m in _MSG] + ["tx" + m for m in _MSG] + ["dm%d" % i for i in range(16)]
 
 
@@ -177,6 +177,9 @@ def rank_program(g, core, T, topo):
         send(nxt if t % 2 == 0 else prv, "s%d" % t, T.SLAND[:, 256 * t:256 * t + 256], s, ["SS0_%d" % t, "SS1_%d" % t])
         landed(prv if t % 2 == 0 else nxt, "s%d" % t, ["SLAND%d" % t])
 
+    def starters_on(t):
+        send(nxt if t % 2 == 0 else prv, "f%d" % t, T.FLAND[:, 256 * t:256 * t + 256], T.SLAND[:, 256 * t:256 * t + 256], ["SLAND%d" % t])
+
     def dead_list(t):
         near, nk = (T.TA, "TA") if t % 2 == 0 else (T.TB, "TB")
         to_list(lambda b: near[:, 2048 * (b % 2) + 16 * (b // 2) + t:2048 * (b % 2) + 2048:128], [nk])
@@ -194,13 +197,11 @@ def rank_program(g, core, T, topo):
 
     def near_send(t):
         hi, lo = T.RSND[:, 32 * t:32 * t + 16], T.RSND[:, 32 * t + 16:32 * t + 32]
-        ts(T.W1[:], T.RES[:], DEAD, A.is_lt, ["RES"], ["W1"])
-        cp(T.LXJ[:], T.RES[:], ["RES"], ["LXJ"])
-        ts(T.W2[:], T.RES[:], 1.0, A.add, ["RES"], ["W2"])
+        ts(T.LXJ[:], T.RES[:], 0.0, A.max, ["RES"], ["LXJ"])
+        ts(T.W3[:], T.RES[:], 1.0, A.add, ["RES"], ["W3"], 0.0, A.max)
         ts(T.LXI[:], T.LXJ[:], 4, A.arith_shift_right, ["LXJ"], ["LXI"])
-        tt(T.W3[:], T.W1[:], T.W2[:], A.mult, ["W1", "W2"], ["W3"])
-        tt(hi, T.LXI[:], T.W1[:], A.mult, ["LXI", "W1"], ["RSH%d" % t])
-        ts(T.W2[:], hi, -16.0, A.mult, ["RSH%d" % t], ["W2"])
+        cp(hi, T.LXI[:], ["LXI"], ["RSH%d" % t])
+        ts(T.W2[:], T.LXI[:], -16.0, A.mult, ["LXI"], ["W2"])
         tt(lo, T.W3[:], T.W2[:], A.add, ["W3", "W2"], ["RSL%d" % t])
         send(prv if t % 2 == 0 else nxt, "r%d" % t, T.RLAND[:, 32 * t:32 * t + 32], T.RSND[:, 32 * t:32 * t + 32], ["RSH%d" % t, "RSL%d" % t])
 
@@ -239,9 +240,10 @@ def rank_program(g, core, T, topo):
     ts(T.PC[:, 8:12], T.CF[:, 12:16], PLOW, A.is_equal, ["CF", "PC"], ["PCI"])
     I12, I14, I15 = T.PC[:, 8:9], T.PC[:, 10:11], T.PC[:, 11:12]
     ts(T.SG[:, 0:12], T.LT[:, 0:12], -1.0, A.add, ["LT"], ["SG"])
-    for r in range(12):
+    for r in range(11):
         n = 1 << r
         act(T.TB[:, n:2 * n], T.TB[:, 0:n], F.Copy, ["TBb", "SG"], ["TBb"], scale=T.SG[:, r:r + 1])
+    act(T.TB[:, 2048:3072], T.TB[:, 0:1024], F.Copy, ["TBb", "SG"], ["TBc"], scale=T.SG[:, 11:12])
     ts(T.PC[:, 12:13], PGRP, 2.0, A.mult, ["PC"], ["PC12"])
     ts(T.PC[:, 13:14], PGRP, 2.0, A.mult, ["PC"], ["PC13"], 1.0, A.add)
     for ch in range(2):
@@ -265,6 +267,7 @@ def rank_program(g, core, T, topo):
             ts(T[wm][:, 128 * ll:128 * ll + 128], T.C8[:], T.PC[:, 12 + ll:13 + ll], A.is_equal, ["C8", "PC12", "PC13", "WF%d" % c], ["%s%d" % (wm, ll)], T.WF[:, c:c + 1], A.mult)
     ms(T.CQ[:, 256:512], 2 * MAGIC, ["CQ1"])
     ms(T.CQ[:, 512:640], -2 * MAGIC, ["CQ2"])
+    ms(T.CQ[:, 640:896], 4096.0, ["CQ3"])
     ts(IB, T.CF[:, 0:128], PP, A.is_equal, ["CF", "PC"], ["IB"])
     ts(T.IDF[:], T.CF[:, 0:128], PP, A.is_equal, ["CF", "PC"], ["IDF"])
     for i in range(2):
@@ -301,8 +304,10 @@ def rank_program(g, core, T, topo):
     rows_b[3]()
     ts(T.PC[:, 19:20], I14, SC, A.mult, ["PCI", "PC17"], ["PC19"], T.PC[:, 17:18], A.add)
     ts(T.PC[:, 20:23], T.CF[:, 1:4], I14, A.mult, ["CF", "PCI"], ["PC20"])
+    ts(T.TB[:, 3072:W], T.TB[:, 1024:2048], T.SG[:, 11:12], A.mult, ["TBb", "SG"], ["TBd"])
     need("y", deps([], ["SS0_0"]))
     fill_rows("TB", 1)
+    starters_on(0)
     need("g", deps(["TBd"], []))
     records_send(0)
     ts(T.WB[:, 0:8], T.CF[:, 0:8], PL7, A.is_equal, ["CF", "PC"], ["WB0"])
@@ -321,7 +326,10 @@ def rank_program(g, core, T, topo):
         for o in range(2):
             op("p", mm(T.C7[:, 32 + o:48:2], T.E3[:, 128 * o:128 * o + 128], T.WB[:, 0:8], True, True), ["E3_%d" % o, "WB0"], ["@C7"])
 
-    op("g", lambda: g.iota(T.TH[:], [[0, 512]], 0, 0, allow_small_or_imprecise_dtypes=True), [], ["TH"])
+    tt(T.MSP[:], T.M1[:], T.SPI[:], A.mult, ["M1", "SPI"], ["MSP"])
+    iota("TH", [[0, 512]], 0, 0)
+    op("g", lambda: g.iota(T.FL[:, 1792:2056], [[0, 264]], 0, 0, allow_small_or_imprecise_dtypes=True), [], ["FL4", "FL5", "FL6", "FL7", "FL8"])
+    iota("DIAG", [[1, 2], [0, 16], [2, 8]], 0, 0)
 
     def scalar_constants():
         spare_columns("TB")
@@ -331,22 +339,21 @@ def rank_program(g, core, T, topo):
 
     def first_constants():
         yield lambda: ms(T.CQ[:, 0:256], -0.5, ["CQ0"])
-        yield lambda: tt(T.MSP[:], T.M1[:], T.SPI[:], A.mult, ["M1", "SPI"], ["MSP"])
         yield lambda: ts(T.LX3[:], T.CF[:, 0:16:2], PLL, A.add, ["CF", "PC"], ["LX3"])
-        yield lambda: ts(T.TH[:, 255:256], PP, SC, A.mult, ["PC", "TH"], ["TH1"], (128 - 1536) * SC, A.add)
-        for c in (383, 511):
-            yield lambda c=c: ts(T.TH[:, c:c + 1], PP, SC, A.mult, ["PC", "TH"], ["TH%d" % c], -1536 * SC, A.add)
-        yield lambda: join("THS", ["TH", "TH1", "TH383", "TH511"])
-        for i, (c0, step, base) in enumerate(((0, 512.0, 383.0), (1, 512.0, 511.0), (8, 512.0, 255.0), (9, 1.0, 2048.0))):
+        yield lambda: ts(T.PC[:, 24:25], PP, SC, A.mult, ["PC"], ["PC24"])
+        yield lambda: ts(T.RSN[:], T.RS1[:], -SC, A.mult, ["RS1"], ["RSN"])
+        yield lambda: (ts(T.TH[:, 127:256:128], T.ZB[:, 0:2], T.PC[:, 24:25], A.add, ["ZB", "PC24", "TH"], ["THa"], -1536 * SC, A.add),
+                       ts(T.TH[:, 511:512], T.PC[:, 24:25], (128 - 1536) * SC, A.add, ["PC24", "TH"], ["THb"]))
+        yield lambda: join("THS", ["TH", "THa", "THb"])
+        for i, (c0, step, base) in enumerate(((0, 512.0, 127.0), (1, 512.0, 255.0), (8, 1.0, 2048.0), (9, 512.0, 511.0))):
             yield lambda i=i, c0=c0, step=step, base=base: ts(T.LT[:, 16 + c0:16 + c0 + 7:2], T.CF[:, 0:4], step, A.mult, ["CF"], ["LT%d" % i], base, A.add)
-        yield lambda: (ms(T.FL[:, 2048:2056], 0.0, ["FL4", "FL5", "FL6", "FL7"]), ms(T.FL[:, 384:512], 0.0, ["FL8"]))
         yield lambda: tt(T.LT[:, 32:40], T.LT[:, 24:32], T.LT[:, 16:24], A.subtract, ["LT0", "LT1", "LT2", "LT3"], ["LT4"])
         yield lambda: ts(T.LT[:, 40:48], T.LT[:, 32:40], P1, A.mult, ["LT4", "PC"], ["LT5"])
         yield lambda: tt(T.LT[:, 32:40], T.LT[:, 40:48], T.LT[:, 16:24], A.add, ["LT5", "LT0", "LT1"], ["LT4"])
         yield lambda: cp(T.LX2[:], T.LT[:, 32:40], ["LT4"], ["LX2"])
+        yield lambda: ms(T.XC0[:, W:WX], 0.0, ["XC0x"])
         yield lambda: ts(T.PC[:, 14:15], PGRP, 16.0, A.mult, ["PC"], ["PC14"], 16.0, A.add)
         yield lambda: ts(T.PC[:, 15:16], I15, 16.0, A.mult, ["PCI"], ["PC15"], I14, A.add)
-        yield lambda: ms(T.XC0[:, W:WX], 0.0, ["XC0x"])
         yield lambda: ts(T.SW[:], T.CF[:, 0:144], T.PC[:, 14:15], A.is_equal, ["CF", "PC14", "PC15"], ["SW"], T.PC[:, 15:16], A.mult)
         for d in range(ND):
             yield lambda d=d: ts(T.ABASE[:, 2 * d:2 * d + 2], T.SCOL[:, 2:4], -1.0, A.mult, ["SCOL2"], ["ABASE%d" % d], 262144.0 - 12.0 + 32.0 * 97 * d, A.add)
@@ -354,20 +361,9 @@ def rank_program(g, core, T, topo):
     def late_constants():
         for f in table_rows(T.PAI, "PAI", 0):
             yield f
-        yield lambda: ts(T.GBH[:], T.C8[:], T.PC[:, 12:13], A.subtract, ["C8", "PC12"], ["GBH"])
-        yield lambda: cp(T.CT1[:], T.CF[:, 0:256], ["CF"], ["CT1"])
-        yield lambda: ts(T.CB[:, 0:128], T.GBH[:], 0.0, A.is_ge, ["GBH"], ["CB"])
-        yield lambda: ts(T.CB[:, 128:256], T.GBH[:], 1.0, A.is_le, ["GBH"], ["CBb"])
-        yield lambda: ts(T.CT2[:, 0:128], T.CT1[:, 0:128], 7, A.bitwise_and, ["CT1"], ["CT2"])
-        yield lambda: tt(T.GBH[:], T.CB[:, 0:128], T.CB[:, 128:256], A.mult, ["CB", "CBb"], ["GBH"])
-        yield lambda: ts(T.CT2[:, 128:256], T.CT1[:, 0:128], 15, A.bitwise_and, ["CT1"], ["CT2b"])
-        for ll in range(2):
-            yield lambda ll=ll: ts(T.CB[:, 128 * ll:128 * ll + 128], T.CT2[:, 0:128], 2.0, A.mult, ["CT2"], ["CB" if ll == 0 else "CBb"], float(ll), A.add)
-        yield lambda: ts(T.DIAG[:], T.CB[:], PLOW, A.is_equal, ["CB", "CBb", "PC"], ["DIAG"])
+        yield lambda: ts(T.DIAG[:], T.DIAG[:], PLOW, A.is_equal, ["DIAG", "PC"], ["DIAG"])
         for i in range(2):
-            yield lambda i=i: ts(T.CB[:, 128 * i:128 * i + 128], T.CT2[:, 128:256], 15.0 - i, A.is_equal, ["CT2b"], ["CB" if i == 0 else "CBb"])
-        for i in range(2):
-            yield lambda i=i: tt(T.SRB[:, 128 * i:128 * i + 128], T.CB[:, 128 * i:128 * i + 128], T.GBH[:], A.mult, ["CB", "CBb", "GBH"], ["SRB%d" % i])
+            yield lambda i=i: ts(T.SRB[:, 128 * i:128 * i + 128], T.CF[:, 0:128], 1.0 + i, A.add, ["CF", "PC14"], ["SRB%d" % i], T.PC[:, 14:15], A.is_equal)
         for h in range(4):
             yield lambda h=h: ts(T.LX4[:, 8 * h:8 * h + 8], T.CF[:, 0:16:2], PLL, A.add, ["CF", "PC"], ["LX4_%d" % h], 16.0 * (h // 2), A.add)
         yield lambda: join("LX4", ["LX4_%d" % h for h in range(4)])
@@ -376,13 +372,17 @@ def rank_program(g, core, T, topo):
         yield lambda: ts(T.D16[:, 0:8], T.CF[:, 0:8], T.WF[:, 2:3], A.is_equal, ["CF", "WF2"], ["D16"])
         for o in range(2):
             yield lambda o=o: ts(T.LX5[:, 8 * o:8 * o + 8], T.ZB[:, 0:8], T.LT[:, o:o + 1], A.add, ["ZB", "LT"], ["LX5_%d" % o])
+        for i in range(2):
+            yield lambda i=i: ts(T.CB[:], T.HL[:, 512 * i:512 * i + 256], 16.0, A.mult, ["HI%d" % i], ["CB", "CBb"], -1.0, A.add)
+            yield lambda i=i: tt(T.PF[:, 256 * i:256 * i + 256], T.CB[:], T.HL[:, 512 * i + 256:512 * i + 512], A.add, ["CB", "CBb", "LO%d" % i], ["PF%d" % i])
+        yield lambda: dma("y", [(T.FO[0:128:16, 0:W], T.PF[:, 256:512])], ["PF1"], ["FO"])
+        yield lambda: act(T.DIAG[:], T.LANE[:], F.Copy, ["LANE"], ["DIAG"], scale=16.0, bias=NB - 1.0)
 
     late = list(late_constants())
     first = list(first_constants())
-    gaps = {(0, 0): first[0:13], (0, 3): first[13:14], (0, 4): first[14:15], (0, 5): first[15:16], (0, 6): first[16:18], (0, 1): first[18:20],
-            (0, 2): first[20:23] + late[0:1],
-            (1, 0): late[1:4], (1, 1): late[4:6], (1, 2): late[6:7], (2, 0): late[7:13], (2, 1): late[13:15],
-            (2, 2): late[15:23], (4, 0): late[23:26], (4, 1): late[26:28]}
+    gaps = {(0, 0): first[0:11], (0, 3): first[11:12], (0, 4): first[12:13], (0, 5): first[13:14], (0, 6): first[14:15], (0, 1): first[15:17],
+            (0, 2): first[17:21],
+            (0, 7): late[0:1], (1, 0): late[1:4], (2, 0): late[4:12], (4, 0): late[12:17], (7, 0): late[17:19], (8, 0): late[19:23]}
 
     for t in range(NB):
         frm, to = (prv, nxt) if t % 2 == 0 else (nxt, prv)
@@ -399,112 +399,111 @@ def rank_program(g, core, T, topo):
                 for f in gaps.get((m, i), []):
                     f()
 
-            hs = T.G4[:, 0:128]
-            op("p", mm(hs, IH, T.ONES[:], True, False), ["IH", "ONES"], ["@G4"])
-            op("p", [mm(hs, T.WN[:, 128 * ll:128 * ll + 128], z[:, ll:256:2], False, False) for ll in range(2)] +
-               [mm(hs, IH, T.CQ[:, c:c + 128], False, False) for c in (256, 512)] +
-               [mm(hs, T.WP[:, 128 * ll:128 * ll + 128], z[:, ll:256:2], False, ll == 1) for ll in range(2)],
-               ["WN0", "WN1", "WP0", "WP1", "CQ1", "CQ2", zk], ["@G4"])
-            if m == 0:
-                first_dead_list()
+            hs = [(T.C7[:, 64:128], "@C7"), (T.G4[:, 0:64], "@G4")]
+            zks = [zk, zk] if d == 0 else ["Z0", "Z1"]
+            for h in (1, 0):
+                op("p", mm(hs[h][0], IH, T.ONES[:, 0:64], True, False), ["IH", "ONES"], [hs[h][1]])
+            for h in (1, 0):
+                zs = [z[:, 128 * h + ll:128 * h + 128:2] for ll in range(2)]
+                op("p", [mm(hs[h][0], T.WN[:, 128 * ll:128 * ll + 128], zs[ll], False, False) for ll in range(2)] +
+                   [mm(hs[h][0], IH, T.CQ[:, c:c + 64], False, False) for c in (256, 512)] +
+                   [mm(hs[h][0], T.WP[:, 128 * ll:128 * ll + 128], zs[ll], False, ll == 1) for ll in range(2)],
+                   ["WN0", "WN1", "WP0", "WP1", "CQ1", "CQ2", zks[h]], [hs[h][1]])
             Z8 = ["Z8_%d" % cl for cl in range(8)]
 
+            def part(ap, ch, h):
+                return ap[:, 128 * ch + 64 * h:128 * ch + 64 * h + 64]
+
+            def floors(ch, h):
+                ts(part(T.FI, ch, h), part(T.SQ, ch, h), T.ACOL[:, ch:ch + 1], A.add, ["SQ%d%d" % (ch, h), "ACOL%d" % ch], ["FI%d%d" % (ch, h)], 1.0 / 32, A.mult)
+
+            def places(ch, h):
+                ts(part(T.CI, ch, h), part(T.FI, ch, h), 4095, A.bitwise_and, ["FI%d%d" % (ch, h)], ["CI%d%d" % (ch, h)])
+
+            def lists(ch, h):
+                cp(part(T.OFF, ch, h), part(T.CI, ch, h), ["CI%d%d" % (ch, h)], ["OFF%d%d" % (ch, h)])
+
+            for h in (1, 0):
+                for ch in range(2):
+                    act(part(T.SQ, ch, h), hs[h][0], F.Square, [hs[h][1], "SCOL%d" % ch], ["SQ%d%d" % (ch, h)], bias=T.SCOL[:, ch:ch + 1], scale=4096.0)
+            if m == 0:
+                first_dead_list()
             def z8(cl):
-                cp(T.Z8[:, cl:16 * NV:8], z[:, 0:2 * NV], [zk], ["Z8_%d" % cl])
+                cp(T.Z8[:, cl:16 * NV[0]:8], z[:, 0:2 * NV[0]], zks, ["Z8_%d" % cl])
 
-            def floors(ch):
-                ts(T.FI[:, 128 * ch:128 * ch + 128], T.SQ[:, 128 * ch:128 * ch + 128], T.ACOL[:, ch:ch + 1], A.add, ["SQ%d" % ch, "ACOL%d" % ch], ["FI%d" % ch], 1.0 / 32, A.mult)
+            for cl in range(3):
+                act(T.Z8[:, cl:16 * NV[0]:8], z[:, 0:2 * NV[0]], F.Copy, zks, ["Z8_%d" % cl])
+            z8(3); z8(4)
+            floors(0, 1); floors(1, 1); z8(5); floors(0, 0); places(0, 1); floors(1, 0); places(0, 0); lists(0, 1)
+            places(1, 1); places(1, 0); lists(0, 0); z8(6); z8(7); lists(1, 1); lists(1, 0)
 
-            def places(ch):
-                ts(T.CI[:, 128 * ch:128 * ch + 128], T.FI[:, 128 * ch:128 * ch + 128], 4095, A.bitwise_and, ["FI%d" % ch], ["CI%d" % ch])
-
-            def lists(ch):
-                cp(T.OFF[:, 128 * ch:128 * ch + 128], T.CI[:, 128 * ch:128 * ch + 128], ["CI%d" % ch], ["OFF%d" % ch])
-
-            for cl in range(2):
-                act(T.Z8[:, cl:16 * NV:8], z[:, 0:2 * NV], F.Copy, [zk], ["Z8_%d" % cl])
-            for ch in range(2):
-                act(T.SQ[:, 128 * ch:128 * ch + 128], hs, F.Square, ["@G4", "SCOL%d" % ch], ["SQ%d" % ch], bias=T.SCOL[:, ch:ch + 1], scale=4096.0)
-            for cl in range(2, 5):
-                act(T.Z8[:, cl:16 * NV:8], z[:, 0:2 * NV], F.Copy, [zk], ["Z8_%d" % cl])
-            for cl in range(5, 8):
-                z8(cl)
-            floors(0)
-            floors(1)
-            places(0)
-            places(1)
-            lists(0)
+            def offs(ch, c0, c1):
+                return ["OFF%d%d" % (ch, h) for h in range(c0 // 64, (c1 - 1) // 64 + 1)]
 
             def v_gather(ch, c0, c1):
                 a, b = 2048 * ch + 16 * c0, 2048 * ch + 16 * c1
                 tt(T.DF[:, a:b], T.X[:, 0:WX].indirect(T.OFF[:, 128 * ch + c0:128 * ch + c1]), T.Z8[:, 16 * c0:16 * c1], A.subtract,
-                   ["X", "OFF%d" % ch] + Z8, ["DF%d_%d" % (ch, c0)])
+                   ["X"] + offs(ch, c0, c1) + Z8, ["DF%d_%d" % (ch, c0)])
 
-            def v_half(ch, c0, c1):
-                a, b = 2048 * ch + 16 * c0, 2048 * ch + 16 * c1
-                ts(T.AB[:, a:b], T.DF[:, a:b], 0.0, A.max, ["DF%d_%d" % (ch, c0)], ["AB%d_%d" % (ch, c0)], 2.0, A.mult)
+            def v_half(ch, c0, c1, keys, odd=None):
+                a, b, st = 2048 * ch + 16 * c0 + (odd or 0), 2048 * ch + 16 * c1, (1 if odd is None else 2)
+                ts(T.AB[:, a:b:st], T.DF[:, a:b:st], 0.0, A.max, keys, ["AB%d_%d_%s" % (ch, c0, odd)], 2.0, A.mult)
 
             def s_gather(ch, c0, c1):
                 a, b = 2048 * ch + 16 * c0, 2048 * ch + 16 * c1
-                act(T.DF[:, a:b], T.X[:, 0:WX].indirect(T.OFF[:, 128 * ch + c0:128 * ch + c1]), F.Copy, ["X", "OFF%d" % ch], ["DF%d_%d" % (ch, c0)])
+                act(T.DF[:, a:b], T.X[:, 0:WX].indirect(T.OFF[:, 128 * ch + c0:128 * ch + c1]), F.Copy, ["X"] + offs(ch, c0, c1), ["DF%d_%d" % (ch, c0)])
 
             def p_diff(ch, c0, c1, bk):
                 a, b = 2048 * ch + 16 * c0, 2048 * ch + 16 * c1
-                op("p", mm(T[bk][:, 0:b - a], IB, T.DF[:, a:b], False, True), ["IB", "DF%d_%d" % (ch, c0)], ["@" + bk])
+                op("p", mm(T[bk][:, 0:b - a], IB, T.DF[:, a:b], False, True), ["IB", "DF%d_%d" % (ch, NV[ch])], ["@" + bk])
 
-            def s_abs(ch, c0, c1, bk):
-                a, b = 2048 * ch + 16 * c0, 2048 * ch + 16 * c1
-                act(T.AB[:, a:b], T[bk][:, 0:b - a], F.Abs, ["@" + bk], ["AB%d_%d" % (ch, c0)])
+            def s_abs(ch, c0, c1, bk, odd=None):
+                a, b, o, st = 2048 * ch + 16 * c0, 2048 * ch + 16 * c1, (odd or 0), (1 if odd is None else 2)
+                act(T.AB[:, a + o:b:st], T[bk][:, o:b - a:st], F.Abs, ["@" + bk], ["AB%d_%d_%s" % (ch, c0, odd)])
 
-            def dsum(src, ch, c0, c1, ob, keys):
+            def dsum(src, ch, c0, c1, ob, keys, parts=range(16)):
                 op("p", [mm(T.K6[c0:c1, 2 * b + ch:256:32], src[:, 2048 * ch + 16 * c0 + b:2048 * ch + 16 * c1:16], T.OB[:, 8 * ob:8 * ob + 8], False, False)
-                         for b in range(16)], keys + ["OB%d" % ob], ["@K6"])
+                         for b in parts], keys + ["OB%d" % ob], ["@K6"])
 
             def unbarred(ch):
                 if d > 0:
-                    tt(T.NE[:, 128 * ch:128 * ch + 128], T.LB[:, 0:128], T.CI[:, 128 * ch:128 * ch + 128], A.not_equal, ["@LB", "CI%d" % ch], ["NE%d" % ch])
+                    tt(T.NE[:, 128 * ch:128 * ch + 128], T.LB[:, 0:128], T.CI[:, 128 * ch:128 * ch + 128], A.not_equal,
+                       ["@LB", "CI%d0" % ch, "CI%d1" % ch], ["NE%d" % ch])
 
             def number(ch):
-                op("p", mm(T.K6[:, ch:256:2], T.CFL[:, 128 * ch:128 * ch + 128], T.IDF[:], False, False), ["CFL", "IDF"], ["@K6"])
+                op("p", mm(T.K6[:, ch:256:2], T.CFL[:, 128 * ch:128 * ch + 128], IB, False, False), ["CFL", "IB"], ["@K6"])
 
-            H, SM = NV // 2, NV + 32
-            sc = [(0, NV, SM, "G0"), (0, SM, 128, "G1"), (1, NV, SM, "G2"), (1, SM, 128, "G3")]
-            op("p", mm(T.K6[:, 0:256], T.ZB[:], T.PEN[:, 0:256], True, False), ["ZB", "PEN"], ["@K6"])
+            sc = [(0, NV[0], NV[0] + 32, "G0"), (0, NV[0] + 32, 128, "G1"), (1, NV[1], NV[1] + 32, "G2"), (1, NV[1] + 32, 128, "G3")]
+            op("p", mm(T.K6[:, 0:256], IH, T.CQ[:, 640:896], True, False), ["IH", "CQ3"], ["@K6"])
             for ch, c0, c1, bk in sc:
-                op("p", [mm(T[bk][:, cl:16 * (c1 - c0):8], IN, z[:, 2 * c0:2 * c1], cl == 0, False) for cl in range(8)], ["IN", zk], ["@" + bk])
-            s_gather(*sc[0][:3])
-            lists(1)
-            s_gather(*sc[1][:3])
-            p_diff(*sc[0])
-            v_gather(0, 0, NV)
-            s_abs(*sc[0])
-            p_diff(*sc[1])
-            cp(T.CFL[:], T.CI[:], ["CI0", "CI1"], ["CFL"])
-            dsum(T.DF, 0, 0, NV, 1, ["DF0_0"])
-            s_gather(*sc[2][:3])
-            v_gather(1, 0, H)
-            s_abs(*sc[1])
-            number(0)
+                op("p", [mm(T[bk][:, cl:16 * (c1 - c0):8], IN, z[:, 2 * c0:2 * c1], cl == 0, False) for cl in range(8)], ["IN", zks[1]], ["@" + bk])
+            for ch in range(2):
+                v_gather(ch, 0, NV[ch])
+                s_gather(ch, NV[ch], 128)
+            ts(T.CFL[:], T.CI[:], -2048.0, A.add, ["CI00", "CI01", "CI10", "CI11"], ["CFL"])
+            for i in range(2):
+                p_diff(*sc[i])
+            dsum(T.DF, 0, 0, NV[0], 1, ["DF0_0"])
             p_diff(*sc[2])
-            number(1)
-            v_half(0, 0, NV)
-            s_gather(*sc[3][:3])
-            dsum(T.AB, 0, 0, 128, 0, ["AB0_0", "AB0_%d" % NV, "AB0_%d" % SM])
             p_diff(*sc[3])
-            v_gather(1, H, NV)
-            s_abs(*sc[2])
-            dsum(T.DF, 1, 0, NV, 1, ["DF1_0", "DF1_%d" % H])
-            v_half(1, 0, H)
-            s_abs(*sc[3])
-            v_half(1, H, NV)
-            unbarred(0)
-            unbarred(1)
+            dsum(T.DF, 1, 0, NV[1], 1, ["DF1_0"])
+            for i in range(2):
+                number(i)
+            v_half(0, 0, NV[0], ["DF0_0"])
+            for c in sc[0:3]:
+                s_abs(*c)
+            dsum(T.AB, 0, 0, 128, 0, ["AB0_0_None", "AB0_%d_None" % sc[0][1], "AB0_%d_None" % sc[1][1]])
+            for odd in range(2):
+                unbarred(odd)
+                v_half(1, 0, NV[1], ["DF1_0"], odd)
+                s_abs(*sc[3], odd)
             if m == 0:
                 cp(T.DLAND[:, 0:16], T.C7[:, 32:48], ["@C7"], ["DLAND0"])
-            dsum(T.AB, 1, 0, 128, 0, ["AB1_0", "AB1_%d" % H, "AB1_%d" % NV, "AB1_%d" % SM])
             if d > 0:
                 op("p", mm(T.K6[:, 0:256:2], T.NE[:, 0:128], T.PEN[:, 1:256:2], False, False), ["NE0", "PEN"], ["@K6"])
-            op("p", mm(T.K6[:, 0:256], T.NE[:, 128:256] if d > 0 else T.ZB[:], T.PEN[:, 0:256], False, True), ["NE1" if d > 0 else "ZB", "PEN"], ["@K6"])
+            for odd in range(2):
+                dsum(T.AB, 1, 0, 128, 0, ["AB1_0_%d" % odd, "AB1_%d_None" % sc[2][1], "AB1_%d_%d" % (sc[3][1], odd)], range(odd, 16, 2))
+            op("p", mm(T.K6[:, 1:256:2], T.NE[:, 128:256] if d > 0 else T.ZB[:], T.PEN[:, 1:256:2], False, True), ["NE1" if d > 0 else "ZB", "PEN"], ["@K6"])
             dead = [(T.DLAND[:, 16 * t:16 * t + 16], "DLAND%d" % t)] + [(T.WB[:, 16 * i:16 * i + 16], "WB%d" % i) for i in range(d)]
             op("p", [mm(T.C7[:, 0:16], IB, a, i == 0, False) for i, (a, k) in enumerate(dead)], ["IB"] + [k for a, k in dead], ["@C7"])
             if d == 0 and t > 0:
@@ -532,10 +531,12 @@ def rank_program(g, core, T, topo):
                 near_add(t - 1)
             else:
                 tt(T.DE[:], T.MSP[:], T.E1[:], A.subtract, ["MSP", "E1"], ["DE"])
-            ts(T.YU[:], T.C7[:, 0:16], DEAD, A.min, ["@C7"], ["YU"])
-            act(T.UP[:], far[:, 0:WX].indirect(T.YU[:]), F.Copy, [fk, "YU"], ["UP"])
-            tt(T.QR[:], far[:, 0:WX].indirect(T.YU[:]), T.CR[:], A.mult, [fk, "YU", "CR"], ["QR"])
-            act(T.GX[:], T.X[:, 0:WX].indirect(T.YU[:]), F.Copy, ["X", "YU"], ["GX"])
+            yu, yk = T.YSND[:, 16 * m:16 * m + 16], "YSND%d" % m
+            ts(yu, T.C7[:, 0:16], DEAD, A.min, ["@C7"], [yk])
+            if not tail:
+                send(to, "y%d%d" % (t, d), T.YLAND[:, 16 * m:16 * m + 16], yu, [yk])
+            act(T.UP[:], far[:, 0:WX].indirect(yu), F.Copy, [fk, yk], ["UP"])
+            tt(T.QR[:], far[:, 0:WX].indirect(yu), T.CR[:], A.mult, [fk, yk, "CR"], ["QR"])
             gap(6)
             ts(T.QO[:], T.QR[:], OCOL, A.mult, ["QR", "PC"], ["QO"])
             if d == 0 and t > 0:
@@ -546,48 +547,65 @@ def rank_program(g, core, T, topo):
                 q = "QO" if gr % 2 else "QR"
                 op("p", mm(T[bk][:, c:c + 128 + 128 * ll], T.UP[p0:p0 + k, ll:256:2], T[q][p0:p0 + k, 0:256:2 - ll], True, True), ["UP", q], ["@" + bk])
 
-            def pv(q):
-                unit(2 * q, 1, "G%d" % q, 0)
-                unit(2 * q, 0, "G%d" % q, 256)
-                if q > 0:
-                    unit(2 * q + 1, 0, "G%d" % q, 384)
+            def by_vector(i):
+                q = min(i, 3)
+                units, c0 = ([(2 * q, 0), (2 * q + 1, 0), (2 * q + 1, 1)], 0) if i < 3 else ([(3 + i, 0)], 128 * (i - 3))
+                n = c0
+                for gr, ll in units:
+                    unit(gr, ll, "G%d" % q, n)
+                    n += 128 + 128 * ll
+                scan(T.FL[:, 512 * q + c0:512 * q + n], T["G%d" % q][:, c0:n], T.TH[:, c0:n], A.max, A.add, ["@G%d" % q, "THS"], ["FL%d" % (i if i < 4 else 9)])
 
-            def vv(q):
-                n = 512 if q > 0 else 384
-                scan(T.FL[:, 512 * q:512 * q + n], T["G%d" % q][:, 0:n], T.TH[:, 0:n], A.max, A.add, ["@G%d" % q, "THS"], ["FL%d" % q])
+            def by_scalar(i):
+                bk, c = ("G4", "K6", "G4", "K6", "G0")[i], (2048 + i if i < 4 else 2047)
+                unit((0, 2, 4, 6, 7)[i], 1, bk, 0)
+                act(T.JK[:, 256 * i:256 * i + 256], T[bk][:, 0:256], F.Relu, ["@" + bk, "THS"], ["JK%d" % i, "FL%d" % (4 + i)],
+                    bias=T.TH[:, 511:512], accum_out=T.FL[:, c:c + 1])
 
-            def ps(q):
-                unit(2 * q + 1, 1, ("G4", "K6")[q % 2], 0)
-                if q == 0:
-                    unit(1, 0, "G4", 256)
+            def new_records(win, wk, ys, yk_, st, stk, bk, c, out, key, opened):
+                gx = T.GX[:, 0:256] if opened else T.GX[:, 256:512]
+                act(gx, win[:, 0:WX].indirect(ys), F.Copy, [wk, yk_], ["G" + key])
+                if not opened:
+                    op("p", [mm(T[bk][:, c:c + 256], IH, a, i == 0, False) for i, a in enumerate((st, T.CQ[:, 0:256]))], ["IH", stk, "CQ0"], ["@" + bk])
+                return (lambda: op("p", [mm(T[bk][:, c:c + 256], IH, a, False, i == 1) for i, a in enumerate((gx, T.CQ[:, 256:512]))],
+                                   ["IH", "G" + key, "CQ1"], ["@" + bk]),
+                        lambda: act(out, T[bk][:, c:c + 256], F.Copy, ["@" + bk], [key], bias=-MAGIC))
 
-            def ss(q):
-                bk = ("G4", "K6")[q % 2]
-                act(T.JK[:, 256 * q:256 * q + 256], T[bk][:, 0:256], F.Relu, ["@" + bk, "THS"], ["JK%d" % q, "FL%d" % (4 + q)],
-                    bias=T.TH[:, 255:256], accum_out=T.FL[:, 2048 + q:2049 + q])
-                if q == 0:
-                    act(T.JK[:, 1024:1152], T.G4[:, 256:384], F.Relu, ["@G4", "THS"], ["JK4", "FL8"], bias=T.TH[:, 383:384], accum_out=T.FL[:, 511:512])
-
-            ns = T.NSND[:, 256 * m:256 * m + 256]
-
-            def pn():
-                op("p", [mm(T.LB[:, 256:512], IH, a, False, i == 1) for i, a in enumerate((T.GX[:], T.CQ[:, 256:512]))], ["IH", "GX", "CQ1"], ["@LB"])
-
-            def sn():
-                act(ns, T.LB[:, 256:512], F.Copy, ["@LB"], ["NSND%d" % m], bias=-MAGIC)
-                if not tail:
-                    send(to, "n%d%d" % (t, d), T.NLAND[:, 256 * m:256 * m + 256], ns, ["NSND%d" % m])
-
-            pv(0); vv(0); ps(0); ss(0); pv(1); vv(1); ps(1); ss(1); pv(2); vv(2); ps(2); ss(2); pv(3); vv(3); ps(3); ss(3); pn(); sn()
+            own_new = new_records(T.X, "X", yu, yk, s_, sk, "LB", 256, T.NS[:, 0:256], "NS", True)
+            by_vector(3); by_scalar(0); by_vector(0); by_scalar(1); by_vector(1); by_scalar(2); by_vector(2); by_scalar(3); by_vector(4); by_scalar(4)
             op("p", mm(T.C7[:, 16:32], T.E1[:], T.RS1[:], True, False), ["E1", "RS1"], ["@C7"])
-            tt(T.E2[:], T.FL[:, 0:2056].indirect(T.LX2[:]), T.DE[:], A.min, ["FL%d" % i for i in range(9)] + ["LX2", "DE"], ["E2"])
-            op("p", mm(T.C7[:, 16:32], T.E2[:], T.RS1[:], False, True), ["E2", "RS1"], ["@C7"])
+            own_new[0]()
+            own_new[1]()
             if not tail:
+                if d == 0:
+                    landed(frm, "b%d" % t, [xk + "b"])
+                    join(xk, [xk + "b", xk + "x"])
+                    landed(frm, "f%d" % t, ["FLAND%d" % t])
+                landed(frm, "y%d%d" % (t, d), ["YLAND%d" % m])
+                home_new = new_records(XC, xk, T.YLAND[:, 16 * m:16 * m + 16], "YLAND%d" % m, T.FLAND[:, 256 * t:256 * t + 256], "FLAND%d" % t,
+                                       "G1", 0, T.NS[:, 256:512], "NH", False)
+            op("p", mm(T.G2[:, 0:16], T.E1[:], T.RS1[:], True, False), ["E1", "RS1"], ["@G2"])
+            tt(T.E2[:], T.FL[:, 0:2056].indirect(T.LX2[:]), T.DE[:], A.min, ["FL%d" % i for i in range(10)] + ["LX2", "DE"], ["E2"])
+            ends = [lambda: op("p", mm(T.C7[:, 16:32], T.E2[:], T.RS1[:], False, True), ["E2", "RS1"], ["@C7"]),
+                    lambda: op("p", mm(T.G2[:, 0:16], T.E2[:], T.RSN[:], False, True), ["E2", "RSN"], ["@G2"])]
+            for f in (ends[::-1] if end else ends):
+                f()
+            if not tail:
+                home_new[0]()
+                home_new[1]()
                 cp(T.R4[:], T.RA[:, 0:16].indirect(T.LX3[:]), ["RA", "LX3"], ["R4"])
-                op("p", mm(T.LB[:, 0:128], T.R4[:], T.IDF[:], True, True), ["R4", "IDF"], ["@LB"])
             gap(1)
+
+            def result(out, key):
+                if d == 0:
+                    cp(out, T.G2[:, 0:16], ["@G2"], [key])
+                else:
+                    tt(out, T.G2[:, 0:16], T.RES[:], A.max, ["@G2", "RES"], [key])
+
             if end:
-                ts(T.CB[:], T.HL[:, 0:256], 16.0, A.mult, ["HI0"], ["CB", "CBb"], -1.0, A.add)
+                r_ = T.RSND[:, 32 * t:32 * t + 16]
+                result(r_, "RSH")
+                send(frm, "r%d" % t, T.RLAND[:, 32 * t:32 * t + 16], r_, ["RSH"])
             ls = T.LSND[:, 16 * m:16 * m + 16]
             lk = "LSND%d" % m
             cp(ls, T.C7[:, 16:32], ["@C7"], [lk])
@@ -595,25 +613,17 @@ def rank_program(g, core, T, topo):
                 send(to, "l%d%d" % (t, d), T.LLAND[:, 16 * m:16 * m + 16], ls, [lk])
             wb = T.WB[:, 16 * d:16 * d + 16]
 
-            def result(out, key):
-                if d == 0:
-                    cp(out, T.C7[:, 16:32], ["@C7"], [key])
-                else:
-                    tt(out, T.C7[:, 16:32], T.RES[:], A.min, ["@C7", "RES"], [key])
-
             def own_records():
-                cp(T.X[:, 0:WX].indirect(ls), ns, [lk, "NSND%d" % m], ["X"])
+                cp(T.X[:, 0:WX].indirect(ls), T.NS[:, 0:256], [lk, "NS"], ["X"])
 
             def far_table():
                 tt(far[:, 0:WX].indirect(ls), T.UP[:], T.RC[:, 256 * t:256 * t + 256], A.add, ["UP", "RC%d" % t, lk], [fk])
 
             if end:
-                r_ = T.RSND[:, 32 * t:32 * t + 16]
-                result(r_, "RSH")
-                send(frm, "r%d" % t, T.RLAND[:, 32 * t:32 * t + 16], r_, ["RSH"])
                 own_records()
                 dma("y", [(T.yx[:], T.X[:, 0:W])], ["X"], ["yx"])
-                far_table()
+                cp(T.FO[:, 0:WX].indirect(ls), T.DIAG[:], [lk, "DIAG"], ["FO"])
+                dma("s", [(T.yb[:], T.FO[0:128:16, 0:W])], ["FO"], ["yb"])
                 break
             ts(wb, T.C7[:, 16:32], DEAD, A.is_lt, ["@C7"], ["WB%d" % d], DEAD, A.mult)
             op("p", mm(T.G0[:, 0:16], T.ONES[:], wb, True, True), ["ONES", "WB%d" % d], ["@G0"])
@@ -633,50 +643,42 @@ def rank_program(g, core, T, topo):
                 near_send(t)
                 kappa[1]()
                 dead_send(t + 1)
+                starters_on(t + 1)
                 records_send(t + 1)
                 kappa[2]()
                 kappa[3]()
                 gap(2)
                 continue
             far_table()
-            act(T.PG[:], far[:, 0:WX].indirect(T.YU[:]), F.Copy, [fk, "YU"], ["PG"])
+            gap(2)
+            act(T.PG[:], far[:, 0:WX].indirect(yu), F.Copy, [fk, yk], ["PG"])
             result(T.RES[:], "RES")
             to_list(lambda b: T.PG[:, b:256:16], ["PG"])
+            op("p", mm(T.LB[:, 0:128], T.R4[:], T.IDF[:], True, True), ["R4", "IDF"], ["@LB"])
             kappa[0]()
+            gap(7)
+            for k in kappa[1:]:
+                k()
             if m == 1:
                 spare_columns("TA")
                 fill_rows("TA", 0)
                 join("TA", ["TAd", "TAx"])
-            if m == ND * NB - 2:
-                dma("y", [(T.HL[:, 0:256], T.TA[15:128:16, 0:W]), (T.HL[:, 256:512], T.TA[14:128:16, 0:W])], ["TA"], ["HI0", "LO0"])
-            kappa[1]()
-            gap(2)
-            msg = "%d%d" % (t, d)
-            if d == 0:
-                landed(frm, "b%d" % t, [xk + "b"])
-                join(xk, [xk + "b", xk + "x"])
-            landed(frm, "n" + msg, ["NLAND%d" % m])
-            landed(frm, "l" + msg, ["LLAND%d" % m])
-            cp(XC[:, 0:WX].indirect(T.LLAND[:, 16 * m:16 * m + 16]), T.NLAND[:, 256 * m:256 * m + 256], ["NLAND%d" % m, "LLAND%d" % m], [xk])
+            if m >= ND * NB - 3:
+                tab, i = (("TA", 0), ("TB", 1))[m - (ND * NB - 3)]
+                dma("y", [(T.HL[:, 512 * i:512 * i + 256], T[tab][15:128:16, 0:W]), (T.HL[:, 512 * i + 256:512 * i + 512], T[tab][14:128:16, 0:W])],
+                    [tab], ["HI%d" % i, "LO%d" % i])
+            landed(frm, "l%d%d" % (t, d), ["LLAND%d" % m])
+            cp(XC[:, 0:WX].indirect(T.LLAND[:, 16 * m:16 * m + 16]), T.NS[:, 256:512], ["NH", "LLAND%d" % m], [xk])
             ts(T.PU[:], T.C7[:, 32:48], -1.0, A.add, ["@C7"], ["PU"])
-            kappa[2]()
-            kappa[3]()
-            act(T.Z[:], XC[:, 0:WX].indirect(T.PU[:]), F.Copy, [xk, "PU"], ["Z"])
+            for h in (1, 0):
+                act(T.Z[:, 128 * h:128 * h + 128], XC[:, 0:WX].indirect(T.PU[:, 8 * h:8 * h + 8]), F.Copy, [xk, "PU"], ["Z%d" % h])
             own_records()
-    op("p", [mm(T.G0[:, 0:256], T.SW[:, 16 - k:144 - k], T.TB[:, 256 * k:256 * k + 256], k == 0, k == 15) for k in range(16)], ["SW", "TB"], ["@G0"])
     t = NB - 1
-    tt(T.PF[:, 0:256], T.CB[:], T.HL[:, 256:512], A.add, ["CB", "CBb", "LO0"], ["YA0"])
     landed(nxt if t % 2 == 0 else prv, "r%d" % t, ["RLAND%d" % t])
-    r_ = T.RLAND[:, 32 * t:32 * t + 16]
-    ts(T.W1[:], r_, DEAD, A.is_lt, ["RLAND%d" % t], ["W1"])
-    ts(T.W2[:], r_, 1.0, A.add, ["RLAND%d" % t], ["W2"])
-    tt(T.W3[:], T.W1[:], T.W2[:], A.mult, ["W1", "W2"], ["W3"])
     for o, e in enumerate(("E1", "E2")):
-        tt(T[e][:], T.W3[:, 0:16].indirect(T.LX5[:, 8 * o:8 * o + 8]), T.CB1[:], A.mult, ["W3", "LX5_%d" % o, "CB1"], [e])
+        tt(T[e][:], T.RLAND[:, 32 * t:32 * t + 16].indirect(T.LX5[:, 8 * o:8 * o + 8]), T.CB1[:], A.mult, ["RLAND%d" % t, "LX5_%d" % o, "CB1"], [e])
         op("p", mm(T.G4[:, 8 * o:8 * o + 8], T[e][:], T.D16[:, 0:8], True, True), [e, "D16"], ["@G4"])
-    act(T.PF[:, 256:512], T.G0[:, 0:256], F.Copy, ["@G0"], ["YB0"], bias=-1.0)
-    dma("s", [(T.yb[:], T.PF[:, 256:512])], ["YB0"], ["yb"])
-    tt(T.PF[:, t:256:16], T.G4[:, 0:16], T.PF[:, t:256:16], A.add, ["@G4", "YA0"], ["YA0"])
-    dma("y", [(T.ya[:], T.PF[:, 0:256])], ["YA0"], ["ya"])
+    tt(T.PF[:, t:256:16], T.G4[:, 0:16], T.PF[:, t:256:16], A.max, ["@G4", "PF0"], ["PF0"])
+    dma("y", [(T.ya[:], T.PF[:, 0:256])], ["PF0"], ["ya"])
     for sem in sorted(last):
         need("g", {sem: last[sem]})

@@ -6,8 +6,9 @@ DUM = 4112
 WX = DUM + 256
 NB, ND = 3, 3
 SC = 8192.0
+FH = 1032
 MAGIC = 1.5 * 2 ** 23
-NV = (66, 64)
+NV = (70, 64)
 
 _B = {}
 
@@ -24,9 +25,9 @@ _sb("WI", 8, "int32"); _sb("WF", 8, "float32")
 _sb("PI", 8, "int32"); _sb("PT", 8, "int32"); _sb("PC", 32, "float32"); _sb("SG", 16, "float32")
 _sb("CF", 264, "float32"); _sb("LANE", 256, "float32"); _sb("C8", 128, "float32"); _sb("CB1", 128, "float32"); _sb("SPI", 128, "float32")
 _sb("CG", 128, "float32"); _sb("WP", 256, "float16"); _sb("WN", 256, "float16")
-_sb("OB", 16, "bfloat16"); _sb("IDF", 128, "float32"); _sb("PEN", 264, "bfloat16"); _sb("ZB", 128, "bfloat16")
+_sb("OB", 16, "bfloat16"); _sb("IDF", 128, "float32"); _sb("IDN", 128, "float32"); _sb("PEN", 128, "bfloat16"); _sb("EK", 128, "float32"); _sb("PAIR", 128, "bfloat16"); _sb("RSX", 32, "float32"); _sb("FBC", 16, "float32"); _sb("LX6", 8, "uint16"); _sb("ZB", 128, "bfloat16")
 _sb("IBN", 384, "bfloat16")
-_sb("CQ", 896, "bfloat16")
+_sb("CQ", 928, "bfloat16")
 _sb("M1", 128, "float32"); _sb("MSP", 128, "float32"); _sb("RS1", 16, "float32"); _sb("RSN", 16, "float32"); _sb("RS", 256, "float32")
 _sb("CR", 256, "bfloat16"); _sb("RC", 256 * NB, "bfloat16"); _sb("TH", 512, "float32"); _sb("SW", 144, "bfloat16")
 _sb("ONES", 128, "bfloat16"); _sb("DIAG", 256, "float32"); _sb("SRB", 256, "bfloat16"); _sb("D16", 16, "float32")
@@ -40,19 +41,19 @@ _sb("LSND", 16 * NB * ND, "uint16"); _sb("LLAND", 16 * NB * ND, "uint16")
 _sb("RSND", 32 * NB, "float32"); _sb("RLAND", 32 * NB, "float32")
 _sb("Z", 256, "bfloat16"); _sb("Z8", 2048, "bfloat16")
 _sb("SQ", 256, "float32"); _sb("FI", 256, "int32"); _sb("CI", 256, "int32")
-_sb("OFF", 256, "uint16"); _sb("CFL", 256, "float16"); _sb("NE", 256, "bfloat16")
+_sb("OFF", 256, "uint16"); _sb("CFL", 256, "float16"); _sb("EQ", 256, "bfloat16")
 _sb("DF", 4096, "bfloat16"); _sb("AB", 4096, "bfloat16")
 _sb("R", 256, "float32"); _sb("RI", 16, "int32"); _sb("RA", 16, "int32"); _sb("E1", 128, "float32"); _sb("DE", 128, "float32")
 _sb("R4", 128, "float32"); _sb("E2", 128, "float32"); _sb("NS", 512, "bfloat16"); _sb("FO", WX, "float32")
 _sb("UP", 256, "bfloat16"); _sb("QR", 256, "bfloat16"); _sb("QO", 256, "bfloat16"); _sb("GX", 512, "bfloat16")
-_sb("FL", 2056, "float32"); _sb("JK", 1280, "bfloat16"); _sb("PG", 256, "bfloat16"); _sb("PU", 16, "uint16"); _sb("E3", 512, "bfloat16")
+_sb("FL", 2 * FH, "float32"); _sb("JK", 1280, "bfloat16"); _sb("PG", 256, "bfloat16"); _sb("PU", 16, "uint16"); _sb("E3", 512, "bfloat16")
 _sb("WB", 16 * ND, "bfloat16"); _sb("RES", 16, "float32"); _sb("W1", 16, "float32"); _sb("W2", 16, "float32"); _sb("W3", 16, "float32")
-_sb("KP", 8, "float32"); _sb("KJ", 16, "float32"); _sb("KI", 8, "int32")
+_sb("KP", 8, "float32"); _sb("KJ", 16, "float32")
 for _n in ["G0", "G1", "G2", "G3", "G4", "K6", "C7", "LB"]:
     _B[_n] = ("psum", [128, 512], "float32")
 SCRATCH = _B
 
-_MSG = []
+_MSG = ["q"]
 for _t in range(NB):
     _MSG += ["s%d" % _t, "f%d" % _t, "b%d" % _t, "e%d" % _t, "r%d" % _t]
     for _d in range(ND - 1):
@@ -122,15 +123,21 @@ def rank_program(g, core, T, topo):
             Q[q].dma_start(out, in_).then_inc(T.sem[sem], 16)
         note(reads, writes, sem, 16 * len(pieces))
 
+    def engines(frm, to, msg):
+        es = topo.engines(T.cores[frm], T.cores[to])
+        if msg == "s1":
+            es = [e for e in es if e in topo.engines(T.cores[frm], T.cores[(frm + 1) % n_ranks])]
+        return es
+
     def send(to, msg, out, in_, reads):
         need("g", deps(reads, []))
-        dst = T.cores[to]
-        rid, pid, _se = topo.addr(dst)
-        g.remote_dma(out, in_, T.sem["rx" + msg], T.sem["tx" + msg], pid, rid, topo.mask(core, dst))
-        note(reads, [], "tx" + msg, len(topo.engines(core, dst)))
+        rid, pid, _se = topo.addr(T.cores[to])
+        es = engines(rank, to, msg)
+        g.remote_dma(out, in_, T.sem["rx" + msg], T.sem["tx" + msg], pid, rid, sum(1 << e for e in es))
+        note(reads, [], "tx" + msg, len(es))
 
     def landed(frm, msg, keys):
-        note([], keys, "rx" + msg, len(topo.engines(T.cores[frm], core)))
+        note([], keys, "rx" + msg, len(engines(frm, rank, msg)))
 
     def join(key, parts):
         wr[key] = deps(parts, [])
@@ -158,6 +165,9 @@ def rank_program(g, core, T, topo):
 
     def iota(key, pattern, base, mult):
         op("g", lambda: g.iota(T[key][:], pattern, base, mult, allow_small_or_imprecise_dtypes=True), [], [key])
+
+    def zeros(ap, keys):
+        op("g", lambda: g.iota(ap, [[0, ap.shape[1]]], 0, 0, allow_small_or_imprecise_dtypes=True), [], keys)
 
     def mm(out, lhsT, rhs, start, stop):
         return lambda: g.tensor.matmul(out, lhsT, rhs, start, stop)
@@ -195,6 +205,12 @@ def rank_program(g, core, T, topo):
         xc = T.XC0 if t % 2 == 0 else T.XC1
         send(nxt if t % 2 == 0 else prv, "b%d" % t, xc[:, 0:W], T.X[:, 0:W], ["X"])
 
+    def result(out, key, d):
+        if d == 0:
+            cp(out, T.LB[:, 128:144], ["@LB"], [key])
+        else:
+            tt(out, T.LB[:, 128:144], T.RES[:], A.max, ["@LB", "RES"], [key])
+
     def near_send(t):
         hi, lo = T.RSND[:, 32 * t:32 * t + 16], T.RSND[:, 32 * t + 16:32 * t + 32]
         ts(T.LXJ[:], T.RES[:], 0.0, A.max, ["RES"], ["LXJ"])
@@ -214,6 +230,15 @@ def rank_program(g, core, T, topo):
             op("p", [mm(T.LB[:, 0:256], T.SRB[:, 128 * h:128 * h + 128], T.E3[:, 256 * h:256 * h + 256], h == 0, h == 1) for h in range(2)],
                ["SRB0", "SRB1", "E3_0", "E3_1"], ["@LB"])
 
+    def last_pairs(i):
+        t = NB - 1
+        msg, c, tiles = (("q", 32 * t + 16, (["R4"], ["EK", "EK0", "EK1"])), ("r%d" % t, 32 * t, (["E1"], ["E2", "E2b"])))[i]
+        landed(nxt if t % 2 == 0 else prv, msg, ["L" + msg])
+        for o, e in enumerate(tiles):
+            tt(T[e[0]][:], T.RLAND[:, c:c + 16].indirect(T.LX5[:, 8 * o:8 * o + 8]), T.CB1[:], A.mult, ["L" + msg, "LX5_%d" % o, "CB1"], e)
+        return lambda: [op("p", mm(T.G4[:, 8 * o:8 * o + 8], T[e[0]][:], T.D16[:, 0:8], i + o == 0, i + o == 2), [e[0], "D16"], ["@G4"])
+                        for o, e in enumerate(tiles)]
+
     def near_add(t):
         near, nk = (T.TA, "TA") if t % 2 == 0 else (T.TB, "TB")
         tt(near[:, t:W:16], T.LB[:, 0:256], near[:, t:W:16], A.add, ["@LB", nk], [nk])
@@ -221,7 +246,7 @@ def rank_program(g, core, T, topo):
     dma("y", [(T.PAI[:], T.pa[:])], [], ["PAI"])
     dma("s", [(T.WI[:, 0:1], T.wt[:])], [], ["WI"])
     dma("y", [(T.X[:, 0:W], T.x[:])], [], ["Xd"])
-    dma("s", [(T.PBI[:], T.pb[:])], [], ["PBI"])
+    dma("y", [(T.PBI[:], T.pb[:])], [], ["PBI"])
     op("g", lambda: g.iota(T.PI[:, 0:1], [[0, 1]], 0, 1), [], ["PI"])
     iota("CF", [[1, 264]], 0, 0)
     iota("C8", [[1, 16], [0, 8]], 0, 0)
@@ -235,7 +260,6 @@ def rank_program(g, core, T, topo):
     ms(T.ZB[:], 0.0, ["ZB"])
     cp(T.PC[:, 0:8], T.PT[:, 0:8], ["PT%d" % c for c in range(8)], ["PC"])
     PGRP, PLOW, PL7, P8, P1, PLL, OCOL, PP = [T.PC[:, c:c + 1] for c in range(8)]
-    ms(T.RS[:], -2.0 ** 26, ["RS"])
     ts(T.LT[:, 0:12], T.CF[:, 0:12], PLOW, A.not_equal, ["CF", "PC"], ["LT"], 2.0, A.mult)
     ts(T.PC[:, 8:12], T.CF[:, 12:16], PLOW, A.is_equal, ["CF", "PC"], ["PCI"])
     I12, I14, I15 = T.PC[:, 8:9], T.PC[:, 10:11], T.PC[:, 11:12]
@@ -248,20 +272,18 @@ def rank_program(g, core, T, topo):
     ts(T.PC[:, 13:14], PGRP, 2.0, A.mult, ["PC"], ["PC13"], 1.0, A.add)
     for ch in range(2):
         ts(T.SCOL[:, ch:ch + 1], PL7, 32.0, A.mult, ["PC"], ["SCOL%d" % ch], 256.0 * ch + 16.0, A.add)
-    ts(T.PC[:, 23:24], PP, 2.0, A.mult, ["PC"], ["PC23"], 1.0, A.add)
     ts(IH, T.CF[:, 0:128], PP, A.is_equal, ["CF", "PC"], ["IH"], 0.5, A.mult)
     tt(T.SCOL[:, 2:4], T.SCOL[:, 0:2], T.SCOL[:, 0:2], A.mult, ["SCOL0", "SCOL1"], ["SCOL2"])
     ts(IN, T.CF[:, 0:128], PP, A.is_equal, ["CF", "PC"], ["IN"], -1.0, A.mult)
     ts(T.ACOL[:, 0:2], T.SCOL[:, 2:4], -1.0, A.mult, ["SCOL2"], ["ACOL0", "ACOL1"], 262144.0 - 12.0, A.add)
     ts(T.WF[:, 3:4], T.WI[:, 0:1], 2048.0, A.is_gt, ["WI"], ["WF3"], -4096.0, A.mult)
     ms(T.ONES[:], 1.0, ["ONES"])
-    ts(T.WF[:, 0:1], T.WI[:, 0:1], T.WF[:, 3:4], A.add, ["WI", "WF3"], ["WF0"], 1.0 / 4096, A.mult)
-    ts(T.WF[:, 1:2], T.WI[:, 0:1], T.WF[:, 3:4], A.add, ["WI", "WF3"], ["WF1"], -1.0 / 4096, A.mult)
     ts(T.DSND[:, 0:16], T.PAI[:, 0:256:16], 0.0, A.is_ge, ["PAI"], ["DSND0"], DEAD, A.mult)
-    iota("SPI", [[0, 64], [1, 2]], DUM, 2)
     iota("CG", [[2, 8], [0, 8], [1, 2]], 0, 0)
     send(nxt, "e0", T.DLAND[:, 16 * NB:16 * NB + 16], T.DSND[:, 0:16], ["DSND0"])
     landed(prv, "e0", ["DRAW"])
+    ts(T.WF[:, 0:1], T.WI[:, 0:1], T.WF[:, 3:4], A.add, ["WI", "WF3"], ["WF0"], 1.0 / 4096, A.mult)
+    ts(T.WF[:, 1:2], T.WI[:, 0:1], T.WF[:, 3:4], A.add, ["WI", "WF3"], ["WF1"], -1.0 / 4096, A.mult)
     for ll in range(2):
         for wm, c in (("WP", 0), ("WN", 1)):
             ts(T[wm][:, 128 * ll:128 * ll + 128], T.C8[:], T.PC[:, 12 + ll:13 + ll], A.is_equal, ["C8", "PC12", "PC13", "WF%d" % c], ["%s%d" % (wm, ll)], T.WF[:, c:c + 1], A.mult)
@@ -269,10 +291,8 @@ def rank_program(g, core, T, topo):
     ms(T.CQ[:, 512:640], -2 * MAGIC, ["CQ2"])
     ms(T.CQ[:, 640:896], 4096.0, ["CQ3"])
     ts(IB, T.CF[:, 0:128], PP, A.is_equal, ["CF", "PC"], ["IB"])
-    ts(T.IDF[:], T.CF[:, 0:128], PP, A.is_equal, ["CF", "PC"], ["IDF"])
     for i in range(2):
         ts(T.OB[:, 8 * i:8 * i + 8], T.CF[:, 0:8], PGRP, A.is_equal, ["CF", "PC"], ["OB%d" % i], 4096.0 * (1 - 2 * i), A.mult)
-    ts(T.PEN[:], T.CF[:], T.PC[:, 23:24], A.is_equal, ["CF", "PC23"], ["PEN"], -2.0 ** 24, A.mult)
 
     def table_rows(pin, pk, i):
         hi, lo = T.HL[:, 512 * i:512 * i + 256], T.HL[:, 512 * i + 256:512 * i + 512]
@@ -292,32 +312,36 @@ def rank_program(g, core, T, topo):
         act(T.RC[:, 256 * t:256 * t + 256], T.LANE[:], F.Identity, ["LANE", "PCI", "PC20"], ["RC%d" % t], scale=I15, bias=T.PC[:, 20 + t:21 + t])
 
     rows_b = table_rows(T.PBI, "PBI", 1)
-    rows_b[0]()
     ts(T.WF[:, 2:3], PLOW, P1, A.subtract, ["PC"], ["WF2"], 0.5, A.mult)
-    ts(T.PC[:, 16:17], I14, 40.0, A.mult, ["PCI"], ["PC16"])
-    rows_b[1]()
-    ms(T.XC1[:, W:WX], 0.0, ["XC1x"])
-    rows_b[2]()
+    ts(T.RS1[:], T.CF[:, 0:16], P8, A.is_equal, ["CF", "PC"], ["RS1"])
+    ts(T.LX1[:], T.CF[:, 0:16:2], P1, A.add, ["CF", "PC"], ["LX1"])
+    ts(T.LT[:, 48:56], T.CF[:, 0:16:2], P1, A.add, ["CF", "PC"], ["LT6"], 16.0, A.mult)
+    ts(T.M1[:], T.CB1[:], PL7, A.is_equal, ["CB1", "PC"], ["M1"])
     ts(T.PC[:, 17:18], PLOW, 12.0, A.is_lt, ["PC"], ["PC17"], 128.0 * SC, A.mult)
     ts(T.PC[:, 18:19], I12, -SC, A.mult, ["PCI"], ["PC18"])
-    starters_send(0)
-    rows_b[3]()
+    ts(T.LX6[:], T.LT[:, 48:56], 15.0, A.add, ["LT6"], ["LX6"])
+    ts(T.PC[:, 16:17], I14, 40.0, A.mult, ["PCI"], ["PC16"])
     ts(T.PC[:, 19:20], I14, SC, A.mult, ["PCI", "PC17"], ["PC19"], T.PC[:, 17:18], A.add)
+    starters_send(0)
     ts(T.PC[:, 20:23], T.CF[:, 1:4], I14, A.mult, ["CF", "PCI"], ["PC20"])
+    ts(T.PC[:, 25:26], P1, 2 * MAGIC - 4096.0, A.mult, ["PC"], ["PC25"], -2 * MAGIC, A.add)
+    ts(T.PC[:, 26:27], PP, P1, A.subtract, ["PC"], ["PC26"], 0.5, A.mult)
+    rows_b[0]()
+    ts(T.WB[:, 0:8], T.CF[:, 0:8], PL7, A.is_equal, ["CF", "PC"], ["WB0"])
+    rows_b[1]()
+    ts(T.R4[:], T.CG[:], P8, A.is_equal, ["CG", "PC"], ["R4"])
+    rows_b[2]()
+    for o in range(2):
+        ts(T.LX0[:, 8 * o:8 * o + 8], T.ZB[:, 0:8], T.WF[:, 2:3], A.add, ["ZB", "WF2"], ["LX0_%d" % o], 8.0 * o, A.add)
+    rows_b[3]()
     ts(T.TB[:, 3072:W], T.TB[:, 1024:2048], T.SG[:, 11:12], A.mult, ["TBb", "SG"], ["TBd"])
     need("y", deps([], ["SS0_0"]))
     fill_rows("TB", 1)
+    zeros(T.RS[:], ["RS"])
     starters_on(0)
+    zeros(T.XC1[:, W:WX], ["XC1x"])
     need("g", deps(["TBd"], []))
     records_send(0)
-    ts(T.WB[:, 0:8], T.CF[:, 0:8], PL7, A.is_equal, ["CF", "PC"], ["WB0"])
-    ts(T.R4[:], T.CG[:], P8, A.is_equal, ["CG", "PC"], ["R4"])
-    for o in range(2):
-        ts(T.LX0[:, 8 * o:8 * o + 8], T.ZB[:, 0:8], T.WF[:, 2:3], A.add, ["ZB", "WF2"], ["LX0_%d" % o], 8.0 * o, A.add)
-    ms(T.RS[:, 0:256:16], 2.0 ** 26, ["RS"])
-    ts(T.M1[:], T.CB1[:], PL7, A.is_equal, ["CB1", "PC"], ["M1"])
-    ts(T.RS1[:], T.CF[:, 0:16], P8, A.is_equal, ["CF", "PC"], ["RS1"])
-    ts(T.LX1[:], T.CF[:, 0:16:2], P1, A.add, ["CF", "PC"], ["LX1"])
     for o in range(2):
         tt(T.E3[:, 128 * o:128 * o + 128], T.DLAND[:, 16 * NB:16 * NB + 16].indirect(T.LX0[:, 8 * o:8 * o + 8]), T.R4[:], A.mult,
            ["DRAW", "LX0_%d" % o, "R4"], ["E3_%d" % o])
@@ -326,32 +350,46 @@ def rank_program(g, core, T, topo):
         for o in range(2):
             op("p", mm(T.C7[:, 32 + o:48:2], T.E3[:, 128 * o:128 * o + 128], T.WB[:, 0:8], True, True), ["E3_%d" % o, "WB0"], ["@C7"])
 
-    tt(T.MSP[:], T.M1[:], T.SPI[:], A.mult, ["M1", "SPI"], ["MSP"])
+    iota("FBC", [[0, 2], [4096, 8]], 4081 * 4096, 0)
+    iota("SPI", [[0, 64], [1, 2]], DUM, 2)
+    iota("PAIR", [[1, 64], [0, 2]], 0, 0)
     iota("TH", [[0, 512]], 0, 0)
-    op("g", lambda: g.iota(T.FL[:, 1792:2056], [[0, 264]], 0, 0, allow_small_or_imprecise_dtypes=True), [], ["FL4", "FL5", "FL6", "FL7", "FL8"])
+    for key, ap, pattern, base in (("LT0", T.LT[:, 16:24], [[512, 4], [128, 2]], 127), ("LT1", T.LT[:, 24:32:2], [[-511, 4]], 897), ("LT2", T.LT[:, 25:32:2], [[0, 4]], 256)):
+        op("g", lambda: g.iota(ap, pattern, base, 0, allow_small_or_imprecise_dtypes=True), [], [key])
+    zeros(T.FL[:, 1024:FH], ["FL4", "FL5"])
+    zeros(T.FL[:, FH + 768:2 * FH], ["FL6", "FL7", "FL8"])
+    zeros(T.XC0[:, W:WX], ["XC0x"])
     iota("DIAG", [[1, 2], [0, 16], [2, 8]], 0, 0)
 
     def scalar_constants():
+        for i in range(2):
+            act(T.RSX[:, 16 * i:16 * i + 16], T.RS1[:], F.Copy, ["RS1"], ["RSX%d" % i], scale=(2 * i - 1) / 4096.0)
+        act(T.CQ[:, 896:912], T.RS1[:], F.Copy, ["RS1"], ["CQ896"], scale=0.0, bias=-2.0 ** -12)
+        act(T.CQ[:, 912:928], T.RS1[:], F.Identity, ["RS1", "PC25"], ["CQ912"], scale=0.0, bias=T.PC[:, 25:26])
+        join("RSX", ["RSX0", "RSX1"])
+        join("CQ4", ["CQ896", "CQ912"])
+        act(T.CR[:], T.LANE[:], F.Identity, ["LANE", "PC18", "PC19"], ["CR"], scale=T.PC[:, 18:19], bias=T.PC[:, 19:20])
         spare_columns("TB")
         join("TB", ["TBd", "TBx"])
-        act(T.CR[:], T.LANE[:], F.Identity, ["LANE", "PC18", "PC19"], ["CR"], scale=T.PC[:, 18:19], bias=T.PC[:, 19:20])
+        act(T.RSN[:], T.RS1[:], F.Copy, ["RS1"], ["RSN"], scale=-SC)
         starter_rows(0)
+        act(T.IDF[:], IB, F.Copy, ["IB"], ["IDF"])
+        act(T.IDN[:], IB, F.Copy, ["IB"], ["IDN"], scale=-1.0)
+        act(T.PEN[:], IB, F.Copy, ["IB"], ["PEN"], scale=2.0 ** 25)
 
     def first_constants():
+        yield lambda: (cp(T.RS[:, 0:256:16], T.FBC[:], ["FBC"], ["RS"]),
+                       ts(T.PAIR[:], T.PAIR[:], T.PC[:, 26:27], A.is_equal, ["PAIR", "PC26"], ["PAIR"], 0.5, A.mult))
         yield lambda: ms(T.CQ[:, 0:256], -0.5, ["CQ0"])
-        yield lambda: ts(T.LX3[:], T.CF[:, 0:16:2], PLL, A.add, ["CF", "PC"], ["LX3"])
         yield lambda: ts(T.PC[:, 24:25], PP, SC, A.mult, ["PC"], ["PC24"])
-        yield lambda: ts(T.RSN[:], T.RS1[:], -SC, A.mult, ["RS1"], ["RSN"])
+        yield lambda: ts(T.LX3[:], T.CF[:, 0:16:2], PLL, A.add, ["CF", "PC"], ["LX3"])
         yield lambda: (ts(T.TH[:, 127:256:128], T.ZB[:, 0:2], T.PC[:, 24:25], A.add, ["ZB", "PC24", "TH"], ["THa"], -1536 * SC, A.add),
                        ts(T.TH[:, 511:512], T.PC[:, 24:25], (128 - 1536) * SC, A.add, ["PC24", "TH"], ["THb"]))
         yield lambda: join("THS", ["TH", "THa", "THb"])
-        for i, (c0, step, base) in enumerate(((0, 512.0, 127.0), (1, 512.0, 255.0), (8, 1.0, 2048.0), (9, 512.0, 511.0))):
-            yield lambda i=i, c0=c0, step=step, base=base: ts(T.LT[:, 16 + c0:16 + c0 + 7:2], T.CF[:, 0:4], step, A.mult, ["CF"], ["LT%d" % i], base, A.add)
-        yield lambda: tt(T.LT[:, 32:40], T.LT[:, 24:32], T.LT[:, 16:24], A.subtract, ["LT0", "LT1", "LT2", "LT3"], ["LT4"])
-        yield lambda: ts(T.LT[:, 40:48], T.LT[:, 32:40], P1, A.mult, ["LT4", "PC"], ["LT5"])
-        yield lambda: tt(T.LT[:, 32:40], T.LT[:, 40:48], T.LT[:, 16:24], A.add, ["LT5", "LT0", "LT1"], ["LT4"])
+        yield lambda: ts(T.LT[:, 40:48], T.LT[:, 24:32], P1, A.mult, ["LT1", "LT2", "PC"], ["LT5"])
+        yield lambda: tt(T.MSP[:], T.M1[:], T.SPI[:], A.mult, ["M1", "SPI"], ["MSP"])
+        yield lambda: tt(T.LT[:, 32:40], T.LT[:, 40:48], T.LT[:, 16:24], A.add, ["LT5", "LT0"], ["LT4"])
         yield lambda: cp(T.LX2[:], T.LT[:, 32:40], ["LT4"], ["LX2"])
-        yield lambda: ms(T.XC0[:, W:WX], 0.0, ["XC0x"])
         yield lambda: ts(T.PC[:, 14:15], PGRP, 16.0, A.mult, ["PC"], ["PC14"], 16.0, A.add)
         yield lambda: ts(T.PC[:, 15:16], I15, 16.0, A.mult, ["PCI"], ["PC15"], I14, A.add)
         yield lambda: ts(T.SW[:], T.CF[:, 0:144], T.PC[:, 14:15], A.is_equal, ["CF", "PC14", "PC15"], ["SW"], T.PC[:, 15:16], A.mult)
@@ -380,9 +418,8 @@ def rank_program(g, core, T, topo):
 
     late = list(late_constants())
     first = list(first_constants())
-    gaps = {(0, 0): first[0:11], (0, 3): first[11:12], (0, 4): first[12:13], (0, 5): first[13:14], (0, 6): first[14:15], (0, 1): first[15:17],
-            (0, 2): first[17:21],
-            (0, 7): late[0:1], (1, 0): late[1:4], (2, 0): late[4:12], (4, 0): late[12:17], (7, 0): late[17:19], (8, 0): late[19:23]}
+    gaps = {(0, 0): first[0:8], (0, 3): first[8:9], (0, 4): first[9:10], (0, 1): first[10:12], (0, 2): first[12:16],
+            (0, 7): late[0:1], (1, 0): late[1:3], (1, 7): late[3:4], (2, 0): late[4:12], (4, 0): late[12:17], (7, 0): late[17:19], (8, 0): late[19:23]}
 
     for t in range(NB):
         frm, to = (prv, nxt) if t % 2 == 0 else (nxt, prv)
@@ -431,11 +468,16 @@ def rank_program(g, core, T, topo):
             def z8(cl):
                 cp(T.Z8[:, cl:16 * NV[0]:8], z[:, 0:2 * NV[0]], zks, ["Z8_%d" % cl])
 
-            for cl in range(3):
+            for cl in range(2):
                 act(T.Z8[:, cl:16 * NV[0]:8], z[:, 0:2 * NV[0]], F.Copy, zks, ["Z8_%d" % cl])
-            z8(3); z8(4)
-            floors(0, 1); floors(1, 1); z8(5); floors(0, 0); places(0, 1); floors(1, 0); places(0, 0); lists(0, 1)
-            places(1, 1); places(1, 0); lists(0, 0); z8(6); z8(7); lists(1, 1); lists(1, 0)
+            for cl in (5, 6, 7):
+                if d > 0:
+                    op("g", lambda: g.affine_select(T.Z8[:, cl:16 * NV[0]:8], z[:, 0:2 * NV[0]], [[0, 2 * NV[0]]], A.is_gt, 0.0, 1, 0), zks, ["Z8_%d" % cl])
+                else:
+                    z8(cl)
+            z8(2); z8(3); z8(4)
+            floors(0, 1); floors(1, 1); floors(0, 0); places(0, 1); floors(1, 0); places(0, 0); lists(0, 1)
+            places(1, 1); places(1, 0); lists(0, 0); lists(1, 1); lists(1, 0)
 
             def offs(ch, c0, c1):
                 return ["OFF%d%d" % (ch, h) for h in range(c0 // 64, (c1 - 1) // 64 + 1)]
@@ -461,14 +503,18 @@ def rank_program(g, core, T, topo):
                 a, b, o, st = 2048 * ch + 16 * c0, 2048 * ch + 16 * c1, (odd or 0), (1 if odd is None else 2)
                 act(T.AB[:, a + o:b:st], T[bk][:, o:b - a:st], F.Abs, ["@" + bk], ["AB%d_%d_%s" % (ch, c0, odd)])
 
-            def dsum(src, ch, c0, c1, ob, keys, parts=range(16)):
-                op("p", [mm(T.K6[c0:c1, 2 * b + ch:256:32], src[:, 2048 * ch + 16 * c0 + b:2048 * ch + 16 * c1:16], T.OB[:, 8 * ob:8 * ob + 8], False, False)
+            def dsum(src, ch, c0, c1, ob, keys, parts=range(16), close=False):
+                op("p", [mm(T.K6[c0:c1, 2 * b + ch:256:32], src[:, 2048 * ch + 16 * c0 + b:2048 * ch + 16 * c1:16], T.OB[:, 8 * ob:8 * ob + 8], False, close and b == 15)
                          for b in parts], keys + ["OB%d" % ob], ["@K6"])
 
-            def unbarred(ch):
+            def barred(ch):
                 if d > 0:
-                    tt(T.NE[:, 128 * ch:128 * ch + 128], T.LB[:, 0:128], T.CI[:, 128 * ch:128 * ch + 128], A.not_equal,
-                       ["@LB", "CI%d0" % ch, "CI%d1" % ch], ["NE%d" % ch])
+                    tt(T.EQ[:, 128 * ch:128 * ch + 128], T.LB[:, 0:128], T.CI[:, 128 * ch:128 * ch + 128], A.is_equal,
+                       ["@LB", "CI%d0" % ch, "CI%d1" % ch], ["EQ%d" % ch])
+
+            def bar(ch):
+                if d > 0:
+                    op("p", mm(T.K6[:, ch:256:2], T.EQ[:, 128 * ch:128 * ch + 128], T.PEN[:], False, False), ["EQ%d" % ch, "PEN"], ["@K6"])
 
             def number(ch):
                 op("p", mm(T.K6[:, ch:256:2], T.CFL[:, 128 * ch:128 * ch + 128], IB, False, False), ["CFL", "IB"], ["@K6"])
@@ -479,8 +525,9 @@ def rank_program(g, core, T, topo):
                 op("p", [mm(T[bk][:, cl:16 * (c1 - c0):8], IN, z[:, 2 * c0:2 * c1], cl == 0, False) for cl in range(8)], ["IN", zks[1]], ["@" + bk])
             for ch in range(2):
                 v_gather(ch, 0, NV[ch])
-                s_gather(ch, NV[ch], 128)
-            ts(T.CFL[:], T.CI[:], -2048.0, A.add, ["CI00", "CI01", "CI10", "CI11"], ["CFL"])
+            s_gather(0, NV[0], 128)
+            s_gather(1, NV[1], 128)
+            ts(T.CFL[:], T.OFF[:], -2048.0, A.add, ["OFF00", "OFF01", "OFF10", "OFF11"], ["CFL"])
             for i in range(2):
                 p_diff(*sc[i])
             dsum(T.DF, 0, 0, NV[0], 1, ["DF0_0"])
@@ -493,19 +540,26 @@ def rank_program(g, core, T, topo):
             for c in sc[0:3]:
                 s_abs(*c)
             dsum(T.AB, 0, 0, 128, 0, ["AB0_0_None", "AB0_%d_None" % sc[0][1], "AB0_%d_None" % sc[1][1]])
+            barred(0)
+            barred(1)
             for odd in range(2):
-                unbarred(odd)
                 v_half(1, 0, NV[1], ["DF1_0"], odd)
                 s_abs(*sc[3], odd)
             if m == 0:
                 cp(T.DLAND[:, 0:16], T.C7[:, 32:48], ["@C7"], ["DLAND0"])
             if d > 0:
-                op("p", mm(T.K6[:, 0:256:2], T.NE[:, 0:128], T.PEN[:, 1:256:2], False, False), ["NE0", "PEN"], ["@K6"])
+                result(T.RES[:], "RES", d - 1)
+            if end:
+                q_ = T.RSND[:, 32 * t + 16:32 * t + 32]
+                act(q_, T.RES[:], F.Relu, ["RES"], ["RSQ"], bias=1.0)
+                send(frm, "q", T.RLAND[:, 32 * t + 16:32 * t + 32], q_, ["RSQ"])
+            bar(0)
+            bar(1)
             for odd in range(2):
-                dsum(T.AB, 1, 0, 128, 0, ["AB1_0_%d" % odd, "AB1_%d_None" % sc[2][1], "AB1_%d_%d" % (sc[3][1], odd)], range(odd, 16, 2))
-            op("p", mm(T.K6[:, 1:256:2], T.NE[:, 128:256] if d > 0 else T.ZB[:], T.PEN[:, 1:256:2], False, True), ["NE1" if d > 0 else "ZB", "PEN"], ["@K6"])
+                dsum(T.AB, 1, 0, 128, 0, ["AB1_0_%d" % odd, "AB1_%d_None" % sc[2][1], "AB1_%d_%d" % (sc[3][1], odd)], range(odd, 16, 2), odd == 1)
             dead = [(T.DLAND[:, 16 * t:16 * t + 16], "DLAND%d" % t)] + [(T.WB[:, 16 * i:16 * i + 16], "WB%d" % i) for i in range(d)]
-            op("p", [mm(T.C7[:, 0:16], IB, a, i == 0, False) for i, (a, k) in enumerate(dead)], ["IB"] + [k for a, k in dead], ["@C7"])
+            op("p", [mm(T.C7[:, 0:16], IH, T.CQ[:, 640:656], True, False), mm(T.C7[:, 0:16], IH, T.ONES[:, 0:16], False, False)] +
+               [mm(T.C7[:, 0:16], IB, a, False, False) for a, k in dead], ["IB", "IH", "CQ3", "ONES"] + [k for a, k in dead], ["@C7"])
             if d == 0 and t > 0:
                 near_rows(t - 1, 0)
                 near_rows(t - 1, 1)
@@ -513,34 +567,41 @@ def rank_program(g, core, T, topo):
             op("p", [mm(T.LB[:, 256:512], IH, a, i == 0, False) for i, a in enumerate((s_, T.CQ[:, 0:256]))], ["IH", sk, "CQ0"], ["@LB"])
             if m == 0:
                 scalar_constants()
-            if m < 2:
-                c0, c1 = ((0, 1536), (1536, W))[m]
-                act(T.TA[:, c0:c1], T.TB[:, c0:c1], F.Copy, ["TB"], ["TA" + "bc"[m]])
+            if m in (1, 2):
+                c0 = 2048 * (m - 1)
+                act(T.TA[:, c0:c0 + 2048], T.TB[:, c0:c0 + 2048], F.Copy, ["TB"], ["TA" + "bc"[m - 1]])
             if m == 2:
-                starter_rows(1)
-                starter_rows(2)
-            scan(T.R[:], T.RS[:], T.K6[:, 0:256], A.max, A.min, ["RS", "@K6"], ["R"])
+                fill_rows("TA", 0)
+            if m == 3:
+                spare_columns("TA")
+                join("TA", ["TAd", "TAx"])
+            if m in (3, 4):
+                starter_rows(m - 2)
+            for h in range(2):
+                scan(T.R[:, 128 * h:128 * h + 128], T.RS[:, 128 * h:128 * h + 128], T.K6[:, 128 * h:128 * h + 128], A.max, A.min, ["RS", "@K6"], ["R%d" % h])
+            for h in range(2):
+                tt(T.EK[:, 64 * h:64 * h + 64], T.R[:, 128 * h:128 * h + 128].indirect(T.LX6[:, 0:4]), T.M1[:, 0:64], A.mult, ["R%d" % h, "LX6", "M1"], ["EK%d" % h])
             gap(3)
-            cp(T.RI[:], T.R[:, 15:256:16], ["R"], ["RI"])
+            op("p", [mm(T.C7[:, 0:16], T.EK[:], T.RSX[:, 0:16], False, False)] +
+               [mm(T.C7[:, 0:16], a, T.CQ[:, c:c + 16], False, False) for a, c in ((IH, 896), (IH, 256), (T.PAIR[:], 912))] +
+               [mm(T.C7[:, 0:16], T.EK[:], T.RSX[:, 16:32], False, True)], ["EK0", "EK1", "RSX", "IH", "PAIR", "CQ1", "CQ4"], ["@C7"])
+            cp(T.RI[:], T.R[:, 15:256:16], ["R0", "R1"], ["RI"])
             gap(4)
+            if d == 0 and t > 0:
+                near_add(t - 1)
             ts(T.RA[:], T.RI[:], 4095, A.bitwise_and, ["RI"], ["RA"])
             gap(5)
             tt(T.E1[:], T.RA[:, 0:16].indirect(T.LX1[:]), T.M1[:], A.mult, ["RA", "LX1", "M1"], ["E1"])
-            op("p", mm(T.C7[:, 0:16], T.E1[:], T.RS1[:], False, True), ["E1", "RS1"], ["@C7"])
-            if d == 0 and t > 0:
-                near_add(t - 1)
-            else:
-                tt(T.DE[:], T.MSP[:], T.E1[:], A.subtract, ["MSP", "E1"], ["DE"])
             yu, yk = T.YSND[:, 16 * m:16 * m + 16], "YSND%d" % m
-            ts(yu, T.C7[:, 0:16], DEAD, A.min, ["@C7"], [yk])
+            ts(yu, T.C7[:, 0:16], 4096.0, A.mult, ["@C7"], [yk], DEAD, A.min)
             if not tail:
                 send(to, "y%d%d" % (t, d), T.YLAND[:, 16 * m:16 * m + 16], yu, [yk])
             act(T.UP[:], far[:, 0:WX].indirect(yu), F.Copy, [fk, yk], ["UP"])
             tt(T.QR[:], far[:, 0:WX].indirect(yu), T.CR[:], A.mult, [fk, yk, "CR"], ["QR"])
             gap(6)
+            if not tail:
+                tt(T.RS[:, 0:256:16], T.RA[:], T.FBC[:], A.add, ["RA", "FBC"], ["RS"])
             ts(T.QO[:], T.QR[:], OCOL, A.mult, ["QR", "PC"], ["QO"])
-            if d == 0 and t > 0:
-                tt(T.DE[:], T.MSP[:], T.E1[:], A.subtract, ["MSP", "E1"], ["DE"])
 
             def unit(gr, ll, bk, c):
                 p0, k = 32 * (gr // 2), 16 + 16 * (gr % 2)
@@ -554,10 +615,11 @@ def rank_program(g, core, T, topo):
                 for gr, ll in units:
                     unit(gr, ll, "G%d" % q, n)
                     n += 128 + 128 * ll
-                scan(T.FL[:, 512 * q + c0:512 * q + n], T["G%d" % q][:, c0:n], T.TH[:, c0:n], A.max, A.add, ["@G%d" % q, "THS"], ["FL%d" % (i if i < 4 else 9)])
+                f0 = FH * (q // 2) + 512 * (q % 2)
+                scan(T.FL[:, f0 + c0:f0 + n], T["G%d" % q][:, c0:n], T.TH[:, c0:n], A.max, A.add, ["@G%d" % q, "THS"], ["FL%d" % (i if i < 4 else 9)])
 
             def by_scalar(i):
-                bk, c = ("G4", "K6", "G4", "K6", "G0")[i], (2048 + i if i < 4 else 2047)
+                bk, c = ("G4", "K6", "G4", "K6", "G0")[i], (FH * (i // 2) + 1024 + i % 2 if i < 4 else FH + 1023)
                 unit((0, 2, 4, 6, 7)[i], 1, bk, 0)
                 act(T.JK[:, 256 * i:256 * i + 256], T[bk][:, 0:256], F.Relu, ["@" + bk, "THS"], ["JK%d" % i, "FL%d" % (4 + i)],
                     bias=T.TH[:, 511:512], accum_out=T.FL[:, c:c + 1])
@@ -572,7 +634,9 @@ def rank_program(g, core, T, topo):
                         lambda: act(out, T[bk][:, c:c + 256], F.Copy, ["@" + bk], [key], bias=-MAGIC))
 
             own_new = new_records(T.X, "X", yu, yk, s_, sk, "LB", 256, T.NS[:, 0:256], "NS", True)
-            by_vector(3); by_scalar(0); by_vector(0); by_scalar(1); by_vector(1); by_scalar(2); by_vector(2); by_scalar(3); by_vector(4); by_scalar(4)
+            by_vector(3)
+            tt(T.DE[:], T.MSP[:], T.E1[:], A.subtract, ["MSP", "E1"], ["DE"])
+            by_scalar(0); by_vector(0); by_scalar(1); by_vector(1); by_scalar(2); by_vector(2); by_scalar(3); by_vector(4); by_scalar(4)
             op("p", mm(T.C7[:, 16:32], T.E1[:], T.RS1[:], True, False), ["E1", "RS1"], ["@C7"])
             own_new[0]()
             own_new[1]()
@@ -584,28 +648,22 @@ def rank_program(g, core, T, topo):
                 landed(frm, "y%d%d" % (t, d), ["YLAND%d" % m])
                 home_new = new_records(XC, xk, T.YLAND[:, 16 * m:16 * m + 16], "YLAND%d" % m, T.FLAND[:, 256 * t:256 * t + 256], "FLAND%d" % t,
                                        "G1", 0, T.NS[:, 256:512], "NH", False)
-            op("p", mm(T.G2[:, 0:16], T.E1[:], T.RS1[:], True, False), ["E1", "RS1"], ["@G2"])
-            tt(T.E2[:], T.FL[:, 0:2056].indirect(T.LX2[:]), T.DE[:], A.min, ["FL%d" % i for i in range(10)] + ["LX2", "DE"], ["E2"])
-            ends = [lambda: op("p", mm(T.C7[:, 16:32], T.E2[:], T.RS1[:], False, True), ["E2", "RS1"], ["@C7"]),
-                    lambda: op("p", mm(T.G2[:, 0:16], T.E2[:], T.RSN[:], False, True), ["E2", "RSN"], ["@G2"])]
-            for f in (ends[::-1] if end else ends):
-                f()
+            for h, done in enumerate(((0, 1, 4, 5), (2, 3, 6, 7, 8, 9))):
+                tt(T.E2[:, 64 * h:64 * h + 64], T.FL[:, FH * h:FH * h + FH].indirect(T.LX2[:, 0:4]), T.DE[:, 64 * h:64 * h + 64], A.min,
+                   ["FL%d" % i for i in done] + ["LX2", "DE"], ["E2", "E2b"][h:h + 1])
+            lists_ = [lambda: op("p", mm(T.C7[:, 16:32], T.E2[:], T.RS1[:], False, True), ["E2", "E2b", "RS1"], ["@C7"]),
+                      lambda: op("p", mm(T.LB[:, 128:144], T.E1[:], T.RS1[:], True, False), ["E1", "RS1"], ["@LB"]),
+                      lambda: op("p", mm(T.LB[:, 128:144], T.E2[:], T.RSN[:], False, True), ["E2", "E2b", "RSN"], ["@LB"])]
+            for i in ((1, 2, 0) if end else (0, 1, 2)):
+                lists_[i]()
             if not tail:
                 home_new[0]()
                 home_new[1]()
                 cp(T.R4[:], T.RA[:, 0:16].indirect(T.LX3[:]), ["RA", "LX3"], ["R4"])
             gap(1)
-
-            def result(out, key):
-                if d == 0:
-                    cp(out, T.G2[:, 0:16], ["@G2"], [key])
-                else:
-                    tt(out, T.G2[:, 0:16], T.RES[:], A.max, ["@G2", "RES"], [key])
-
             if end:
-                r_ = T.RSND[:, 32 * t:32 * t + 16]
-                result(r_, "RSH")
-                send(frm, "r%d" % t, T.RLAND[:, 32 * t:32 * t + 16], r_, ["RSH"])
+                last_pairs(0)()
+
             ls = T.LSND[:, 16 * m:16 * m + 16]
             lk = "LSND%d" % m
             cp(ls, T.C7[:, 16:32], ["@C7"], [lk])
@@ -620,6 +678,9 @@ def rank_program(g, core, T, topo):
                 tt(far[:, 0:WX].indirect(ls), T.UP[:], T.RC[:, 256 * t:256 * t + 256], A.add, ["UP", "RC%d" % t, lk], [fk])
 
             if end:
+                r_ = T.RSND[:, 32 * t:32 * t + 16]
+                act(r_, T.LB[:, 128:144], F.Relu, ["@LB"], ["RSH"], bias=1.0)
+                send(frm, "r%d" % t, T.RLAND[:, 32 * t:32 * t + 16], r_, ["RSH"])
                 own_records()
                 dma("y", [(T.yx[:], T.X[:, 0:W])], ["X"], ["yx"])
                 cp(T.FO[:, 0:WX].indirect(ls), T.DIAG[:], [lk, "DIAG"], ["FO"])
@@ -627,42 +688,37 @@ def rank_program(g, core, T, topo):
                 break
             ts(wb, T.C7[:, 16:32], DEAD, A.is_lt, ["@C7"], ["WB%d" % d], DEAD, A.mult)
             op("p", mm(T.G0[:, 0:16], T.ONES[:], wb, True, True), ["ONES", "WB%d" % d], ["@G0"])
-            act(T.KJ[:], T.G0[:, 0:16], F.Copy, ["@G0"], ["KJ", "KP"], scale=1.0 / DEAD, accum_out=T.KP[:, 0:1])
+            act(T.KJ[:], T.G0[:, 0:16], F.Copy, ["@G0"], ["KJ", "KP"], scale=1.0 / (32 * DEAD), accum_out=T.KP[:, 0:1])
+            kp = T.G0[:, 16:17]
+            op("p", [mm(kp, IH, T.ONES[:, 0:1], True, False), mm(kp, T.IDN[:], T.KP[:, 0:1], False, False)] +
+               [mm(kp, IH, T.CQ[:, c:c + 1], False, False) for c in (896, 256, 512)] + [mm(kp, T.IDF[:], T.KP[:, 0:1], False, True)],
+               ["IH", "ONES", "IDF", "IDN", "KP", "CQ1", "CQ2", "CQ4"], ["@G0"])
             dn = (d + 1) % ND
-            kappa = [lambda: cp(T.KI[:, 0:1], T.KP[:, 0:1], ["KP"], ["KI0"]),
-                     lambda: ts(T.KI[:, 1:2], T.KI[:, 0:1], 31, A.bitwise_and, ["KI0"], ["KI1"])]
-            kappa += [lambda ch=ch: ts(T.ACOL[:, ch:ch + 1], T.KI[:, 1:2], 32.0, A.mult, ["KI1", "ABASE%d" % dn], ["ACOL%d" % ch],
-                                       T.ABASE[:, 2 * dn + ch:2 * dn + ch + 1], A.add) for ch in range(2)]
+
+            def kappa():
+                for ch in range(2):
+                    act(T.ACOL[:, ch:ch + 1], kp, F.Identity, ["@G0", "ABASE%d" % dn], ["ACOL%d" % ch], scale=1024.0, bias=T.ABASE[:, 2 * dn + ch:2 * dn + ch + 1])
+
             if tail:
                 own_records()
-                result(T.RES[:], "RES")
+                result(T.RES[:], "RES", d)
                 starters_send(t + 1)
+                kappa()
                 far_table()
                 dead_list(t + 1)
-                kappa[0]()
                 near_send(t)
-                kappa[1]()
                 dead_send(t + 1)
                 starters_on(t + 1)
                 records_send(t + 1)
-                kappa[2]()
-                kappa[3]()
                 gap(2)
                 continue
             far_table()
             gap(2)
             act(T.PG[:], far[:, 0:WX].indirect(yu), F.Copy, [fk, yk], ["PG"])
-            result(T.RES[:], "RES")
+            kappa()
             to_list(lambda b: T.PG[:, b:256:16], ["PG"])
             op("p", mm(T.LB[:, 0:128], T.R4[:], T.IDF[:], True, True), ["R4", "IDF"], ["@LB"])
-            kappa[0]()
             gap(7)
-            for k in kappa[1:]:
-                k()
-            if m == 1:
-                spare_columns("TA")
-                fill_rows("TA", 0)
-                join("TA", ["TAd", "TAx"])
             if m >= ND * NB - 3:
                 tab, i = (("TA", 0), ("TB", 1))[m - (ND * NB - 3)]
                 dma("y", [(T.HL[:, 512 * i:512 * i + 256], T[tab][15:128:16, 0:W]), (T.HL[:, 512 * i + 256:512 * i + 512], T[tab][14:128:16, 0:W])],
@@ -674,11 +730,10 @@ def rank_program(g, core, T, topo):
                 act(T.Z[:, 128 * h:128 * h + 128], XC[:, 0:WX].indirect(T.PU[:, 8 * h:8 * h + 8]), F.Copy, [xk, "PU"], ["Z%d" % h])
             own_records()
     t = NB - 1
-    landed(nxt if t % 2 == 0 else prv, "r%d" % t, ["RLAND%d" % t])
-    for o, e in enumerate(("E1", "E2")):
-        tt(T[e][:], T.RLAND[:, 32 * t:32 * t + 16].indirect(T.LX5[:, 8 * o:8 * o + 8]), T.CB1[:], A.mult, ["RLAND%d" % t, "LX5_%d" % o, "CB1"], [e])
-        op("p", mm(T.G4[:, 8 * o:8 * o + 8], T[e][:], T.D16[:, 0:8], True, True), [e, "D16"], ["@G4"])
-    tt(T.PF[:, t:256:16], T.G4[:, 0:16], T.PF[:, t:256:16], A.max, ["@G4", "PF0"], ["PF0"])
+    last_pairs(1)()
+    tt(T.PF[:, t:256:16], T.G4[:, 0:16], T.PF[:, t:256:16], A.add, ["@G4", "PF0"], ["PF0"])
     dma("y", [(T.ya[:], T.PF[:, 0:256])], ["PF0"], ["ya"])
-    for sem in sorted(last):
-        need("g", {sem: last[sem]})
+    outs = [s for k in ("yx", "yb", "ya") for s in wr[k]]
+    for sem in [s for s in sorted(last) if s not in outs] + outs:
+        if max(waited[q].get(sem, 0) for q in Q) < last[sem]:
+            need("g", {sem: last[sem]})

@@ -3,12 +3,15 @@ from concourse.mybir import AluOpType, ActivationFunctionType
 W = 4096
 DEAD = 4096.0
 DUM = 4112
-WX = DUM + 256
+WX = DUM + 1024
 NB, ND = 3, 3
-SC = 8192.0
+SC = 16384.0
+SAME = 12 * SC
+OFFR = 448.0
 FH = 1032
 MAGIC = 1.5 * 2 ** 23
-NV = (70, 64)
+NVS = ((74, 68), (72, 66))
+ZSPLIT = ((2, 2), (3, 2))
 
 _B = {}
 
@@ -20,45 +23,47 @@ def _sb(name, cols, dtype):
 for _n in ("X", "XC0", "XC1", "TA", "TB"):
     _sb(_n, WX, "bfloat16")
 _sb("PAI", 256, "int32"); _sb("PBI", 256, "int32"); _sb("CT1", 256, "int32")
-_sb("HL", 1024, "bfloat16"); _sb("CB", 256, "float32"); _sb("PF", 512, "float32")
+_sb("HL", 1024, "bfloat16"); _sb("I16", 128, "bfloat16"); _sb("PF", 512, "float32")
 _sb("WI", 8, "int32"); _sb("WF", 8, "float32")
-_sb("PI", 8, "int32"); _sb("PT", 8, "int32"); _sb("PC", 32, "float32"); _sb("SG", 16, "float32")
-_sb("CF", 264, "float32"); _sb("LANE", 256, "float32"); _sb("C8", 128, "float32"); _sb("CB1", 128, "float32"); _sb("SPI", 128, "float32")
+_sb("PI", 8, "int32"); _sb("PT", 8, "int32"); _sb("PC", 40, "float32"); _sb("SG", 16, "float32"); _sb("SGB", 8, "bfloat16"); _sb("WC", 8, "bfloat16")
+_sb("CF", 264, "float32"); _sb("LANE", 256, "float32"); _sb("C8", 128, "float32"); _sb("CB1", 128, "float32")
+_sb("SPK", 16, "float32"); _sb("RB", 16, "float32"); _sb("BW", 256, "bfloat16")
 _sb("CG", 128, "float32"); _sb("WP", 256, "float16"); _sb("WN", 256, "float16")
-_sb("OB", 16, "bfloat16"); _sb("IDF", 128, "float32"); _sb("IDN", 128, "float32"); _sb("PEN", 128, "bfloat16"); _sb("EK", 128, "float32"); _sb("PAIR", 128, "bfloat16"); _sb("RSX", 32, "float32"); _sb("FBC", 16, "float32"); _sb("LX6", 8, "uint16"); _sb("ZB", 128, "bfloat16")
+_sb("OB", 16, "bfloat16"); _sb("KN", 256, "float32"); _sb("PEN", 128, "bfloat16"); _sb("EK", 128, "float32")
+_sb("FBC", 16, "float32"); _sb("ZB", 128, "bfloat16"); _sb("PAIR", 128, "bfloat16"); _sb("RSX", 32, "float32"); _sb("LX6", 8, "uint16")
 _sb("IBN", 384, "bfloat16")
 _sb("CQ", 928, "bfloat16")
-_sb("M1", 128, "float32"); _sb("MSP", 128, "float32"); _sb("RS1", 16, "float32"); _sb("RSN", 16, "float32"); _sb("RS", 256, "float32")
-_sb("CR", 256, "bfloat16"); _sb("RC", 256 * NB, "bfloat16"); _sb("TH", 512, "float32"); _sb("SW", 144, "bfloat16")
+_sb("M1", 128, "float32"); _sb("RS1", 16, "float32"); _sb("RS4", 16, "bfloat16"); _sb("RSN", 16, "bfloat16"); _sb("RS", 256, "float32")
+_sb("CR", 256, "bfloat16"); _sb("RC", 256 * NB, "bfloat16"); _sb("TH", 520, "float32"); _sb("SW", 144, "bfloat16")
 _sb("ONES", 128, "bfloat16"); _sb("DIAG", 256, "float32"); _sb("SRB", 256, "bfloat16"); _sb("D16", 16, "float32")
-_sb("LX0", 16, "uint16"); _sb("LX1", 8, "uint16"); _sb("LX2", 8, "uint16"); _sb("LX3", 8, "uint16"); _sb("LX4", 32, "uint16"); _sb("LX5", 16, "uint16")
-_sb("LT", 64, "float32"); _sb("LXI", 16, "int32"); _sb("LXJ", 16, "int32")
+_sb("LX0", 16, "uint16"); _sb("LX1", 8, "uint16"); _sb("LX2", 8, "uint16"); _sb("LN", 16, "uint16"); _sb("LX5", 16, "uint16")
+_sb("LT", 64, "float32"); _sb("PW", 48, "float32")
 _sb("SCOL", 4, "float32"); _sb("ABASE", 8, "float32"); _sb("ACOL", 4, "float32")
 _sb("SSND", 256 * NB, "bfloat16"); _sb("SLAND", 256 * NB, "bfloat16")
-_sb("DSND", 16 * NB, "bfloat16"); _sb("DLAND", 16 * (NB + 1), "bfloat16")
+_sb("DSND", 16 * NB, "bfloat16"); _sb("DLAND", 16 * NB, "bfloat16")
 _sb("FLAND", 256 * NB, "bfloat16"); _sb("YSND", 16 * NB * ND, "uint16"); _sb("YLAND", 16 * NB * ND, "uint16")
 _sb("LSND", 16 * NB * ND, "uint16"); _sb("LLAND", 16 * NB * ND, "uint16")
-_sb("RSND", 32 * NB, "float32"); _sb("RLAND", 32 * NB, "float32")
+_sb("RSND", 32, "float32"); _sb("RLAND", 32, "float32"); _sb("NSND", 256 * (NB - 1), "bfloat16"); _sb("NLAND", 256 * (NB - 1), "bfloat16")
 _sb("Z", 256, "bfloat16"); _sb("Z8", 2048, "bfloat16")
 _sb("SQ", 256, "float32"); _sb("FI", 256, "int32"); _sb("CI", 256, "int32")
 _sb("OFF", 256, "uint16"); _sb("CFL", 256, "float16"); _sb("EQ", 256, "bfloat16")
 _sb("DF", 4096, "bfloat16"); _sb("AB", 4096, "bfloat16")
-_sb("R", 256, "float32"); _sb("RI", 16, "int32"); _sb("RA", 16, "int32"); _sb("E1", 128, "float32"); _sb("DE", 128, "float32")
-_sb("R4", 128, "float32"); _sb("E2", 128, "float32"); _sb("NS", 512, "bfloat16"); _sb("FO", WX, "float32")
-_sb("UP", 256, "bfloat16"); _sb("QR", 256, "bfloat16"); _sb("QO", 256, "bfloat16"); _sb("GX", 512, "bfloat16")
-_sb("FL", 2 * FH, "float32"); _sb("JK", 1280, "bfloat16"); _sb("PG", 256, "bfloat16"); _sb("PU", 16, "uint16"); _sb("E3", 512, "bfloat16")
-_sb("WB", 16 * ND, "bfloat16"); _sb("RES", 16, "float32"); _sb("W1", 16, "float32"); _sb("W2", 16, "float32"); _sb("W3", 16, "float32")
-_sb("KP", 8, "float32"); _sb("KJ", 16, "float32")
+_sb("R", 256, "float32"); _sb("RI", 16, "int32"); _sb("RA", 16, "int32"); _sb("RQ", 16, "int32"); _sb("E1", 128, "float32"); _sb("DE", 128, "float32")
+_sb("R4", 128, "float32"); _sb("E2", 128, "float16"); _sb("NS", 512, "bfloat16"); _sb("FO", WX, "float32")
+_sb("UP", 256, "bfloat16"); _sb("QR", 256, "bfloat16"); _sb("GX", 512, "bfloat16")
+_sb("FL", 2 * FH, "float32"); _sb("JK", 1280, "bfloat16"); _sb("PG", 256, "bfloat16"); _sb("PU", 16, "uint16"); _sb("E3", 256, "bfloat16")
+_sb("WB", 16 * ND, "bfloat16"); _sb("RES", 16, "float32")
+_sb("KP", 8, "float32")
 for _n in ["G0", "G1", "G2", "G3", "G4", "K6", "C7", "LB"]:
     _B[_n] = ("psum", [128, 512], "float32")
 SCRATCH = _B
 
-_MSG = ["q"]
+_MSG = ["q", "s0"]
 for _t in range(NB):
-    _MSG += ["s%d" % _t, "f%d" % _t, "b%d" % _t, "e%d" % _t, "r%d" % _t]
-    for _d in range(ND - 1):
+    _MSG += ["f%d" % _t, "b%d" % _t, "e%d" % _t, "r%d" % _t]
+    for _d in range(ND - 1 if _t == NB - 1 else ND):
         _MSG += ["y%d%d" % (_t, _d), "l%d%d" % (_t, _d)]
-SEMAPHORES = ["cv", "cs", "cp", "cg"] + ["rx" + m for m in _MSG] + ["tx" + m for m in _MSG] + ["dm%d" % i for i in range(16)]
+SEMAPHORES = ["cv", "cs", "cp", "cg"] + ["rx" + m for m in _MSG] + ["tx" + m for m in _MSG] + ["dm%d" % i for i in range(20)]
 
 
 def rank_program(g, core, T, topo):
@@ -124,10 +129,7 @@ def rank_program(g, core, T, topo):
         note(reads, writes, sem, 16 * len(pieces))
 
     def engines(frm, to, msg):
-        es = topo.engines(T.cores[frm], T.cores[to])
-        if msg == "s1":
-            es = [e for e in es if e in topo.engines(T.cores[frm], T.cores[(frm + 1) % n_ranks])]
-        return es
+        return topo.engines(T.cores[frm], T.cores[to])
 
     def send(to, msg, out, in_, reads):
         need("g", deps(reads, []))
@@ -177,15 +179,10 @@ def rank_program(g, core, T, topo):
     def to_list(cols, keys):
         op("p", [mm(T.C7[:, 32:48], T.SW[:, 16 - b:144 - b], cols(b), b == 0, b == 15) for b in range(16)], ["SW"] + keys, ["@C7"])
 
-    def starters_send(t):
-        s = T.SSND[:, 256 * t:256 * t + 256]
-        cp(s[:, 0:256:2], T.X[:, t:W // 2:16], ["X"], ["SS0_%d" % t])
-        if t == 0:
-            cp(s[:, 1:256:2], T.X[:, W // 2 + t:W:16], ["X"], ["SS1_%d" % t])
-        else:
-            act(s[:, 1:256:2], T.X[:, W // 2 + t:W:16], F.Copy, ["X"], ["SS1_%d" % t])
-        send(nxt if t % 2 == 0 else prv, "s%d" % t, T.SLAND[:, 256 * t:256 * t + 256], s, ["SS0_%d" % t, "SS1_%d" % t])
-        landed(prv if t % 2 == 0 else nxt, "s%d" % t, ["SLAND%d" % t])
+    def starters(name, win, t):
+        for ll in range(2):
+            cp(T[name][:, 256 * t + ll:256 * t + 256:2], T[win][:, W // 2 * ll + t:W // 2 * (ll + 1):16], [win], ["%s%d_%d" % (name, t, ll)])
+        join("%s%d" % (name, t), ["%s%d_%d" % (name, t, ll) for ll in range(2)])
 
     def starters_on(t):
         send(nxt if t % 2 == 0 else prv, "f%d" % t, T.FLAND[:, 256 * t:256 * t + 256], T.SLAND[:, 256 * t:256 * t + 256], ["SLAND%d" % t])
@@ -205,43 +202,37 @@ def rank_program(g, core, T, topo):
         xc = T.XC0 if t % 2 == 0 else T.XC1
         send(nxt if t % 2 == 0 else prv, "b%d" % t, xc[:, 0:W], T.X[:, 0:W], ["X"])
 
-    def result(out, key, d):
+    def result(t, d):
+        src, bk, o = (T.G2[:, 0:16], "@G2", A.max) if t == NB - 1 else (T.C7[:, 16:32], "@C7", A.min)
         if d == 0:
-            cp(out, T.LB[:, 128:144], ["@LB"], [key])
+            cp(T.RES[:], src, [bk], ["RES"])
         else:
-            tt(out, T.LB[:, 128:144], T.RES[:], A.max, ["@LB", "RES"], [key])
+            tt(T.RES[:], src, T.RES[:], o, [bk, "RES"], ["RES"])
 
     def near_send(t):
-        hi, lo = T.RSND[:, 32 * t:32 * t + 16], T.RSND[:, 32 * t + 16:32 * t + 32]
-        ts(T.LXJ[:], T.RES[:], 0.0, A.max, ["RES"], ["LXJ"])
-        ts(T.W3[:], T.RES[:], 1.0, A.add, ["RES"], ["W3"], 0.0, A.max)
-        ts(T.LXI[:], T.LXJ[:], 4, A.arith_shift_right, ["LXJ"], ["LXI"])
-        cp(hi, T.LXI[:], ["LXI"], ["RSH%d" % t])
-        ts(T.W2[:], T.LXI[:], -16.0, A.mult, ["LXI"], ["W2"])
-        tt(lo, T.W3[:], T.W2[:], A.add, ["W3", "W2"], ["RSL%d" % t])
-        send(prv if t % 2 == 0 else nxt, "r%d" % t, T.RLAND[:, 32 * t:32 * t + 32], T.RSND[:, 32 * t:32 * t + 32], ["RSH%d" % t, "RSL%d" % t])
+        tab, tk = (T.TA, "TA") if t % 2 == 0 else (T.TB, "TB")
+        bits = T.NSND[:, 256 * t:256 * t + 256]
+        ts(T.LN[:], T.RES[:], DEAD, A.min, ["RES"], ["LN"])
+        act(bits, tab[:, 0:DUM].indirect(T.LN[:]), F.Copy, [tk, "LN"], ["NSND%d" % t])
+        send(prv if t % 2 == 0 else nxt, "r%d" % t, T.NLAND[:, 256 * t:256 * t + 256], bits, ["NSND%d" % t])
 
-    def near_rows(t, i):
-        if i == 0:
-            landed(nxt if t % 2 == 0 else prv, "r%d" % t, ["RLAND%d" % t])
-        tt(T.E3[:, 256 * i:256 * i + 256], T.RLAND[:, 32 * t:32 * t + 32].indirect(T.LX4[:, 16 * i:16 * i + 16]), T.DIAG[:], A.mult,
-           ["RLAND%d" % t, "LX4", "DIAG"], ["E3_%d" % i])
-        if i == 1:
-            op("p", [mm(T.LB[:, 0:256], T.SRB[:, 128 * h:128 * h + 128], T.E3[:, 256 * h:256 * h + 256], h == 0, h == 1) for h in range(2)],
-               ["SRB0", "SRB1", "E3_0", "E3_1"], ["@LB"])
-
-    def last_pairs(i):
-        t = NB - 1
-        msg, c, tiles = (("q", 32 * t + 16, (["R4"], ["EK", "EK0", "EK1"])), ("r%d" % t, 32 * t, (["E1"], ["E2", "E2b"])))[i]
-        landed(nxt if t % 2 == 0 else prv, msg, ["L" + msg])
-        for o, e in enumerate(tiles):
-            tt(T[e[0]][:], T.RLAND[:, c:c + 16].indirect(T.LX5[:, 8 * o:8 * o + 8]), T.CB1[:], A.mult, ["L" + msg, "LX5_%d" % o, "CB1"], e)
-        return lambda: [op("p", mm(T.G4[:, 8 * o:8 * o + 8], T[e[0]][:], T.D16[:, 0:8], i + o == 0, i + o == 2), [e[0], "D16"], ["@G4"])
-                        for o, e in enumerate(tiles)]
+    def near_rows(t):
+        landed(nxt if t % 2 == 0 else prv, "r%d" % t, ["NLAND%d" % t])
+        op("p", [mm(T.LB[:, 128 * ll:128 * ll + 128], T.SRB[:, 128 * h:128 * h + 128], T.NLAND[:, 256 * t + ll:256 * t + 256:2], ll + h == 0, ll + h == 2)
+                 for ll in range(2) for h in range(2)], ["SRB0", "SRB1", "NLAND%d" % t], ["@LB"])
 
     def near_add(t):
         near, nk = (T.TA, "TA") if t % 2 == 0 else (T.TB, "TB")
         tt(near[:, t:W:16], T.LB[:, 0:256], near[:, t:W:16], A.add, ["@LB", nk], [nk])
+
+    def last_pairs(i):
+        t = NB - 1
+        msg, c, tiles = (("q", 16, ("R4", "CG")), ("r%d" % t, 0, ("E1", "DE")))[i]
+        landed(nxt if t % 2 == 0 else prv, msg, ["L" + msg])
+        spread = [lambda o=o, e=e: tt(T[e][:], T.RLAND[:, c:c + 16].indirect(T.LX5[:, 8 * o:8 * o + 8]), T.CB1[:], A.mult, ["L" + msg, "LX5_%d" % o, "CB1"], [e])
+                  for o, e in enumerate(tiles)]
+        return spread + [lambda: [op("p", mm(T.G4[:, 8 * o:8 * o + 8], T[e][:], T.D16[:, 0:8], i + o == 0, i + o == 2), [e, "D16"], ["@G4"])
+                                  for o, e in enumerate(tiles)]]
 
     dma("y", [(T.PAI[:], T.pa[:])], [], ["PAI"])
     dma("s", [(T.WI[:, 0:1], T.wt[:])], [], ["WI"])
@@ -252,22 +243,39 @@ def rank_program(g, core, T, topo):
     iota("C8", [[1, 16], [0, 8]], 0, 0)
     iota("CB1", [[0, 8], [1, 8], [0, 2]], 0, 0)
     iota("LANE", [[1, 128], [128, 2]], 0, 0)
-    ms(T.TB[:, 0:1], 1.0, ["TBb"])
-    ms(T.X[:, W:WX], 0.0, ["Xx"])
+    ms(T.X[:, W:DUM], 0.0, ["Xx"])
     join("X", ["Xd", "Xx"])
-    for c, (sh, mask) in enumerate(((4, 7), (0, 15), (0, 7), (3, 15), (0, 1), (3, 1), (4, 1), (0, 127))):
+    for c, (sh, mask) in enumerate(((4, 7), (0, 15), (0, 7), (3, 15), (0, 1), (4, 1), (0, 127))):
         ts(T.PT[:, c:c + 1], T.PI[:, 0:1], sh, A.arith_shift_right, ["PI"], ["PT%d" % c], mask, A.bitwise_and)
     ms(T.ZB[:], 0.0, ["ZB"])
-    cp(T.PC[:, 0:8], T.PT[:, 0:8], ["PT%d" % c for c in range(8)], ["PC"])
-    PGRP, PLOW, PL7, P8, P1, PLL, OCOL, PP = [T.PC[:, c:c + 1] for c in range(8)]
+    ms(T.CQ[:, 0:256], -0.5, ["CQ0"])
+    cp(T.PC[:, 0:7], T.PT[:, 0:7], ["PT%d" % c for c in range(7)], ["PC"])
+    ms(T.CQ[:, 512:640], -2 * MAGIC, ["CQ2"])
+    ms(T.CQ[:, 640:896], 4096.0, ["CQ3"])
+    ms(T.CQ[:, 896:912], -2.0 ** -12, ["CQ896"])
+    PGRP, PLOW, PL7, P8, P1, OCOL, PP = [T.PC[:, c:c + 1] for c in range(7)]
     ts(T.LT[:, 0:12], T.CF[:, 0:12], PLOW, A.not_equal, ["CF", "PC"], ["LT"], 2.0, A.mult)
     ts(T.PC[:, 8:12], T.CF[:, 12:16], PLOW, A.is_equal, ["CF", "PC"], ["PCI"])
-    I12, I14, I15 = T.PC[:, 8:9], T.PC[:, 10:11], T.PC[:, 11:12]
+    I12, I13, I14, I15 = [T.PC[:, c:c + 1] for c in range(8, 12)]
+    ts(T.PC[:, 17:18], PLOW, 12.0, A.is_lt, ["PC"], ["PC17"], SC, A.mult)
+    ms(T.ONES[:], 1.0, ["ONES"])
+    ts(T.PC[:, 29:30], I12, 128.0, A.mult, ["PCI"], ["PC29"])
     ts(T.SG[:, 0:12], T.LT[:, 0:12], -1.0, A.add, ["LT"], ["SG"])
-    for r in range(11):
+    ms(T.CQ[:, 256:512], 2 * MAGIC, ["CQ1"])
+    ts(T.TB[:, 0:1], I13, T.PC[:, 29:30], A.add, ["PCI", "PC17", "PC29"], ["TBb"], T.PC[:, 17:18], A.add)
+    for r in range(9):
         n = 1 << r
         act(T.TB[:, n:2 * n], T.TB[:, 0:n], F.Copy, ["TBb", "SG"], ["TBb"], scale=T.SG[:, r:r + 1])
-    act(T.TB[:, 2048:3072], T.TB[:, 0:1024], F.Copy, ["TBb", "SG"], ["TBc"], scale=T.SG[:, 11:12])
+    for r in range(3):
+        act(T.TB[:, 512 << r:(512 << r) + 512], T.TB[:, 0:512], F.Copy, ["TBb", "SG"], ["TB_%d" % (1 << r)], scale=T.SG[:, 9 + r:10 + r])
+
+    def bits_block(b, src, r0, r1):
+        ts(T.TB[:, 512 * b:512 * b + 512], T.TB[:, 512 * src:512 * src + 512], T.SGB[:, r0:r0 + 1], A.mult, ["TB_1" if src else "TBb", "SGB"], ["TB_%d" % b],
+           T.SGB[:, r1:r1 + 1], A.mult)
+
+    ts(T.DSND[:, 0:16], T.PAI[:, 0:256:16], 0.0, A.is_ge, ["PAI"], ["DSND0"], DEAD, A.mult)
+    send(nxt, "e0", T.DLAND[:, 0:16], T.DSND[:, 0:16], ["DSND0"])
+    landed(prv, "e0", ["DRAW"])
     ts(T.PC[:, 12:13], PGRP, 2.0, A.mult, ["PC"], ["PC12"])
     ts(T.PC[:, 13:14], PGRP, 2.0, A.mult, ["PC"], ["PC13"], 1.0, A.add)
     for ch in range(2):
@@ -277,19 +285,16 @@ def rank_program(g, core, T, topo):
     ts(IN, T.CF[:, 0:128], PP, A.is_equal, ["CF", "PC"], ["IN"], -1.0, A.mult)
     ts(T.ACOL[:, 0:2], T.SCOL[:, 2:4], -1.0, A.mult, ["SCOL2"], ["ACOL0", "ACOL1"], 262144.0 - 12.0, A.add)
     ts(T.WF[:, 3:4], T.WI[:, 0:1], 2048.0, A.is_gt, ["WI"], ["WF3"], -4096.0, A.mult)
-    ms(T.ONES[:], 1.0, ["ONES"])
-    ts(T.DSND[:, 0:16], T.PAI[:, 0:256:16], 0.0, A.is_ge, ["PAI"], ["DSND0"], DEAD, A.mult)
     iota("CG", [[2, 8], [0, 8], [1, 2]], 0, 0)
-    send(nxt, "e0", T.DLAND[:, 16 * NB:16 * NB + 16], T.DSND[:, 0:16], ["DSND0"])
-    landed(prv, "e0", ["DRAW"])
+    iota("PAIR", [[1, 64], [0, 2]], 0, 0)
+    iota("FBC", [[0, 2], [4096, 8]], 4081 * 4096, 0)
+    for key, ap, pattern, base in (("LT0", T.LT[:, 16:24], [[512, 4], [128, 2]], 127), ("LT1", T.LT[:, 24:32:2], [[-511, 4]], 897), ("LT2", T.LT[:, 25:32:2], [[0, 4]], 256)):
+        op("g", lambda: g.iota(ap, pattern, base, 0, allow_small_or_imprecise_dtypes=True), [], [key])
     ts(T.WF[:, 0:1], T.WI[:, 0:1], T.WF[:, 3:4], A.add, ["WI", "WF3"], ["WF0"], 1.0 / 4096, A.mult)
     ts(T.WF[:, 1:2], T.WI[:, 0:1], T.WF[:, 3:4], A.add, ["WI", "WF3"], ["WF1"], -1.0 / 4096, A.mult)
     for ll in range(2):
         for wm, c in (("WP", 0), ("WN", 1)):
             ts(T[wm][:, 128 * ll:128 * ll + 128], T.C8[:], T.PC[:, 12 + ll:13 + ll], A.is_equal, ["C8", "PC12", "PC13", "WF%d" % c], ["%s%d" % (wm, ll)], T.WF[:, c:c + 1], A.mult)
-    ms(T.CQ[:, 256:512], 2 * MAGIC, ["CQ1"])
-    ms(T.CQ[:, 512:640], -2 * MAGIC, ["CQ2"])
-    ms(T.CQ[:, 640:896], 4096.0, ["CQ3"])
     ts(IB, T.CF[:, 0:128], PP, A.is_equal, ["CF", "PC"], ["IB"])
     for i in range(2):
         ts(T.OB[:, 8 * i:8 * i + 8], T.CF[:, 0:8], PGRP, A.is_equal, ["CF", "PC"], ["OB%d" % i], 4096.0 * (1 - 2 * i), A.mult)
@@ -298,128 +303,140 @@ def rank_program(g, core, T, topo):
         hi, lo = T.HL[:, 512 * i:512 * i + 256], T.HL[:, 512 * i + 256:512 * i + 512]
         return [lambda: ts(T.CT1[:], pin[:], 4, A.arith_shift_right, [pk], ["CT1"]),
                 lambda: ts(hi, T.CT1[:], 0.0, A.max, ["CT1"], ["HI%d" % i]),
-                lambda: ts(T.CB[:], hi, -16.0, A.mult, ["HI%d" % i], ["CB", "CBb"], 1.0, A.add),
-                lambda: tt(lo, T.CB[:], pin[:], A.add, ["CB", "CBb", pk], ["LO%d" % i])]
+                lambda: ts(T.PF[:, 0:256], hi, -16.0, A.mult, ["HI%d" % i], ["PF0"], 1.0, A.add),
+                lambda: tt(lo, T.PF[:, 0:256], pin[:], A.add, ["PF0", pk], ["LO%d" % i])]
 
     def fill_rows(tab, i):
         dma("y", [(T[tab][15:128:16, 0:W], T.HL[:, 512 * i:512 * i + 256]), (T[tab][14:128:16, 0:W], T.HL[:, 512 * i + 256:512 * i + 512])],
             ["HI%d" % i, "LO%d" % i], [tab + "b", tab + "c", tab + "d"])
 
     def spare_columns(tab):
-        act(T[tab][:, W:WX], T.XC1[:, W:WX], F.Identity, ["XC1x", "PC16"], [tab + "x"], bias=T.PC[:, 16:17])
+        act(T[tab][:, W:DUM], T.XC1[:, W:DUM], F.Identity, ["XC1x", "PC16"], [tab + "x"], bias=T.PC[:, 16:17])
 
     def starter_rows(t):
-        act(T.RC[:, 256 * t:256 * t + 256], T.LANE[:], F.Identity, ["LANE", "PCI", "PC20"], ["RC%d" % t], scale=I15, bias=T.PC[:, 20 + t:21 + t])
+        act(T.RC[:, 256 * t:256 * t + 256], T.LANE[:], F.Identity, ["LANE", "PC27", "PC20"], ["RC%d" % t], scale=T.PC[:, 27:28], bias=T.PC[:, 20 + t:21 + t])
 
+    first = [lambda: ts(T.PC[:, 14:15], PGRP, 16.0, A.mult, ["PC"], ["PC14"], 16.0, A.add),
+             lambda: ts(T.PC[:, 15:16], I15, 16.0, A.mult, ["PCI"], ["PC15"], I14, A.add),
+             lambda: ts(T.SW[:], T.CF[:, 0:144], T.PC[:, 14:15], A.is_equal, ["CF", "PC14", "PC15"], ["SW"], T.PC[:, 15:16], A.mult)] + [
+             lambda d=d: ts(T.ABASE[:, 2 * d:2 * d + 2], T.SCOL[:, 2:4], -1.0, A.mult, ["SCOL2"], ["ABASE%d" % d], 262144.0 - 12.0 + 32.0 * 97 * d, A.add)
+             for d in range(ND)]
     rows_b = table_rows(T.PBI, "PBI", 1)
+    ts(T.LT[:, 48:56], T.CF[:, 0:16:2], P1, A.add, ["CF", "PC"], ["LT6"], 16.0, A.mult)
     ts(T.WF[:, 2:3], PLOW, P1, A.subtract, ["PC"], ["WF2"], 0.5, A.mult)
     ts(T.RS1[:], T.CF[:, 0:16], P8, A.is_equal, ["CF", "PC"], ["RS1"])
     ts(T.LX1[:], T.CF[:, 0:16:2], P1, A.add, ["CF", "PC"], ["LX1"])
-    ts(T.LT[:, 48:56], T.CF[:, 0:16:2], P1, A.add, ["CF", "PC"], ["LT6"], 16.0, A.mult)
-    ts(T.M1[:], T.CB1[:], PL7, A.is_equal, ["CB1", "PC"], ["M1"])
-    ts(T.PC[:, 17:18], PLOW, 12.0, A.is_lt, ["PC"], ["PC17"], 128.0 * SC, A.mult)
-    ts(T.PC[:, 18:19], I12, -SC, A.mult, ["PCI"], ["PC18"])
+    ts(T.PC[:, 28:29], I14, 127.0, A.mult, ["PCI"], ["PC28"], 1.0, A.add)
     ts(T.LX6[:], T.LT[:, 48:56], 15.0, A.add, ["LT6"], ["LX6"])
-    ts(T.PC[:, 16:17], I14, 40.0, A.mult, ["PCI"], ["PC16"])
-    ts(T.PC[:, 19:20], I14, SC, A.mult, ["PCI", "PC17"], ["PC19"], T.PC[:, 17:18], A.add)
-    starters_send(0)
-    ts(T.PC[:, 20:23], T.CF[:, 1:4], I14, A.mult, ["CF", "PCI"], ["PC20"])
-    ts(T.PC[:, 25:26], P1, 2 * MAGIC - 4096.0, A.mult, ["PC"], ["PC25"], -2 * MAGIC, A.add)
-    ts(T.PC[:, 26:27], PP, P1, A.subtract, ["PC"], ["PC26"], 0.5, A.mult)
-    rows_b[0]()
-    ts(T.WB[:, 0:8], T.CF[:, 0:8], PL7, A.is_equal, ["CF", "PC"], ["WB0"])
-    rows_b[1]()
+    cp(T.SGB[:, 0:3], T.SG[:, 9:12], ["SG"], ["SGB"])
+    ts(T.LT[:, 40:48], T.LT[:, 24:32], P1, A.mult, ["LT1", "LT2", "PC"], ["LT5"])
     ts(T.R4[:], T.CG[:], P8, A.is_equal, ["CG", "PC"], ["R4"])
+    starters("SSND", "X", 0)
+    send(nxt, "s0", T.SLAND[:, 0:256], T.SSND[:, 0:256], ["SSND0"])
+    landed(prv, "s0", ["SLAND0"])
+    ts(T.PC[:, 33:34], I12, -255.0 * 128, A.mult, ["PCI"], ["PC33"])
+    ts(T.PC[:, 18:19], I12, -1.0, A.mult, ["PCI"], ["PC18"])
+    ts(T.PC[:, 19:20], I12, 255.0, A.mult, ["PCI", "PC28"], ["PC19"], T.PC[:, 28:29], A.add)
+    ts(T.PC[:, 16:17], I14, OFFR, A.mult, ["PCI", "PC29"], ["PC16"], T.PC[:, 29:30], A.add)
+    ts(T.PC[:, 27:28], I15, T.PC[:, 29:30], A.add, ["PCI", "PC29"], ["PC27"])
+    ts(T.PC[:, 31:32], OCOL, T.PC[:, 28:29], A.mult, ["PC", "PC28"], ["PC31"])
+    rows_b[0]()
+    ts(T.PC[:, 24:25], P1, 2 * MAGIC, A.mult, ["PC"], ["PC24"], -2 * MAGIC, A.add)
+    ts(T.PC[:, 26:27], PP, P1, A.subtract, ["PC"], ["PC26"], 0.5, A.mult)
+    ts(T.PC[:, 23:24], P1, 22.5, A.mult, ["PC"], ["PC23"], 0.5, A.add)
+    ts(T.PC[:, 20:23], T.CF[:, 1:4], I14, A.mult, ["CF", "PCI", "PC33"], ["PC20"], T.PC[:, 33:34], A.add)
+    rows_b[1]()
+    ts(T.PC[:, 25:26], P1, -89.0, A.mult, ["PC", "PC24"], ["PC25"], T.PC[:, 24:25], A.add)
+    ts(T.PAIR[:], T.PAIR[:], T.PC[:, 26:27], A.is_equal, ["PAIR", "PC26", "PC23"], ["PAIR"], T.PC[:, 23:24], A.mult)
+    ts(T.M1[:], T.CB1[:], PL7, A.is_equal, ["CB1", "PC"], ["M1"])
+    bits_block(3, 0, 0, 1)
     rows_b[2]()
+    bits_block(5, 0, 0, 2)
+    ts(T.WC[:, 0:8], T.CF[:, 0:8], PL7, A.is_equal, ["CF", "PC"], ["WC"])
     for o in range(2):
         ts(T.LX0[:, 8 * o:8 * o + 8], T.ZB[:, 0:8], T.WF[:, 2:3], A.add, ["ZB", "WF2"], ["LX0_%d" % o], 8.0 * o, A.add)
+    ts(T.KP[:, 4:6], T.CF[:, 0:129:128], PP, A.add, ["CF", "PC"], ["KP4"], -256.0, A.add)
     rows_b[3]()
-    ts(T.TB[:, 3072:W], T.TB[:, 1024:2048], T.SG[:, 11:12], A.mult, ["TBb", "SG"], ["TBd"])
-    need("y", deps([], ["SS0_0"]))
+    bits_block(6, 0, 1, 2)
+    bits_block(7, 1, 1, 2)
+    join("TBc", ["TB_%d" % b for b in range(1, 8)])
+    second = [lambda: tt(T.KP[:, 6:8], T.KP[:, 4:6], T.KP[:, 4:6], A.mult, ["KP4"], ["KP6"]),
+              lambda: ts(T.TH[:, 255:512:256], T.KP[:, 4:6], -SAME, A.add, ["KP4", "TH"], ["THa"], SC, A.mult),
+              lambda: tt(T.LT[:, 32:40], T.LT[:, 40:48], T.LT[:, 16:24], A.add, ["LT5", "LT0"], ["LT4"]),
+              lambda: (ts(T.TH[:, 127:513:385], T.KP[:, 6:8], SAME, A.add, ["KP6", "TH"], ["THb"], -SC, A.mult), join("THS", ["TH", "THa", "THb"])),
+              lambda: cp(T.LX2[:], T.LT[:, 32:40], ["LT4"], ["LX2"])]
+    third = [lambda: ts(T.PW[:, 0:12], T.CF[:, 0:12], PLOW, A.add, ["CF", "PC"], ["PW0"], 11.0, A.is_equal),
+             lambda: ts(T.PW[:, 34:35], I13, -0.5, A.mult, ["PCI"], ["PW34"]),
+             lambda: ts(T.PW[:, 12:24], T.PW[:, 0:12], -2.0, A.mult, ["PW0"], ["PW12"], 2.0, A.add),
+             lambda: scan(T.PW[:, 36:48], T.PW[:, 12:24], T.PW[:, 0:12], A.mult, A.add, ["PW0", "PW12"], ["PW36"]),
+             lambda: ts(T.PW[:, 35:36], T.PW[:, 47:48], -1.0 / (2 * SC), A.mult, ["PW36", "PW34"], ["PW35"], T.PW[:, 34:35], A.add)] + [
+             lambda ll=ll: ts(T.BW[:, 128 * ll:128 * ll + 128], T.C8[:], T.PC[:, 12 + ll:13 + ll], A.is_equal, ["C8", "PC12", "PC13", "PW35"], ["BW%d" % ll], T.PW[:, 35:36], A.mult)
+             for ll in range(2)]
+    need("y", deps([], ["SSND0"]))
     fill_rows("TB", 1)
     zeros(T.RS[:], ["RS"])
-    starters_on(0)
-    zeros(T.XC1[:, W:WX], ["XC1x"])
-    need("g", deps(["TBd"], []))
-    records_send(0)
-    for o in range(2):
-        tt(T.E3[:, 128 * o:128 * o + 128], T.DLAND[:, 16 * NB:16 * NB + 16].indirect(T.LX0[:, 8 * o:8 * o + 8]), T.R4[:], A.mult,
-           ["DRAW", "LX0_%d" % o, "R4"], ["E3_%d" % o])
+    op("g", lambda: g.iota(T.RS[:, 0:256:16], [[0, 2], [4096, 8]], 4081 * 4096, 0, allow_small_or_imprecise_dtypes=True), [], ["RS"])
+    zeros(T.XC1[:, W:DUM], ["XC1x"])
+    zeros(T.XC0[:, W:DUM], ["XC0x"])
 
-    def first_dead_list():
-        for o in range(2):
-            op("p", mm(T.C7[:, 32 + o:48:2], T.E3[:, 128 * o:128 * o + 128], T.WB[:, 0:8], True, True), ["E3_%d" % o, "WB0"], ["@C7"])
+    def late_fills():
+        need("g", deps(["LO1", "TB_7"], []))
+        iota("SPK", [[0, 8], [1, 2]], DUM // 4, 2)
+        zeros(T.FL[:, 1024:FH], ["FL4", "FL5"])
+        records_send(0)
+        zeros(T.TH[:], ["TH"])
+        zeros(T.FL[:, FH + 768:2 * FH], ["FL6", "FL7", "FL8"])
+        for i in range(2):
+            op("g", lambda: g.affine_select(T.KN[:, 128 * i:128 * i + 128], T.C8[:], [[0, 128]], A.is_gt, (2 * i - 1) / 64.0, 0, 0), ["C8"], ["KN%d" % i])
+        op("g", lambda: g.affine_select(T.PEN[:], T.ZB[:], [[-1, 128]], A.not_equal, 2.0 ** 25, 0, 1), ["ZB"], ["PEN"])
 
-    iota("FBC", [[0, 2], [4096, 8]], 4081 * 4096, 0)
-    iota("SPI", [[0, 64], [1, 2]], DUM, 2)
-    iota("PAIR", [[1, 64], [0, 2]], 0, 0)
-    iota("TH", [[0, 512]], 0, 0)
-    for key, ap, pattern, base in (("LT0", T.LT[:, 16:24], [[512, 4], [128, 2]], 127), ("LT1", T.LT[:, 24:32:2], [[-511, 4]], 897), ("LT2", T.LT[:, 25:32:2], [[0, 4]], 256)):
-        op("g", lambda: g.iota(ap, pattern, base, 0, allow_small_or_imprecise_dtypes=True), [], [key])
-    zeros(T.FL[:, 1024:FH], ["FL4", "FL5"])
-    zeros(T.FL[:, FH + 768:2 * FH], ["FL6", "FL7", "FL8"])
-    zeros(T.XC0[:, W:WX], ["XC0x"])
-    iota("DIAG", [[1, 2], [0, 16], [2, 8]], 0, 0)
+    first_dead = [lambda o=o: tt(T.E3[:, 128 * o:128 * o + 128], T.DLAND[:, 0:16].indirect(T.LX0[:, 8 * o:8 * o + 8]), T.R4[:], A.mult,
+                                 ["DRAW", "LX0_%d" % o, "R4"], ["E3_%d" % o]) for o in range(2)]
 
     def scalar_constants():
         for i in range(2):
             act(T.RSX[:, 16 * i:16 * i + 16], T.RS1[:], F.Copy, ["RS1"], ["RSX%d" % i], scale=(2 * i - 1) / 4096.0)
-        act(T.CQ[:, 896:912], T.RS1[:], F.Copy, ["RS1"], ["CQ896"], scale=0.0, bias=-2.0 ** -12)
         act(T.CQ[:, 912:928], T.RS1[:], F.Identity, ["RS1", "PC25"], ["CQ912"], scale=0.0, bias=T.PC[:, 25:26])
         join("RSX", ["RSX0", "RSX1"])
         join("CQ4", ["CQ896", "CQ912"])
         act(T.CR[:], T.LANE[:], F.Identity, ["LANE", "PC18", "PC19"], ["CR"], scale=T.PC[:, 18:19], bias=T.PC[:, 19:20])
         spare_columns("TB")
         join("TB", ["TBd", "TBx"])
-        act(T.RSN[:], T.RS1[:], F.Copy, ["RS1"], ["RSN"], scale=-SC)
         starter_rows(0)
-        act(T.IDF[:], IB, F.Copy, ["IB"], ["IDF"])
-        act(T.IDN[:], IB, F.Copy, ["IB"], ["IDN"], scale=-1.0)
-        act(T.PEN[:], IB, F.Copy, ["IB"], ["PEN"], scale=2.0 ** 25)
-
-    def first_constants():
-        yield lambda: (cp(T.RS[:, 0:256:16], T.FBC[:], ["FBC"], ["RS"]),
-                       ts(T.PAIR[:], T.PAIR[:], T.PC[:, 26:27], A.is_equal, ["PAIR", "PC26"], ["PAIR"], 0.5, A.mult))
-        yield lambda: ms(T.CQ[:, 0:256], -0.5, ["CQ0"])
-        yield lambda: ts(T.PC[:, 24:25], PP, SC, A.mult, ["PC"], ["PC24"])
-        yield lambda: ts(T.LX3[:], T.CF[:, 0:16:2], PLL, A.add, ["CF", "PC"], ["LX3"])
-        yield lambda: (ts(T.TH[:, 127:256:128], T.ZB[:, 0:2], T.PC[:, 24:25], A.add, ["ZB", "PC24", "TH"], ["THa"], -1536 * SC, A.add),
-                       ts(T.TH[:, 511:512], T.PC[:, 24:25], (128 - 1536) * SC, A.add, ["PC24", "TH"], ["THb"]))
-        yield lambda: join("THS", ["TH", "THa", "THb"])
-        yield lambda: ts(T.LT[:, 40:48], T.LT[:, 24:32], P1, A.mult, ["LT1", "LT2", "PC"], ["LT5"])
-        yield lambda: tt(T.MSP[:], T.M1[:], T.SPI[:], A.mult, ["M1", "SPI"], ["MSP"])
-        yield lambda: tt(T.LT[:, 32:40], T.LT[:, 40:48], T.LT[:, 16:24], A.add, ["LT5", "LT0"], ["LT4"])
-        yield lambda: cp(T.LX2[:], T.LT[:, 32:40], ["LT4"], ["LX2"])
-        yield lambda: ts(T.PC[:, 14:15], PGRP, 16.0, A.mult, ["PC"], ["PC14"], 16.0, A.add)
-        yield lambda: ts(T.PC[:, 15:16], I15, 16.0, A.mult, ["PCI"], ["PC15"], I14, A.add)
-        yield lambda: ts(T.SW[:], T.CF[:, 0:144], T.PC[:, 14:15], A.is_equal, ["CF", "PC14", "PC15"], ["SW"], T.PC[:, 15:16], A.mult)
-        for d in range(ND):
-            yield lambda d=d: ts(T.ABASE[:, 2 * d:2 * d + 2], T.SCOL[:, 2:4], -1.0, A.mult, ["SCOL2"], ["ABASE%d" % d], 262144.0 - 12.0 + 32.0 * 97 * d, A.add)
+        act(T.RS4[:], T.RS1[:, 0:16], F.Copy, ["RS1"], ["RS4"], scale=4.0)
 
     def late_constants():
         for f in table_rows(T.PAI, "PAI", 0):
             yield f
-        yield lambda: ts(T.DIAG[:], T.DIAG[:], PLOW, A.is_equal, ["DIAG", "PC"], ["DIAG"])
+        yield lambda: ts(T.PW[:, 32:33], PLOW, 4.0, A.is_ge, ["PC"], ["PW32"], -1.0 / (32 * SC), A.mult)
+        yield lambda: ts(T.PW[:, 33:34], PLOW, 4.0, A.is_lt, ["PC"], ["PW33"], -1.0 / (2 * SC), A.mult)
+        yield lambda: ts(T.PW[:, 24:26], T.CF[:, 17:256:238], I13, A.mult, ["CF", "PCI"], ["PW24"], 0.5, A.mult)
+        yield lambda: ts(T.PW[:, 26:28], T.CF[:, 1:3], -1.0, A.mult, ["CF", "PC14"], ["PW26"], T.PC[:, 14:15], A.add)
         for i in range(2):
-            yield lambda i=i: ts(T.SRB[:, 128 * i:128 * i + 128], T.CF[:, 0:128], 1.0 + i, A.add, ["CF", "PC14"], ["SRB%d" % i], T.PC[:, 14:15], A.is_equal)
-        for h in range(4):
-            yield lambda h=h: ts(T.LX4[:, 8 * h:8 * h + 8], T.CF[:, 0:16:2], PLL, A.add, ["CF", "PC"], ["LX4_%d" % h], 16.0 * (h // 2), A.add)
-        yield lambda: join("LX4", ["LX4_%d" % h for h in range(4)])
+            yield lambda i=i: ts(T.PW[:, 28 + i:29 + i], T.PW[:, 47:48], T.PW[:, 32 + i:33 + i], A.mult, ["PW36", "PW32", "PW33", "PW24"], ["PW%d" % (28 + i)],
+                                 T.PW[:, 25 - i:26 - i], A.add)
+        for i in range(2):
+            yield lambda i=i: ts(T.SRB[:, 128 * i:128 * i + 128], T.CF[:, 0:128], T.PW[:, 26 + i:27 + i], A.is_equal, ["CF", "PW26", "PW%d" % (28 + i)], ["SRB%d" % i],
+                                 T.PW[:, 28 + i:29 + i], A.mult)
         yield lambda: ts(T.CB1[:], T.C8[:], T.PC[:, 12:13], A.subtract, ["C8", "PC12"], ["CB1"], P1, A.is_equal)
         yield lambda: ts(T.LT[:, 0:2], T.CF[:, 0:2], PL7, A.add, ["CF", "PC"], ["LT"], PL7, A.add)
         yield lambda: ts(T.D16[:, 0:8], T.CF[:, 0:8], T.WF[:, 2:3], A.is_equal, ["CF", "WF2"], ["D16"])
         for o in range(2):
             yield lambda o=o: ts(T.LX5[:, 8 * o:8 * o + 8], T.ZB[:, 0:8], T.LT[:, o:o + 1], A.add, ["ZB", "LT"], ["LX5_%d" % o])
         for i in range(2):
-            yield lambda i=i: ts(T.CB[:], T.HL[:, 512 * i:512 * i + 256], 16.0, A.mult, ["HI%d" % i], ["CB", "CBb"], -1.0, A.add)
-            yield lambda i=i: tt(T.PF[:, 256 * i:256 * i + 256], T.CB[:], T.HL[:, 512 * i + 256:512 * i + 512], A.add, ["CB", "CBb", "LO%d" % i], ["PF%d" % i])
+            yield lambda i=i: (op("p", [mm(T.G1[:, 0:256], a, T.HL[:, 512 * i + 256 * h:512 * i + 256 * h + 256], h == 0, h == 1) for h, a in enumerate((T.I16[:], IB))],
+                                  ["I16", "IB", "HI%d" % i, "LO%d" % i], ["@G1"]),
+                               act(T.PF[:, 256 * i:256 * i + 256], T.G1[:, 0:256], F.Copy, ["@G1"], ["PF%d" % i], bias=-1.0))
         yield lambda: dma("y", [(T.FO[0:128:16, 0:W], T.PF[:, 256:512])], ["PF1"], ["FO"])
+        yield lambda: act(T.I16[:], IB, F.Copy, ["IB"], ["I16"], scale=16.0)
+        yield lambda: act(T.RSN[:], T.RS1[:, 0:16], F.Copy, ["RS1"], ["RSN"], scale=-SC)
         yield lambda: act(T.DIAG[:], T.LANE[:], F.Copy, ["LANE"], ["DIAG"], scale=16.0, bias=NB - 1.0)
 
     late = list(late_constants())
-    first = list(first_constants())
-    gaps = {(0, 0): first[0:8], (0, 3): first[8:9], (0, 4): first[9:10], (0, 1): first[10:12], (0, 2): first[12:16],
-            (0, 7): late[0:1], (1, 0): late[1:3], (1, 7): late[3:4], (2, 0): late[4:12], (4, 0): late[12:17], (7, 0): late[17:19], (8, 0): late[19:23]}
+    gaps = {(0, 0): first_dead, (0, 3): second[0:3], (0, 4): second[3:5],
+            (0, 2): first[0:2] + third[0:2] + first[3:5] + third[2:3] + first[2:3] + first[5:6] + third[3:4] + late[0:1] + third[4:5],
+            (0, 7): third[5:7], (1, 0): late[4:8], (1, 3): late[1:2], (1, 2): late[2:3] + late[8:10] + late[12:14] + late[3:4],
+            (2, 3): late[10:12], (4, 3): late[14:17], (5, 1): late[20:23], (7, 1): late[17:18], (8, 1): late[18:20]}
 
     for t in range(NB):
         frm, to = (prv, nxt) if t % 2 == 0 else (nxt, prv)
@@ -430,7 +447,10 @@ def rank_program(g, core, T, topo):
             m = t * ND + d
             tail = d == ND - 1
             end = m == NB * ND - 1
+            NV = NVS[d > 0]
             z, zk = (s_, sk) if d == 0 else (T.Z[:], "Z")
+            dst, src = (frm, to) if tail else (to, frm)
+            CP, ck = (T.XC0, "XC0") if (t + tail) % 2 == 0 else (T.XC1, "XC1")
 
             def gap(i):
                 for f in gaps.get((m, i), []):
@@ -442,41 +462,52 @@ def rank_program(g, core, T, topo):
                 op("p", mm(hs[h][0], IH, T.ONES[:, 0:64], True, False), ["IH", "ONES"], [hs[h][1]])
             for h in (1, 0):
                 zs = [z[:, 128 * h + ll:128 * h + 128:2] for ll in range(2)]
+                if d == 0 and t > 0:
+                    zs = [XC[:, 2048 * ll + 1024 * h + t:2048 * ll + 1024 * h + 1024:16] for ll in range(2)]
                 op("p", [mm(hs[h][0], T.WN[:, 128 * ll:128 * ll + 128], zs[ll], False, False) for ll in range(2)] +
                    [mm(hs[h][0], IH, T.CQ[:, c:c + 64], False, False) for c in (256, 512)] +
                    [mm(hs[h][0], T.WP[:, 128 * ll:128 * ll + 128], zs[ll], False, ll == 1) for ll in range(2)],
-                   ["WN0", "WN1", "WP0", "WP1", "CQ1", "CQ2", zks[h]], [hs[h][1]])
+                   ["WN0", "WN1", "WP0", "WP1", "CQ1", "CQ2", xk if d == 0 and t > 0 else zks[h]], [hs[h][1]])
             Z8 = ["Z8_%d" % cl for cl in range(8)]
 
             def part(ap, ch, h):
-                return ap[:, 128 * ch + 64 * h:128 * ch + 64 * h + 64]
+                return ap[:, 128 * ch + 64 * (h % 2):128 * ch + 64 * min(h, 1) + 64]
+
+            def keys(name, ch, h):
+                return ["%s%d%d" % (name, ch, i) for i in ((0, 1) if h == 2 else (h,))]
 
             def floors(ch, h):
-                ts(part(T.FI, ch, h), part(T.SQ, ch, h), T.ACOL[:, ch:ch + 1], A.add, ["SQ%d%d" % (ch, h), "ACOL%d" % ch], ["FI%d%d" % (ch, h)], 1.0 / 32, A.mult)
+                ts(part(T.FI, ch, h), part(T.SQ, ch, h), T.ACOL[:, ch:ch + 1], A.add, keys("SQ", ch, h) + ["ACOL%d" % ch], keys("FI", ch, h), 1.0 / 32, A.mult)
 
             def places(ch, h):
-                ts(part(T.CI, ch, h), part(T.FI, ch, h), 4095, A.bitwise_and, ["FI%d%d" % (ch, h)], ["CI%d%d" % (ch, h)])
+                ts(part(T.CI, ch, h), part(T.FI, ch, h), 4095, A.bitwise_and, keys("FI", ch, h), keys("CI", ch, h))
 
             def lists(ch, h):
-                cp(part(T.OFF, ch, h), part(T.CI, ch, h), ["CI%d%d" % (ch, h)], ["OFF%d%d" % (ch, h)])
+                cp(part(T.OFF, ch, h), part(T.CI, ch, h), keys("CI", ch, h), keys("OFF", ch, h))
 
             for h in (1, 0):
                 for ch in range(2):
                     act(part(T.SQ, ch, h), hs[h][0], F.Square, [hs[h][1], "SCOL%d" % ch], ["SQ%d%d" % (ch, h)], bias=T.SCOL[:, ch:ch + 1], scale=4096.0)
-            if m == 0:
-                first_dead_list()
+
             def z8(cl):
                 cp(T.Z8[:, cl:16 * NV[0]:8], z[:, 0:2 * NV[0]], zks, ["Z8_%d" % cl])
 
-            for cl in range(2):
+            ns, ng = ZSPLIT[m > 0]
+            if tail and not end:
+                records_send(t + 1)
+            for cl in range(ns):
                 act(T.Z8[:, cl:16 * NV[0]:8], z[:, 0:2 * NV[0]], F.Copy, zks, ["Z8_%d" % cl])
-            for cl in (5, 6, 7):
-                if d > 0:
-                    op("g", lambda: g.affine_select(T.Z8[:, cl:16 * NV[0]:8], z[:, 0:2 * NV[0]], [[0, 2 * NV[0]]], A.is_gt, 0.0, 1, 0), zks, ["Z8_%d" % cl])
-                else:
-                    z8(cl)
-            z8(2); z8(3); z8(4)
-            floors(0, 1); floors(1, 1); floors(0, 0); places(0, 1); floors(1, 0); places(0, 0); lists(0, 1)
+            for cl in range(8 - ng, 8):
+                op("g", lambda: g.affine_select(T.Z8[:, cl:16 * NV[0]:8], z[:, 0:2 * NV[0]], [[0, 2 * NV[0]]], A.is_gt, 0.0, 1, 0), zks, ["Z8_%d" % cl])
+            if d == 0:
+                starters_on(t)
+            if m == 0:
+                late_fills()
+            zv = list(range(ns, 8 - ng))
+            held = [zv.pop(), zv.pop()] if d == 0 and t > 0 else []
+            for cl in zv:
+                z8(cl)
+            floors(0, 1); floors(1, 1); floors(0, 0); [z8(cl) for cl in held[0:1]]; places(0, 1); floors(1, 0); [z8(cl) for cl in held[1:2]]; places(0, 0); lists(0, 1)
             places(1, 1); places(1, 0); lists(0, 0); lists(1, 1); lists(1, 0)
 
             def offs(ch, c0, c1):
@@ -484,16 +515,16 @@ def rank_program(g, core, T, topo):
 
             def v_gather(ch, c0, c1):
                 a, b = 2048 * ch + 16 * c0, 2048 * ch + 16 * c1
-                tt(T.DF[:, a:b], T.X[:, 0:WX].indirect(T.OFF[:, 128 * ch + c0:128 * ch + c1]), T.Z8[:, 16 * c0:16 * c1], A.subtract,
+                tt(T.DF[:, a:b], T.X[:, 0:W].indirect(T.OFF[:, 128 * ch + c0:128 * ch + c1]), T.Z8[:, 16 * c0:16 * c1], A.subtract,
                    ["X"] + offs(ch, c0, c1) + Z8, ["DF%d_%d" % (ch, c0)])
 
-            def v_half(ch, c0, c1, keys, odd=None):
-                a, b, st = 2048 * ch + 16 * c0 + (odd or 0), 2048 * ch + 16 * c1, (1 if odd is None else 2)
-                ts(T.AB[:, a:b:st], T.DF[:, a:b:st], 0.0, A.max, keys, ["AB%d_%d_%s" % (ch, c0, odd)], 2.0, A.mult)
+            def v_half(ch, odd=None):
+                a, b, st = 2048 * ch + (odd or 0), 2048 * ch + 16 * NV[ch], (1 if odd is None else 2)
+                ts(T.AB[:, a:b:st], T.DF[:, a:b:st], 0.0, A.max, ["DF%d_0" % ch], ["AB%d_0_%s" % (ch, odd)], 2.0, A.mult)
 
             def s_gather(ch, c0, c1):
                 a, b = 2048 * ch + 16 * c0, 2048 * ch + 16 * c1
-                act(T.DF[:, a:b], T.X[:, 0:WX].indirect(T.OFF[:, 128 * ch + c0:128 * ch + c1]), F.Copy, ["X"] + offs(ch, c0, c1), ["DF%d_%d" % (ch, c0)])
+                act(T.DF[:, a:b], T.X[:, 0:W].indirect(T.OFF[:, 128 * ch + c0:128 * ch + c1]), F.Copy, ["X"] + offs(ch, c0, c1), ["DF%d_%d" % (ch, c0)])
 
             def p_diff(ch, c0, c1, bk):
                 a, b = 2048 * ch + 16 * c0, 2048 * ch + 16 * c1
@@ -507,22 +538,23 @@ def rank_program(g, core, T, topo):
                 op("p", [mm(T.K6[c0:c1, 2 * b + ch:256:32], src[:, 2048 * ch + 16 * c0 + b:2048 * ch + 16 * c1:16], T.OB[:, 8 * ob:8 * ob + 8], False, close and b == 15)
                          for b in parts], keys + ["OB%d" % ob], ["@K6"])
 
-            def barred(ch):
-                if d > 0:
-                    tt(T.EQ[:, 128 * ch:128 * ch + 128], T.LB[:, 0:128], T.CI[:, 128 * ch:128 * ch + 128], A.is_equal,
-                       ["@LB", "CI%d0" % ch, "CI%d1" % ch], ["EQ%d" % ch])
-
             def bar(ch):
                 if d > 0:
-                    op("p", mm(T.K6[:, ch:256:2], T.EQ[:, 128 * ch:128 * ch + 128], T.PEN[:], False, False), ["EQ%d" % ch, "PEN"], ["@K6"])
+                    op("p", mm(T.K6[:, ch:256:2], T.EQ[:, 128 * ch:128 * ch + 128], T.PEN[:], False, False), ["EQ", "PEN"], ["@K6"])
 
             def number(ch):
                 op("p", mm(T.K6[:, ch:256:2], T.CFL[:, 128 * ch:128 * ch + 128], IB, False, False), ["CFL", "IB"], ["@K6"])
 
-            sc = [(0, NV[0], NV[0] + 32, "G0"), (0, NV[0] + 32, 128, "G1"), (1, NV[1], NV[1] + 32, "G2"), (1, NV[1] + 32, 128, "G3")]
+            sc = [(ch, c0, min(c0 + 32, 128)) for ch in range(2) for c0 in range(NV[ch], 128, 32)]
+            sc = [c + ("G%d" % i,) for i, c in enumerate(sc)]
             op("p", mm(T.K6[:, 0:256], IH, T.CQ[:, 640:896], True, False), ["IH", "CQ3"], ["@K6"])
             for ch, c0, c1, bk in sc:
                 op("p", [mm(T[bk][:, cl:16 * (c1 - c0):8], IN, z[:, 2 * c0:2 * c1], cl == 0, False) for cl in range(8)], ["IN", zks[1]], ["@" + bk])
+            if d == 0 and t > 0:
+                near_rows(t - 1)
+            if d > 0:
+                op("p", [mm(T.LB[:, 128 * ch:128 * ch + 128], T.BW[:, 128 * ll:128 * ll + 128], T.QR[:, ll:256:2], ch + ll == 0, ch + ll == 2)
+                         for ch in range(2) for ll in range(2)], ["BW0", "BW1", "QR"], ["@LB"])
             for ch in range(2):
                 v_gather(ch, 0, NV[ch])
             s_gather(0, NV[0], 128)
@@ -536,201 +568,202 @@ def rank_program(g, core, T, topo):
             dsum(T.DF, 1, 0, NV[1], 1, ["DF1_0"])
             for i in range(2):
                 number(i)
-            v_half(0, 0, NV[0], ["DF0_0"])
+            v_half(0)
             for c in sc[0:3]:
                 s_abs(*c)
             dsum(T.AB, 0, 0, 128, 0, ["AB0_0_None", "AB0_%d_None" % sc[0][1], "AB0_%d_None" % sc[1][1]])
-            barred(0)
-            barred(1)
-            for odd in range(2):
-                v_half(1, 0, NV[1], ["DF1_0"], odd)
-                s_abs(*sc[3], odd)
-            if m == 0:
-                cp(T.DLAND[:, 0:16], T.C7[:, 32:48], ["@C7"], ["DLAND0"])
             if d > 0:
-                result(T.RES[:], "RES", d - 1)
-            if end:
-                q_ = T.RSND[:, 32 * t + 16:32 * t + 32]
-                act(q_, T.RES[:], F.Relu, ["RES"], ["RSQ"], bias=1.0)
-                send(frm, "q", T.RLAND[:, 32 * t + 16:32 * t + 32], q_, ["RSQ"])
+                tt(T.EQ[:], T.LB[:, 0:256], T.CFL[:], A.is_equal, ["@LB", "CFL"], ["EQ"])
+            for odd in range(2):
+                v_half(1, odd)
+                s_abs(*sc[3], odd)
+            gap(0)
             bar(0)
             bar(1)
             for odd in range(2):
                 dsum(T.AB, 1, 0, 128, 0, ["AB1_0_%d" % odd, "AB1_%d_None" % sc[2][1], "AB1_%d_%d" % (sc[3][1], odd)], range(odd, 16, 2), odd == 1)
-            dead = [(T.DLAND[:, 16 * t:16 * t + 16], "DLAND%d" % t)] + [(T.WB[:, 16 * i:16 * i + 16], "WB%d" % i) for i in range(d)]
-            op("p", [mm(T.C7[:, 0:16], IH, T.CQ[:, 640:656], True, False), mm(T.C7[:, 0:16], IH, T.ONES[:, 0:16], False, False)] +
-               [mm(T.C7[:, 0:16], IB, a, False, False) for a, k in dead], ["IB", "IH", "CQ3", "ONES"] + [k for a, k in dead], ["@C7"])
-            if d == 0 and t > 0:
-                near_rows(t - 1, 0)
-                near_rows(t - 1, 1)
-            gap(0)
-            op("p", [mm(T.LB[:, 256:512], IH, a, i == 0, False) for i, a in enumerate((s_, T.CQ[:, 0:256]))], ["IH", sk, "CQ0"], ["@LB"])
+            dead = [(T.DLAND[:, 16 * t:16 * t + 16], "DLAND%d" % t)][0:min(t, 1)] + [(T.WB[:, 16 * i:16 * i + 16], "WB%d" % i) for i in range(d)]
+            op("p", [mm(T.C7[:, 0:16], IB, T.CQ[:, 0:16], True, False), mm(T.C7[:, 0:16], IH, T.CQ[:, 896:912], False, False), mm(T.C7[:, 0:16], IH, T.CQ[:, 640:656], False, False)] +
+               [mm(T.C7[:, 0:16], IB, a, False, False) for a, k in dead + [(T.ONES[:, 0:16], "ONES")] * d],
+               ["IB", "IH", "CQ0", "CQ3", "CQ896", "ONES"] + [k for a, k in dead], ["@C7"])
+            if t == 0:
+                op("p", [mm(T.C7[:, o:16:2], T.E3[:, 128 * o:128 * o + 128], T.WC[:, 0:8], False, False) for o in range(2)], ["E3_0", "E3_1", "WC"], ["@C7"])
+            gap(1)
             if m == 0:
                 scalar_constants()
-            if m in (1, 2):
-                c0 = 2048 * (m - 1)
-                act(T.TA[:, c0:c0 + 2048], T.TB[:, c0:c0 + 2048], F.Copy, ["TB"], ["TA" + "bc"[m - 1]])
-            if m == 2:
-                fill_rows("TA", 0)
-            if m == 3:
+            if m == 1:
                 spare_columns("TA")
-                join("TA", ["TAd", "TAx"])
             if m in (3, 4):
                 starter_rows(m - 2)
             for h in range(2):
                 scan(T.R[:, 128 * h:128 * h + 128], T.RS[:, 128 * h:128 * h + 128], T.K6[:, 128 * h:128 * h + 128], A.max, A.min, ["RS", "@K6"], ["R%d" % h])
             for h in range(2):
                 tt(T.EK[:, 64 * h:64 * h + 64], T.R[:, 128 * h:128 * h + 128].indirect(T.LX6[:, 0:4]), T.M1[:, 0:64], A.mult, ["R%d" % h, "LX6", "M1"], ["EK%d" % h])
-            gap(3)
             op("p", [mm(T.C7[:, 0:16], T.EK[:], T.RSX[:, 0:16], False, False)] +
-               [mm(T.C7[:, 0:16], a, T.CQ[:, c:c + 16], False, False) for a, c in ((IH, 896), (IH, 256), (T.PAIR[:], 912))] +
+               [mm(T.C7[:, 0:16], a, T.CQ[:, c:c + 16], False, False) for a, c in ((IH, 256), (T.PAIR[:], 912))] +
                [mm(T.C7[:, 0:16], T.EK[:], T.RSX[:, 16:32], False, True)], ["EK0", "EK1", "RSX", "IH", "PAIR", "CQ1", "CQ4"], ["@C7"])
             cp(T.RI[:], T.R[:, 15:256:16], ["R0", "R1"], ["RI"])
-            gap(4)
             if d == 0 and t > 0:
                 near_add(t - 1)
+            gap(3)
+            if end:
+                pairs_so_far = last_pairs(0)
+                pairs_so_far[0]()
             ts(T.RA[:], T.RI[:], 4095, A.bitwise_and, ["RI"], ["RA"])
-            gap(5)
-            tt(T.E1[:], T.RA[:, 0:16].indirect(T.LX1[:]), T.M1[:], A.mult, ["RA", "LX1", "M1"], ["E1"])
-            yu, yk = T.YSND[:, 16 * m:16 * m + 16], "YSND%d" % m
-            ts(yu, T.C7[:, 0:16], 4096.0, A.mult, ["@C7"], [yk], DEAD, A.min)
-            if not tail:
-                send(to, "y%d%d" % (t, d), T.YLAND[:, 16 * m:16 * m + 16], yu, [yk])
-            act(T.UP[:], far[:, 0:WX].indirect(yu), F.Copy, [fk, yk], ["UP"])
-            tt(T.QR[:], far[:, 0:WX].indirect(yu), T.CR[:], A.mult, [fk, yk, "CR"], ["QR"])
-            gap(6)
+            ts(T.RQ[:], T.RI[:], 2, A.arith_shift_right, ["RI"], ["RQ"], 1023, A.bitwise_and)
+            gap(4)
             if not tail:
                 tt(T.RS[:, 0:256:16], T.RA[:], T.FBC[:], A.add, ["RA", "FBC"], ["RS"])
-            ts(T.QO[:], T.QR[:], OCOL, A.mult, ["QR", "PC"], ["QO"])
+            tt(T.RB[:], T.SPK[:], T.RQ[:], A.subtract, ["SPK", "RQ"], ["RB"])
+            yu, yk = T.YSND[:, 16 * m:16 * m + 16], "YSND%d" % m
+            ts(yu, T.C7[:, 0:16], 4096.0, A.mult, ["@C7"], [yk], DEAD, A.min)
+            if not end:
+                send(dst, "y%d%d" % (t, d), T.YLAND[:, 16 * m:16 * m + 16], yu, [yk])
+            act(T.UP[:], far[:, 0:DUM].indirect(yu), F.Copy, [fk, yk, "PC31"], ["UP"], scale=T.PC[:, 31:32])
+            tt(T.QR[:], far[:, 0:DUM].indirect(yu), T.CR[:], A.mult, [fk, yk, "CR"], ["QR"])
+            tt(T.DE[:], T.RB[:, 0:16].indirect(T.LX1[:]), T.M1[:], A.mult, ["RB", "LX1", "M1"], ["DE"])
+            tt(T.E1[:], T.RA[:, 0:16].indirect(T.LX1[:]), T.M1[:], A.mult, ["RA", "LX1", "M1"], ["E1"])
 
             def unit(gr, ll, bk, c):
                 p0, k = 32 * (gr // 2), 16 + 16 * (gr % 2)
-                q = "QO" if gr % 2 else "QR"
-                op("p", mm(T[bk][:, c:c + 128 + 128 * ll], T.UP[p0:p0 + k, ll:256:2], T[q][p0:p0 + k, 0:256:2 - ll], True, True), ["UP", q], ["@" + bk])
+                q = "UP" if gr % 2 else "QR"
+                op("p", mm(T[bk][:, c:c + 128 + 128 * ll], T[q][p0:p0 + k, ll:256:2], T.QR[p0:p0 + k, 0:256:2 - ll], True, True), ["QR", q], ["@" + bk])
 
-            def by_vector(i):
-                q = min(i, 3)
-                units, c0 = ([(2 * q, 0), (2 * q + 1, 0), (2 * q + 1, 1)], 0) if i < 3 else ([(3 + i, 0)], 128 * (i - 3))
-                n = c0
-                for gr, ll in units:
+            def by_vector(q):
+                n = 0
+                for gr, ll in [(2 * q, 0), (2 * q + 1, 0), (2 * q + 1, 1)][0:3 if q < 3 else 2]:
                     unit(gr, ll, "G%d" % q, n)
                     n += 128 + 128 * ll
                 f0 = FH * (q // 2) + 512 * (q % 2)
-                scan(T.FL[:, f0 + c0:f0 + n], T["G%d" % q][:, c0:n], T.TH[:, c0:n], A.max, A.add, ["@G%d" % q, "THS"], ["FL%d" % (i if i < 4 else 9)])
+                scan(T.FL[:, f0:f0 + n], T["G%d" % q][:, 0:n], T.TH[:, 0:n], A.max, A.add, ["@G%d" % q, "THS"], ["FL%d" % q])
 
             def by_scalar(i):
-                bk, c = ("G4", "K6", "G4", "K6", "G0")[i], (FH * (i // 2) + 1024 + i % 2 if i < 4 else FH + 1023)
+                bk, c = ("G4", "K6", "LB", "G4", "K6")[i], (FH * (i // 2) + 1024 + i % 2 if i < 4 else FH + 1023)
                 unit((0, 2, 4, 6, 7)[i], 1, bk, 0)
                 act(T.JK[:, 256 * i:256 * i + 256], T[bk][:, 0:256], F.Relu, ["@" + bk, "THS"], ["JK%d" % i, "FL%d" % (4 + i)],
-                    bias=T.TH[:, 511:512], accum_out=T.FL[:, c:c + 1])
+                    bias=T.TH[:, 512 - i // 4:513 - i // 4], accum_out=T.FL[:, c:c + 1])
 
-            def new_records(win, wk, ys, yk_, st, stk, bk, c, out, key, opened):
-                gx = T.GX[:, 0:256] if opened else T.GX[:, 256:512]
-                act(gx, win[:, 0:WX].indirect(ys), F.Copy, [wk, yk_], ["G" + key])
-                if not opened:
-                    op("p", [mm(T[bk][:, c:c + 256], IH, a, i == 0, False) for i, a in enumerate((st, T.CQ[:, 0:256]))], ["IH", stk, "CQ0"], ["@" + bk])
-                return (lambda: op("p", [mm(T[bk][:, c:c + 256], IH, a, False, i == 1) for i, a in enumerate((gx, T.CQ[:, 256:512]))],
-                                   ["IH", "G" + key, "CQ1"], ["@" + bk]),
-                        lambda: act(out, T[bk][:, c:c + 256], F.Copy, ["@" + bk], [key], bias=-MAGIC))
+            def targets(h):
+                tt(T.E2[:, 64 * h:64 * h + 64], T.FL[:, FH * h:FH * h + FH].indirect(T.LX2[:, 0:4]), T.DE[:, 64 * h:64 * h + 64], A.min,
+                   ["FL%d" % i for i in ((0, 1, 4, 5), (2, 3, 6, 7, 8))[h]] + ["LX2", "DE"], ["E2", "E2b"][h:h + 1])
 
-            own_new = new_records(T.X, "X", yu, yk, s_, sk, "LB", 256, T.NS[:, 0:256], "NS", True)
-            by_vector(3)
-            tt(T.DE[:], T.MSP[:], T.E1[:], A.subtract, ["MSP", "E1"], ["DE"])
-            by_scalar(0); by_vector(0); by_scalar(1); by_vector(1); by_scalar(2); by_vector(2); by_scalar(3); by_vector(4); by_scalar(4)
+            def new_records(win, wk, ys, yk_, st, stk, bk, c, key):
+                gx, out = T.GX[:, c:c + 256], T.NS[:, c:c + 256]
+                act(gx, win[:, 0:DUM].indirect(ys), F.Copy, [wk, yk_], ["G" + key])
+                return (lambda: op("p", [mm(T[bk][:, 0:256], IH, a, i == 0, i == 3) for i, a in enumerate((st, T.CQ[:, 0:256], gx, T.CQ[:, 256:512]))],
+                                   ["IH", stk, "CQ0", "G" + key, "CQ1"], ["@" + bk]),
+                        lambda: act(out, T[bk][:, 0:256], F.Copy, ["@" + bk], [key], bias=-MAGIC))
+
+            own_new = new_records(T.X, "X", yu, yk, s_, sk, "LB", 0, "NS")
+            by_scalar(0); by_vector(3); by_vector(0); by_scalar(1); by_vector(1); by_scalar(2); by_scalar(3); by_vector(2); by_scalar(4); targets(0)
             op("p", mm(T.C7[:, 16:32], T.E1[:], T.RS1[:], True, False), ["E1", "RS1"], ["@C7"])
             own_new[0]()
-            own_new[1]()
-            if not tail:
-                if d == 0:
-                    landed(frm, "b%d" % t, [xk + "b"])
-                    join(xk, [xk + "b", xk + "x"])
-                    landed(frm, "f%d" % t, ["FLAND%d" % t])
-                landed(frm, "y%d%d" % (t, d), ["YLAND%d" % m])
-                home_new = new_records(XC, xk, T.YLAND[:, 16 * m:16 * m + 16], "YLAND%d" % m, T.FLAND[:, 256 * t:256 * t + 256], "FLAND%d" % t,
-                                       "G1", 0, T.NS[:, 256:512], "NH", False)
-            for h, done in enumerate(((0, 1, 4, 5), (2, 3, 6, 7, 8, 9))):
-                tt(T.E2[:, 64 * h:64 * h + 64], T.FL[:, FH * h:FH * h + FH].indirect(T.LX2[:, 0:4]), T.DE[:, 64 * h:64 * h + 64], A.min,
-                   ["FL%d" % i for i in done] + ["LX2", "DE"], ["E2", "E2b"][h:h + 1])
-            lists_ = [lambda: op("p", mm(T.C7[:, 16:32], T.E2[:], T.RS1[:], False, True), ["E2", "E2b", "RS1"], ["@C7"]),
-                      lambda: op("p", mm(T.LB[:, 128:144], T.E1[:], T.RS1[:], True, False), ["E1", "RS1"], ["@LB"]),
-                      lambda: op("p", mm(T.LB[:, 128:144], T.E2[:], T.RSN[:], False, True), ["E2", "E2b", "RSN"], ["@LB"])]
-            for i in ((1, 2, 0) if end else (0, 1, 2)):
-                lists_[i]()
-            if not tail:
-                home_new[0]()
-                home_new[1]()
-                cp(T.R4[:], T.RA[:, 0:16].indirect(T.LX3[:]), ["RA", "LX3"], ["R4"])
-            gap(1)
             if end:
-                last_pairs(0)()
+                own_new[1]()
+            else:
+                if m == 0 or tail:
+                    landed(src, "b%d" % (t + tail), [ck + "b"])
+                    join(ck, [ck + "b", ck + "x"])
+                if d == 0:
+                    landed(frm, "f%d" % t, ["FLAND%d" % t])
+                landed(src, "y%d%d" % (t, d), ["YLAND%d" % m])
+                served = "SSND" if tail else "FLAND"
+                home_new = new_records(CP, ck, T.YLAND[:, 16 * m:16 * m + 16], "YLAND%d" % m, T[served][:, 256 * t:256 * t + 256], "%s%d" % (served, t), "G1", 256, "NH")
+            targets(1)
+            lists_ = [lambda: op("p", mm(T.C7[:, 16:32], T.E2[:], T.RS4[:], False, True), ["E2", "E2b", "RS4"], ["@C7"]),
+                      lambda: op("p", mm(T.G2[:, 0:16], T.E1[:], T.RS1[:, 0:16], True, False), ["E1", "RS1"], ["@G2"]),
+                      lambda: op("p", mm(T.G2[:, 0:16], T.E2[:], T.RSN[:], False, True), ["E2", "E2b", "RSN"], ["@G2"])]
+            for i in ((1, 2, 0) if end else (0, 1, 2) if t == NB - 1 else (0,)):
+                lists_[i]()
+            if not end:
+                home_new[0]()
+                own_new[1]()
+            if end:
+                pairs_so_far[1]()
+                pairs_so_far[2]()
 
             ls = T.LSND[:, 16 * m:16 * m + 16]
             lk = "LSND%d" % m
             cp(ls, T.C7[:, 16:32], ["@C7"], [lk])
-            if not tail:
-                send(to, "l%d%d" % (t, d), T.LLAND[:, 16 * m:16 * m + 16], ls, [lk])
+            if not end:
+                send(dst, "l%d%d" % (t, d), T.LLAND[:, 16 * m:16 * m + 16], ls, [lk])
             wb = T.WB[:, 16 * d:16 * d + 16]
 
-            def own_records():
-                cp(T.X[:, 0:WX].indirect(ls), T.NS[:, 0:256], [lk, "NS"], ["X"])
+            def own_records(k0=0, k1=16):
+                cp(T.X[:, 0:WX].indirect(ls[:, k0:k1]), T.NS[:, 16 * k0:16 * k1], [lk, "NS"], ["X"])
 
             def far_table():
-                tt(far[:, 0:WX].indirect(ls), T.UP[:], T.RC[:, 256 * t:256 * t + 256], A.add, ["UP", "RC%d" % t, lk], [fk])
+                tt(far[:, 0:WX].indirect(ls), T.QR[:], T.RC[:, 256 * t:256 * t + 256], A.add, ["QR", "RC%d" % t, lk], [fk])
 
             if end:
-                r_ = T.RSND[:, 32 * t:32 * t + 16]
-                act(r_, T.LB[:, 128:144], F.Relu, ["@LB"], ["RSH"], bias=1.0)
-                send(frm, "r%d" % t, T.RLAND[:, 32 * t:32 * t + 16], r_, ["RSH"])
+                r_ = T.RSND[:, 0:16]
+                act(r_, T.G2[:, 0:16], F.Relu, ["@G2"], ["RSH"], bias=1.0)
+                send(frm, "r%d" % t, T.RLAND[:, 0:16], r_, ["RSH"])
                 own_records()
                 dma("y", [(T.yx[:], T.X[:, 0:W])], ["X"], ["yx"])
                 cp(T.FO[:, 0:WX].indirect(ls), T.DIAG[:], [lk, "DIAG"], ["FO"])
                 dma("s", [(T.yb[:], T.FO[0:128:16, 0:W])], ["FO"], ["yb"])
                 break
-            ts(wb, T.C7[:, 16:32], DEAD, A.is_lt, ["@C7"], ["WB%d" % d], DEAD, A.mult)
-            op("p", mm(T.G0[:, 0:16], T.ONES[:], wb, True, True), ["ONES", "WB%d" % d], ["@G0"])
-            act(T.KJ[:], T.G0[:, 0:16], F.Copy, ["@G0"], ["KJ", "KP"], scale=1.0 / (32 * DEAD), accum_out=T.KP[:, 0:1])
+            act(wb, T.C7[:, 16:32], F.Sign, ["@C7"], ["WB%d" % d, "KP"], scale=-1.0, bias=DEAD, accum_out=T.KP[:, 0:1])
             kp = T.G0[:, 16:17]
-            op("p", [mm(kp, IH, T.ONES[:, 0:1], True, False), mm(kp, T.IDN[:], T.KP[:, 0:1], False, False)] +
-               [mm(kp, IH, T.CQ[:, c:c + 1], False, False) for c in (896, 256, 512)] + [mm(kp, T.IDF[:], T.KP[:, 0:1], False, True)],
-               ["IH", "ONES", "IDF", "IDN", "KP", "CQ1", "CQ2", "CQ4"], ["@G0"])
+            op("p", [mm(kp, IH, T.ONES[:, 0:1], True, False), mm(kp, T.KN[:, 0:128], T.KP[:, 0:1], False, False)] +
+               [mm(kp, IH, T.CQ[:, c:c + 1], False, False) for c in (896, 256, 512)] + [mm(kp, T.KN[:, 128:256], T.KP[:, 0:1], False, True)],
+               ["IH", "ONES", "KN0", "KN1", "KP", "CQ1", "CQ2", "CQ4"], ["@G0"])
             dn = (d + 1) % ND
+            home_new[1]()
 
             def kappa():
                 for ch in range(2):
                     act(T.ACOL[:, ch:ch + 1], kp, F.Identity, ["@G0", "ABASE%d" % dn], ["ACOL%d" % ch], scale=1024.0, bias=T.ABASE[:, 2 * dn + ch:2 * dn + ch + 1])
 
+            def copy_records():
+                landed(src, "l%d%d" % (t, d), ["LLAND%d" % m])
+                cp(CP[:, 0:WX].indirect(T.LLAND[:, 16 * m:16 * m + 16]), T.NS[:, 256:512], ["NH", "LLAND%d" % m], [ck])
+
             if tail:
-                own_records()
-                result(T.RES[:], "RES", d)
-                starters_send(t + 1)
-                kappa()
                 far_table()
+                result(t, d)
+                kappa()
                 dead_list(t + 1)
                 near_send(t)
-                dead_send(t + 1)
-                starters_on(t + 1)
-                records_send(t + 1)
+                own_records(0, 6)
                 gap(2)
+                copy_records()
+                dead_send(t + 1)
+                own_records(6, 10)
+                starters("SLAND", ck, t + 1)
+                own_records(10, 16)
                 continue
             far_table()
+            result(t, d)
+            if m == ND:
+                starters("SSND", "X", t)
             gap(2)
-            act(T.PG[:], far[:, 0:WX].indirect(yu), F.Copy, [fk, yk], ["PG"])
+            act(T.PG[:], far[:, 0:DUM].indirect(yu), F.Copy, [fk, yk], ["PG"])
             kappa()
+            if m == ND * NB - 2:
+                act(T.RSND[:, 16:32], T.RES[:], F.Relu, ["RES"], ["RSQ"], bias=1.0)
+                send(frm, "q", T.RLAND[:, 16:32], T.RSND[:, 16:32], ["RSQ"])
             to_list(lambda b: T.PG[:, b:256:16], ["PG"])
-            op("p", mm(T.LB[:, 0:128], T.R4[:], T.IDF[:], True, True), ["R4", "IDF"], ["@LB"])
-            gap(7)
+            copy_records()
             if m >= ND * NB - 3:
                 tab, i = (("TA", 0), ("TB", 1))[m - (ND * NB - 3)]
                 dma("y", [(T.HL[:, 512 * i:512 * i + 256], T[tab][15:128:16, 0:W]), (T.HL[:, 512 * i + 256:512 * i + 512], T[tab][14:128:16, 0:W])],
-                    [tab], ["HI%d" % i, "LO%d" % i])
-            landed(frm, "l%d%d" % (t, d), ["LLAND%d" % m])
-            cp(XC[:, 0:WX].indirect(T.LLAND[:, 16 * m:16 * m + 16]), T.NS[:, 256:512], ["NH", "LLAND%d" % m], [xk])
+                    [tab, "LLAND%d" % m], ["HI%d" % i, "LO%d" % i])
+            if m == 1:
+                need("y", deps(["LLAND1"], []))
+                fill_rows("TA", 0)
+                join("TA", ["TAd", "TAx"])
+            if m == 0:
+                dma("y", [(T.TA[:, 0:W], T.TB[:, 0:W])], ["TB", "LLAND0"], ["TAb", "TAc"])
             ts(T.PU[:], T.C7[:, 32:48], -1.0, A.add, ["@C7"], ["PU"])
+            gap(7)
             for h in (1, 0):
-                act(T.Z[:, 128 * h:128 * h + 128], XC[:, 0:WX].indirect(T.PU[:, 8 * h:8 * h + 8]), F.Copy, [xk, "PU"], ["Z%d" % h])
+                act(T.Z[:, 128 * h:128 * h + 128], XC[:, 0:W].indirect(T.PU[:, 8 * h:8 * h + 8]), F.Copy, [xk, "PU"], ["Z%d" % h])
             own_records()
     t = NB - 1
-    last_pairs(1)()
+    for f in last_pairs(1):
+        f()
     tt(T.PF[:, t:256:16], T.G4[:, 0:16], T.PF[:, t:256:16], A.add, ["@G4", "PF0"], ["PF0"])
     dma("y", [(T.ya[:], T.PF[:, 0:256])], ["PF0"], ["ya"])
     outs = [s for k in ("yx", "yb", "ya") for s in wr[k]]

from concourse.mybir import AluOpType, ActivationFunctionType

W = 4096
DEAD = 4096.0
DUM = 4112
WX = DUM + 1024
NB, ND = 3, 3
SC = 16384.0
SAME = 12 * SC
OFFR = 448.0
FH = 1032
MAGIC = 1.5 * 2 ** 23
NVS = ((74, 68), (72, 66))
ZSPLIT = ((2, 2), (3, 2))

_B = {}


def _sb(name, cols, dtype):
    _B[name] = ("sbuf", [128, cols], dtype)


for _n in ("X", "XC0", "XC1", "TA", "TB"):
    _sb(_n, WX, "bfloat16")
_sb("PAI", 256, "int32"); _sb("PBI", 256, "int32"); _sb("CT1", 256, "int32")
_sb("HL", 1024, "bfloat16"); _sb("I16", 128, "bfloat16"); _sb("PF", 512, "float32")
_sb("WI", 8, "int32"); _sb("WF", 8, "float32")
_sb("PI", 8, "int32"); _sb("PT", 8, "int32"); _sb("PC", 40, "float32"); _sb("SG", 16, "float32"); _sb("SGB", 8, "bfloat16"); _sb("WC", 8, "bfloat16")
_sb("CF", 264, "float32"); _sb("LANE", 256, "float32"); _sb("C8", 128, "float32"); _sb("CB1", 128, "float32")
_sb("SPK", 16, "float32"); _sb("RB", 16, "float32"); _sb("BW", 256, "bfloat16")
_sb("CG", 128, "float32"); _sb("WP", 256, "float16"); _sb("WN", 256, "float16")
_sb("OB", 16, "bfloat16"); _sb("KN", 256, "float32"); _sb("PEN", 128, "bfloat16"); _sb("EK", 128, "float32")
_sb("FBC", 16, "float32"); _sb("ZB", 128, "bfloat16"); _sb("PAIR", 128, "bfloat16"); _sb("RSX", 32, "float32"); _sb("LX6", 8, "uint16")
_sb("IBN", 384, "bfloat16")
_sb("CQ", 928, "bfloat16")
_sb("M1", 128, "float32"); _sb("RS1", 16, "float32"); _sb("RS4", 16, "bfloat16"); _sb("RSN", 16, "bfloat16"); _sb("RS", 256, "float32")
_sb("CR", 256, "bfloat16"); _sb("RC", 256 * NB, "bfloat16"); _sb("TH", 520, "float32"); _sb("SW", 144, "bfloat16")
_sb("ONES", 128, "bfloat16"); _sb("DIAG", 256, "float32"); _sb("SRB", 256, "bfloat16"); _sb("D16", 16, "float32")
_sb("LX0", 16, "uint16"); _sb("LX1", 8, "uint16"); _sb("LX2", 8, "uint16"); _sb("LN", 16, "uint16"); _sb("LX5", 16, "uint16")
_sb("LT", 64, "float32"); _sb("PW", 48, "float32")
_sb("SCOL", 4, "float32"); _sb("ABASE", 8, "float32"); _sb("ACOL", 4, "float32")
_sb("SSND", 256 * NB, "bfloat16"); _sb("SLAND", 256 * NB, "bfloat16")
_sb("DSND", 16 * NB, "bfloat16"); _sb("DLAND", 16 * NB, "bfloat16")
_sb("FLAND", 256 * NB, "bfloat16"); _sb("YSND", 16 * NB * ND, "uint16"); _sb("YLAND", 16 * NB * ND, "uint16")
_sb("LSND", 16 * NB * ND, "uint16"); _sb("LLAND", 16 * NB * ND, "uint16")
_sb("RSND", 32, "float32"); _sb("RLAND", 32, "float32"); _sb("NSND", 256 * (NB - 1), "bfloat16"); _sb("NLAND", 256 * (NB - 1), "bfloat16")
_sb("Z", 256, "bfloat16"); _sb("Z8", 2048, "bfloat16")
_sb("SQ", 256, "float32"); _sb("FI", 256, "int32"); _sb("CI", 256, "int32")
_sb("OFF", 256, "uint16"); _sb("CFL", 256, "float16"); _sb("EQ", 256, "bfloat16")
_sb("DF", 4096, "bfloat16"); _sb("AB", 4096, "bfloat16")
_sb("R", 256, "float32"); _sb("RI", 16, "int32"); _sb("RA", 16, "int32"); _sb("RQ", 16, "int32"); _sb("E1", 128, "float32"); _sb("DE", 128, "float32")
_sb("R4", 128, "float32"); _sb("E2", 128, "float16"); _sb("NS", 512, "bfloat16"); _sb("FO", WX, "float32")
_sb("UP", 256, "bfloat16"); _sb("QR", 256, "bfloat16"); _sb("GX", 512, "bfloat16")
_sb("FL", 2 * FH, "float32"); _sb("JK", 1280, "bfloat16"); _sb("PG", 256, "bfloat16"); _sb("PU", 16, "uint16"); _sb("E3", 256, "bfloat16")
_sb("WB", 16 * ND, "bfloat16"); _sb("RES", 16, "float32")
_sb("KP", 8, "float32")
for _n in ["G0", "G1", "G2", "G3", "G4", "K6", "C7", "LB"]:
    _B[_n] = ("psum", [128, 512], "float32")
SCRATCH = _B

_MSG = ["q", "s0"]
for _t in range(NB):
    _MSG += ["f%d" % _t, "b%d" % _t, "e%d" % _t, "r%d" % _t]
    for _d in range(ND - 1 if _t == NB - 1 else ND):
        _MSG += ["y%d%d" % (_t, _d), "l%d%d" % (_t, _d)]
SEMAPHORES = ["cv", "cs", "cp", "cg"] + ["rx" + m for m in _MSG] + ["tx" + m for m in _MSG] + ["dm%d" % i for i in range(20)]


def rank_program(g, core, T, topo):
    rank = T.rank_of(core)
    if rank is None:
        return
    A = AluOpType
    F = ActivationFunctionType
    n_ranks = len(T.cores)
    nxt, prv = (rank + 1) % n_ranks, (rank - 1) % n_ranks
    Q = {"v": g.vector, "s": g.scalar, "p": g.tensor, "g": g, "y": g.sync}
    cnt = {"v": 0, "s": 0, "p": 0, "g": 0}
    waited = {q: {} for q in Q}
    wr = {}
    rd = {}
    bank = {}
    nd = [0]
    last = {}

    def need(q, toks):
        for sem in sorted(toks):
            if waited[q].get(sem, 0) < toks[sem]:
                Q[q].wait_ge(T.sem[sem], toks[sem])
                waited[q][sem] = toks[sem]

    def deps(reads, writes, own=None):
        toks = {}
        for k in reads + writes:
            if k[0] == "@":
                ms_ = [{s: v for s, v in bank.get(k, {}).items() if s != own}]
            else:
                ms_ = [wr.get(k, {})] + ([rd.get(k, {})] if k in writes else [])
            for m in ms_:
                for s, v in m.items():
                    toks[s] = max(toks.get(s, 0), v)
        return toks

    def note(reads, writes, sem, val):
        for k in reads + writes:
            if k[0] == "@":
                bank.setdefault(k, {})[sem] = val
            elif k in writes:
                wr[k] = {sem: val}
                rd[k] = {}
            else:
                m = rd.setdefault(k, {})
                m[sem] = max(m.get(sem, 0), val)
        last[sem] = max(last.get(sem, 0), val)

    def op(q, fns, reads, writes):
        need(q, deps(reads, writes, "c" + q))
        for fn in (fns if isinstance(fns, list) else [fns]):
            cnt[q] += 1
            fn().then_inc(T.sem["c" + q], 1)
        note(reads, writes, "c" + q, cnt[q])

    def dma(q, pieces, reads, writes):
        need(q, deps(reads, writes))
        sem = "dm%d" % nd[0]
        nd[0] += 1
        for out, in_ in pieces:
            Q[q].dma_start(out, in_).then_inc(T.sem[sem], 16)
        note(reads, writes, sem, 16 * len(pieces))

    def engines(frm, to, msg):
        return topo.engines(T.cores[frm], T.cores[to])

    def send(to, msg, out, in_, reads):
        need("g", deps(reads, []))
        rid, pid, _se = topo.addr(T.cores[to])
        es = engines(rank, to, msg)
        g.remote_dma(out, in_, T.sem["rx" + msg], T.sem["tx" + msg], pid, rid, sum(1 << e for e in es))
        note(reads, [], "tx" + msg, len(es))

    def landed(frm, msg, keys):
        note([], keys, "rx" + msg, len(engines(frm, rank, msg)))

    def join(key, parts):
        wr[key] = deps(parts, [])

    def ts(out, in0, s1, o0, r, w, s2=None, o1=None):
        if o1 is None:
            op("v", lambda: g.vector.tensor_scalar(out, in0, s1, None, o0), r, w)
        else:
            op("v", lambda: g.vector.tensor_scalar(out, in0, s1, s2, o0, o1), r, w)

    def tt(out, a, b, o, r, w):
        op("v", lambda: g.vector.tensor_tensor(out, a, b, o), r, w)

    def cp(out, a, r, w):
        op("v", lambda: g.vector.tensor_copy(out, a), r, w)

    def scan(out, d0, d1, o0, o1, r, w):
        op("v", lambda: g.vector.tensor_tensor_scan(out, d0, d1, 0.0, o0, o1), r, w)

    def ms(ap, c, w):
        op("v", lambda: g.vector.memset(ap, c), [], w)

    def act(out, in_, f, r, w, **kw):
        op("s", lambda: g.scalar.activation(out, in_, f, **kw), r, w)

    def iota(key, pattern, base, mult):
        op("g", lambda: g.iota(T[key][:], pattern, base, mult, allow_small_or_imprecise_dtypes=True), [], [key])

    def zeros(ap, keys):
        op("g", lambda: g.iota(ap, [[0, ap.shape[1]]], 0, 0, allow_small_or_imprecise_dtypes=True), [], keys)

    def mm(out, lhsT, rhs, start, stop):
        return lambda: g.tensor.matmul(out, lhsT, rhs, start, stop)

    IB, IN, IH = T.IBN[:, 0:128], T.IBN[:, 128:256], T.IBN[:, 256:384]

    def to_list(cols, keys):
        op("p", [mm(T.C7[:, 32:48], T.SW[:, 16 - b:144 - b], cols(b), b == 0, b == 15) for b in range(16)], ["SW"] + keys, ["@C7"])

    def starters(name, win, t):
        for ll in range(2):
            cp(T[name][:, 256 * t + ll:256 * t + 256:2], T[win][:, W // 2 * ll + t:W // 2 * (ll + 1):16], [win], ["%s%d_%d" % (name, t, ll)])
        join("%s%d" % (name, t), ["%s%d_%d" % (name, t, ll) for ll in range(2)])

    def starters_on(t):
        send(nxt if t % 2 == 0 else prv, "f%d" % t, T.FLAND[:, 256 * t:256 * t + 256], T.SLAND[:, 256 * t:256 * t + 256], ["SLAND%d" % t])

    def dead_list(t):
        near, nk = (T.TA, "TA") if t % 2 == 0 else (T.TB, "TB")
        to_list(lambda b: near[:, 2048 * (b % 2) + 16 * (b // 2) + t:2048 * (b % 2) + 2048:128], [nk])

    def dead_send(t):
        to = nxt if t % 2 == 0 else prv
        e = T.DSND[:, 16 * t:16 * t + 16]
        ts(e, T.C7[:, 32:48], 1.0, A.min, ["@C7"], ["DSND%d" % t], DEAD, A.mult)
        send(to, "e%d" % t, T.DLAND[:, 16 * t:16 * t + 16], e, ["DSND%d" % t])
        landed(prv if t % 2 == 0 else nxt, "e%d" % t, ["DLAND%d" % t])

    def records_send(t):
        xc = T.XC0 if t % 2 == 0 else T.XC1
        send(nxt if t % 2 == 0 else prv, "b%d" % t, xc[:, 0:W], T.X[:, 0:W], ["X"])

    def result(t, d):
        src, bk, o = (T.G2[:, 0:16], "@G2", A.max) if t == NB - 1 else (T.C7[:, 16:32], "@C7", A.min)
        if d == 0:
            cp(T.RES[:], src, [bk], ["RES"])
        else:
            tt(T.RES[:], src, T.RES[:], o, [bk, "RES"], ["RES"])

    def near_send(t):
        tab, tk = (T.TA, "TA") if t % 2 == 0 else (T.TB, "TB")
        bits = T.NSND[:, 256 * t:256 * t + 256]
        ts(T.LN[:], T.RES[:], DEAD, A.min, ["RES"], ["LN"])
        act(bits, tab[:, 0:DUM].indirect(T.LN[:]), F.Copy, [tk, "LN"], ["NSND%d" % t])
        send(prv if t % 2 == 0 else nxt, "r%d" % t, T.NLAND[:, 256 * t:256 * t + 256], bits, ["NSND%d" % t])

    def near_rows(t):
        landed(nxt if t % 2 == 0 else prv, "r%d" % t, ["NLAND%d" % t])
        op("p", [mm(T.LB[:, 128 * ll:128 * ll + 128], T.SRB[:, 128 * h:128 * h + 128], T.NLAND[:, 256 * t + ll:256 * t + 256:2], ll + h == 0, ll + h == 2)
                 for ll in range(2) for h in range(2)], ["SRB0", "SRB1", "NLAND%d" % t], ["@LB"])

    def near_add(t):
        near, nk = (T.TA, "TA") if t % 2 == 0 else (T.TB, "TB")
        tt(near[:, t:W:16], T.LB[:, 0:256], near[:, t:W:16], A.add, ["@LB", nk], [nk])

    def last_pairs(i):
        t = NB - 1
        msg, c, tiles = (("q", 16, ("R4", "CG")), ("r%d" % t, 0, ("E1", "DE")))[i]
        landed(nxt if t % 2 == 0 else prv, msg, ["L" + msg])
        spread = [lambda o=o, e=e: tt(T[e][:], T.RLAND[:, c:c + 16].indirect(T.LX5[:, 8 * o:8 * o + 8]), T.CB1[:], A.mult, ["L" + msg, "LX5_%d" % o, "CB1"], [e])
                  for o, e in enumerate(tiles)]
        return spread + [lambda: [op("p", mm(T.G4[:, 8 * o:8 * o + 8], T[e][:], T.D16[:, 0:8], i + o == 0, i + o == 2), [e, "D16"], ["@G4"])
                                  for o, e in enumerate(tiles)]]

    dma("y", [(T.PAI[:], T.pa[:])], [], ["PAI"])
    dma("s", [(T.WI[:, 0:1], T.wt[:])], [], ["WI"])
    dma("y", [(T.X[:, 0:W], T.x[:])], [], ["Xd"])
    dma("y", [(T.PBI[:], T.pb[:])], [], ["PBI"])
    op("g", lambda: g.iota(T.PI[:, 0:1], [[0, 1]], 0, 1), [], ["PI"])
    iota("CF", [[1, 264]], 0, 0)
    iota("C8", [[1, 16], [0, 8]], 0, 0)
    iota("CB1", [[0, 8], [1, 8], [0, 2]], 0, 0)
    iota("LANE", [[1, 128], [128, 2]], 0, 0)
    ms(T.X[:, W:DUM], 0.0, ["Xx"])
    join("X", ["Xd", "Xx"])
    for c, (sh, mask) in enumerate(((4, 7), (0, 15), (0, 7), (3, 15), (0, 1), (4, 1), (0, 127))):
        ts(T.PT[:, c:c + 1], T.PI[:, 0:1], sh, A.arith_shift_right, ["PI"], ["PT%d" % c], mask, A.bitwise_and)
    ms(T.ZB[:], 0.0, ["ZB"])
    ms(T.CQ[:, 0:256], -0.5, ["CQ0"])
    cp(T.PC[:, 0:7], T.PT[:, 0:7], ["PT%d" % c for c in range(7)], ["PC"])
    ms(T.CQ[:, 512:640], -2 * MAGIC, ["CQ2"])
    ms(T.CQ[:, 640:896], 4096.0, ["CQ3"])
    ms(T.CQ[:, 896:912], -2.0 ** -12, ["CQ896"])
    PGRP, PLOW, PL7, P8, P1, OCOL, PP = [T.PC[:, c:c + 1] for c in range(7)]
    ts(T.LT[:, 0:12], T.CF[:, 0:12], PLOW, A.not_equal, ["CF", "PC"], ["LT"], 2.0, A.mult)
    ts(T.PC[:, 8:12], T.CF[:, 12:16], PLOW, A.is_equal, ["CF", "PC"], ["PCI"])
    I12, I13, I14, I15 = [T.PC[:, c:c + 1] for c in range(8, 12)]
    ts(T.PC[:, 17:18], PLOW, 12.0, A.is_lt, ["PC"], ["PC17"], SC, A.mult)
    ms(T.ONES[:], 1.0, ["ONES"])
    ts(T.PC[:, 29:30], I12, 128.0, A.mult, ["PCI"], ["PC29"])
    ts(T.SG[:, 0:12], T.LT[:, 0:12], -1.0, A.add, ["LT"], ["SG"])
    ms(T.CQ[:, 256:512], 2 * MAGIC, ["CQ1"])
    ts(T.TB[:, 0:1], I13, T.PC[:, 29:30], A.add, ["PCI", "PC17", "PC29"], ["TBb"], T.PC[:, 17:18], A.add)
    for r in range(9):
        n = 1 << r
        act(T.TB[:, n:2 * n], T.TB[:, 0:n], F.Copy, ["TBb", "SG"], ["TBb"], scale=T.SG[:, r:r + 1])
    for r in range(3):
        act(T.TB[:, 512 << r:(512 << r) + 512], T.TB[:, 0:512], F.Copy, ["TBb", "SG"], ["TB_%d" % (1 << r)], scale=T.SG[:, 9 + r:10 + r])

    def bits_block(b, src, r0, r1):
        ts(T.TB[:, 512 * b:512 * b + 512], T.TB[:, 512 * src:512 * src + 512], T.SGB[:, r0:r0 + 1], A.mult, ["TB_1" if src else "TBb", "SGB"], ["TB_%d" % b],
           T.SGB[:, r1:r1 + 1], A.mult)

    ts(T.DSND[:, 0:16], T.PAI[:, 0:256:16], 0.0, A.is_ge, ["PAI"], ["DSND0"], DEAD, A.mult)
    send(nxt, "e0", T.DLAND[:, 0:16], T.DSND[:, 0:16], ["DSND0"])
    landed(prv, "e0", ["DRAW"])
    ts(T.PC[:, 12:13], PGRP, 2.0, A.mult, ["PC"], ["PC12"])
    ts(T.PC[:, 13:14], PGRP, 2.0, A.mult, ["PC"], ["PC13"], 1.0, A.add)
    for ch in range(2):
        ts(T.SCOL[:, ch:ch + 1], PL7, 32.0, A.mult, ["PC"], ["SCOL%d" % ch], 256.0 * ch + 16.0, A.add)
    ts(IH, T.CF[:, 0:128], PP, A.is_equal, ["CF", "PC"], ["IH"], 0.5, A.mult)
    tt(T.SCOL[:, 2:4], T.SCOL[:, 0:2], T.SCOL[:, 0:2], A.mult, ["SCOL0", "SCOL1"], ["SCOL2"])
    ts(IN, T.CF[:, 0:128], PP, A.is_equal, ["CF", "PC"], ["IN"], -1.0, A.mult)
    ts(T.ACOL[:, 0:2], T.SCOL[:, 2:4], -1.0, A.mult, ["SCOL2"], ["ACOL0", "ACOL1"], 262144.0 - 12.0, A.add)
    ts(T.WF[:, 3:4], T.WI[:, 0:1], 2048.0, A.is_gt, ["WI"], ["WF3"], -4096.0, A.mult)
    iota("CG", [[2, 8], [0, 8], [1, 2]], 0, 0)
    iota("PAIR", [[1, 64], [0, 2]], 0, 0)
    iota("FBC", [[0, 2], [4096, 8]], 4081 * 4096, 0)
    for key, ap, pattern, base in (("LT0", T.LT[:, 16:24], [[512, 4], [128, 2]], 127), ("LT1", T.LT[:, 24:32:2], [[-511, 4]], 897), ("LT2", T.LT[:, 25:32:2], [[0, 4]], 256)):
        op("g", lambda: g.iota(ap, pattern, base, 0, allow_small_or_imprecise_dtypes=True), [], [key])
    ts(T.WF[:, 0:1], T.WI[:, 0:1], T.WF[:, 3:4], A.add, ["WI", "WF3"], ["WF0"], 1.0 / 4096, A.mult)
    ts(T.WF[:, 1:2], T.WI[:, 0:1], T.WF[:, 3:4], A.add, ["WI", "WF3"], ["WF1"], -1.0 / 4096, A.mult)
    for ll in range(2):
        for wm, c in (("WP", 0), ("WN", 1)):
            ts(T[wm][:, 128 * ll:128 * ll + 128], T.C8[:], T.PC[:, 12 + ll:13 + ll], A.is_equal, ["C8", "PC12", "PC13", "WF%d" % c], ["%s%d" % (wm, ll)], T.WF[:, c:c + 1], A.mult)
    ts(IB, T.CF[:, 0:128], PP, A.is_equal, ["CF", "PC"], ["IB"])
    for i in range(2):
        ts(T.OB[:, 8 * i:8 * i + 8], T.CF[:, 0:8], PGRP, A.is_equal, ["CF", "PC"], ["OB%d" % i], 4096.0 * (1 - 2 * i), A.mult)

    def table_rows(pin, pk, i):
        hi, lo = T.HL[:, 512 * i:512 * i + 256], T.HL[:, 512 * i + 256:512 * i + 512]
        return [lambda: ts(T.CT1[:], pin[:], 4, A.arith_shift_right, [pk], ["CT1"]),
                lambda: ts(hi, T.CT1[:], 0.0, A.max, ["CT1"], ["HI%d" % i]),
                lambda: ts(T.PF[:, 0:256], hi, -16.0, A.mult, ["HI%d" % i], ["PF0"], 1.0, A.add),
                lambda: tt(lo, T.PF[:, 0:256], pin[:], A.add, ["PF0", pk], ["LO%d" % i])]

    def fill_rows(tab, i):
        dma("y", [(T[tab][15:128:16, 0:W], T.HL[:, 512 * i:512 * i + 256]), (T[tab][14:128:16, 0:W], T.HL[:, 512 * i + 256:512 * i + 512])],
            ["HI%d" % i, "LO%d" % i], [tab + "b", tab + "c", tab + "d"])

    def spare_columns(tab):
        act(T[tab][:, W:DUM], T.XC1[:, W:DUM], F.Identity, ["XC1x", "PC16"], [tab + "x"], bias=T.PC[:, 16:17])

    def starter_rows(t):
        act(T.RC[:, 256 * t:256 * t + 256], T.LANE[:], F.Identity, ["LANE", "PC27", "PC20"], ["RC%d" % t], scale=T.PC[:, 27:28], bias=T.PC[:, 20 + t:21 + t])

    first = [lambda: ts(T.PC[:, 14:15], PGRP, 16.0, A.mult, ["PC"], ["PC14"], 16.0, A.add),
             lambda: ts(T.PC[:, 15:16], I15, 16.0, A.mult, ["PCI"], ["PC15"], I14, A.add),
             lambda: ts(T.SW[:], T.CF[:, 0:144], T.PC[:, 14:15], A.is_equal, ["CF", "PC14", "PC15"], ["SW"], T.PC[:, 15:16], A.mult)] + [
             lambda d=d: ts(T.ABASE[:, 2 * d:2 * d + 2], T.SCOL[:, 2:4], -1.0, A.mult, ["SCOL2"], ["ABASE%d" % d], 262144.0 - 12.0 + 32.0 * 97 * d, A.add)
             for d in range(ND)]
    rows_b = table_rows(T.PBI, "PBI", 1)
    ts(T.LT[:, 48:56], T.CF[:, 0:16:2], P1, A.add, ["CF", "PC"], ["LT6"], 16.0, A.mult)
    ts(T.WF[:, 2:3], PLOW, P1, A.subtract, ["PC"], ["WF2"], 0.5, A.mult)
    ts(T.RS1[:], T.CF[:, 0:16], P8, A.is_equal, ["CF", "PC"], ["RS1"])
    ts(T.LX1[:], T.CF[:, 0:16:2], P1, A.add, ["CF", "PC"], ["LX1"])
    ts(T.PC[:, 28:29], I14, 127.0, A.mult, ["PCI"], ["PC28"], 1.0, A.add)
    ts(T.LX6[:], T.LT[:, 48:56], 15.0, A.add, ["LT6"], ["LX6"])
    cp(T.SGB[:, 0:3], T.SG[:, 9:12], ["SG"], ["SGB"])
    ts(T.LT[:, 40:48], T.LT[:, 24:32], P1, A.mult, ["LT1", "LT2", "PC"], ["LT5"])
    ts(T.R4[:], T.CG[:], P8, A.is_equal, ["CG", "PC"], ["R4"])
    starters("SSND", "X", 0)
    send(nxt, "s0", T.SLAND[:, 0:256], T.SSND[:, 0:256], ["SSND0"])
    landed(prv, "s0", ["SLAND0"])
    ts(T.PC[:, 33:34], I12, -255.0 * 128, A.mult, ["PCI"], ["PC33"])
    ts(T.PC[:, 18:19], I12, -1.0, A.mult, ["PCI"], ["PC18"])
    ts(T.PC[:, 19:20], I12, 255.0, A.mult, ["PCI", "PC28"], ["PC19"], T.PC[:, 28:29], A.add)
    ts(T.PC[:, 16:17], I14, OFFR, A.mult, ["PCI", "PC29"], ["PC16"], T.PC[:, 29:30], A.add)
    ts(T.PC[:, 27:28], I15, T.PC[:, 29:30], A.add, ["PCI", "PC29"], ["PC27"])
    ts(T.PC[:, 31:32], OCOL, T.PC[:, 28:29], A.mult, ["PC", "PC28"], ["PC31"])
    rows_b[0]()
    ts(T.PC[:, 24:25], P1, 2 * MAGIC, A.mult, ["PC"], ["PC24"], -2 * MAGIC, A.add)
    ts(T.PC[:, 26:27], PP, P1, A.subtract, ["PC"], ["PC26"], 0.5, A.mult)
    ts(T.PC[:, 23:24], P1, 22.5, A.mult, ["PC"], ["PC23"], 0.5, A.add)
    ts(T.PC[:, 20:23], T.CF[:, 1:4], I14, A.mult, ["CF", "PCI", "PC33"], ["PC20"], T.PC[:, 33:34], A.add)
    rows_b[1]()
    ts(T.PC[:, 25:26], P1, -89.0, A.mult, ["PC", "PC24"], ["PC25"], T.PC[:, 24:25], A.add)
    ts(T.PAIR[:], T.PAIR[:], T.PC[:, 26:27], A.is_equal, ["PAIR", "PC26", "PC23"], ["PAIR"], T.PC[:, 23:24], A.mult)
    ts(T.M1[:], T.CB1[:], PL7, A.is_equal, ["CB1", "PC"], ["M1"])
    bits_block(3, 0, 0, 1)
    rows_b[2]()
    bits_block(5, 0, 0, 2)
    ts(T.WC[:, 0:8], T.CF[:, 0:8], PL7, A.is_equal, ["CF", "PC"], ["WC"])
    for o in range(2):
        ts(T.LX0[:, 8 * o:8 * o + 8], T.ZB[:, 0:8], T.WF[:, 2:3], A.add, ["ZB", "WF2"], ["LX0_%d" % o], 8.0 * o, A.add)
    ts(T.KP[:, 4:6], T.CF[:, 0:129:128], PP, A.add, ["CF", "PC"], ["KP4"], -256.0, A.add)
    rows_b[3]()
    bits_block(6, 0, 1, 2)
    bits_block(7, 1, 1, 2)
    join("TBc", ["TB_%d" % b for b in range(1, 8)])
    second = [lambda: tt(T.KP[:, 6:8], T.KP[:, 4:6], T.KP[:, 4:6], A.mult, ["KP4"], ["KP6"]),
              lambda: ts(T.TH[:, 255:512:256], T.KP[:, 4:6], -SAME, A.add, ["KP4", "TH"], ["THa"], SC, A.mult),
              lambda: tt(T.LT[:, 32:40], T.LT[:, 40:48], T.LT[:, 16:24], A.add, ["LT5", "LT0"], ["LT4"]),
              lambda: (ts(T.TH[:, 127:513:385], T.KP[:, 6:8], SAME, A.add, ["KP6", "TH"], ["THb"], -SC, A.mult), join("THS", ["TH", "THa", "THb"])),
              lambda: cp(T.LX2[:], T.LT[:, 32:40], ["LT4"], ["LX2"])]
    third = [lambda: ts(T.PW[:, 0:12], T.CF[:, 0:12], PLOW, A.add, ["CF", "PC"], ["PW0"], 11.0, A.is_equal),
             lambda: ts(T.PW[:, 34:35], I13, -0.5, A.mult, ["PCI"], ["PW34"]),
             lambda: ts(T.PW[:, 12:24], T.PW[:, 0:12], -2.0, A.mult, ["PW0"], ["PW12"], 2.0, A.add),
             lambda: scan(T.PW[:, 36:48], T.PW[:, 12:24], T.PW[:, 0:12], A.mult, A.add, ["PW0", "PW12"], ["PW36"]),
             lambda: ts(T.PW[:, 35:36], T.PW[:, 47:48], -1.0 / (2 * SC), A.mult, ["PW36", "PW34"], ["PW35"], T.PW[:, 34:35], A.add)] + [
             lambda ll=ll: ts(T.BW[:, 128 * ll:128 * ll + 128], T.C8[:], T.PC[:, 12 + ll:13 + ll], A.is_equal, ["C8", "PC12", "PC13", "PW35"], ["BW%d" % ll], T.PW[:, 35:36], A.mult)
             for ll in range(2)]
    need("y", deps([], ["SSND0"]))
    fill_rows("TB", 1)
    zeros(T.RS[:], ["RS"])
    op("g", lambda: g.iota(T.RS[:, 0:256:16], [[0, 2], [4096, 8]], 4081 * 4096, 0, allow_small_or_imprecise_dtypes=True), [], ["RS"])
    zeros(T.XC1[:, W:DUM], ["XC1x"])
    zeros(T.XC0[:, W:DUM], ["XC0x"])

    def late_fills():
        need("g", deps(["LO1", "TB_7"], []))
        iota("SPK", [[0, 8], [1, 2]], DUM // 4, 2)
        zeros(T.FL[:, 1024:FH], ["FL4", "FL5"])
        records_send(0)
        zeros(T.TH[:], ["TH"])
        zeros(T.FL[:, FH + 768:2 * FH], ["FL6", "FL7", "FL8"])
        for i in range(2):
            op("g", lambda: g.affine_select(T.KN[:, 128 * i:128 * i + 128], T.C8[:], [[0, 128]], A.is_gt, (2 * i - 1) / 64.0, 0, 0), ["C8"], ["KN%d" % i])
        op("g", lambda: g.affine_select(T.PEN[:], T.ZB[:], [[-1, 128]], A.not_equal, 2.0 ** 25, 0, 1), ["ZB"], ["PEN"])

    first_dead = [lambda o=o: tt(T.E3[:, 128 * o:128 * o + 128], T.DLAND[:, 0:16].indirect(T.LX0[:, 8 * o:8 * o + 8]), T.R4[:], A.mult,
                                 ["DRAW", "LX0_%d" % o, "R4"], ["E3_%d" % o]) for o in range(2)]

    def scalar_constants():
        for i in range(2):
            act(T.RSX[:, 16 * i:16 * i + 16], T.RS1[:], F.Copy, ["RS1"], ["RSX%d" % i], scale=(2 * i - 1) / 4096.0)
        act(T.CQ[:, 912:928], T.RS1[:], F.Identity, ["RS1", "PC25"], ["CQ912"], scale=0.0, bias=T.PC[:, 25:26])
        join("RSX", ["RSX0", "RSX1"])
        join("CQ4", ["CQ896", "CQ912"])
        act(T.CR[:], T.LANE[:], F.Identity, ["LANE", "PC18", "PC19"], ["CR"], scale=T.PC[:, 18:19], bias=T.PC[:, 19:20])
        spare_columns("TB")
        join("TB", ["TBd", "TBx"])
        starter_rows(0)
        act(T.RS4[:], T.RS1[:, 0:16], F.Copy, ["RS1"], ["RS4"], scale=4.0)

    def late_constants():
        for f in table_rows(T.PAI, "PAI", 0):
            yield f
        yield lambda: ts(T.PW[:, 32:33], PLOW, 4.0, A.is_ge, ["PC"], ["PW32"], -1.0 / (32 * SC), A.mult)
        yield lambda: ts(T.PW[:, 33:34], PLOW, 4.0, A.is_lt, ["PC"], ["PW33"], -1.0 / (2 * SC), A.mult)
        yield lambda: ts(T.PW[:, 24:26], T.CF[:, 17:256:238], I13, A.mult, ["CF", "PCI"], ["PW24"], 0.5, A.mult)
        yield lambda: ts(T.PW[:, 26:28], T.CF[:, 1:3], -1.0, A.mult, ["CF", "PC14"], ["PW26"], T.PC[:, 14:15], A.add)
        for i in range(2):
            yield lambda i=i: ts(T.PW[:, 28 + i:29 + i], T.PW[:, 47:48], T.PW[:, 32 + i:33 + i], A.mult, ["PW36", "PW32", "PW33", "PW24"], ["PW%d" % (28 + i)],
                                 T.PW[:, 25 - i:26 - i], A.add)
        for i in range(2):
            yield lambda i=i: ts(T.SRB[:, 128 * i:128 * i + 128], T.CF[:, 0:128], T.PW[:, 26 + i:27 + i], A.is_equal, ["CF", "PW26", "PW%d" % (28 + i)], ["SRB%d" % i],
                                 T.PW[:, 28 + i:29 + i], A.mult)
        yield lambda: ts(T.CB1[:], T.C8[:], T.PC[:, 12:13], A.subtract, ["C8", "PC12"], ["CB1"], P1, A.is_equal)
        yield lambda: ts(T.LT[:, 0:2], T.CF[:, 0:2], PL7, A.add, ["CF", "PC"], ["LT"], PL7, A.add)
        yield lambda: ts(T.D16[:, 0:8], T.CF[:, 0:8], T.WF[:, 2:3], A.is_equal, ["CF", "WF2"], ["D16"])
        for o in range(2):
            yield lambda o=o: ts(T.LX5[:, 8 * o:8 * o + 8], T.ZB[:, 0:8], T.LT[:, o:o + 1], A.add, ["ZB", "LT"], ["LX5_%d" % o])
        for i in range(2):
            yield lambda i=i: (op("p", [mm(T.G1[:, 0:256], a, T.HL[:, 512 * i + 256 * h:512 * i + 256 * h + 256], h == 0, h == 1) for h, a in enumerate((T.I16[:], IB))],
                                  ["I16", "IB", "HI%d" % i, "LO%d" % i], ["@G1"]),
                               act(T.PF[:, 256 * i:256 * i + 256], T.G1[:, 0:256], F.Copy, ["@G1"], ["PF%d" % i], bias=-1.0))
        yield lambda: dma("y", [(T.FO[0:128:16, 0:W], T.PF[:, 256:512])], ["PF1"], ["FO"])
        yield lambda: act(T.I16[:], IB, F.Copy, ["IB"], ["I16"], scale=16.0)
        yield lambda: act(T.RSN[:], T.RS1[:, 0:16], F.Copy, ["RS1"], ["RSN"], scale=-SC)
        yield lambda: act(T.DIAG[:], T.LANE[:], F.Copy, ["LANE"], ["DIAG"], scale=16.0, bias=NB - 1.0)

    late = list(late_constants())
    gaps = {(0, 0): first_dead, (0, 3): second[0:3], (0, 4): second[3:5],
            (0, 2): first[0:2] + third[0:2] + first[3:5] + third[2:3] + first[2:3] + first[5:6] + third[3:4] + late[0:1] + third[4:5],
            (0, 7): third[5:7], (1, 0): late[4:8], (1, 3): late[1:2], (1, 2): late[2:3] + late[8:10] + late[12:14] + late[3:4],
            (2, 3): late[10:12], (4, 3): late[14:17], (5, 1): late[20:23], (7, 1): late[17:18], (8, 1): late[18:20]}

    for t in range(NB):
        frm, to = (prv, nxt) if t % 2 == 0 else (nxt, prv)
        far, fk = (T.TB, "TB") if t % 2 == 0 else (T.TA, "TA")
        XC, xk = (T.XC0, "XC0") if t % 2 == 0 else (T.XC1, "XC1")
        s_, sk = T.SLAND[:, 256 * t:256 * t + 256], "SLAND%d" % t
        for d in range(ND):
            m = t * ND + d
            tail = d == ND - 1
            end = m == NB * ND - 1
            NV = NVS[d > 0]
            z, zk = (s_, sk) if d == 0 else (T.Z[:], "Z")
            dst, src = (frm, to) if tail else (to, frm)
            CP, ck = (T.XC0, "XC0") if (t + tail) % 2 == 0 else (T.XC1, "XC1")

            def gap(i):
                for f in gaps.get((m, i), []):
                    f()

            hs = [(T.C7[:, 64:128], "@C7"), (T.G4[:, 0:64], "@G4")]
            zks = [zk, zk] if d == 0 else ["Z0", "Z1"]
            for h in (1, 0):
                op("p", mm(hs[h][0], IH, T.ONES[:, 0:64], True, False), ["IH", "ONES"], [hs[h][1]])
            for h in (1, 0):
                zs = [z[:, 128 * h + ll:128 * h + 128:2] for ll in range(2)]
                if d == 0 and t > 0:
                    zs = [XC[:, 2048 * ll + 1024 * h + t:2048 * ll + 1024 * h + 1024:16] for ll in range(2)]
                op("p", [mm(hs[h][0], T.WN[:, 128 * ll:128 * ll + 128], zs[ll], False, False) for ll in range(2)] +
                   [mm(hs[h][0], IH, T.CQ[:, c:c + 64], False, False) for c in (256, 512)] +
                   [mm(hs[h][0], T.WP[:, 128 * ll:128 * ll + 128], zs[ll], False, ll == 1) for ll in range(2)],
                   ["WN0", "WN1", "WP0", "WP1", "CQ1", "CQ2", xk if d == 0 and t > 0 else zks[h]], [hs[h][1]])
            Z8 = ["Z8_%d" % cl for cl in range(8)]

            def part(ap, ch, h):
                return ap[:, 128 * ch + 64 * (h % 2):128 * ch + 64 * min(h, 1) + 64]

            def keys(name, ch, h):
                return ["%s%d%d" % (name, ch, i) for i in ((0, 1) if h == 2 else (h,))]

            def floors(ch, h):
                ts(part(T.FI, ch, h), part(T.SQ, ch, h), T.ACOL[:, ch:ch + 1], A.add, keys("SQ", ch, h) + ["ACOL%d" % ch], keys("FI", ch, h), 1.0 / 32, A.mult)

            def places(ch, h):
                ts(part(T.CI, ch, h), part(T.FI, ch, h), 4095, A.bitwise_and, keys("FI", ch, h), keys("CI", ch, h))

            def lists(ch, h):
                cp(part(T.OFF, ch, h), part(T.CI, ch, h), keys("CI", ch, h), keys("OFF", ch, h))

            for h in (1, 0):
                for ch in range(2):
                    act(part(T.SQ, ch, h), hs[h][0], F.Square, [hs[h][1], "SCOL%d" % ch], ["SQ%d%d" % (ch, h)], bias=T.SCOL[:, ch:ch + 1], scale=4096.0)

            def z8(cl):
                cp(T.Z8[:, cl:16 * NV[0]:8], z[:, 0:2 * NV[0]], zks, ["Z8_%d" % cl])

            ns, ng = ZSPLIT[m > 0]
            if tail and not end:
                records_send(t + 1)
            for cl in range(ns):
                act(T.Z8[:, cl:16 * NV[0]:8], z[:, 0:2 * NV[0]], F.Copy, zks, ["Z8_%d" % cl])
            for cl in range(8 - ng, 8):
                op("g", lambda: g.affine_select(T.Z8[:, cl:16 * NV[0]:8], z[:, 0:2 * NV[0]], [[0, 2 * NV[0]]], A.is_gt, 0.0, 1, 0), zks, ["Z8_%d" % cl])
            if d == 0:
                starters_on(t)
            if m == 0:
                late_fills()
            zv = list(range(ns, 8 - ng))
            held = [zv.pop(), zv.pop()] if d == 0 and t > 0 else []
            for cl in zv:
                z8(cl)
            floors(0, 1); floors(1, 1); floors(0, 0); [z8(cl) for cl in held[0:1]]; places(0, 1); floors(1, 0); [z8(cl) for cl in held[1:2]]; places(0, 0); lists(0, 1)
            places(1, 1); places(1, 0); lists(0, 0); lists(1, 1); lists(1, 0)

            def offs(ch, c0, c1):
                return ["OFF%d%d" % (ch, h) for h in range(c0 // 64, (c1 - 1) // 64 + 1)]

            def v_gather(ch, c0, c1):
                a, b = 2048 * ch + 16 * c0, 2048 * ch + 16 * c1
                tt(T.DF[:, a:b], T.X[:, 0:W].indirect(T.OFF[:, 128 * ch + c0:128 * ch + c1]), T.Z8[:, 16 * c0:16 * c1], A.subtract,
                   ["X"] + offs(ch, c0, c1) + Z8, ["DF%d_%d" % (ch, c0)])

            def v_half(ch, odd=None):
                a, b, st = 2048 * ch + (odd or 0), 2048 * ch + 16 * NV[ch], (1 if odd is None else 2)
                ts(T.AB[:, a:b:st], T.DF[:, a:b:st], 0.0, A.max, ["DF%d_0" % ch], ["AB%d_0_%s" % (ch, odd)], 2.0, A.mult)

            def s_gather(ch, c0, c1):
                a, b = 2048 * ch + 16 * c0, 2048 * ch + 16 * c1
                act(T.DF[:, a:b], T.X[:, 0:W].indirect(T.OFF[:, 128 * ch + c0:128 * ch + c1]), F.Copy, ["X"] + offs(ch, c0, c1), ["DF%d_%d" % (ch, c0)])

            def p_diff(ch, c0, c1, bk):
                a, b = 2048 * ch + 16 * c0, 2048 * ch + 16 * c1
                op("p", mm(T[bk][:, 0:b - a], IB, T.DF[:, a:b], False, True), ["IB", "DF%d_%d" % (ch, NV[ch])], ["@" + bk])

            def s_abs(ch, c0, c1, bk, odd=None):
                a, b, o, st = 2048 * ch + 16 * c0, 2048 * ch + 16 * c1, (odd or 0), (1 if odd is None else 2)
                act(T.AB[:, a + o:b:st], T[bk][:, o:b - a:st], F.Abs, ["@" + bk], ["AB%d_%d_%s" % (ch, c0, odd)])

            def dsum(src, ch, c0, c1, ob, keys, parts=range(16), close=False):
                op("p", [mm(T.K6[c0:c1, 2 * b + ch:256:32], src[:, 2048 * ch + 16 * c0 + b:2048 * ch + 16 * c1:16], T.OB[:, 8 * ob:8 * ob + 8], False, close and b == 15)
                         for b in parts], keys + ["OB%d" % ob], ["@K6"])

            def bar(ch):
                if d > 0:
                    op("p", mm(T.K6[:, ch:256:2], T.EQ[:, 128 * ch:128 * ch + 128], T.PEN[:], False, False), ["EQ", "PEN"], ["@K6"])

            def number(ch):
                op("p", mm(T.K6[:, ch:256:2], T.CFL[:, 128 * ch:128 * ch + 128], IB, False, False), ["CFL", "IB"], ["@K6"])

            sc = [(ch, c0, min(c0 + 32, 128)) for ch in range(2) for c0 in range(NV[ch], 128, 32)]
            sc = [c + ("G%d" % i,) for i, c in enumerate(sc)]
            op("p", mm(T.K6[:, 0:256], IH, T.CQ[:, 640:896], True, False), ["IH", "CQ3"], ["@K6"])
            for ch, c0, c1, bk in sc:
                op("p", [mm(T[bk][:, cl:16 * (c1 - c0):8], IN, z[:, 2 * c0:2 * c1], cl == 0, False) for cl in range(8)], ["IN", zks[1]], ["@" + bk])
            if d == 0 and t > 0:
                near_rows(t - 1)
            if d > 0:
                op("p", [mm(T.LB[:, 128 * ch:128 * ch + 128], T.BW[:, 128 * ll:128 * ll + 128], T.QR[:, ll:256:2], ch + ll == 0, ch + ll == 2)
                         for ch in range(2) for ll in range(2)], ["BW0", "BW1", "QR"], ["@LB"])
            for ch in range(2):
                v_gather(ch, 0, NV[ch])
            s_gather(0, NV[0], 128)
            s_gather(1, NV[1], 128)
            ts(T.CFL[:], T.OFF[:], -2048.0, A.add, ["OFF00", "OFF01", "OFF10", "OFF11"], ["CFL"])
            for i in range(2):
                p_diff(*sc[i])
            dsum(T.DF, 0, 0, NV[0], 1, ["DF0_0"])
            p_diff(*sc[2])
            p_diff(*sc[3])
            dsum(T.DF, 1, 0, NV[1], 1, ["DF1_0"])
            for i in range(2):
                number(i)
            v_half(0)
            for c in sc[0:3]:
                s_abs(*c)
            dsum(T.AB, 0, 0, 128, 0, ["AB0_0_None", "AB0_%d_None" % sc[0][1], "AB0_%d_None" % sc[1][1]])
            if d > 0:
                tt(T.EQ[:], T.LB[:, 0:256], T.CFL[:], A.is_equal, ["@LB", "CFL"], ["EQ"])
            for odd in range(2):
                v_half(1, odd)
                s_abs(*sc[3], odd)
            gap(0)
            bar(0)
            bar(1)
            for odd in range(2):
                dsum(T.AB, 1, 0, 128, 0, ["AB1_0_%d" % odd, "AB1_%d_None" % sc[2][1], "AB1_%d_%d" % (sc[3][1], odd)], range(odd, 16, 2), odd == 1)
            dead = [(T.DLAND[:, 16 * t:16 * t + 16], "DLAND%d" % t)][0:min(t, 1)] + [(T.WB[:, 16 * i:16 * i + 16], "WB%d" % i) for i in range(d)]
            op("p", [mm(T.C7[:, 0:16], IB, T.CQ[:, 0:16], True, False), mm(T.C7[:, 0:16], IH, T.CQ[:, 896:912], False, False), mm(T.C7[:, 0:16], IH, T.CQ[:, 640:656], False, False)] +
               [mm(T.C7[:, 0:16], IB, a, False, False) for a, k in dead + [(T.ONES[:, 0:16], "ONES")] * d],
               ["IB", "IH", "CQ0", "CQ3", "CQ896", "ONES"] + [k for a, k in dead], ["@C7"])
            if t == 0:
                op("p", [mm(T.C7[:, o:16:2], T.E3[:, 128 * o:128 * o + 128], T.WC[:, 0:8], False, False) for o in range(2)], ["E3_0", "E3_1", "WC"], ["@C7"])
            gap(1)
            if m == 0:
                scalar_constants()
            if m == 1:
                spare_columns("TA")
            if m in (3, 4):
                starter_rows(m - 2)
            for h in range(2):
                scan(T.R[:, 128 * h:128 * h + 128], T.RS[:, 128 * h:128 * h + 128], T.K6[:, 128 * h:128 * h + 128], A.max, A.min, ["RS", "@K6"], ["R%d" % h])
            for h in range(2):
                tt(T.EK[:, 64 * h:64 * h + 64], T.R[:, 128 * h:128 * h + 128].indirect(T.LX6[:, 0:4]), T.M1[:, 0:64], A.mult, ["R%d" % h, "LX6", "M1"], ["EK%d" % h])
            op("p", [mm(T.C7[:, 0:16], T.EK[:], T.RSX[:, 0:16], False, False)] +
               [mm(T.C7[:, 0:16], a, T.CQ[:, c:c + 16], False, False) for a, c in ((IH, 256), (T.PAIR[:], 912))] +
               [mm(T.C7[:, 0:16], T.EK[:], T.RSX[:, 16:32], False, True)], ["EK0", "EK1", "RSX", "IH", "PAIR", "CQ1", "CQ4"], ["@C7"])
            cp(T.RI[:], T.R[:, 15:256:16], ["R0", "R1"], ["RI"])
            if d == 0 and t > 0:
                near_add(t - 1)
            gap(3)
            if end:
                pairs_so_far = last_pairs(0)
                pairs_so_far[0]()
            ts(T.RA[:], T.RI[:], 4095, A.bitwise_and, ["RI"], ["RA"])
            ts(T.RQ[:], T.RI[:], 2, A.arith_shift_right, ["RI"], ["RQ"], 1023, A.bitwise_and)
            gap(4)
            if not tail:
                tt(T.RS[:, 0:256:16], T.RA[:], T.FBC[:], A.add, ["RA", "FBC"], ["RS"])
            tt(T.RB[:], T.SPK[:], T.RQ[:], A.subtract, ["SPK", "RQ"], ["RB"])
            yu, yk = T.YSND[:, 16 * m:16 * m + 16], "YSND%d" % m
            ts(yu, T.C7[:, 0:16], 4096.0, A.mult, ["@C7"], [yk], DEAD, A.min)
            if not end:
                send(dst, "y%d%d" % (t, d), T.YLAND[:, 16 * m:16 * m + 16], yu, [yk])
            act(T.UP[:], far[:, 0:DUM].indirect(yu), F.Copy, [fk, yk, "PC31"], ["UP"], scale=T.PC[:, 31:32])
            tt(T.QR[:], far[:, 0:DUM].indirect(yu), T.CR[:], A.mult, [fk, yk, "CR"], ["QR"])
            tt(T.DE[:], T.RB[:, 0:16].indirect(T.LX1[:]), T.M1[:], A.mult, ["RB", "LX1", "M1"], ["DE"])
            tt(T.E1[:], T.RA[:, 0:16].indirect(T.LX1[:]), T.M1[:], A.mult, ["RA", "LX1", "M1"], ["E1"])

            def unit(gr, ll, bk, c):
                p0, k = 32 * (gr // 2), 16 + 16 * (gr % 2)
                q = "UP" if gr % 2 else "QR"
                op("p", mm(T[bk][:, c:c + 128 + 128 * ll], T[q][p0:p0 + k, ll:256:2], T.QR[p0:p0 + k, 0:256:2 - ll], True, True), ["QR", q], ["@" + bk])

            def by_vector(q):
                n = 0
                for gr, ll in [(2 * q, 0), (2 * q + 1, 0), (2 * q + 1, 1)][0:3 if q < 3 else 2]:
                    unit(gr, ll, "G%d" % q, n)
                    n += 128 + 128 * ll
                f0 = FH * (q // 2) + 512 * (q % 2)
                scan(T.FL[:, f0:f0 + n], T["G%d" % q][:, 0:n], T.TH[:, 0:n], A.max, A.add, ["@G%d" % q, "THS"], ["FL%d" % q])

            def by_scalar(i):
                bk, c = ("G4", "K6", "LB", "G4", "K6")[i], (FH * (i // 2) + 1024 + i % 2 if i < 4 else FH + 1023)
                unit((0, 2, 4, 6, 7)[i], 1, bk, 0)
                act(T.JK[:, 256 * i:256 * i + 256], T[bk][:, 0:256], F.Relu, ["@" + bk, "THS"], ["JK%d" % i, "FL%d" % (4 + i)],
                    bias=T.TH[:, 512 - i // 4:513 - i // 4], accum_out=T.FL[:, c:c + 1])

            def targets(h):
                tt(T.E2[:, 64 * h:64 * h + 64], T.FL[:, FH * h:FH * h + FH].indirect(T.LX2[:, 0:4]), T.DE[:, 64 * h:64 * h + 64], A.min,
                   ["FL%d" % i for i in ((0, 1, 4, 5), (2, 3, 6, 7, 8))[h]] + ["LX2", "DE"], ["E2", "E2b"][h:h + 1])

            def new_records(win, wk, ys, yk_, st, stk, bk, c, key):
                gx, out = T.GX[:, c:c + 256], T.NS[:, c:c + 256]
                act(gx, win[:, 0:DUM].indirect(ys), F.Copy, [wk, yk_], ["G" + key])
                return (lambda: op("p", [mm(T[bk][:, 0:256], IH, a, i == 0, i == 3) for i, a in enumerate((st, T.CQ[:, 0:256], gx, T.CQ[:, 256:512]))],
                                   ["IH", stk, "CQ0", "G" + key, "CQ1"], ["@" + bk]),
                        lambda: act(out, T[bk][:, 0:256], F.Copy, ["@" + bk], [key], bias=-MAGIC))

            own_new = new_records(T.X, "X", yu, yk, s_, sk, "LB", 0, "NS")
            by_scalar(0); by_vector(3); by_vector(0); by_scalar(1); by_vector(1); by_scalar(2); by_scalar(3); by_vector(2); by_scalar(4); targets(0)
            op("p", mm(T.C7[:, 16:32], T.E1[:], T.RS1[:], True, False), ["E1", "RS1"], ["@C7"])
            own_new[0]()
            if end:
                own_new[1]()
            else:
                if m == 0 or tail:
                    landed(src, "b%d" % (t + tail), [ck + "b"])
                    join(ck, [ck + "b", ck + "x"])
                if d == 0:
                    landed(frm, "f%d" % t, ["FLAND%d" % t])
                landed(src, "y%d%d" % (t, d), ["YLAND%d" % m])
                served = "SSND" if tail else "FLAND"
                home_new = new_records(CP, ck, T.YLAND[:, 16 * m:16 * m + 16], "YLAND%d" % m, T[served][:, 256 * t:256 * t + 256], "%s%d" % (served, t), "G1", 256, "NH")
            targets(1)
            lists_ = [lambda: op("p", mm(T.C7[:, 16:32], T.E2[:], T.RS4[:], False, True), ["E2", "E2b", "RS4"], ["@C7"]),
                      lambda: op("p", mm(T.G2[:, 0:16], T.E1[:], T.RS1[:, 0:16], True, False), ["E1", "RS1"], ["@G2"]),
                      lambda: op("p", mm(T.G2[:, 0:16], T.E2[:], T.RSN[:], False, True), ["E2", "E2b", "RSN"], ["@G2"])]
            for i in ((1, 2, 0) if end else (0, 1, 2) if t == NB - 1 else (0,)):
                lists_[i]()
            if not end:
                home_new[0]()
                own_new[1]()
            if end:
                pairs_so_far[1]()
                pairs_so_far[2]()

            ls = T.LSND[:, 16 * m:16 * m + 16]
            lk = "LSND%d" % m
            cp(ls, T.C7[:, 16:32], ["@C7"], [lk])
            if not end:
                send(dst, "l%d%d" % (t, d), T.LLAND[:, 16 * m:16 * m + 16], ls, [lk])
            wb = T.WB[:, 16 * d:16 * d + 16]

            def own_records(k0=0, k1=16):
                cp(T.X[:, 0:WX].indirect(ls[:, k0:k1]), T.NS[:, 16 * k0:16 * k1], [lk, "NS"], ["X"])

            def far_table():
                tt(far[:, 0:WX].indirect(ls), T.QR[:], T.RC[:, 256 * t:256 * t + 256], A.add, ["QR", "RC%d" % t, lk], [fk])

            if end:
                r_ = T.RSND[:, 0:16]
                act(r_, T.G2[:, 0:16], F.Relu, ["@G2"], ["RSH"], bias=1.0)
                send(frm, "r%d" % t, T.RLAND[:, 0:16], r_, ["RSH"])
                own_records()
                dma("y", [(T.yx[:], T.X[:, 0:W])], ["X"], ["yx"])
                cp(T.FO[:, 0:WX].indirect(ls), T.DIAG[:], [lk, "DIAG"], ["FO"])
                dma("s", [(T.yb[:], T.FO[0:128:16, 0:W])], ["FO"], ["yb"])
                break
            act(wb, T.C7[:, 16:32], F.Sign, ["@C7"], ["WB%d" % d, "KP"], scale=-1.0, bias=DEAD, accum_out=T.KP[:, 0:1])
            kp = T.G0[:, 16:17]
            op("p", [mm(kp, IH, T.ONES[:, 0:1], True, False), mm(kp, T.KN[:, 0:128], T.KP[:, 0:1], False, False)] +
               [mm(kp, IH, T.CQ[:, c:c + 1], False, False) for c in (896, 256, 512)] + [mm(kp, T.KN[:, 128:256], T.KP[:, 0:1], False, True)],
               ["IH", "ONES", "KN0", "KN1", "KP", "CQ1", "CQ2", "CQ4"], ["@G0"])
            dn = (d + 1) % ND
            home_new[1]()

            def kappa():
                for ch in range(2):
                    act(T.ACOL[:, ch:ch + 1], kp, F.Identity, ["@G0", "ABASE%d" % dn], ["ACOL%d" % ch], scale=1024.0, bias=T.ABASE[:, 2 * dn + ch:2 * dn + ch + 1])

            def copy_records():
                landed(src, "l%d%d" % (t, d), ["LLAND%d" % m])
                cp(CP[:, 0:WX].indirect(T.LLAND[:, 16 * m:16 * m + 16]), T.NS[:, 256:512], ["NH", "LLAND%d" % m], [ck])

            if tail:
                far_table()
                result(t, d)
                kappa()
                dead_list(t + 1)
                near_send(t)
                own_records(0, 6)
                gap(2)
                copy_records()
                dead_send(t + 1)
                own_records(6, 10)
                starters("SLAND", ck, t + 1)
                own_records(10, 16)
                continue
            far_table()
            result(t, d)
            if m == ND:
                starters("SSND", "X", t)
            gap(2)
            act(T.PG[:], far[:, 0:DUM].indirect(yu), F.Copy, [fk, yk], ["PG"])
            kappa()
            if m == ND * NB - 2:
                act(T.RSND[:, 16:32], T.RES[:], F.Relu, ["RES"], ["RSQ"], bias=1.0)
                send(frm, "q", T.RLAND[:, 16:32], T.RSND[:, 16:32], ["RSQ"])
            to_list(lambda b: T.PG[:, b:256:16], ["PG"])
            copy_records()
            if m >= ND * NB - 3:
                tab, i = (("TA", 0), ("TB", 1))[m - (ND * NB - 3)]
                dma("y", [(T.HL[:, 512 * i:512 * i + 256], T[tab][15:128:16, 0:W]), (T.HL[:, 512 * i + 256:512 * i + 512], T[tab][14:128:16, 0:W])],
                    [tab, "LLAND%d" % m], ["HI%d" % i, "LO%d" % i])
            if m == 1:
                need("y", deps(["LLAND1"], []))
                fill_rows("TA", 0)
                join("TA", ["TAd", "TAx"])
            if m == 0:
                dma("y", [(T.TA[:, 0:W], T.TB[:, 0:W])], ["TB", "LLAND0"], ["TAb", "TAc"])
            ts(T.PU[:], T.C7[:, 32:48], -1.0, A.add, ["@C7"], ["PU"])
            gap(7)
            for h in (1, 0):
                act(T.Z[:, 128 * h:128 * h + 128], XC[:, 0:W].indirect(T.PU[:, 8 * h:8 * h + 8]), F.Copy, [xk, "PU"], ["Z%d" % h])
            own_records()
    t = NB - 1
    for f in last_pairs(1):
        f()
    tt(T.PF[:, t:256:16], T.G4[:, 0:16], T.PF[:, t:256:16], A.add, ["@G4", "PF0"], ["PF0"])
    dma("y", [(T.ya[:], T.PF[:, 0:256])], ["PF0"], ["ya"])
    outs = [s for k in ("yx", "yb", "ya") for s in wr[k]]
    for sem in [s for s in sorted(last) if s not in outs] + outs:
        if max(waited[q].get(sem, 0) for q in Q) < last[sem]:
            need("g", {sem: last[sem]})
